import numpy as np, ml_dtypes
CORES = [6,15,38,47]
N = 4
BF = ml_dtypes.bfloat16
W, M, TV, S, B = 4096, 256, 5, 1, 8
QN = W // 16
def parts(rng):
    X = rng.integers(0, 256, (N, 8, 16, W)); z = rng.integers(0, 256, (N, 8, 16, M))
    o = np.argsort(rng.random((8, W)), axis=1); A, H, Q = o[:, :8], o[:, 8:40], o[:, 40:40 + QN]; gi = np.arange(8)[None, :, None, None]
    e = rng.integers(0, W, (N, 8, 16, W)); l = rng.integers(0, W, (N, 8, 16, M))
    e = np.where(rng.random(e.shape) < 0.2, H[gi, rng.integers(0, 32, e.shape)], e)
    l[:, :, 0] = H[gi[..., 0], rng.integers(0, 32, (N, 8, M))]
    for q in range(N):
        for g in range(8):
            lanes = rng.permutation(16)[:8]; sub = e[q, g]; sub[lanes[:, None], Q[g][None, :]] = A[g][:, None]
    barred = rng.random((N, 8, M)) < 0.06; barred[:, :, 5] = True
    lb = Q[gi, rng.integers(0, QN, (N, 8, 16, M))]; lb[:, :, 0] = A[gi[..., 0], rng.integers(0, 8, (N, 8, M))]
    keep = (rng.random((N, 8, 1, M)) < 0.5) & (np.arange(16)[None, None, :, None] == rng.integers(1, 16, (N, 8, 1, M)))
    l = np.where(barred[:, :, None, :] & ~keep, lb, l)
    return X, e, l, z, rng.integers(800, 1501, (N, 8))
def pack(X, e, l, z, th):
    return {"xt": np.ascontiguousarray(X.reshape(N, 128, W)).astype(np.float32).astype(BF), "ex": np.ascontiguousarray(e.reshape(N, 128, W)).astype(np.int32),
            "l0": np.ascontiguousarray(l.reshape(N, 128, M)).astype(np.int32), "z0": np.ascontiguousarray(z.reshape(N, 128, M)).astype(np.float32).astype(BF),
            "th": np.ascontiguousarray(th.reshape(N, 8, 1)).astype(np.int32)}
def setup_inputs(rng):
    return pack(*parts(rng))
def setup_inputs_spread(rng):
    def skew(top, rows, n):
        return np.minimum((top * rng.random((N, 8, rows, n)) ** np.exp2(rng.integers(-3, 4, (N, 8, 1, n)))).astype(np.int64), top - 1)
    return pack(skew(256, 16, W), skew(W, 16, W), skew(W, 16, M), skew(256, 16, M), rng.integers(0, 4081, (N, 8)))
def setup_inputs_ends(rng):
    ends = np.array([0, W - 1])
    def bits(n):
        u = rng.random((N, 8, 1, n)); return np.where(u < 0.3, 0, np.where(u < 0.6, 255, 255 * rng.integers(0, 2, (N, 8, 16, n))))
    X = bits(W); z = bits(M); sw = (np.arange(N)[:, None, None] + np.arange(8)[None, :, None]) % 2
    X[..., 0] = 255 * sw; X[..., W - 1] = 255 * (1 - sw); z[..., M - 1] = 0; z[..., 0] = 255
    u = rng.random((N, 8, 1, W)); u[..., 0] *= 0.7; u[..., W - 1] *= 0.7
    e = np.where(u < 0.25, 0, np.where(u < 0.5, W - 1, np.where(u < 0.7, ends[rng.integers(0, 2, (N, 8, 16, W))], rng.integers(0, W, (N, 8, 16, W)))))
    l = np.where(rng.random((N, 8, 16, M)) < 0.7, ends[rng.integers(0, 2, (N, 8, 16, M))], rng.integers(0, W, (N, 8, 16, M)))
    l[:, :, [2, 7, 15], M - 1] = W - 1; l[:, :, 0, M - 1] = 0
    th = np.stack([rng.permutation(np.array([0, 4080] * 4)) for q in range(N)]); th[N - 1] = np.array([0, 4080] * 4)
    return pack(X, e, l, z, th)
def setup_inputs_corners(rng):
    X, e, l, z, th = parts(rng); v = [int(a) for a in rng.permutation(8)]; i = np.arange(M); c = np.arange(W)
    e[:, v[0]] = np.where(rng.random((N, 16, W)) < 0.5, c, e[:, v[0]])
    l[:, v[0]] = np.where(rng.random((N, 16, M)) < 0.4, l[:, v[0], :1], l[:, v[0]]); l[:, v[0], :, ::8] = l[:, v[0], :1, ::8].copy()
    th[:, v[0]] = 4080
    o = rng.permutation(W); A, full, free = o[:8], o[8:8 + W // 2], o[8 + W // 2:]
    for g in (v[1], v[2]):
        e[:, g] = rng.choice(free, (N, 16, W))
        for q in range(N):
            lanes = rng.permutation(16)[:8]; sub = e[q, g]; sub[lanes[:, None], full[None, :]] = A[:, None]
        l[:, g] = rng.choice(full, (N, 16, M)); l[:, g, 0] = rng.choice(A, (N, M))
    l[:, v[2], 1 + i % 15, i] = rng.choice(free, (N, M)); j = i[1::2]
    l[:, v[2], 1 + (j + 7) % 15, j] = rng.choice(free, (N, len(j)))
    th[:, v[1]] = rng.choice(np.array([1, 4079]), N)
    l[:, v[3], 1:] = rng.integers(0, W, (N, 1, M)); th[:, v[3]] = 0
    X[:, v[4]] = X[:, v[4], :, :4].copy()[:, :, rng.integers(0, 4, W)]
    tips = np.array([0, 1, W - 2, W - 1]); e[:, v[5]] = rng.choice(tips, (N, 16, W)); l[:, v[5]] = rng.choice(tips, (N, 16, M))
    l[:, v[6], 1:] = rng.choice(o[-3:], (N, 15, M)); th[:, v[6]] = 4080
    e[:, v[7]] = (c[None, :] + 1 + np.arange(16)[:, None]) % W; l[:, v[7]] = rng.integers(W - 20, W, (N, 16, M))
    return pack(X, e, l, z, th)
def setup_inputs_crowd(rng):
    X, e, l, z, th = parts(rng); X = np.minimum(np.maximum(X, 1), 254)
    sizes = rng.permutation(np.array([1, 2, 3, 16, 64, 256, W, W]))
    for g in range(8):
        pool = rng.permutation(W)[:int(sizes[g])]
        e[:, g] = rng.choice(pool, (N, 16, W)); l[:, g, 1:] = rng.choice(pool, (N, 15, M))
    th[::2] = 4080; th[1::2] = 0
    return pack(X, e, l, z, th)
def setup_inputs_lull(rng):
    X = np.zeros((N, 8, 16, W), np.int64); e = np.zeros((N, 8, 16, W), np.int64); l = rng.integers(0, W, (N, 8, 16, M)); z = rng.integers(107, 149, (N, 8, 16, M))
    for g in range(8):
        o = rng.permutation(W); bar, grey = int(o[0]), int(o[1]); dl, dh, bl, bh = [o[2 + j::4] for j in range(4)]
        dark = np.concatenate([dl, dh]); bright = np.concatenate([bl, bh]); low = np.concatenate([dl, bl]); high = np.concatenate([dh, bh, o[:2]])
        x = X[:, g]; s = e[:, g]; m = l[:, g]; v = z[:, g]
        x[:, :, dark] = rng.integers(60, 101, (N, 16, len(dark))); x[:, :, bright] = rng.integers(155, 196, (N, 16, len(bright)))
        x[:, :, bar] = 255 * rng.integers(0, 2, (N, 16)); x[:, :, grey] = rng.integers(107, 149, (N, 16))
        s[:, :, low] = rng.choice(dark, (N, 16, len(low))); s[:, :, high] = rng.choice(bright, (N, 16, len(high)))
        s[:, 1, high] = rng.choice(bl, (N, len(high))); s[:, 2, high] = rng.choice(bh, (N, len(high)))
        np.put_along_axis(s, rng.integers(3, 15, (N, 1, W)), bar, 1)
        m[:, 0] = bar; m[:, 1] = np.stack([rng.permutation(low)[:M] for q in range(N)]); m[:, 2] = rng.choice(high[:-2], (N, M))
        m[:, 3:, 3::16] = grey; m[:, 4:, 11::16] = grey
        v[:, :, 3::16] = x[:, :, grey][:, :, None]; v[:, :, 11::16] = x[:, :, grey][:, :, None]
    th = np.zeros((N, 8), np.int64); th[::2] = rng.integers(1310, 1361, th[::2].shape); th[::2, rng.permutation(8)[:3]] = 4080
    return pack(X, e, l, z, th)
def check_inputs(d):
    bad = []
    for k, lo, hi in (("xt", 0, 255), ("ex", 0, W - 1), ("l0", 0, W - 1), ("z0", 0, 255), ("th", 0, 4080)):
        v = np.asarray(d[k]).astype(np.float64)
        if not (np.min(v) >= lo and np.max(v) <= hi): bad.append("range of " + k)
        elif not np.all(v == np.floor(v)): bad.append("whole numbers of " + k)
    return bad
def pick(w, ix):
    return np.take_along_axis(w, ix.reshape(8, 1, -1), 2).reshape((8, 16) + ix.shape[1:])
def at(l, k):
    return np.take_along_axis(l, k[:, None, :], 1)[:, 0]
def reference(xt, ex, l0, z0, th):
    X = xt.astype(np.float32).astype(np.int32).reshape(N, 8, 16, W); R = ex.astype(np.int64).reshape(N, 8, 16, W)
    L = l0.astype(np.int64).reshape(N, 8, 16, M); Z = z0.astype(np.float32).astype(np.int32).reshape(N, 8, 16, M); limit = th.astype(np.int64).reshape(N, 8, 1)
    count = [0] * N; kk = np.arange(16)[None, :, None]; gg = np.arange(8)[:, None] + np.zeros((8, M), np.int64); ii = np.arange(M)[None, :] + np.zeros((8, M), np.int64)
    for t in range(TV):
        for h in range(N):
            q = (h + S * t) % N; x = X[q]; l = L[h].copy(); z = Z[h].copy()
            d = np.add.reduce(np.abs(pick(x, l) - z[:, :, None, :]), axis=1).astype(np.int64)
            conf = np.any(pick(R[q], l) == l[:, None, :1, :], axis=1)
            key = np.where(conf, 2 ** 16 + kk, 16 * d + kk); key[:, 0] = 2 ** 20
            o = np.argsort(key, axis=1, kind="stable"); ra = o[:, 0]; rb = o[:, 1]
            la = at(l, ra); lb = at(l, rb); e = []
            Ea = pick(R[q], la); Eb = pick(R[q], lb)
            for E in (Ea, Eb):
                de = np.add.reduce(np.abs(pick(x, E) - z[:, :, None, :]), axis=1)
                e.append(at(E, np.argmin(de, axis=1)))
            far = 16 * d + 15 - kk; far[:, 0] = -1
            np.put_along_axis(far, ra[:, None, :], -1, 1); np.put_along_axis(far, rb[:, None, :], -1, 1)
            new = l.copy()
            for v in e:
                p = np.argmax(far, axis=1); np.put_along_axis(far, p[:, None, :], -1, 1); np.put_along_axis(new, p[:, None, :], v[:, None, :], 1)
            xa = pick(x, e[0]); xb = pick(x, e[1])
            acc = np.add.reduce(np.abs(xa - xb), axis=1) < limit[q] + (count[h] & 63)
            new[:, 1:] = np.where(acc[:, None, :], Eb[:, 1:], new[:, 1:])
            first = np.full((8, W), M); np.minimum.at(first, (gg[acc], la[acc]), ii[acc])
            win = acc & (first[gg, la] == ii)
            R[q][gg[win], (ii[win] + t) & 15, la[win]] = l[:, 0][win]
            L[h] = new; Z[h] = (xa + xb) >> 1; count[h] = int(np.count_nonzero(acc))
    home = [(q - S * (TV - 1)) % N for q in range(N)]
    return {"yl": L[home].reshape(N, 128, M).astype(np.float32), "yz": Z[home].reshape(N, 128, M).astype(np.float32).astype(BF),
            "yr": np.add.reduce(R.reshape(N, 128, B, W // B), axis=2).astype(np.float32)}

@@ -1,0 +1,698 @@
+from concourse.bass import DstId, RemoteDMATransfer
+from concourse.mybir import AluOpType as A, ActivationFunctionType as F, AxisListType
+
+N, TV, W, M = 4, 5, 4096, 256
+CYC = 0.83
+SCRATCH = {
+    "X": ("sbuf", [128, 4096], "bfloat16"), "R": ("sbuf", [128, 4352], "float32"),
+    "LI": ("sbuf", [128, 256], "int32"), "THI": ("sbuf", [128, 8], "int32"), "THB": ("sbuf", [128, 8], "int32"), "TH": ("sbuf", [128, 8], "float32"),
+    "THN": ("sbuf", [128, 8], "float32"), "NF": ("sbuf", [128, 4], "float32"), "NI": ("sbuf", [128, 4], "int32"), "NM": ("sbuf", [128, 4], "float32"),
+    "ONEB": ("sbuf", [128, 256], "bfloat16"), "IDB": ("sbuf", [128, 128], "bfloat16"), "NIDB": ("sbuf", [128, 128], "bfloat16"),
+    "ID32": ("sbuf", [128, 128], "float32"), "ID16": ("sbuf", [128, 128], "float16"), "NID16": ("sbuf", [128, 128], "float16"), "BOF": ("sbuf", [128, 128], "bfloat16"),
+    "BO1": ("sbuf", [128, 8], "bfloat16"), "BOK": ("sbuf", [128, 16], "bfloat16"), "BOC": ("sbuf", [128, 8], "bfloat16"),
+    "BOD": ("sbuf", [128, 16], "bfloat16"), "BON": ("sbuf", [128, 16], "bfloat16"), "ONEB3": ("sbuf", [128, 16, 16], "bfloat16"),
+    "PB2": ("sbuf", [128, 16, 16], "bfloat16"), "PM2": ("sbuf", [128, 32, 16], "float16"), "IOT2": ("sbuf", [128, 16, 16], "float32"),
+    "PERM": ("sbuf", [128, 128], "bfloat16"), "PM": ("sbuf", [128, 256], "float16"), "SELB": ("sbuf", [128, 768], "bfloat16"),
+    "SEL": ("sbuf", [128, 768], "float16"), "RXB": ("sbuf", [128, 128], "bfloat16"), "RX": ("sbuf", [128, 128], "float16"),
+    "CKL": ("sbuf", [128, 128], "float16"), "CK1": ("sbuf", [128, 256], "float16"), "CK2": ("sbuf", [128, 32, 16], "float16"), "SELF": ("sbuf", [128, 256], "float16"),
+    "IOT": ("sbuf", [128, 128], "float32"), "CF": ("sbuf", [128, 128], "float32"), "PI": ("sbuf", [128, 4], "int32"),
+    "KC": ("sbuf", [128, 4], "float32"), "SC": ("sbuf", [128, 4], "float32"), "IJ": ("sbuf", [128, 640], "int32"), "MT": ("sbuf", [128, 640], "bfloat16"),
+    "CI": ("sbuf", [128, 16], "float32"), "CI2": ("sbuf", [128, 16], "float32"), "IOS": ("sbuf", [128, 8, 16], "float32"),
+    "TRI": ("sbuf", [128, 8, 16], "bfloat16"), "PT": ("sbuf", [128, 256], "float32"), "PS": ("sbuf", [128, 384], "float32"), "RS": ("sbuf", [128, 256], "float32"),
+    "BPD": ("sbuf", [128, 143], "bfloat16"), "BOS": ("sbuf", [128, 128], "bfloat16"), "ACL": ("sbuf", [128, 16], "float32"), "THC": ("sbuf", [128, 4], "float32"), "WC": ("sbuf", [128, 16], "float32"),
+    "ZERO": ("sbuf", [128, 256], "bfloat16"), "ONEF": ("sbuf", [128, 128], "float16"),
+    "LAB": ("sbuf", [128, 256], "float16"), "LML": ("sbuf", [128, 16], "float32"), "E": ("sbuf", [128, 16, 272], "bfloat16"),
+    "WA": ("sbuf", [128, 16], "float32"), "WB": ("sbuf", [128, 16], "float32"), "WO": ("sbuf", [128, 16], "uint16"),
+    "SV": ("sbuf", [128, 256], "float32"), "YL": ("sbuf", [128, 256], "float32"), "YR": ("sbuf", [128, 512], "float32"),
+    "R16": ("sbuf", [128, 4096], "float16"),
+}
+for _q in range(4):
+    SCRATCH["RI%d" % _q] = ("sbuf", [128, 1024], "int32")
+for _n, _d in (("LV", "uint16"), ("ZV", "bfloat16"), ("SL", "uint16"), ("SZ", "bfloat16")):
+    SCRATCH[_n] = ("sbuf", [128, 2 * TV + 2, 136], _d)
+PER_BLOCK = {
+    "XY": ([128, 2, 128], "float32"), "SVD": ([128, 128], "float32"), "LTA": ([128, 128], "float16"), "XG": ([128, 2048], "bfloat16"), "XA": ([128, 4096], "bfloat16"), "RG": ([128, 2048], "float32"), "CE": ([128, 2048], "bfloat16"),
+    "LP": ([128, 128], "float16"), "HM": ([128, 128], "float16"), "KC4": ([128, 384], "float32"),
+    "KT": ([128, 2, 128], "float32"), "T1": ([128, 4, 2, 64], "float32"), "KI": ([128, 4, 8], "int32"), "FT": ([128, 4, 64], "float32"),
+    "FI": ([128, 16], "int32"), "FF": ([128, 16], "float32"), "TA": ([128, 2, 8], "float32"), "KB": ([128, 128], "float32"),
+    "BA": ([128, 142], "float16"), "BE": ([128, 142], "float16"), "BM": ([128, 143], "float16"), "VT": ([128, 128], "float16"), "VTT": ([128, 128], "float16"),
+    "OL": ([128, 16], "uint16"), "RAB": ([128, 256], "float16"), "OF": ([128, 256], "uint16"), "HM2": ([128, 256], "float16"),
+    "KE": ([128, 2, 128], "float32"), "KJ": ([128, 2, 16], "int32"), "OE": ([128, 16], "uint16"), "XE": ([128, 256], "bfloat16"),
+    "XD": ([128, 128], "bfloat16"), "ZT": ([128, 128], "float16"), "SM": ([128, 4, 8], "float32"), "MM": ([128, 256], "float16"),
+    "P12": ([128, 256], "float16"), "P34": ([128, 256], "float16"),
+}
+_small = {}
+for _n, (_s, _d) in PER_BLOCK.items():
+    SCRATCH[_n] = ("sbuf", [128, 2] + _s[1:], _d)
+SCRATCH["AB"] = ("sbuf", [128, 4, 512], "bfloat16")
+SCRATCH["MX"] = ("sbuf", [128, 3, 512], "bfloat16")
+for _b in range(8):
+    SCRATCH["Q%d" % _b] = ("psum", [128, 512], "float32")
+SEMAPHORES = ["sv", "sa", "sp", "sg", "dz", "dl", "dt", "ls", "do", "dx0", "dx1", "dr0", "dr1", "dr2", "dr3"] + ["ar%d%d" % (t, h) for t in range(1, TV) for h in range(2)]
+SEMOF = {"v": "sv", "a": "sa", "p": "sp", "g": "sg"}
+DEP = 100.0
+GA = 1.45
+S2V = ((3,), ())
+MAXV = {(1, 0): (1, 3), (1, 1): (), (2, 0): (0, 1, 2, 3, 4, 5, 6, 7), (2, 1): (0, 1, 2, 3, 4, 5, 6, 7)}
+PEC = 0.71
+BONUS = {"far0": -3000, "far1": -1000, "sum0": 4000, "sum1": -4000, "end0": 2000, "end1": -1000, "wr0": -3000, "wr1": -3500,
+         "one0": -1500, "one1": -1000, "prep": 0, "sel0": 1000, "sel1": 3000}
+KBA = True
+SVV = False
+RGA = (64, 112)
+KEA = (False, True)
+SEED, SPREAD = 1, 0.0
+
+
+def plan():
+    ops = []
+
+    sec = [""]
+
+    def op(eng, cost, reads, writes, fn):
+        ops.append({"e": eng, "c": cost, "r": reads, "w": writes, "f": fn, "p": BONUS.get(sec[0], 0.0), "i": len(ops)})
+
+    def V(n, reads, writes, fn):
+        op("v", max(64, n) * CYC, reads, writes, fn)
+
+    def AC(n, reads, writes, fn):
+        op("a", 20 + max(64, n) * CYC, reads, writes, fn)
+
+    def P(n, reads, writes, fn):
+        op("p", n * PEC, reads, writes, fn)
+
+    def gather(eng, n, reads, writes, fn):
+        op(eng, 55 + GA * n * CYC, reads, writes, fn)
+
+    def G(n, reads, writes, fn):
+        op("g", 170 + 2 * n * CYC, reads, writes, fn)
+
+    def load(q, sem, cost, writes, fn):
+        op(q, cost, [], writes, fn)
+        ops[-1]["s"] = (sem, 16)
+    load("s", "dl", 2500, ["LI"], lambda k, T: k.sync.dma_start(T.LI[:, :], T.l0[:, :]))
+    load("s", "dx0", 3500, ["Xa"], lambda k, T: k.sync.dma_start(T.X[:, 0:2048], T.xt[:, 0:2048]))
+    load("t", "dx1", 3500, ["Xb"], lambda k, T: k.scalar.dma_start(T.X[:, 2048:4096], T.xt[:, 2048:4096]))
+    load("s", "dz", 4000, ["Z00", "Z01"], lambda k, T: (k.sync.dma_start(T.ZV[:, 0, 0:128], T.z0[:, 0:128]), k.sync.dma_start(T.ZV[:, 1, 0:128], T.z0[:, 128:256])))
+    ops[-1]["s"] = ("dz", 32)
+    for q in range(4):
+        load("s" if q % 2 else "t", "dr%d" % q, 6000 + 1500 * q, ["RI%d" % q],
+             (lambda q: lambda k, T: (k.sync if q % 2 else k.scalar).dma_start(T["RI%d" % q][:, :], T.ex[:, 1024 * q:1024 * q + 1024]))(q))
+    load("s", "dt", 9000, ["THI"], lambda k, T: k.sync.dma_start(T.THI[0:1, :], T.th[:, :]))
+
+    V(128, [], ["ONEB"], lambda k, T: k.vector.memset(T.ONEB[:, :], 1.0))
+    V(256, ["LI"], ["L00", "L01"], lambda k, T: (k.vector.tensor_copy(T.LV[:, 0, 0:128], T.LI[:, 0:128]), k.vector.tensor_copy(T.LV[:, 1, 0:128], T.LI[:, 128:256]))[-1])
+    V(1400, [], ["SLP"], lambda k, T: k.vector.memset(T.SL[:, :, :], 0))
+    V(700, [], ["SZP"], lambda k, T: k.vector.memset(T.SZ[:, :, :], 0.0))
+    G(128, ["ONEB"], ["IDB"], lambda k, T: k.affine_select(T.IDB[:, :], T.ONEB[:, 0:128], [[-1, 128]], A.is_equal, 0.0, 0, 1))
+    G(128, ["ONEB"], ["PERM"], lambda k, T: k.affine_select(T.PERM[:, :], T.ONEB[:, 0:128], [[-1, 16], [-16, 8]], A.is_equal, 0.0, 0, 1))
+    G(128, ["ONEB"], ["BOF"], lambda k, T: k.affine_select(T.BOF[:, :], T.ONEB[:, 0:128], [[-16, 8], [0, 16]], A.is_ge, 0.0, 0, 1))
+    G(128, ["BOF"], ["BOF"], lambda k, T: k.affine_select(T.BOF[:, :], T.BOF[:, :], [[16, 8], [0, 16]], A.is_ge, 0.0, 15, -1))
+    for s in range(6):
+        G(128, ["ONEB"], ["SELB%d" % s], (lambda s: lambda k, T: k.affine_select(T.SELB[:, 128 * s:128 * s + 128], T.ONEB[:, 0:128], [[-16, 8], [0, 16]], A.is_equal, 0.0, -s, 1))(s))
+    G(128, [], ["IOT"], lambda k, T: k.iota(T.IOT[:, :], [[64, 16], [0, 8]], 0, 0, allow_small_or_imprecise_dtypes=True))
+    G(256, [], ["IOT2"], lambda k, T: k.iota(T.IOT2[:, :, :], [[64, 16], [0, 16]], 0, 0, allow_small_or_imprecise_dtypes=True))
+    G(256, ["ONEB"], ["PB2"], lambda k, T: k.affine_select(T.PB2[:, :, :], T.ONEB3[:, :, :], [[-1, 16], [0, 2], [-16, 8]], A.is_equal, 0.0, 0, 1))
+    ops[-1]["r"] = ["ONEB3"]
+    V(256, [], ["ONEB3"], lambda k, T: k.vector.memset(T.ONEB3[:, :, :], 1.0))
+    ops[-1], ops[-2] = ops[-2], ops[-1]
+    ops[-1]["i"], ops[-2]["i"] = len(ops) - 1, len(ops) - 2
+    G(128, ["ONEB"], ["RXB"], lambda k, T: k.affine_select(T.RXB[:, :], T.ONEB[:, 0:128], [[-1, 8], [-8, 16]], A.is_equal, 0.0, 0, 1))
+    G(4, [], ["PI"], lambda k, T: k.iota(T.PI[:, :], [[0, 4]], 0, 1))
+    G(16, [], ["CI"], lambda k, T: k.iota(T.CI[:, :], [[16, 16]], 2048, 0, allow_small_or_imprecise_dtypes=True))
+    G(128, [], ["IOS"], lambda k, T: k.iota(T.IOS[:, :, :], [[0, 8], [1, 16]], 0, 0, allow_small_or_imprecise_dtypes=True))
+    for t in range(TV):
+        G(128, [], ["IJ%d" % t], (lambda t: lambda k, T: k.iota(T.IJ[:, 128 * t:128 * t + 128], [[1, 128]], 128 + t, -1))(t))
+    G(8, ["THI"], ["THB"], lambda k, T: k.partition_broadcast(T.THB[:, :], T.THI[0:1, :], 128))
+    cp = lambda o, i: (lambda k, T: k.vector.tensor_copy(o(T), i(T)))
+    ts = lambda o, i, s1, s2, o0, o1=None: (lambda k, T: k.vector.tensor_scalar(o(T), i(T), s1(T) if callable_(s1) else s1, s2, o0, o1) if o1 is not None
+                                            else k.vector.tensor_scalar(o(T), i(T), s1(T) if callable_(s1) else s1, None, o0))
+    tt = lambda o, x, y, f: (lambda k, T: k.vector.tensor_tensor(o(T), x(T), y(T), f))
+    V(64, ["IDB"], ["NIDB"], ts(lambda T: T.NIDB[:, :], lambda T: T.IDB[:, :], -1.0, None, A.mult))
+    AC(128, ["IDB"], ["ID32"], lambda k, T: k.scalar.activation(T.ID32[:, :], T.IDB[:, :], F.Copy))
+    V(64, ["IDB"], ["ID16"], cp(lambda T: T.ID16[:, :], lambda T: T.IDB[:, :]))
+    V(64, ["IDB"], ["NID16"], cp(lambda T: T.NID16[:, :], lambda T: T.NIDB[:, :]))
+    ops[-1]["r"] = ["NIDB"]
+    for nm, x in (("BO1", 1.0), ("BOK", 1024.0), ("BOC", 8388608.0), ("BOD", 2048.0), ("BON", -1024.0)):
+        V(128, ["BOF"], [nm], (lambda nm, x: lambda k, T: [k.vector.tensor_scalar(T[nm][:, c:c + 8], T.BOF[:, 0::16], x, None, A.mult) for c in ((0, 8) if nm in ("BOK", "BOD", "BON") else (0,))][-1])(nm, x))
+    V(128, [], ["CK2"], lambda k, T: k.vector.memset(T.CK2[:, :, :], 0.0))
+    V(128, ["CK2", "IOT2"], ["CK2"], lambda k, T: [k.vector.tensor_copy(T.CK2[0:1, c:c + 16, :], T.IOT2[0:1, :, :]) for c in (0, 16)][-1])
+    V(256, ["CK2", "IOT2"], ["CK2"], lambda k, T: ([k.vector.tensor_scalar(T.CK2[0:1, c:c + 16, 0:8], T.IOT2[0:1, :, 0:8], -1025.0, None, A.add) for c in (0, 16)],
+                                             k.vector.memset(T.CK2[32:33, :, 8:16], 33824.0), k.vector.memset(T.CK2[64:65, :, 8:16], 33824.0))[-1])
+    V(256, ["PB2"], ["PM2"], lambda k, T: (k.vector.tensor_copy(T.PM2[:, 0:16, 0:8], T.PB2[:, :, 0:8]), k.vector.tensor_scalar(T.PM2[:, 0:16, 8:16], T.PB2[:, :, 8:16], -64.0, None, A.mult),
+                                       k.vector.memset(T.PM2[:, 16:32, 0:8], 0.0), k.vector.tensor_copy(T.PM2[:, 16:32, 8:16], T.PB2[:, :, 8:16]))[-1])
+    V(64, ["PERM"], ["PMa"], cp(lambda T: T.PM[:, 0:128], lambda T: T.PERM[:, :]))
+    V(64, ["PERM"], ["PMb"], ts(lambda T: T.PM[:, 128:256], lambda T: T.PERM[:, :], -64.0, None, A.mult))
+    for s in range(6):
+        V(64, ["SELB%d" % s], ["SEL%d" % s], cp((lambda s: lambda T: T.SEL[:, 128 * s:128 * s + 128])(s), (lambda s: lambda T: T.SELB[:, 128 * s:128 * s + 128])(s)))
+    V(64, [], ["SEL4"], lambda k, T: k.vector.memset(T.SEL[:, 512:640:16], 0.0))
+    V(128, [], ["BPD"], lambda k, T: k.vector.memset(T.BPD[:, :], 0.0))
+    V(64, ["BOF", "BPD"], ["BPD"], lambda k, T: k.vector.tensor_copy(T.BPD[:, 15::16], T.BOF[:, 0::16]))
+    V(64, ["BOF"], ["BOS"], lambda k, T: k.vector.tensor_scalar(T.BOS[:, :], T.BOF[:, :], 8192.0, None, A.mult))
+    V(256, [], ["RS"], lambda k, T: k.vector.memset(T.RS[:, :], 1.0))
+    V(64, ["RS"], ["RS"], lambda k, T: k.vector.memset(T.RS[:, 0::16], 0.0))
+    V(128, ["SELB4"], ["SELF"], lambda k, T: [k.vector.tensor_scalar(T.SELF[:, 128 * v:128 * v + 128], T.SELB[:, 512:640], 32.0, None, A.mult) for v in range(2)][-1])
+    V(256, ["SELF", "SELB2", "SELB3"], ["SELF"], lambda k, T: k.vector.tensor_tensor(T.SELF[:, :], T.SELF[:, :], T.SELB[:, 256:512], A.add))
+    V(64, ["RXB"], ["RX"], cp(lambda T: T.RX[:, :], lambda T: T.RXB[:, :]))
+    V(64, [], ["CKL"], lambda k, T: k.vector.memset(T.CKL[:, :], 0.0))
+    V(64, ["CKL"], ["CKL"], lambda k, T: [k.vector.memset(T.CKL[b:b + 1, :], x) for b, x in ((0, 1.0), (32, 1.0), (64, 1.0), (96, 256.0))][-1])
+    for nm in ("CK1",):
+        g_ = (lambda nm: lambda T: T[nm])(nm)
+        V(128, [], [nm], (lambda g_: lambda k, T: k.vector.memset(g_(T)[:, :], 0.0))(g_))
+        V(128, [nm, "IOT"], [nm], (lambda g_: lambda k, T: (k.vector.tensor_scalar(g_(T)[0:1, 0:128], T.IOT[0:1, :], -1025.0, None, A.add),
+                                                       k.vector.tensor_copy(g_(T)[0:1, 128:256], T.IOT[0:1, :]),
+                                                       k.vector.memset(g_(T)[32:33, 128:256], 33824.0), k.vector.memset(g_(T)[64:65, 128:256], 33824.0))[-1])(g_))
+    V(128, ["CK1"], ["CK1"], lambda k, T: (k.vector.memset(T.CK1[96:97, 0:8], 49152.0), k.vector.memset(T.CK1[96:97, 128:136], 49152.0))[-1])
+    V(128, ["IOT"], ["CF"], ts(lambda T: T.CF[:, :], lambda T: T.IOT[:, :], -1.0, 1024.0, A.mult, A.add))
+    V(64, ["CF"], ["CF"], lambda k, T: k.vector.memset(T.CF[:, 0:8], -8388608.0))
+    V(64, ["PI"], ["PI"], ts(lambda T: T.PI[:, :], lambda T: T.PI[:, :], 15, None, A.bitwise_and))
+    V(64, ["PI"], ["SC"], cp(lambda T: T.SC[:, :], lambda T: T.PI[:, :]))
+    V(64, ["SC"], ["KC"], ts(lambda T: T.KC[:, :], lambda T: T.SC[:, :], -1.0, 16.0, A.mult, A.add))
+    V(64, ["CI", "SC"], ["CI"], ts(lambda T: T.CI[:, :], lambda T: T.CI[:, :], lambda T: T.SC[:, 0:1], None, A.add))
+    V(64, ["CI"], ["CI2"], ts(lambda T: T.CI2[:, :], lambda T: T.CI[:, :], 2048.0, None, A.add))
+    V(512, ["IOS", "SC"], ["TRI"], lambda k, T: [k.vector.tensor_scalar(T.TRI[:, m, :], T.IOS[:, m, :], T.SC[:, 0:1], None, A.is_gt) for m in range(8)][-1])
+    for t in range(TV):
+        sl = (lambda t: slice(128 * t, 128 * t + 128))(t)
+        V(128, ["IJ%d" % t], ["IJ%d" % t], (lambda sl: ts(lambda T: T.IJ[:, sl], lambda T: T.IJ[:, sl], 15, None, A.bitwise_and))(sl))
+        V(128, ["IJ%d" % t], ["MT%d" % t], (lambda sl: ts(lambda T: T.MT[:, sl], lambda T: T.IJ[:, sl], 0.0, None, A.is_equal))(sl))
+    V(128, [], ["ZERO"], lambda k, T: k.vector.memset(T.ZERO[:, :], 0.0))
+    V(64, [], ["ONEF"], lambda k, T: k.vector.memset(T.ONEF[:, :], 1.0))
+    V(256, [], ["Rd"], lambda k, T: k.vector.memset(T.R[:, 4096:4352], 0.0))
+    for nm in ("BA", "BE", "BM", "VT"):
+        V(128, [], [nm + "0", nm + "1"], (lambda nm: lambda k, T: k.vector.memset(T[nm][:, :, :], 0.0))(nm))
+    for q in range(4):
+        V(1024, ["RI%d" % q], ["R%d" % q], (lambda q: ts(lambda T: T.R[:, 1024 * q:1024 * q + 1024], lambda T: T["RI%d" % q][:, :], -2048.0, None, A.add))(q))
+    V(64, ["THB"], ["TH"], cp(lambda T: T.TH[:, :], lambda T: T.THB[:, :]))
+    V(64, ["TH", "BO1"], ["THN"], lambda k, T: k.vector.tensor_tensor(T.THN[:, :], T.TH[:, :], T.BO1[:, :], A.mult))
+    V(64, ["THN"], ["THC0"], lambda k, T: k.vector.tensor_reduce(T.THC[:, 0:1], T.THN[:, :], AxisListType.X, A.add))
+    RT = ["R0", "R1", "R2", "R3", "Rd"]
+    XT = ["Xa", "Xb"]
+    nab = [0]
+
+    nmx = [0]
+    P(64, ["IDB", "ZERO"], ["Q3.z"], lambda k, T: k.tensor.matmul(T.Q3[:, 0:8], T.IDB[:, :], T.ZERO[:, 0:8], True, True))
+
+    def subsum(t, h, which, x3, base, zk, bo_out, reads, vmax=False):
+        b = nab[0] % 2
+        a4 = nab[0] % 4
+        nab[0] += 1
+        bank = "Q%d" % (1 + b)
+
+        zi = 2 * t + h
+        nw, one = 8 * which, which == 1
+        skip = 1 if which == 1 and base == 0 else 0
+        if vmax:
+            nab[0] -= 1
+            m4 = nmx[0] % 3
+            nmx[0] += 1
+            nosz = len(MAXV[which, h]) == 4 * which
+            V(512 - 128 * skip, reads + ["Q0.z%d" % h], ["MX%d" % m4], lambda k, T: [k.vector.tensor_tensor(
+                T.MX[:, m4, 128 * kk:128 * kk + 128], x3(T, base + kk), T.Q0[:, 256 + 128 * h:384 + 128 * h], A.max) for kk in range(skip, 4)][-1])
+
+            def sums(k, T):
+                for kk in range(skip, 4):
+                    k.tensor.matmul(bo_out[1](T, kk), T.MX[:, m4, 128 * kk:128 * kk + 128], T.BOD[:, 0:nw], one, False)
+                    last = k.tensor.matmul(bo_out[1](T, kk), x3(T, base + kk), T.BON[:, 0:nw], False, one and nosz)
+                    if not nosz:
+                        last = k.tensor.matmul(bo_out[1](T, kk), T.ZV[:, zi, 0:128], T.BON[:, 0:nw], False, one)
+                return last
+            P((4 - skip) * (128 if nosz else 192), ["MX%d" % m4, "BOD", "BON", zk] + reads, [bo_out[0]], sums)
+            return
+
+        def sub(k, T):
+            for kk in range(skip, 4):
+                o = T[bank][:, 128 * kk:128 * kk + 128]
+                k.tensor.matmul(o, T.IDB[:, :], x3(T, base + kk), True, False)
+                last = k.tensor.matmul(o, T.NIDB[:, :], T.ZV[:, zi, 0:128], False, True)
+            return last
+        P(1024 - 256 * skip, reads + [zk, "IDB", "NIDB"], [bank], sub)
+        AC(512 - 128 * skip, [bank], ["AB%d" % a4], lambda k, T: k.scalar.activation(T.AB[:, a4, 128 * skip:512], T[bank][:, 128 * skip:512], F.Abs))
+        P(256 - 64 * skip, ["AB%d" % a4, "BOK"], [bo_out[0]], lambda k, T: [k.tensor.matmul(bo_out[1](T, kk), T.AB[:, a4, 128 * kk:128 * kk + 128], T.BOK[:, 0:nw], one, one) for kk in range(skip, 4)][-1])
+
+    def lists(T, k, out, B, width, step, xs, rhs, rw):
+        for x in range(xs):
+            last = k.tensor.matmul(out, B[:, width - step * x:width - step * x + 128], rhs[:, rw * x:rw * x + rw], x == 0, x == xs - 1)
+        return last
+
+    for t in range(TV):
+        if t:
+            for h in range(2):
+                op("x", 0, ["send%d%d" % (t - 1, h)], ["L%d%d" % (t, h), "Z%d%d" % (t, h)], None)
+                ops[-1]["s"] = ("ar%d%d" % (t, h), 8)
+                ops[-1]["c"] = 3000
+        hh = []
+        for h in range(2):
+            H = str(h)
+            Lk, Zk = "L%d%d" % (t, h), "Z%d%d" % (t, h)
+
+            def prep(t, h, H, Lk, Zk):
+                li = 2 * t + h
+                V(64, [Lk], ["LP" + H], lambda k, T: k.vector.tensor_scalar(T.LP[:, h, :], T.LV[:, li, 0:128], -2048.0, None, A.add))
+                V(64, [Lk], ["HM" + H], lambda k, T: k.vector.tensor_scalar(T.HM[:, h, :], T.LV[:, li, 0:128], 0.015625, 1025 - 0.4921875, A.mult, A.add))
+                P(128, ["LP" + H, "SEL0"], ["Q0.l" + H], lambda k, T: k.tensor.matmul(T.Q0[:, 128 * h:128 * h + 128], T.SEL[:, 0:128], T.LP[:, h, :], True, True))
+                P(128, [Zk, "IDB"], ["Q0.z" + H], lambda k, T: k.tensor.matmul(T.Q0[:, 256 + 128 * h:384 + 128 * h], T.IDB[:, :], T.ZV[:, li, 0:128], True, True))
+            sec[0] = "prep"
+            prep(t, h, H, Lk, Zk)
+        for h in range(2):
+            H, Lk, Zk = str(h), "L%d%d" % (t, h), "Z%d%d" % (t, h)
+
+            def stage1(t, h, H, Lk, Zk):
+                li = 2 * t + h
+                sec[0] = "one" + H
+                gather("a", 2048, XT + [Lk], ["XG" + H], lambda k, T: k.scalar.activation(T.XG[:, h, :], T.X[:, :].indirect(T.LV[:, li, 0:128]), F.Copy))
+
+                def payload(k, T):
+                    k.tensor.matmul(T.Q3[:, 256:512], T.CKL[:, :], T.CK1[:, :], True, False)
+                    k.tensor.matmul(T.Q3[:, 256:512], T.HM[:, h, :], T.PM[:, :], False, False)
+                    return k.tensor.matmul(T.Q3[:, 384:512], T.LP[:, h, :], T.PM[:, 0:128], False, True)
+                P(640, ["CKL", "CK1", "HM" + H, "LP" + H, "PMa", "PMb"], ["Q3.p"], payload)
+                for q in range(4):
+                    subsum(t, h, 1, lambda T, r: T.XG[:, h, r::16], 4 * q, Zk, ("Q3.d%d" % q, (lambda q: lambda T, kk: T.Q3[:, 8 * (4 * q + kk):8 * (4 * q + kk) + 8])(q)), ["XG" + H], vmax=q in MAXV[1, h])
+                na = RGA[h]
+                gather("a", 16 * na, RT + [Lk], ["RG" + H], lambda k, T: k.scalar.activation(T.RG[:, h, 0:16 * na], T.R[:, :].indirect(T.LV[:, li, 0:na]), F.Copy))
+                if na < 128:
+                    gather("v", 2048 - 16 * na, RT + [Lk], ["RGv" + H], lambda k, T: k.vector.tensor_copy(T.RG[:, h, 16 * na:2048], T.R[:, :].indirect(T.LV[:, li, na:128])))
+                for q in range(3):
+                    V(640, ["RG" + H, "RGv" + H, "Q0.l" + H], ["CE%s%d" % (H, q)], (lambda q: lambda k, T: [k.vector.tensor_tensor(
+                        T.CE[:, h, 128 * kk:128 * kk + 128], T.RG[:, h, kk::16], T.Q0[:, 128 * h:128 * h + 128], A.is_equal) for kk in range(5 * q + 1, 5 * q + 6)][-1])(q))
+                    P(320, ["CE%s%d" % (H, q), "BOC"], ["Q3.c%d" % q], (lambda q: lambda k, T: [k.tensor.matmul(
+                        T.Q3[:, 128 + 8 * kk:136 + 8 * kk], T.CE[:, h, 128 * kk:128 * kk + 128], T.BOC[:, :], True, True) for kk in range(5 * q + 1, 5 * q + 6)][-1])(q))
+                D4 = ["Q3.d0", "Q3.d1", "Q3.d2", "Q3.d3", "Q3.z"]
+                sec[0] = "sel" + H
+                V(120, ["Q3.c0", "Q3.c1", "Q3.c2"], ["KCa" + H], lambda k, T: k.vector.tensor_scalar(T.KC4[:, h, 8:128], T.Q3[:, 136:256], 8388608.0, None, A.min))
+                V(128, D4 + ["CF"], ["KCc" + H], lambda k, T: k.vector.tensor_tensor(T.KC4[:, h, 256:384], T.Q3[:, 0:128], T.CF[:, :], A.add))
+                V(64, [], ["KCz" + H], lambda k, T: k.vector.memset(T.KC4[:, h, 0:8], 0.0)) if t == 0 else None
+                V(128, D4 + ["KCa" + H, "KCz" + H], ["KCb" + H], lambda k, T: k.vector.tensor_tensor(T.KC4[:, h, 128:256], T.Q3[:, 0:128], T.KC4[:, h, 0:128], A.max))
+                for w in range(2):
+                    V(128, ["KCb" + H, "Q3.p"], ["KT%s%d" % (H, w)], (lambda w: lambda k, T: k.vector.tensor_tensor(
+                        T.KT[:, h, w, :], T.Q3[:, 256 + 128 * w:384 + 128 * w], T.KC4[:, h, 128:256], A.add))(w))
+                KT = ["KT" + H + "0", "KT" + H + "1"]
+                V(256, KT, ["m64" + H], lambda k, T: k.vector.tensor_tensor(T.T1[:, h, 0, :, :], T.KT[:, h, :, 0:64], T.KT[:, h, :, 64:128], A.min))
+                V(256, KT, ["s64" + H], lambda k, T: k.vector.tensor_tensor(T.T1[:, h, 1, :, :], T.KT[:, h, :, 0:64], T.KT[:, h, :, 64:128], A.max))
+                for n in (32, 16, 8):
+                    lastlevel = n == 8
+                    o = {32: (2, 0), 16: (2, 32), 8: (2, 48)}[n]
+                    i = {32: (None, 0), 16: (2, 0), 8: (2, 32)}[n]
+                    mi, si = ((0, 1) if n == 32 else (2, 3))
+                    lo = i[1]
+
+                    def lev(n, mi, si, lo, oo, lastlevel):
+                        two = 2 * n
+                        V(4 * n, ["m%d" % two + H], ["x%d" % n + H], lambda k, T: k.vector.tensor_tensor(T.XY[:, h, :, 0:n], T.T1[:, h, mi, :, lo:lo + n], T.T1[:, h, mi, :, lo + n:lo + 2 * n], A.max))
+                        ops[-1]["w"].append("XY" + H)
+                        V(4 * n, ["s%d" % two + H], ["y%d" % n + H], lambda k, T: k.vector.tensor_tensor(T.XY[:, h, :, 64:64 + n], T.T1[:, h, si, :, lo:lo + n], T.T1[:, h, si, :, lo + n:lo + 2 * n], A.min))
+                        ops[-1]["w"].append("XZ" + H)
+                        V(4 * n, ["m%d" % two + H], ["m%d" % n + H], lambda k, T: k.vector.tensor_tensor(
+                            T.KI[:, h, 0:2, :] if lastlevel else T.T1[:, h, 2, :, oo:oo + n], T.T1[:, h, mi, :, lo:lo + n], T.T1[:, h, mi, :, lo + n:lo + 2 * n], A.min))
+                        V(4 * n, ["x%d" % n + H, "y%d" % n + H, "XY" + H, "XZ" + H], ["s%d" % n + H], lambda k, T: k.vector.tensor_tensor(
+                            T.KI[:, h, 2:4, :] if lastlevel else T.T1[:, h, 3, :, oo:oo + n], T.XY[:, h, :, 0:n], T.XY[:, h, :, 64:64 + n], A.min))
+                    lev(n, mi, si, lo, o[1], lastlevel)
+                V(64, ["s8" + H], ["KB" + H], lambda k, T: k.vector.tensor_copy(T.KB[:, h, 0:8], T.KI[:, h, 2, :]))
+                V(64, ["m8" + H, "s8" + H, "KB" + H], ["KJ" + H], lambda k, T: k.vector.tensor_scalar(T.KI[:, h, :, :], T.KI[:, h, :, :], 63, None, A.bitwise_and))
+                ops[-1]["w"].extend(["m8" + H, "s8" + H])
+                V(64, ["KJ" + H], ["TA" + H], lambda k, T: k.vector.tensor_scalar(T.TA[:, h, :, :], T.KI[:, h, 0::2, :], 64.0, -2048.0, A.mult, A.add))
+                V(128, ["TA" + H, "KJ" + H], ["BA" + H], lambda k, T: [k.vector.tensor_tensor(T.BA[:, h, 14 + v:128 + 14:16], T.TA[:, h, v, :], T.KI[:, h, 2 * v + 1, :], A.add) for v in range(2)][-1])
+                P(128, ["BA" + H, "ID16"], ["Q5.vt"], lambda k, T: k.tensor.matmul(T.Q5[:, 384:512], T.BA[:, h, 14:142], T.ID16[:, :], True, True))
+                P(512, ["BA" + H, "RX"], ["Q5.ll" + H], lambda k, T: lists(T, k, T.Q5[:, 256 + 16 * h:272 + 16 * h], T.BA[:, h, :], 14, 2, 8, T.RX, 16))
+                V(64, ["Q5.ll" + H], ["OL" + H], lambda k, T: k.vector.tensor_scalar(T.OL[:, h, :], T.Q5[:, 256 + 16 * h:272 + 16 * h], 2048.0, None, A.add))
+                V(128, ["Q5.vt"], ["LTA" + H], lambda k, T: k.vector.tensor_copy(T.LTA[:, h, :], T.Q5[:, 384:512]))
+                P(128, ["LTA" + H, "SEL0"], ["Q6.a"], lambda k, T: k.tensor.matmul(T.Q6[:, 384:512], T.SEL[:, 0:128], T.LTA[:, h, :], True, True))
+                gather("v", 256, RT + ["OL" + H], ["RAB" + H], lambda k, T: k.vector.tensor_copy(T.RAB[:, h, :], T.R[:, :].indirect(T.OL[:, h, :])))
+                P(256, ["LP" + H, "SEL0", "RAB" + H, "NID16"], ["Q6.c"], lambda k, T: (k.tensor.matmul(T.Q6[:, 256:384], T.SEL[:, 0:128], T.LP[:, h, :], True, False),
+                                                                        k.tensor.matmul(T.Q6[:, 256:384], T.NID16[:, :], T.RAB[:, h, 0::2], False, True))[-1])
+                V(128, ["Q6.a"], ["LAB" + H], lambda k, T: k.vector.tensor_copy(T.LAB[:, 128 * h:128 * h + 128], T.Q6[:, 384:512]))
+                V(128, ["Q6.c", "MT%d" % t], ["SVD" + H], lambda k, T: k.vector.tensor_tensor(T.SVD[:, h, :], T.Q6[:, 256:384], T.MT[:, 128 * t:128 * t + 128], A.mult))
+                P(640, ["SVD" + H, "RAB" + H, "ID16", "ID32"], ["Q6.f"], lambda k, T: (k.tensor.matmul(T.Q6[:, 0:128], T.ID32[:, :], T.SVD[:, h, :], True, False),
+                                                                                 k.tensor.matmul(T.Q6[:, 0:128], T.ID16[:, :], T.RAB[:, h, 0::2], False, True))[-1])
+                if SVV:
+                    V(128, ["Q6.f"], ["SV" + H], lambda k, T: k.vector.tensor_copy(T.SV[:, 128 * h:128 * h + 128], T.Q6[:, 0:128]))
+                else:
+                    AC(128, ["Q6.f"], ["SV" + H], lambda k, T: k.scalar.activation(T.SV[:, 128 * h:128 * h + 128], T.Q6[:, 0:128], F.Copy))
+                V(64, ["BA" + H], ["BM" + H], lambda k, T: k.vector.tensor_copy(T.BM[:, h, 15::16], T.BA[:, h, 14:142:16]))
+                P(1024, ["BM" + H, "PMa"], ["Q5.lm"], lambda k, T: lists(T, k, T.Q5[:, 336:344], T.BM[:, h, :], 15, 1, 16, T.PM, 8))
+                V(64, ["Q5.lm"], ["LML" + H], lambda k, T: k.vector.tensor_copy(T.LML[:, 8 * h:8 * h + 8], T.Q5[:, 336:344]))
+                V(128, ["RAB" + H], ["OF" + H], lambda k, T: k.vector.tensor_scalar(T.OF[:, h, :], T.RAB[:, h, :], 2048.0, None, A.add))
+                V(128, ["RAB" + H], ["HM2" + H], lambda k, T: k.vector.tensor_scalar(T.HM2[:, h, :], T.RAB[:, h, :], 0.015625, 1057 - 0.4921875, A.mult, A.add))
+                b2 = ("Q4", "Q3")[h]
+
+                def payload2(k, T):
+                    k.tensor.matmul(T[b2][:, :], T.CKL[:, :], T.CK2[:, :, :], True, False)
+                    for v in range(2):
+                        k.tensor.matmul(T[b2][:, 256 * v:256 * v + 256], T.HM2[:, h, v::2], T.PM2[:, 0:16, :], False, False)
+                        last = k.tensor.matmul(T[b2][:, 256 * v:256 * v + 256], T.RAB[:, h, v::2], T.PM2[:, 16:32, :], False, False)
+                    return last
+                P(1536, ["CKL", "CK2", "HM2" + H, "RAB" + H, "PM2"], [b2 + ".p"] + [b2 + ".d%d" % j for j in range(8)] + [b2 + ".c%d" % j for j in range(3)], payload2)
+                sec[0] = "far" + H
+                for n in (8, 16, 32, 64):
+                    op("a" if KBA else "v", 60, ["KB" + H], ["KB" + H], (lambda n: lambda k, T: k.scalar.activation(T.KB[:, h, n:2 * n], T.KB[:, h, 0:n], F.Copy) if KBA else
+                                                                         k.vector.tensor_copy(T.KB[:, h, n:2 * n], T.KB[:, h, 0:n]))(n))
+                V(256, ["KB" + H, "KT" + H + "0"], ["KCa" + H, "KCz" + H], lambda k, T: k.vector.tensor_tensor(T.KC4[:, h, 0:128], T.KT[:, h, 0, :], T.KB[:, h, :], A.is_gt))
+                V(256, ["KCa" + H, "KCc" + H], ["KCc" + H], lambda k, T: k.vector.tensor_tensor(T.KC4[:, h, 256:384], T.KC4[:, h, 256:384], T.KC4[:, h, 0:128], A.mult))
+                FT = lambda T, j, a, b: T.FT[:, h, j, a:b]
+                V(128, ["KCc" + H], ["fm64" + H], lambda k, T: k.vector.tensor_tensor(FT(T, 0, 0, 64), T.KC4[:, h, 256:320], T.KC4[:, h, 320:384], A.max))
+                V(128, ["KCc" + H], ["fs64" + H], lambda k, T: k.vector.tensor_tensor(FT(T, 1, 0, 64), T.KC4[:, h, 256:320], T.KC4[:, h, 320:384], A.min))
+                for n, mi, lo, oo in ((32, 0, 0, 0), (16, 2, 0, 32), (8, 2, 32, 48)):
+                    def flev(n, mi, lo, oo):
+                        two = 2 * n
+                        si = mi + 1
+                        V(2 * n, ["fm%d" % two + H, "KCc" + H], ["fx" + H], lambda k, T: k.vector.tensor_tensor(T.KC4[:, h, 0:n], FT(T, mi, lo, lo + n), FT(T, mi, lo + n, lo + 2 * n), A.min))
+                        V(2 * n, ["fs%d" % two + H, "KCc" + H], ["fy" + H], lambda k, T: k.vector.tensor_tensor(T.KC4[:, h, 64:64 + n], FT(T, si, lo, lo + n), FT(T, si, lo + n, lo + 2 * n), A.max))
+                        V(2 * n, ["fm%d" % two + H], ["fm%d" % n + H], lambda k, T: k.vector.tensor_tensor(T.FI[:, h, 0:8] if n == 8 else FT(T, 2, oo, oo + n), FT(T, mi, lo, lo + n), FT(T, mi, lo + n, lo + 2 * n), A.max))
+                        V(2 * n, ["fx" + H, "fy" + H], ["fs%d" % n + H], lambda k, T: k.vector.tensor_tensor(T.FI[:, h, 8:16] if n == 8 else FT(T, 3, oo, oo + n), T.KC4[:, h, 0:n], T.KC4[:, h, 64:64 + n], A.max))
+                    flev(n, mi, lo, oo)
+                V(64, [], ["KCa" + H], lambda k, T: k.vector.memset(T.KC4[:, h, 0:8], 0.0))
+                ops[-1]["r"] = ["fs8" + H]
+                ops[-1]["w"] = ["KCz" + H, "KCa" + H]
+                V(64, ["fm8" + H, "fs8" + H], ["FI" + H], lambda k, T: k.vector.tensor_scalar(T.FI[:, h, :], T.FI[:, h, :], 6, 15, A.logical_shift_right, A.bitwise_and))
+                ops[-1]["w"].extend(["fm8" + H, "fs8" + H])
+                V(128, ["FI" + H, "VT" + H], ["VT2" + H], lambda k, T: [k.vector.tensor_copy(T.VT[:, h, 2 + v::16], T.FI[:, h, 8 * v:8 * v + 8]) for v in range(2)][-1])
+            stage1(t, h, H, Lk, Zk)
+        for h in range(2):
+            def stage2(t, h, H, Lk, Zk):
+                zi = 2 * t + h
+                for q in range(4):
+                    if q in S2V[h]:
+                        gather("v", 1024, XT + ["OF" + H], ["XA%s%d" % (H, q)], (lambda q: lambda k, T: k.vector.tensor_copy(T.XA[:, h, 1024 * q:1024 * q + 1024], T.X[:, :].indirect(T.OF[:, h, 64 * q:64 * q + 64])))(q))
+                    else:
+                        gather("a", 1024, XT + ["OF" + H], ["XA%s%d" % (H, q)], (lambda q: lambda k, T: k.scalar.activation(T.XA[:, h, 1024 * q:1024 * q + 1024], T.X[:, :].indirect(T.OF[:, h, 64 * q:64 * q + 64]), F.Copy))(q))
+
+                sec[0] = "sum" + H
+                bk = ("Q4", "Q3")[h]
+                for q in range(8):
+                    subsum(t, h, 2, lambda T, r: T.XA[:, h, r::32], 4 * q, Zk, (bk + ".d%d" % q, (lambda q: lambda T, kk: T[("Q4", "Q3")[h]][:, 16 * (4 * q + kk):16 * (4 * q + kk) + 16])(q)), ["XA%s%d" % (H, j) for j in range(4)], vmax=q in MAXV[2, h])
+                P(64, [bk + ".d%d" % j for j in range(8)] + ["IDB", "ZERO"], [bk + ".f"], lambda k, T: k.tensor.matmul(T[("Q4", "Q3")[h]][:, 0:16], T.IDB[:, :], T.ZERO[:, 0:16], False, True))
+                if KEA[h]:
+                    AC(276, [bk + ".f"], ["KE" + H], lambda k, T: [k.scalar.activation(T.KE[:, h, v, :], T[("Q4", "Q3")[h]][:, 256 * v:256 * v + 128], F.Copy) for v in range(2)][-1])
+                else:
+                    V(256, [bk + ".f"], ["KE" + H], lambda k, T: [k.vector.tensor_copy(T.KE[:, h, v, :], T[("Q4", "Q3")[h]][:, 256 * v:256 * v + 128]) for v in range(2)][-1])
+                V(256, [bk + ".f", "KE" + H], ["KE" + H], lambda k, T: [k.vector.tensor_tensor(T.KE[:, h, v, :], T.KE[:, h, v, :], T[("Q4", "Q3")[h]][:, 256 * v + 128:256 * v + 256], A.min) for v in range(2)][-1])
+                sec[0] = "end" + H
+                for n in (64, 32):
+                    V(4 * n, ["KE" + H], ["KE" + H], (lambda n: lambda k, T: k.vector.tensor_tensor(T.KE[:, h, :, 0:n], T.KE[:, h, :, 0:n], T.KE[:, h, :, n:2 * n], A.min))(n))
+                V(64, ["KE" + H], ["KI2" + H], lambda k, T: k.vector.tensor_tensor(T.KJ[:, h, :, :], T.KE[:, h, :, 0:16], T.KE[:, h, :, 16:32], A.min))
+                V(64, ["KI2" + H], ["KI2" + H], lambda k, T: k.vector.tensor_scalar(T.KJ[:, h, :, :], T.KJ[:, h, :, :], 63, None, A.bitwise_and))
+                V(64, ["KI2" + H], ["TE" + H], lambda k, T: k.vector.tensor_scalar(T.SM[:, h, 0:2, :], T.KJ[:, h, :, 0:8], 64.0, -2048.0, A.mult, A.add))
+                V(128, ["TE" + H, "KI2" + H], ["BE" + H], lambda k, T: [k.vector.tensor_tensor(T.BE[:, h, 14 + v:128 + 14:16], T.SM[:, h, v, :], T.KJ[:, h, v, 8:16], A.add) for v in range(2)][-1])
+                P(512, ["BE" + H, "RX"], ["Q5.le" + H], lambda k, T: lists(T, k, T.Q5[:, 288 + 16 * h:304 + 16 * h], T.BE[:, h, :], 14, 2, 8, T.RX, 16))
+                V(64, ["Q5.le" + H], ["OE" + H], lambda k, T: k.vector.tensor_scalar(T.OE[:, h, :], T.Q5[:, 288 + 16 * h:304 + 16 * h], 2048.0, None, A.add))
+                gather("v", 256, XT + ["OE" + H], ["XE" + H], lambda k, T: k.vector.tensor_copy(T.XE[:, h, :], T.X[:, :].indirect(T.OE[:, h, :])))
+
+                def sd(k, T):
+                    k.tensor.matmul(T.Q6[:, 128:256], T.IDB[:, :], T.XE[:, h, 0::2], True, False)
+                    k.tensor.matmul(T.Q6[:, 128:256], T.NIDB[:, :], T.XE[:, h, 1::2], False, True)
+                    k.tensor.matmul(T.Q6[:, 0:128], T.IDB[:, :], T.XE[:, h, 0::2], True, False)
+                    return k.tensor.matmul(T.Q6[:, 0:128], T.IDB[:, :], T.XE[:, h, 1::2], False, True)
+                P(512, ["XE" + H, "IDB", "NIDB"], ["Q6.f"], sd)
+                AC(128, ["Q6.f"], ["XD" + H], lambda k, T: k.scalar.activation(T.XD[:, h, :], T.Q6[:, 128:256], F.Abs))
+                V(128, ["Q6.f"], ["ZT" + H], lambda k, T: k.vector.tensor_scalar(T.ZT[:, h, :], T.Q6[:, 0:128], 0.5, 1023.75, A.mult, A.add))
+                zo = "SZ%d%d" % (t, h)
+                V(64, ["ZT" + H, "SZP"], [zo], lambda k, T: k.vector.tensor_scalar(T.SZ[:, zi, 0:128], T.ZT[:, h, :], -1024.0, None, A.add))
+                P(64, ["XD" + H, "BO1"], ["Q5.dt"], lambda k, T: k.tensor.matmul(T.Q5[:, 320:328], T.XD[:, h, :], T.BO1[:, :], True, True))
+                P(1024, ["XD" + H, "BPD"], ["Q5.dl"], lambda k, T: [k.tensor.matmul(T.Q5[:, 352:360], T.BPD[:, 15 - x:143 - x], T.XD[:, h, x::16], x == 0, x == 15) for x in range(16)][-1])
+                if t == 0:
+                    thn = lambda T: T.TH[:, :]
+                    tk = "TH"
+                else:
+                    if h == 0:
+                        nn = ["L%d0" % t, "L%d1" % t]
+                        V(64, nn, ["NF"], lambda k, T: (k.vector.tensor_copy(T.NF[:, 0:1], T.LV[:, 2 * t, 128:129]), k.vector.tensor_copy(T.NF[:, 1:2], T.LV[:, 2 * t + 1, 128:129]))[-1])
+                        V(64, ["NF"], ["NI"], lambda k, T: k.vector.tensor_tensor(T.NI[:, 0:1], T.NF[:, 0:1], T.NF[:, 1:2], A.add))
+                        V(64, ["NI"], ["NI"], lambda k, T: k.vector.tensor_scalar(T.NI[:, 0:1], T.NI[:, 0:1], 63, None, A.bitwise_and))
+                        V(64, ["NI"], ["NM"], lambda k, T: k.vector.tensor_copy(T.NM[:, 0:1], T.NI[:, 0:1]))
+                        V(64, ["NM", "THC0"], ["THC1"], lambda k, T: k.vector.tensor_tensor(T.THC[:, 1:2], T.THC[:, 0:1], T.NM[:, 0:1], A.add))
+                        V(64, ["NM", "TH"], ["THN"], lambda k, T: k.vector.tensor_scalar(T.THN[:, :], T.TH[:, :], T.NM[:, 0:1], None, A.add))
+                    thn = lambda T: T.THN[:, :]
+                    tk = "THN"
+                V(64, ["Q5.dt", tk, "VT" + H], ["VT4" + H], lambda k, T: k.vector.tensor_tensor(T.VT[:, h, 4::16], T.Q5[:, 320:328], thn(T), A.is_lt))
+                tc = 0 if t == 0 else 1
+                V(64, ["Q5.dl", "THC%d" % tc], ["ACL" + H], lambda k, T: k.vector.tensor_scalar(T.ACL[:, 8 * h:8 * h + 8], T.Q5[:, 352:360], T.THC[:, tc:tc + 1], None, A.is_lt))
+                VTK = ["VT%d%s" % (s, H) for s in (2, 4)] + ["VT" + H]
+                P(256, VTK + ["BE" + H, "ID16"], ["Q5.vt"], lambda k, T: (k.tensor.matmul(T.Q5[:, 384:512], T.VT[:, h, :], T.ID16[:, :], True, False),
+                                                                     k.tensor.matmul(T.Q5[:, 384:512], T.BE[:, h, 14:142], T.ID16[:, :], False, True))[-1])
+                V(128, ["Q5.vt"], ["VTT" + H], lambda k, T: k.vector.tensor_copy(T.VTT[:, h, :], T.Q5[:, 384:512]))
+
+                def bc(out, s):
+                    return lambda k, T: k.tensor.matmul(out(T), T.SEL[:, 128 * s:128 * s + 128], T.VTT[:, h, :], True, True)
+                P(256, ["VTT" + H, "SELF"], ["Q6.f"], lambda k, T: [k.tensor.matmul(T.Q6[:, 128 * v:128 * v + 128], T.SELF[:, 128 * v:128 * v + 128], T.VTT[:, h, :], True, True) for v in range(2)][-1])
+                P(128, ["VTT" + H, "SEL4"], ["Q6.c"], bc(lambda T: T.Q6[:, 256:384], 4))
+                P(256, ["VTT" + H, "SEL0", "SEL1"], ["Q7.e"], lambda k, T: (bc(lambda T: T.Q7[:, 0:128], 0)(k, T), bc(lambda T: T.Q7[:, 128:256], 1)(k, T))[-1])
+                V(256, ["Q6.f", "KC"], ["MM" + H], lambda k, T: k.vector.tensor_scalar(T.MM[:, h, :], T.Q6[:, 0:256], T.KC[:, 0:1], None, A.is_equal))
+                V(128, ["Q6.c", "RAB" + H], ["P3" + H], lambda k, T: k.vector.tensor_tensor(T.P34[:, h, 0:128], T.Q6[:, 256:384], T.RAB[:, h, 1::2], A.mult))
+                V(256, ["MM" + H, "Q7.e"], ["P12" + H], lambda k, T: k.vector.tensor_tensor(T.P12[:, h, :], T.MM[:, h, :], T.Q7[:, 0:256], A.mult))
+
+                def kam(k, T):
+                    k.tensor.matmul(T.Q7[:, 256:384], T.ID16[:, :], T.MM[:, h, 0:128], True, False)
+                    k.tensor.matmul(T.Q7[:, 256:384], T.ID16[:, :], T.MM[:, h, 128:256], False, False)
+                    return k.tensor.matmul(T.Q7[:, 256:384], T.SEL[:, 512:640], T.VTT[:, h, :], False, True)
+                P(384, ["MM" + H, "VTT" + H, "ID16", "SEL4"], ["Q7.k"], kam)
+                V(128, ["Q7.k", "LP" + H], ["P4" + H], lambda k, T: k.vector.tensor_tensor(T.P34[:, h, 128:256], T.Q7[:, 256:384], T.LP[:, h, :], A.mult))
+
+                def new(k, T):
+                    o = T.Q7[:, 384:512]
+                    k.tensor.matmul(o, T.ID16[:, :], T.LP[:, h, :], True, False)
+                    k.tensor.matmul(o, T.ID16[:, :], T.P34[:, h, 0:128], False, False)
+                    k.tensor.matmul(o, T.ID16[:, :], T.P12[:, h, 0:128], False, False)
+                    k.tensor.matmul(o, T.ID16[:, :], T.P12[:, h, 128:256], False, False)
+                    return k.tensor.matmul(o, T.NID16[:, :], T.P34[:, h, 128:256], False, True)
+                P(640, ["P12" + H, "P3" + H, "P4" + H, "LP" + H, "ID16", "NID16"], ["Q7.n"], new)
+                if t < TV - 1:
+                    sl = "SL%d%d" % (t, h)
+                    V(128, ["Q7.n", "SLP"], [sl], lambda k, T: k.vector.tensor_scalar(T.SL[:, zi, 0:128], T.Q7[:, 384:512], 2048.0, None, A.add))
+                    P(512, ["VT4" + H, "ONEF"], ["Q5.nc"], lambda k, T: [k.tensor.matmul(T.Q5[:, 328:329], T.ONEF[:, :], T.VT[:, h, 4 + 16 * j:5 + 16 * j], j == 0, j == 7) for j in range(8)][-1])
+                    V(64, ["Q5.nc", "SLP"], [sl + "n"], lambda k, T: k.vector.tensor_copy(T.SL[:, zi, 128:129], T.Q5[:, 328:329]))
+                    op("g", 1200, [sl, sl + "n", zo, "SLP", "SZP"], ["send%d%d" % (t, h)], None)
+                    ops[-1]["send"] = (t, h)
+                else:
+                    V(128, ["Q7.n"], ["YL" + H], lambda k, T: k.vector.tensor_scalar(T.YL[:, 128 * h:128 * h + 128], T.Q7[:, 384:512], 2048.0, None, A.add))
+                    op("s", 50, ["YL" + H], ["yl" + H], lambda k, T: k.sync.dma_start(T.yl[:, 128 * h:128 * h + 128], T.YL[:, 128 * h:128 * h + 128]))
+                    ops[-1]["s"] = ("do", 16)
+                    op("s", 50, [zo], ["yz" + H], lambda k, T: k.sync.dma_start(T.yz[:, 128 * h:128 * h + 128], T.SZ[:, zi, 0:128]))
+                    ops[-1]["s"] = ("do", 16)
+                sec[0] = "wr" + H
+                V(64, ["ACL" + H], ["LU" + H], lambda k, T: k.vector.tensor_scalar(T.WA[:, 8 * h:8 * h + 8], T.ACL[:, 8 * h:8 * h + 8], -16384.0, 18432.0, A.mult, A.add))
+                V(64, ["LU" + H, "LML" + H], ["LV" + H], lambda k, T: k.vector.tensor_tensor(T.WB[:, 8 * h:8 * h + 8], T.WA[:, 8 * h:8 * h + 8], T.LML[:, 8 * h:8 * h + 8], A.add))
+
+                def eq(m, a, b):
+                    return lambda k, T: k.vector.tensor_scalar(T.E[:, m, a - 16 * m:b - 16 * m], T.LAB[:, a:b], T.LML[:, m:m + 1], T.ACL[:, m:m + 1], A.is_equal, A.mult)
+                V(8 * 64 + 300 * (1 - h), ["LAB1", "LAB" + H, "LML" + H, "ACL" + H], ["E%d%d" % (h, h)], lambda k, T: [eq(m, 16 * m, 256)(k, T) for m in range(8 * h, 8 * h + 8)][-1])
+                V(256, ["E%d%d" % (h, h), "TRI"], ["E%d%d" % (h, h)], lambda k, T: k.vector.tensor_tensor(T.E[:, 8 * h:8 * h + 8, 0:16], T.E[:, 8 * h:8 * h + 8, 0:16], T.TRI[:, :, :], A.mult))
+                n = 256 - 128 * h
+                bk = "Q7.e" if h == 0 else "Q7.k"
+                P(1600 - 900 * h, ["E00", "BOS"] if h == 0 else ["E11", "BOS"], [bk],
+                  lambda k, T: [k.tensor.matmul(T.Q7[:, 256 * h + 16 * m:256 * h + n], T.BOS[:, :], T.E[:, 8 * h + m, 0:n - 16 * m], m == 0, m == 7) for m in range(8)][-1])
+                if h == 0:
+                    V(256, [bk, "MT0"], ["PT"], lambda k, T: [k.vector.tensor_tensor(T.PT[:, 128 * j:128 * j + 128], T.Q7[:, 128 * j:128 * j + 128], T.MT[:, 0:128], A.mult) for j in range(2)][-1])
+                else:
+                    V(128, [bk, "MT0"], ["PT"], lambda k, T: k.vector.tensor_tensor(T.PT[:, 0:128], T.Q7[:, 256:384], T.MT[:, 0:128], A.mult))
+                V(n, ["PT", "RS"], ["PS%d" % h], lambda k, T: k.vector.tensor_tensor_scan(T.PS[:, 256 * h:256 * h + n], T.RS[:, 0:n], T.PT[:, 0:n], 0.0, A.mult, A.add))
+                if h == 0:
+                    V(64, ["PS0", "LV0"], ["LW0"], lambda k, T: k.vector.tensor_tensor(T.WB[:, 0:8], T.WB[:, 0:8], T.PS[:, 15:128:16], A.add))
+                else:
+                    V(64, ["PS0", "LV1"], ["LV1"], lambda k, T: k.vector.tensor_tensor(T.WB[:, 8:16], T.WB[:, 8:16], T.PS[:, 143:256:16], A.add))
+                    V(64, ["PS1", "LV1"], ["LW1"], lambda k, T: k.vector.tensor_tensor(T.WB[:, 8:16], T.WB[:, 8:16], T.PS[:, 271:384:16], A.add))
+            stage2(t, h, str(h), "L%d%d" % (t, h), "Z%d%d" % (t, h))
+
+        V(64, ["LW0", "LW1", "CI2"], ["WC"], lambda k, T: k.vector.tensor_tensor(T.WC[:, :], T.WB[:, :], T.CI2[:, :], A.min))
+        ops[-1]["w"].extend(["LV0", "LV1"])
+        V(64, ["WC"], ["WO"], lambda k, T: k.vector.tensor_copy(T.WO[:, :], T.WC[:, :]))
+        op("v", 60 + 256 * 3.5 * CYC, ["WO", "SV0", "SV1"], RT, lambda k, T: k.vector.tensor_copy(T.R[:, :].indirect(T.WO[:, :]), T.SV[:, :]))
+    for b in range(8):
+        if b % 2:
+            V(512, ["R%d" % (b // 2)], ["R16%d" % b], (lambda b: lambda k, T: k.vector.tensor_copy(T.R16[:, 512 * b:512 * b + 512], T.R[:, 512 * b:512 * b + 512]))(b))
+        else:
+            V(512, ["R%d" % (b // 2)], ["R16%d" % b], (lambda b: lambda k, T: k.vector.tensor_copy(T.R16[:, 512 * b:512 * b + 512], T.R[:, 512 * b:512 * b + 512]))(b))
+    for b in range(8):
+        P(512, ["R16%d" % b, "ID16"], ["Q1"], (lambda b: lambda k, T: k.tensor.matmul(T.Q1[:, :], T.ID16[:, :], T.R16[:, 512 * b:512 * b + 512], b == 0, b == 7))(b))
+    V(512, ["Q1"], ["YR"], lambda k, T: k.vector.tensor_scalar(T.YR[:, :], T.Q1[:, :], 16384.0, None, A.add))
+    op("s", 50, ["YR"], ["yr"], lambda k, T: k.sync.dma_start(T.yr[:, :], T.YR[:, :]))
+    ops[-1]["s"] = ("do", 16)
+    return ops
+
+
+def callable_(x):
+    return not isinstance(x, (int, float))
+
+
+def edges(ops):
+    lastw, readers, bank = {}, {}, {}
+    for o in ops:
+        pre = set()
+        for k in o["r"]:
+            if k in lastw:
+                pre.add(lastw[k])
+        for k in o["w"]:
+            if k in lastw:
+                pre.add(lastw[k])
+            pre.update(readers.get(k, ()))
+        for b in set(k.split(".")[0] for k in o["r"] + o["w"] if k[0] == "Q"):
+            d = bank.setdefault(b, [None, [], []])
+            if d[0] != o["e"]:
+                d[0], d[1], d[2] = o["e"], [], d[1]
+            d[1].append(o["i"])
+            pre.update(d[2])
+        for k in o["r"]:
+            readers.setdefault(k, []).append(o["i"])
+        for k in o["w"]:
+            lastw[k] = o["i"]
+            readers[k] = []
+        pre.discard(o["i"])
+        o["pre"] = sorted(pre)
+
+
+def schedule(ops):
+    n = len(ops)
+    succ = [[] for _ in ops]
+    for o in ops:
+        for p in o["pre"]:
+            succ[p].append(o["i"])
+    tail = [0.0] * n
+    rnd = SEED
+    for o in reversed(ops):
+        tail[o["i"]] = o["c"] + max([tail[s] + DEP for s in succ[o["i"]]] or [0.0])
+    for i in range(n):
+        rnd = (rnd * 1103515245 + 12345) % 2147483648
+        tail[i] += ops[i]["p"] + SPREAD * (rnd // 65536) / 32768.0
+    left = [len(o["pre"]) for o in ops]
+    at = [0.0] * n
+    free = {}
+    ready = {}
+    order = {}
+    for o in ops:
+        if not left[o["i"]]:
+            ready.setdefault(o["e"], []).append(o["i"])
+    done = 0
+    end = [0.0] * n
+    while done < n:
+        best = None
+        for e, rs in ready.items():
+            if not rs:
+                continue
+            f = free.get(e, 0.0)
+            st = min(max(f, at[i]) for i in rs)
+            if best is None or st < best[0]:
+                best = (st, e)
+        st, e = best
+        cand = [i for i in ready[e] if max(free.get(e, 0.0), at[i]) <= st + 1e-9]
+        i = max(cand, key=lambda j: (tail[j], -j))
+        if e in ("s", "t"):
+            i = min(ready[e])
+        ready[e].remove(i)
+        o = ops[i]
+        s0 = max(free.get(e, 0.0), at[i])
+        end[i] = s0 + o["c"]
+        free[e] = s0 + (50 if e in ("s", "t", "x") else o["c"])
+        order.setdefault(e, []).append(i)
+        done += 1
+        for s in succ[i]:
+            left[s] -= 1
+            at[s] = max(at[s], end[i] + DEP)
+            if not left[s]:
+                ready.setdefault(ops[s]["e"], []).append(s)
+    seq = sorted(range(n), key=lambda i: (end[i] - ops[i]["c"], i))
+    return order, max(end)
+
+
+def rank_program(g, core, T, topo):
+    rank = T.rank_of(core)
+    if rank is None:
+        return
+    ops = plan()
+    edges(ops)
+    order, _ = schedule(ops)
+    queue = {"v": g.vector, "a": g.scalar, "p": g.tensor, "g": g, "s": g.sync, "t": g.scalar}
+    nxt = T.cores[(rank + 1) % N]
+    count = {}
+    seen = {}
+    for e, li in order.items():
+        c = 0
+        for i in li:
+            o = ops[i]
+            if "s" in o:
+                if o["s"][0] == "do":
+                    continue
+                count[i] = o["s"]
+            elif "send" in o:
+                count[i] = None
+            else:
+                c += 1
+                count[i] = (SEMOF[e], c)
+    total = {e: 0 for e in "vapg"}
+    known = {}
+    clock = {}
+
+    def merge(a, b):
+        for k, v in b.items():
+            if a.get(k, 0) < v:
+                a[k] = v
+
+    pos = {e: 0 for e in order}
+    lists_ = {e: list(li) for e, li in order.items()}
+    if "t" in lists_:
+        lists_["a"] = lists_["t"] + lists_["a"]
+        del lists_["t"]
+    pos = {e: 0 for e in lists_}
+    emitted = set()
+    do = 0
+    ls = 0
+    progress = True
+    while progress:
+        progress = False
+        for e in list(lists_):
+            while pos[e] < len(lists_[e]):
+                i = lists_[e][pos[e]]
+                o = ops[i]
+                if any(p not in emitted for p in o["pre"]):
+                    break
+                pos[e] += 1
+                progress = True
+                emitted.add(i)
+                if e == "x":
+                    clock[i] = {o["s"][0]: o["s"][1]}
+                    continue
+                q = queue[e]
+                kn = known.setdefault(e, {})
+                for p in sorted(o["pre"], reverse=True):
+                    po = ops[p]
+                    if po["e"] == "p" and e == "p":
+                        continue
+                    if po["e"] == "g" and "send" in po:
+                        continue
+                    sem, val = count[p]
+                    if kn.get(sem, 0) < val:
+                        q.wait_ge(T.sem[sem], val)
+                        merge(kn, clock[p])
+                        kn[sem] = max(kn.get(sem, 0), val)
+                if "send" in o:
+                    t, h = o["send"]
+                    rid, pid = topo.addr(nxt)[0:2]
+                    eng = topo.engines(core, nxt)
+                    ma = sum(1 << x for x in eng[0:4])
+                    mb = sum(1 << x for x in eng[4:8])
+                    dst = DstId(rid=rid, pnc=pid)
+                    arr = T.sem["ar%d%d" % (t + 1, h)]
+                    g.remote_dma_fused([
+                        RemoteDMATransfer(dst_ids=[dst], dma_engine_mask=ma, remote_sem=arr, src=T.SL[:, 2 * t + h, :], dst=T.LV[:, 2 * t + 2 + h, :]),
+                        RemoteDMATransfer(dst_ids=[dst], dma_engine_mask=mb, remote_sem=arr, src=T.SZ[:, 2 * t + h, :], dst=T.ZV[:, 2 * t + 2 + h, :]),
+                    ], local_sem=T.sem.ls)
+                    ls += 8
+                    continue
+                last = o["f"](g, T)
+                if "s" in o:
+                    sem, val = o["s"]
+                    if sem == "do":
+                        do += 16
+                    for x in (last if isinstance(last, tuple) else (last,)):
+                        x.then_inc(T.sem[sem], 16)
+                    clock[i] = dict(kn)
+                    clock[i][sem] = val
+                else:
+                    sem, val = count[i]
+                    last.then_inc(T.sem[sem], 1)
+                    total[e] += 1
+                    clock[i] = dict(kn)
+                    clock[i][sem] = val
+    g.wait_ge(T.sem.ls, ls)
+    g.sync.wait_ge(T.sem["do"], do)
+    for e in "vapg":
+        if total[e]:
+            queue[e].wait_ge(T.sem[SEMOF[e]], total[e])

@@ -1,698 +1,568 @@
+import numpy as np
 from concourse.bass import DstId, RemoteDMATransfer
 from concourse.mybir import AluOpType as A, ActivationFunctionType as F, AxisListType
 
-N, TV, W, M = 4, 5, 4096, 256
-CYC = 0.83
-SCRATCH = {
-    "X": ("sbuf", [128, 4096], "bfloat16"), "R": ("sbuf", [128, 4352], "float32"),
-    "LI": ("sbuf", [128, 256], "int32"), "THI": ("sbuf", [128, 8], "int32"), "THB": ("sbuf", [128, 8], "int32"), "TH": ("sbuf", [128, 8], "float32"),
-    "THN": ("sbuf", [128, 8], "float32"), "NF": ("sbuf", [128, 4], "float32"), "NI": ("sbuf", [128, 4], "int32"), "NM": ("sbuf", [128, 4], "float32"),
-    "ONEB": ("sbuf", [128, 256], "bfloat16"), "IDB": ("sbuf", [128, 128], "bfloat16"), "NIDB": ("sbuf", [128, 128], "bfloat16"),
-    "ID32": ("sbuf", [128, 128], "float32"), "ID16": ("sbuf", [128, 128], "float16"), "NID16": ("sbuf", [128, 128], "float16"), "BOF": ("sbuf", [128, 128], "bfloat16"),
-    "BO1": ("sbuf", [128, 8], "bfloat16"), "BOK": ("sbuf", [128, 16], "bfloat16"), "BOC": ("sbuf", [128, 8], "bfloat16"),
-    "BOD": ("sbuf", [128, 16], "bfloat16"), "BON": ("sbuf", [128, 16], "bfloat16"), "ONEB3": ("sbuf", [128, 16, 16], "bfloat16"),
-    "PB2": ("sbuf", [128, 16, 16], "bfloat16"), "PM2": ("sbuf", [128, 32, 16], "float16"), "IOT2": ("sbuf", [128, 16, 16], "float32"),
-    "PERM": ("sbuf", [128, 128], "bfloat16"), "PM": ("sbuf", [128, 256], "float16"), "SELB": ("sbuf", [128, 768], "bfloat16"),
-    "SEL": ("sbuf", [128, 768], "float16"), "RXB": ("sbuf", [128, 128], "bfloat16"), "RX": ("sbuf", [128, 128], "float16"),
-    "CKL": ("sbuf", [128, 128], "float16"), "CK1": ("sbuf", [128, 256], "float16"), "CK2": ("sbuf", [128, 32, 16], "float16"), "SELF": ("sbuf", [128, 256], "float16"),
-    "IOT": ("sbuf", [128, 128], "float32"), "CF": ("sbuf", [128, 128], "float32"), "PI": ("sbuf", [128, 4], "int32"),
-    "KC": ("sbuf", [128, 4], "float32"), "SC": ("sbuf", [128, 4], "float32"), "IJ": ("sbuf", [128, 640], "int32"), "MT": ("sbuf", [128, 640], "bfloat16"),
-    "CI": ("sbuf", [128, 16], "float32"), "CI2": ("sbuf", [128, 16], "float32"), "IOS": ("sbuf", [128, 8, 16], "float32"),
-    "TRI": ("sbuf", [128, 8, 16], "bfloat16"), "PT": ("sbuf", [128, 256], "float32"), "PS": ("sbuf", [128, 384], "float32"), "RS": ("sbuf", [128, 256], "float32"),
-    "BPD": ("sbuf", [128, 143], "bfloat16"), "BOS": ("sbuf", [128, 128], "bfloat16"), "ACL": ("sbuf", [128, 16], "float32"), "THC": ("sbuf", [128, 4], "float32"), "WC": ("sbuf", [128, 16], "float32"),
-    "ZERO": ("sbuf", [128, 256], "bfloat16"), "ONEF": ("sbuf", [128, 128], "float16"),
-    "LAB": ("sbuf", [128, 256], "float16"), "LML": ("sbuf", [128, 16], "float32"), "E": ("sbuf", [128, 16, 272], "bfloat16"),
-    "WA": ("sbuf", [128, 16], "float32"), "WB": ("sbuf", [128, 16], "float32"), "WO": ("sbuf", [128, 16], "uint16"),
-    "SV": ("sbuf", [128, 256], "float32"), "YL": ("sbuf", [128, 256], "float32"), "YR": ("sbuf", [128, 512], "float32"),
-    "R16": ("sbuf", [128, 4096], "float16"),
+N, TV = 4, 5
+CYC, PEC, GA, SCA, DEP = 0.83, 0.71, 1.5, 3.5, 100.0
+EW = 131
+B16, H16, F32, I32, U16 = "bfloat16", "float16", "float32", "int32", "uint16"
+SB = {
+    "X": ([4096], B16), "R": ([4352], F32), "R16": ([4096], H16), "LI": ([256], I32), "ZI": ([256], B16), "THI": ([8], I32), "THB": ([8], I32),
+    "LV": ([2 * TV, 136], U16), "ZV": ([2 * TV, 136], B16), "SL": ([2 * TV, 136], U16), "SZ": ([2 * TV, 136], B16),
+    "ONEB": ([256], B16), "IDB": ([128], B16), "NIDB": ([128], B16), "PID8": ([128], B16), "NID8": ([128], B16), "ID16": ([128], H16), "NID16": ([128], H16),
+    "ID32": ([128], F32), "HID16": ([128], H16), "PEN16": ([128], H16), "BOF": ([128], B16), "BOF16": ([128], H16), "NBOF16": ([128], H16), "BOFS16": ([128], H16),
+    "BPD": ([143], H16), "BOD": ([16], B16), "BON": ([16], B16), "BOC": ([8], B16), "BO1": ([8], F32), "SELB": ([128], B16), "SEL0": ([128], H16),
+    "RX": ([128], B16), "IK": ([256], F32), "PI": ([4], I32), "IM": ([144], I32), "MTW": ([144], B16), "IN": ([16], F32), "CO": ([24], F32),
+    "CL": ([2, 16], B16), "CK": ([512], B16), "CAPK": ([128], F32), "RST": ([256], F32), "RSTN": ([128], F32), "AQ": ([4, 128], B16), "BQ": ([128], B16),
+    "QM": ([6, 128], B16), "KEEP": ([8 * EW], H16), "DG": ([2, 16], H16), "DUM": ([8], F32), "TH": ([8], F32), "TH0": ([128], H16), "THT": ([128], H16),
+    "SN": ([128], B16), "SC2": ([128], B16), "NR": ([2], F32), "YL": ([256], F32), "YZ": ([256], B16), "YR": ([512], F32),
 }
 for _q in range(4):
-    SCRATCH["RI%d" % _q] = ("sbuf", [128, 1024], "int32")
-for _n, _d in (("LV", "uint16"), ("ZV", "bfloat16"), ("SL", "uint16"), ("SZ", "bfloat16")):
-    SCRATCH[_n] = ("sbuf", [128, 2 * TV + 2, 136], _d)
-PER_BLOCK = {
-    "XY": ([128, 2, 128], "float32"), "SVD": ([128, 128], "float32"), "LTA": ([128, 128], "float16"), "XG": ([128, 2048], "bfloat16"), "XA": ([128, 4096], "bfloat16"), "RG": ([128, 2048], "float32"), "CE": ([128, 2048], "bfloat16"),
-    "LP": ([128, 128], "float16"), "HM": ([128, 128], "float16"), "KC4": ([128, 384], "float32"),
-    "KT": ([128, 2, 128], "float32"), "T1": ([128, 4, 2, 64], "float32"), "KI": ([128, 4, 8], "int32"), "FT": ([128, 4, 64], "float32"),
-    "FI": ([128, 16], "int32"), "FF": ([128, 16], "float32"), "TA": ([128, 2, 8], "float32"), "KB": ([128, 128], "float32"),
-    "BA": ([128, 142], "float16"), "BE": ([128, 142], "float16"), "BM": ([128, 143], "float16"), "VT": ([128, 128], "float16"), "VTT": ([128, 128], "float16"),
-    "OL": ([128, 16], "uint16"), "RAB": ([128, 256], "float16"), "OF": ([128, 256], "uint16"), "HM2": ([128, 256], "float16"),
-    "KE": ([128, 2, 128], "float32"), "KJ": ([128, 2, 16], "int32"), "OE": ([128, 16], "uint16"), "XE": ([128, 256], "bfloat16"),
-    "XD": ([128, 128], "bfloat16"), "ZT": ([128, 128], "float16"), "SM": ([128, 4, 8], "float32"), "MM": ([128, 256], "float16"),
-    "P12": ([128, 256], "float16"), "P34": ([128, 256], "float16"),
-}
-_small = {}
-for _n, (_s, _d) in PER_BLOCK.items():
-    SCRATCH[_n] = ("sbuf", [128, 2] + _s[1:], _d)
-SCRATCH["AB"] = ("sbuf", [128, 4, 512], "bfloat16")
-SCRATCH["MX"] = ("sbuf", [128, 3, 512], "bfloat16")
-for _b in range(8):
-    SCRATCH["Q%d" % _b] = ("psum", [128, 512], "float32")
+    SB["RI%d" % _q] = ([1024], I32)
+for _n, (_s, _d) in {
+    "LP": ([128], H16), "XG": ([2048], B16), "MX": ([2048], B16), "RG": ([2048], F32), "CE": ([2048], B16), "XA": ([4096], B16), "MY": ([4096], B16),
+    "KS": ([256], F32), "M2": ([128], F32), "KF": ([512], F32), "M2F": ([128], F32), "FS": ([128], F32), "RR": ([48], F32), "BA": ([144], B16), "BE": ([144], B16),
+    "VT": ([128], B16), "VF": ([256], B16), "VTT": ([128], B16), "VTU": ([128], B16), "OL": ([16], U16), "OE": ([16], U16), "RAB": ([256], H16),
+    "XE": ([256], H16), "OF": ([256], U16), "S1": ([256], H16), "S2": ([256], H16), "LAB": ([128], F32), "LML": ([8], F32), "LABP": ([128], H16),
+    "SVA": ([128], F32), "SVB": ([128], F32), "NL": ([128], H16), "XD": ([128], B16), "RU": ([128], B16), "SG": ([128], B16), "CNT": ([2], F32),
+    "E": ([8 * EW], H16), "ES": ([8 * EW], H16), "WC": ([8], F32), "WO": ([8], U16),
+}.items():
+    SB[_n] = ([2] + _s, _d)
+SCRATCH = {_n: ("sbuf", [128] + _s, _d) for _n, (_s, _d) in SB.items()}
+BANKS = [_b + _h for _b in "ZKMN" for _h in "01"]
+for _b in BANKS:
+    SCRATCH[_b] = ("psum", [128, 512], F32)
 SEMAPHORES = ["sv", "sa", "sp", "sg", "dz", "dl", "dt", "ls", "do", "dx0", "dx1", "dr0", "dr1", "dr2", "dr3"] + ["ar%d%d" % (t, h) for t in range(1, TV) for h in range(2)]
 SEMOF = {"v": "sv", "a": "sa", "p": "sp", "g": "sg"}
-DEP = 100.0
-GA = 1.45
-S2V = ((3,), ())
-MAXV = {(1, 0): (1, 3), (1, 1): (), (2, 0): (0, 1, 2, 3, 4, 5, 6, 7), (2, 1): (0, 1, 2, 3, 4, 5, 6, 7)}
-PEC = 0.71
-BONUS = {"far0": -3000, "far1": -1000, "sum0": 4000, "sum1": -4000, "end0": 2000, "end1": -1000, "wr0": -3000, "wr1": -3500,
-         "one0": -1500, "one1": -1000, "prep": 0, "sel0": 1000, "sel1": 3000}
-KBA = True
-SVV = False
-RGA = (64, 112)
-KEA = (False, True)
-SEED, SPREAD = 1, 0.0
+HBM = ("xt", "z0", "ex", "l0", "th", "yl", "yz", "yr")
+s_ = np.s_
+C7, C6, C0 = 1.5 * 2.0 ** 30, 1.5 * 2.0 ** 29, 1.5 * 2.0 ** 23
+BIG = 2.0 ** 30
+RGP = (((("a", 0, 64), ("a", 64, 128)), ((0, 64), (64, 128))), ((("a", 0, 128),), ((0, 128),)))
+XAP = {(0, 0): (("a", 0, 64), ("a", 64, 128)), (0, 1): (("a", 0, 64), ("a", 64, 128)), (1, 0): (("a", 0, 64), ("a", 64, 128)), (1, 1): (("a", 0, 64), ("a", 64, 128))}
+BONUS = {'arr': -66000, 'cnt': 32000, 'conf0': 15000, 'conf1': 13000, 'end0': 7000, 'end1': 20500, 'far0': 19500, 'far1': 9500, 'init': 2500, 'late': 3000, 'new0': 47000, 'new1': 24000, 'prep0': 500, 'prep1': 19500, 'prew0': 14000, 'prew1': 11000, 'sel0': 37500, 'sel1': 15500, 'sum': 39500, 'two0': 13500, 'two1': 2500, 'wr0': -22500, 'wr1': 74500}
+
+
+def sb(name, *idx):
+    return (name, (slice(None),) + idx)
+
+
+def pt(name, p, *idx):
+    return (name, (p,) + idx)
+
+
+def ind(win, off):
+    return ("@", win, off)
+
+
+def isap(x):
+    return isinstance(x, tuple) and isinstance(x[0], str)
+
+
+def shape_of(name):
+    return SCRATCH[name][1]
+
+
+CELLS = {}
+
+
+def cells(ap):
+    key = (ap[0], str(ap[1]))
+    if key not in CELLS:
+        sh = shape_of(ap[0])[1:]
+        m = np.zeros(sh, bool)
+        m[ap[1][1:]] = True
+        CELLS[key] = (int(m.sum()), int.from_bytes(np.packbits(m.reshape(-1)).tobytes(), "big"))
+    return CELLS[key]
+
+
+def two(ap):
+    return SCRATCH[ap[0]][2] in (B16, H16, U16)
+
+
+def cost(e, c):
+    k, out = c[0], c[1]
+    if k == "mm":
+        return max(min(64, cells(c[2])[0]), cells(c[3])[0]) * PEC * (1 if two(c[2]) else 4)
+    if out[0] == "@":
+        return 50 + 16 * cells(out[2])[0] * SCA * CYC
+    n = cells(out)[0]
+    if e == "g":
+        return 170 + 2 * n * CYC
+    if k != "memset" and c[2][0] == "@":
+        return 60 + n * GA * CYC
+    if e == "a":
+        return 20 + max(64, n) * CYC
+    if k == "tt":
+        f = 1 if c[2][0] in BANKS or c[3][0] in BANKS else 2
+    elif k == "red":
+        n, f = cells(c[2])[0], 1
+    else:
+        f = 0.5 if all(two(x) for x in ((out,) if k == "memset" else c[1:4] if k == "scan" else c[1:3])) else 1
+    return 5 + max(64, n * f) * CYC
 
 
 def plan():
-    ops = []
+    ops, sec, vis = [], ["init"], [0]
 
-    sec = [""]
+    def op(e, calls, **kw):
+        o = {"e": e, "calls": calls, "i": len(ops), "t": vis[0], "sec": sec[0]}
+        o["c"] = kw.pop("c") if "c" in kw else sum(cost(e, c) for c in calls)
+        o.update(kw)
+        ops.append(o)
 
-    def op(eng, cost, reads, writes, fn):
-        ops.append({"e": eng, "c": cost, "r": reads, "w": writes, "f": fn, "p": BONUS.get(sec[0], 0.0), "i": len(ops)})
+    def V(*calls):
+        op("v", list(calls))
 
-    def V(n, reads, writes, fn):
-        op("v", max(64, n) * CYC, reads, writes, fn)
+    def S(*calls):
+        op("a", list(calls))
 
-    def AC(n, reads, writes, fn):
-        op("a", 20 + max(64, n) * CYC, reads, writes, fn)
+    def G(*calls):
+        op("g", list(calls))
 
-    def P(n, reads, writes, fn):
-        op("p", n * PEC, reads, writes, fn)
+    def P(out, pairs, start=True, stop=True):
+        return [("mm", out, l, r, start and j == 0, stop and j == len(pairs) - 1) for j, (l, r) in enumerate(pairs)]
 
-    def gather(eng, n, reads, writes, fn):
-        op(eng, 55 + GA * n * CYC, reads, writes, fn)
+    def PE(*groups):
+        op("p", [c for gr in groups for c in gr])
 
-    def G(n, reads, writes, fn):
-        op("g", 170 + 2 * n * CYC, reads, writes, fn)
+    def ts(o, i, s1, o0, s2=None, o1=None):
+        return ("ts", o, i, s1, s2, o0, o1)
 
-    def load(q, sem, cost, writes, fn):
-        op(q, cost, [], writes, fn)
-        ops[-1]["s"] = (sem, 16)
-    load("s", "dl", 2500, ["LI"], lambda k, T: k.sync.dma_start(T.LI[:, :], T.l0[:, :]))
-    load("s", "dx0", 3500, ["Xa"], lambda k, T: k.sync.dma_start(T.X[:, 0:2048], T.xt[:, 0:2048]))
-    load("t", "dx1", 3500, ["Xb"], lambda k, T: k.scalar.dma_start(T.X[:, 2048:4096], T.xt[:, 2048:4096]))
-    load("s", "dz", 4000, ["Z00", "Z01"], lambda k, T: (k.sync.dma_start(T.ZV[:, 0, 0:128], T.z0[:, 0:128]), k.sync.dma_start(T.ZV[:, 1, 0:128], T.z0[:, 128:256])))
-    ops[-1]["s"] = ("dz", 32)
+    def act(o, i, f, bias=0.0, scale=1.0, acc=None):
+        return ("act", o, i, f, bias, scale, acc)
+
+    def col(j):
+        return sb("CO", s_[j:j + 1])
+
+    al = s_[:]
+    def load(q, sem, c, out, src):
+        op(q, [("dma", out, src)], c=c, s=(sem, 16))
+    load("s", "dl", 2500, sb("LI", al), ("l0", s_[:, :]))
+    load("s", "dx0", 3500, sb("X", s_[0:2048]), ("xt", s_[:, 0:2048]))
+    load("t", "dx1", 3500, sb("X", s_[2048:4096]), ("xt", s_[:, 2048:4096]))
+    load("s", "dz", 4000, sb("ZI", al), ("z0", s_[:, :]))
     for q in range(4):
-        load("s" if q % 2 else "t", "dr%d" % q, 6000 + 1500 * q, ["RI%d" % q],
-             (lambda q: lambda k, T: (k.sync if q % 2 else k.scalar).dma_start(T["RI%d" % q][:, :], T.ex[:, 1024 * q:1024 * q + 1024]))(q))
-    load("s", "dt", 9000, ["THI"], lambda k, T: k.sync.dma_start(T.THI[0:1, :], T.th[:, :]))
+        load("s" if q % 2 else "t", "dr%d" % q, 6000 + 1500 * q, sb("RI%d" % q, al), ("ex", s_[:, 1024 * q:1024 * q + 1024]))
+    load("s", "dt", 9000, pt("THI", s_[0:1], al), ("th", s_[:, :]))
 
-    V(128, [], ["ONEB"], lambda k, T: k.vector.memset(T.ONEB[:, :], 1.0))
-    V(256, ["LI"], ["L00", "L01"], lambda k, T: (k.vector.tensor_copy(T.LV[:, 0, 0:128], T.LI[:, 0:128]), k.vector.tensor_copy(T.LV[:, 1, 0:128], T.LI[:, 128:256]))[-1])
-    V(1400, [], ["SLP"], lambda k, T: k.vector.memset(T.SL[:, :, :], 0))
-    V(700, [], ["SZP"], lambda k, T: k.vector.memset(T.SZ[:, :, :], 0.0))
-    G(128, ["ONEB"], ["IDB"], lambda k, T: k.affine_select(T.IDB[:, :], T.ONEB[:, 0:128], [[-1, 128]], A.is_equal, 0.0, 0, 1))
-    G(128, ["ONEB"], ["PERM"], lambda k, T: k.affine_select(T.PERM[:, :], T.ONEB[:, 0:128], [[-1, 16], [-16, 8]], A.is_equal, 0.0, 0, 1))
-    G(128, ["ONEB"], ["BOF"], lambda k, T: k.affine_select(T.BOF[:, :], T.ONEB[:, 0:128], [[-16, 8], [0, 16]], A.is_ge, 0.0, 0, 1))
-    G(128, ["BOF"], ["BOF"], lambda k, T: k.affine_select(T.BOF[:, :], T.BOF[:, :], [[16, 8], [0, 16]], A.is_ge, 0.0, 15, -1))
-    for s in range(6):
-        G(128, ["ONEB"], ["SELB%d" % s], (lambda s: lambda k, T: k.affine_select(T.SELB[:, 128 * s:128 * s + 128], T.ONEB[:, 0:128], [[-16, 8], [0, 16]], A.is_equal, 0.0, -s, 1))(s))
-    G(128, [], ["IOT"], lambda k, T: k.iota(T.IOT[:, :], [[64, 16], [0, 8]], 0, 0, allow_small_or_imprecise_dtypes=True))
-    G(256, [], ["IOT2"], lambda k, T: k.iota(T.IOT2[:, :, :], [[64, 16], [0, 16]], 0, 0, allow_small_or_imprecise_dtypes=True))
-    G(256, ["ONEB"], ["PB2"], lambda k, T: k.affine_select(T.PB2[:, :, :], T.ONEB3[:, :, :], [[-1, 16], [0, 2], [-16, 8]], A.is_equal, 0.0, 0, 1))
-    ops[-1]["r"] = ["ONEB3"]
-    V(256, [], ["ONEB3"], lambda k, T: k.vector.memset(T.ONEB3[:, :, :], 1.0))
-    ops[-1], ops[-2] = ops[-2], ops[-1]
-    ops[-1]["i"], ops[-2]["i"] = len(ops) - 1, len(ops) - 2
-    G(128, ["ONEB"], ["RXB"], lambda k, T: k.affine_select(T.RXB[:, :], T.ONEB[:, 0:128], [[-1, 8], [-8, 16]], A.is_equal, 0.0, 0, 1))
-    G(4, [], ["PI"], lambda k, T: k.iota(T.PI[:, :], [[0, 4]], 0, 1))
-    G(16, [], ["CI"], lambda k, T: k.iota(T.CI[:, :], [[16, 16]], 2048, 0, allow_small_or_imprecise_dtypes=True))
-    G(128, [], ["IOS"], lambda k, T: k.iota(T.IOS[:, :, :], [[0, 8], [1, 16]], 0, 0, allow_small_or_imprecise_dtypes=True))
-    for t in range(TV):
-        G(128, [], ["IJ%d" % t], (lambda t: lambda k, T: k.iota(T.IJ[:, 128 * t:128 * t + 128], [[1, 128]], 128 + t, -1))(t))
-    G(8, ["THI"], ["THB"], lambda k, T: k.partition_broadcast(T.THB[:, :], T.THI[0:1, :], 128))
-    cp = lambda o, i: (lambda k, T: k.vector.tensor_copy(o(T), i(T)))
-    ts = lambda o, i, s1, s2, o0, o1=None: (lambda k, T: k.vector.tensor_scalar(o(T), i(T), s1(T) if callable_(s1) else s1, s2, o0, o1) if o1 is not None
-                                            else k.vector.tensor_scalar(o(T), i(T), s1(T) if callable_(s1) else s1, None, o0))
-    tt = lambda o, x, y, f: (lambda k, T: k.vector.tensor_tensor(o(T), x(T), y(T), f))
-    V(64, ["IDB"], ["NIDB"], ts(lambda T: T.NIDB[:, :], lambda T: T.IDB[:, :], -1.0, None, A.mult))
-    AC(128, ["IDB"], ["ID32"], lambda k, T: k.scalar.activation(T.ID32[:, :], T.IDB[:, :], F.Copy))
-    V(64, ["IDB"], ["ID16"], cp(lambda T: T.ID16[:, :], lambda T: T.IDB[:, :]))
-    V(64, ["IDB"], ["NID16"], cp(lambda T: T.NID16[:, :], lambda T: T.NIDB[:, :]))
-    ops[-1]["r"] = ["NIDB"]
-    for nm, x in (("BO1", 1.0), ("BOK", 1024.0), ("BOC", 8388608.0), ("BOD", 2048.0), ("BON", -1024.0)):
-        V(128, ["BOF"], [nm], (lambda nm, x: lambda k, T: [k.vector.tensor_scalar(T[nm][:, c:c + 8], T.BOF[:, 0::16], x, None, A.mult) for c in ((0, 8) if nm in ("BOK", "BOD", "BON") else (0,))][-1])(nm, x))
-    V(128, [], ["CK2"], lambda k, T: k.vector.memset(T.CK2[:, :, :], 0.0))
-    V(128, ["CK2", "IOT2"], ["CK2"], lambda k, T: [k.vector.tensor_copy(T.CK2[0:1, c:c + 16, :], T.IOT2[0:1, :, :]) for c in (0, 16)][-1])
-    V(256, ["CK2", "IOT2"], ["CK2"], lambda k, T: ([k.vector.tensor_scalar(T.CK2[0:1, c:c + 16, 0:8], T.IOT2[0:1, :, 0:8], -1025.0, None, A.add) for c in (0, 16)],
-                                             k.vector.memset(T.CK2[32:33, :, 8:16], 33824.0), k.vector.memset(T.CK2[64:65, :, 8:16], 33824.0))[-1])
-    V(256, ["PB2"], ["PM2"], lambda k, T: (k.vector.tensor_copy(T.PM2[:, 0:16, 0:8], T.PB2[:, :, 0:8]), k.vector.tensor_scalar(T.PM2[:, 0:16, 8:16], T.PB2[:, :, 8:16], -64.0, None, A.mult),
-                                       k.vector.memset(T.PM2[:, 16:32, 0:8], 0.0), k.vector.tensor_copy(T.PM2[:, 16:32, 8:16], T.PB2[:, :, 8:16]))[-1])
-    V(64, ["PERM"], ["PMa"], cp(lambda T: T.PM[:, 0:128], lambda T: T.PERM[:, :]))
-    V(64, ["PERM"], ["PMb"], ts(lambda T: T.PM[:, 128:256], lambda T: T.PERM[:, :], -64.0, None, A.mult))
-    for s in range(6):
-        V(64, ["SELB%d" % s], ["SEL%d" % s], cp((lambda s: lambda T: T.SEL[:, 128 * s:128 * s + 128])(s), (lambda s: lambda T: T.SELB[:, 128 * s:128 * s + 128])(s)))
-    V(64, [], ["SEL4"], lambda k, T: k.vector.memset(T.SEL[:, 512:640:16], 0.0))
-    V(128, [], ["BPD"], lambda k, T: k.vector.memset(T.BPD[:, :], 0.0))
-    V(64, ["BOF", "BPD"], ["BPD"], lambda k, T: k.vector.tensor_copy(T.BPD[:, 15::16], T.BOF[:, 0::16]))
-    V(64, ["BOF"], ["BOS"], lambda k, T: k.vector.tensor_scalar(T.BOS[:, :], T.BOF[:, :], 8192.0, None, A.mult))
-    V(256, [], ["RS"], lambda k, T: k.vector.memset(T.RS[:, :], 1.0))
-    V(64, ["RS"], ["RS"], lambda k, T: k.vector.memset(T.RS[:, 0::16], 0.0))
-    V(128, ["SELB4"], ["SELF"], lambda k, T: [k.vector.tensor_scalar(T.SELF[:, 128 * v:128 * v + 128], T.SELB[:, 512:640], 32.0, None, A.mult) for v in range(2)][-1])
-    V(256, ["SELF", "SELB2", "SELB3"], ["SELF"], lambda k, T: k.vector.tensor_tensor(T.SELF[:, :], T.SELF[:, :], T.SELB[:, 256:512], A.add))
-    V(64, ["RXB"], ["RX"], cp(lambda T: T.RX[:, :], lambda T: T.RXB[:, :]))
-    V(64, [], ["CKL"], lambda k, T: k.vector.memset(T.CKL[:, :], 0.0))
-    V(64, ["CKL"], ["CKL"], lambda k, T: [k.vector.memset(T.CKL[b:b + 1, :], x) for b, x in ((0, 1.0), (32, 1.0), (64, 1.0), (96, 256.0))][-1])
-    for nm in ("CK1",):
-        g_ = (lambda nm: lambda T: T[nm])(nm)
-        V(128, [], [nm], (lambda g_: lambda k, T: k.vector.memset(g_(T)[:, :], 0.0))(g_))
-        V(128, [nm, "IOT"], [nm], (lambda g_: lambda k, T: (k.vector.tensor_scalar(g_(T)[0:1, 0:128], T.IOT[0:1, :], -1025.0, None, A.add),
-                                                       k.vector.tensor_copy(g_(T)[0:1, 128:256], T.IOT[0:1, :]),
-                                                       k.vector.memset(g_(T)[32:33, 128:256], 33824.0), k.vector.memset(g_(T)[64:65, 128:256], 33824.0))[-1])(g_))
-    V(128, ["CK1"], ["CK1"], lambda k, T: (k.vector.memset(T.CK1[96:97, 0:8], 49152.0), k.vector.memset(T.CK1[96:97, 128:136], 49152.0))[-1])
-    V(128, ["IOT"], ["CF"], ts(lambda T: T.CF[:, :], lambda T: T.IOT[:, :], -1.0, 1024.0, A.mult, A.add))
-    V(64, ["CF"], ["CF"], lambda k, T: k.vector.memset(T.CF[:, 0:8], -8388608.0))
-    V(64, ["PI"], ["PI"], ts(lambda T: T.PI[:, :], lambda T: T.PI[:, :], 15, None, A.bitwise_and))
-    V(64, ["PI"], ["SC"], cp(lambda T: T.SC[:, :], lambda T: T.PI[:, :]))
-    V(64, ["SC"], ["KC"], ts(lambda T: T.KC[:, :], lambda T: T.SC[:, :], -1.0, 16.0, A.mult, A.add))
-    V(64, ["CI", "SC"], ["CI"], ts(lambda T: T.CI[:, :], lambda T: T.CI[:, :], lambda T: T.SC[:, 0:1], None, A.add))
-    V(64, ["CI"], ["CI2"], ts(lambda T: T.CI2[:, :], lambda T: T.CI[:, :], 2048.0, None, A.add))
-    V(512, ["IOS", "SC"], ["TRI"], lambda k, T: [k.vector.tensor_scalar(T.TRI[:, m, :], T.IOS[:, m, :], T.SC[:, 0:1], None, A.is_gt) for m in range(8)][-1])
-    for t in range(TV):
-        sl = (lambda t: slice(128 * t, 128 * t + 128))(t)
-        V(128, ["IJ%d" % t], ["IJ%d" % t], (lambda sl: ts(lambda T: T.IJ[:, sl], lambda T: T.IJ[:, sl], 15, None, A.bitwise_and))(sl))
-        V(128, ["IJ%d" % t], ["MT%d" % t], (lambda sl: ts(lambda T: T.MT[:, sl], lambda T: T.IJ[:, sl], 0.0, None, A.is_equal))(sl))
-    V(128, [], ["ZERO"], lambda k, T: k.vector.memset(T.ZERO[:, :], 0.0))
-    V(64, [], ["ONEF"], lambda k, T: k.vector.memset(T.ONEF[:, :], 1.0))
-    V(256, [], ["Rd"], lambda k, T: k.vector.memset(T.R[:, 4096:4352], 0.0))
-    for nm in ("BA", "BE", "BM", "VT"):
-        V(128, [], [nm + "0", nm + "1"], (lambda nm: lambda k, T: k.vector.memset(T[nm][:, :, :], 0.0))(nm))
+    ms = lambda o, x: ("memset", o, x)
+    one = sb("ONEB", s_[0:128])
+    V(ms(sb("ONEB", al), 1.0))
+    rev = (s_[255:127:-1], s_[127::-1])
+    for h in range(2):
+        V(("copy", sb("LV", h, s_[0:128]), sb("LI", rev[h])))
+        V(("copy", sb("ZV", h, s_[0:128]), sb("ZI", rev[h])))
+    G(("asel", sb("IDB", al), one, [[-1, 128]], A.is_equal, 0.0, 0, 1))
+    G(("asel", sb("BOF", al), one, [[-16, 8], [0, 16]], A.is_ge, 0.0, 0, 1))
+    G(("asel", sb("BOF", al), sb("BOF", al), [[16, 8], [0, 16]], A.is_ge, 0.0, 15, -1))
+    G(("asel", sb("SELB", al), one, [[-16, 8], [0, 16]], A.is_equal, 0.0, 0, 1))
+    G(("iota", sb("IK", al), [[0, 16], [1, 16]], 0, 0))
+    G(("iota", sb("PI", al), [[0, 4]], 0, 1))
+    G(("asel", sb("RX", al), one, [[-1, 8], [-8, 16]], A.is_equal, 0.0, 0, 1))
+    G(("iota", sb("IN", al), [[128, 16]], 0, 0))
+    G(("iota", sb("IM", al), [[1, 144]], 1, 1))
+    G(("pbc", sb("THB", al), pt("THI", s_[0:1], al), 128))
+    for nm, src, x in (("ID16", "IDB", 1.0), ("ID32", "IDB", 1.0), ("NID16", "IDB", -1.0), ("HID16", "IDB", 0.5 - 2.0 ** -12), ("PEN16", "IDB", -512.0), ("NIDB", "IDB", -1.0),
+                       ("PID8", "IDB", 8192.0), ("NID8", "IDB", -8192.0), ("SEL0", "SELB", 1.0), ("BOF16", "BOF", 1.0), ("NBOF16", "BOF", -1.0),
+                       ("BOFS16", "BOF", 2.0 ** -13)):
+        V(ts(sb(nm, al), sb(src, al), x, A.mult))
+    b8 = sb("BOF", s_[0::16])
+    V(ms(sb("BPD", al), 0.0))
+    V(ts(sb("BPD", s_[15::16]), b8, 2.0 ** -13, A.mult))
+    V(*[ts(sb(nm, s_[c:c + 8]), b8, x, A.mult) for nm, x in (("BOD", 256.0), ("BON", -128.0)) for c in (0, 8)])
+    V(ts(sb("BOC", al), b8, 2.0 ** 21, A.mult), ("copy", sb("BO1", al), b8))
+    V(ts(sb("PI", s_[0:1]), sb("PI", s_[0:1]), 15, A.bitwise_and), ts(sb("PI", s_[1:2]), sb("PI", s_[1:2]), 14, A.bitwise_and),
+      ts(sb("PI", s_[2:3]), sb("PI", s_[2:3]), 1, A.bitwise_and))
+    V(("copy", col(0), sb("PI", s_[0:1])), ts(col(4), sb("PI", s_[1:2]), 8.0, A.mult), ts(col(5), sb("PI", s_[2:3]), 2048.0, A.mult))
+    V(*[ts(col(1 + j), col(0), float(j), A.is_equal) for j in range(3)])
+    V(ts(col(6), col(0), 6.0, A.is_equal, 2.0, A.mult), ts(col(8), col(0), 2.0 ** -12, A.mult, 0.25, A.add))
+    V(ts(col(6), col(6), -1.0, A.add), ts(col(7), col(1), 2.0 ** 26, A.mult))
+    V(ts(sb("CL", 0, al), sb("IN", al), col(4), A.add), ts(sb("CL", 1, al), sb("IN", al), col(4), A.add, col(5), A.add))
+    V(ts(sb("DUM", al), sb("IN", s_[0:8]), 2.0 ** -15, A.mult, col(8), A.add))
+    r0, r32, r64 = s_[0:1], s_[32:33], s_[64:65]
+    V(ms(pt("CK", s_[0:64], al), 0.0))
+    V(("copy", pt("CK", r0, s_[0:128]), pt("IK", r0, s_[0:128])), ts(pt("CK", r0, s_[128:256]), pt("IK", r0, s_[0:128]), -1.0, A.mult, 15.0, A.add),
+      ("copy", pt("CK", r0, s_[256:512]), pt("IK", r0, al)), ms(pt("CK", r32, s_[0:128:16]), 2.0 ** 21), ms(pt("CK", r32, s_[128:256]), -2.0 ** 22))
+    V(ms(pt("CK", r32, s_[128:256:16]), -2.0 ** 23))
+    V(ts(sb("CAPK", al), sb("IK", s_[0:128]), 2.0 ** 20, A.add))
+    V(ms(sb("CAPK", s_[0::16]), 1.5 * 2.0 ** 20))
+    V(ms(sb("RST", al), -BIG), ms(sb("RSTN", al), BIG))
+    V(ms(sb("RST", s_[0::16]), BIG), ms(sb("RSTN", s_[0::16]), -BIG), ms(sb("M2", al, s_[0:1]), BIG), ms(sb("M2F", al, s_[0:1]), -BIG))
+    V(ts(sb("IM", al), sb("IM", al), 15, A.bitwise_and))
+    V(ts(sb("MTW", al), sb("IM", al), 0.0, A.is_equal))
+    for nm in ("BA", "BE", "VT", "VF"):
+        V(ms(sb(nm, al, al), 0.0))
+    V(ms(sb("VT", al, s_[4::16]), 1.0), ms(sb("VF", al, s_[4:128:16]), 1.0), ms(sb("VF", al, s_[6:128:16]), 1.0))
+    V(ms(sb("R", s_[4096:4352]), 0.0), ms(sb("SL", al, s_[128:136]), 0), ms(sb("SZ", al, s_[128:136]), 0.0))
+    sec[0] = "late"
+    V(ms(pt("AQ", s_[0:96], al, al), 0.0), ms(pt("BQ", s_[0:96], al), 0.0))
+    q8 = 8192.0
+    V(*[ms(pt("AQ", r, m, s_[sl::16]), x) for r, m, sl, x in (
+        (r0, 0, 0, 2 * q8), (r0, 1, 1, 2 * q8), (r64, 0, 2, -q8), (r64, 1, 3, -q8), (r32, s_[0:2], 4, -q8),
+        (r0, 2, 9, 2 * q8), (r0, 3, 11, 2 * q8), (r0, s_[2:4], 4, -30 * q8), (r32, s_[2:4], 4, q8), (r64, 2, 9, -30 * q8), (r64, 3, 11, -30 * q8),
+        (r64, 2, 13, q8), (r64, 3, 15, q8), (r64, s_[2:4], 4, 225 * q8), (r64, s_[2:4], 6, 61440.0))])
+    V(("copy", pt("BQ", r0, al), pt("IK", r0, s_[0:128])), ("tt", pt("BQ", r32, al), pt("IK", r32, s_[0:128]), pt("IK", r32, s_[0:128]), A.mult), ms(pt("BQ", r64, al), 1.0))
+    PE(*[P(sb("M1", s_[128 * m:128 * m + 128]), [(pt("AQ", s_[0:96], m, al), pt("BQ", s_[0:96], al))]) for m in range(4)])
+    V(*[("tt", sb("QM", m, al), sb("M1", s_[128 * m:128 * m + 128]), sb("BOF", al), A.mult) for m in range(4)])
+    V(*[ts(sb("QM", 2 + m, al), sb("QM", m, al), col(6), A.mult) for m in (2, 3)])
+    V(ms(sb("KEEP", al), 1.0))
+    V(ms(sb("E", al, al), 0.0))
+    V(ms(sb("E", al, s_[129::EW]), 1.0), ms(sb("KEEP", s_[0::EW + 16]), 0.0))
+    V(ts(sb("DG", 0, al), sb("IK", s_[0:16]), col(0), A.is_gt), ts(sb("DG", 1, al), sb("IK", s_[0:16]), col(0), A.is_equal))
+    V(*[("tt", sb("KEEP", s_[(EW + 16) * m + 1:(EW + 16) * m + 17]), sb("DG", 0, al), sb("DG", 1, al), A.subtract) for m in range(8)])
+    V(("copy", sb("TH", al), sb("THB", al)))
+    V(("tt", sb("TH", al), sb("TH", al), sb("BO1", al), A.mult))
+    V(("red", col(9), sb("TH", al), A.add))
+    V(ts(col(10), col(9), C6, A.add, -C6, A.add))
+    V(("tt", col(11), col(9), col(10), A.subtract), ("tt", col(12), col(10), col(1), A.mult))
+    V(ts(col(11), col(11), -0.5, A.add, col(2), A.mult), ts(col(12), col(3), 31.5, A.mult, col(12), A.add))
+    V(ts(sb("TH0", al), one, col(11), A.mult, col(12), A.add))
+    V(ms(sb("SN", al), 0.0), ms(pt("SC2", r0, al), 0.0))
+    V(ts(sb("SN", s_[2::16]), sb("ONEB", s_[0:8]), col(2), A.mult, -0.5, A.mult), ms(pt("SC2", r0, s_[2::16]), -31.5))
+    sec[0] = "init"
     for q in range(4):
-        V(1024, ["RI%d" % q], ["R%d" % q], (lambda q: ts(lambda T: T.R[:, 1024 * q:1024 * q + 1024], lambda T: T["RI%d" % q][:, :], -2048.0, None, A.add))(q))
-    V(64, ["THB"], ["TH"], cp(lambda T: T.TH[:, :], lambda T: T.THB[:, :]))
-    V(64, ["TH", "BO1"], ["THN"], lambda k, T: k.vector.tensor_tensor(T.THN[:, :], T.TH[:, :], T.BO1[:, :], A.mult))
-    V(64, ["THN"], ["THC0"], lambda k, T: k.vector.tensor_reduce(T.THC[:, 0:1], T.THN[:, :], AxisListType.X, A.add))
-    RT = ["R0", "R1", "R2", "R3", "Rd"]
-    XT = ["Xa", "Xb"]
-    nab = [0]
+        V(ts(sb("R", s_[1024 * q:1024 * q + 1024]), sb("RI%d" % q, al), -2048.0, A.add))
+    IDB, ID16, NID16 = sb("IDB", al), sb("ID16", al), sb("NID16", al)
+    XW, RW = sb("X", al), sb("R", al)
+    ones33 = pt("ONEB", s_[0:33], s_[0:128])
 
-    nmx = [0]
-    P(64, ["IDB", "ZERO"], ["Q3.z"], lambda k, T: k.tensor.matmul(T.Q3[:, 0:8], T.IDB[:, :], T.ZERO[:, 0:8], True, True))
+    def lists(bank, c0, which, tile, h):
+        out = sb(bank, s_[c0:c0 + 16])
+        return P(out, [(IDB, sb("CL", which, al))] + [(sb(tile, h, s_[14 - 2 * x:142 - 2 * x]), sb("RX", s_[16 * x:16 * x + 16])) for x in range(8)])
 
-    def subsum(t, h, which, x3, base, zk, bo_out, reads, vmax=False):
-        b = nab[0] % 2
-        a4 = nab[0] % 4
-        nab[0] += 1
-        bank = "Q%d" % (1 + b)
+    def first(t, h):
+        H, li = str(h), 2 * t + h
+        Z, K, M, Nb = "Z" + H, "K" + H, "M" + H, "N" + H
+        mt = sb("MTW", s_[16 - t:144 - t])
+        LP = sb("LP", h, al)
+        sec[0] = "prep" + H
+        V(ts(LP, sb("LV", li, s_[0:128]), -2048.0, A.add))
+        PE(P(sb(Z, s_[0:128]), [(IDB, sb("ZV", li, s_[0:128]))]), P(sb(Z, s_[128:256]), [(sb("SEL0", al), LP)]))
+        S(act(sb("XG", h, al), ind(XW, sb("LV", li, s_[0:128])), F.Copy))
+        PE(P(sb(K, s_[0:256]), [(ones33, pt("CK", s_[0:33], s_[0:256]))], True, False))
+        for rows in ((1, 2, 3), (4, 5, 6, 7), (8, 9, 10, 11), (12, 13, 14, 15)):
+            V(*[("tt", sb("MX", h, s_[128 * k:128 * k + 128]), sb("XG", h, s_[k::16]), sb(Z, s_[0:128]), A.max) for k in rows])
+            PE(*[P(sb(K, s_[k:256:16]), [(sb("XG", h, s_[k::16]), sb("BON", al)), (sb("MX", h, s_[128 * k:128 * k + 128]), sb("BOD", al))], False, False) for k in rows])
+        sec[0] = "conf" + H
+        for e, a, b in RGP[h][0]:
+            o, i = sb("RG", h, s_[16 * a:16 * b]), ind(RW, sb("LV", li, s_[a:b]))
+            S(act(o, i, F.Copy)) if e == "a" else V(("copy", o, i))
+        for n_, (a, b) in enumerate(RGP[h][1]):
+            last = n_ == len(RGP[h][1]) - 1
+            for rows in (((1, 2, 3, 4, 5), (6, 7, 8, 9, 10), (11, 12, 13), (14, 15)) if last else (tuple(range(1, 16)),)):
+                V(*[("tt", sb("CE", h, s_[128 * k + a:128 * k + b]), sb("RG", h, s_[16 * a + k:16 * b:16]), sb(Z, s_[128 + a:128 + b]), A.is_equal) for k in rows])
+                if last:
+                    PE(*[P(sb(K, s_[k:128:16]), [(sb("CE", h, s_[128 * k:128 * k + 128]), sb("BOC", al))], False, k == 15) for k in rows])
+        sec[0] = "sel" + H
+        V(("tt", sb(K, s_[0:128]), sb(K, s_[0:128]), sb("CAPK", al), A.min))
+        V(("scan", sb("KS", h, s_[0:128]), sb("RST", s_[0:128]), sb(K, s_[0:128]), A.max, A.min))
+        V(("tt", sb("M2", h, s_[1:128]), sb(K, s_[1:128]), sb("KS", h, s_[0:127]), A.max))
+        V(("scan", sb("KS", h, s_[128:256]), sb("RST", s_[0:128]), sb("M2", h, al), A.max, A.min))
+        V(ts(sb("RR", h, s_[0:16]), sb("KS", h, s_[15::16]), C7, A.add, -C7, A.add))
+        V(*[("tt", sb("BA", h, s_[14 + v:142:16]), sb("KS", h, s_[128 * v + 15:128 * v + 128:16]), sb("RR", h, s_[8 * v:8 * v + 8]), A.subtract) for v in range(2)])
+        PE(lists(M, 0, 0, "BA", h))
+        V(("copy", sb("OL", h, al), sb(M, s_[0:16])))
+        V(("copy", sb("RAB", h, al), ind(sb("RG", h, al), sb("OL", h, al))))
+        rab = [sb("RAB", h, s_[v::2]) for v in range(2)]
+        for v in range(2):
+            V(ts(sb("OF", h, s_[128 * v:128 * v + 128]), rab[v], 2048.0, A.add))
+        sec[0] = "far" + H
+        V(*[("tt", sb("VT", h, s_[2 + v::16]), sb("BA", h, s_[14 + v:142:16]), sb("BA", h, s_[14 + v:142:16]), A.mult) for v in range(2)])
+        PE(P(sb(M, s_[128:256]), [(sb("BA", h, s_[14:142]), IDB), (sb("VT", h, al), IDB)]))
+        S(act(sb("VTT", h, al), sb(M, s_[128:256]), F.Copy))
+        PE(*[P(sb(M, s_[256 + 128 * v:384 + 128 * v]), [(sb("QM", v, al), sb("VTT", h, al)), (ID16, LP)]) for v in range(2)])
+        V(ts(sb("S1", h, al), sb(M, s_[256:512]), -4096.0, A.max))
+        S(act(sb("FS", h, al), sb(K, s_[128:256]), F.Copy))
+        PE(P(sb(K, s_[128:256]), [(sb("ID32", al), sb("FS", h, al))], True, False))
+        PE(P(sb(K, s_[128:256]), [(sb("S1", h, s_[128 * v:128 * v + 128]), sb("PEN16", al)) for v in range(2)], False, True))
+        V(("scan", sb("KF", h, s_[256:384]), sb("RSTN", al), sb(K, s_[128:256]), A.min, A.max))
+        V(("tt", sb("M2F", h, s_[1:128]), sb(K, s_[129:256]), sb("KF", h, s_[256:383]), A.min))
+        V(("scan", sb("KF", h, s_[384:512]), sb("RSTN", al), sb("M2F", h, al), A.min, A.max))
+        sec[0] = "prew" + H
+        PE(P(sb(M, s_[128:256]), [(sb("BOFS16", al), sb("S1", h, s_[0:128]))]),
+           P(sb(M, s_[32:40]), [(sb("BPD", s_[15 - x:143 - x]), sb("S1", h, s_[x:128:16])) for x in range(16)]))
+        S(act(sb("LAB", h, al), sb(M, s_[128:256]), F.Identity, 7.5), act(sb("LML", h, al), sb(M, s_[32:40]), F.Identity, 7.5))
+        V(("copy", sb("E", h, s_[130::EW]), sb("LML", h, al)))
+        PE(P(sb(Nb, s_[0:128]), [(sb("SEL0", al), LP), (sb("PID8", al), mt)]), P(sb(Nb, s_[128:256]), [(ID16, rab[0]), (sb("NID8", al), mt)]))
+        S(act(sb("SVB", h, al), sb(Nb, s_[0:128]), F.Identity, -8192.0), act(sb("SVA", h, al), sb(Nb, s_[128:256]), F.Copy))
 
-        zi = 2 * t + h
-        nw, one = 8 * which, which == 1
-        skip = 1 if which == 1 and base == 0 else 0
-        if vmax:
-            nab[0] -= 1
-            m4 = nmx[0] % 3
-            nmx[0] += 1
-            nosz = len(MAXV[which, h]) == 4 * which
-            V(512 - 128 * skip, reads + ["Q0.z%d" % h], ["MX%d" % m4], lambda k, T: [k.vector.tensor_tensor(
-                T.MX[:, m4, 128 * kk:128 * kk + 128], x3(T, base + kk), T.Q0[:, 256 + 128 * h:384 + 128 * h], A.max) for kk in range(skip, 4)][-1])
+    def count(t):
+        sec[0] = "cnt"
+        v = sb("M1", s_[40:41])
+        PE(P(v, [(pt("SC2", r0, al), pt("ONEB", r0, s_[0:1]))] + ([(sb("SN", al), sb("ZV", 2 * t + h, s_[128:129])) for h in range(2)] if t else [])))
+        V(ts(sb("NR", s_[0:1]), v, C6, A.add, -C6, A.add))
+        V(ts(sb("THT", al), sb("TH0", al), v, A.add, sb("NR", s_[0:1]), A.subtract))
 
-            def sums(k, T):
-                for kk in range(skip, 4):
-                    k.tensor.matmul(bo_out[1](T, kk), T.MX[:, m4, 128 * kk:128 * kk + 128], T.BOD[:, 0:nw], one, False)
-                    last = k.tensor.matmul(bo_out[1](T, kk), x3(T, base + kk), T.BON[:, 0:nw], False, one and nosz)
-                    if not nosz:
-                        last = k.tensor.matmul(bo_out[1](T, kk), T.ZV[:, zi, 0:128], T.BON[:, 0:nw], False, one)
-                return last
-            P((4 - skip) * (128 if nosz else 192), ["MX%d" % m4, "BOD", "BON", zk] + reads, [bo_out[0]], sums)
-            return
-
-        def sub(k, T):
-            for kk in range(skip, 4):
-                o = T[bank][:, 128 * kk:128 * kk + 128]
-                k.tensor.matmul(o, T.IDB[:, :], x3(T, base + kk), True, False)
-                last = k.tensor.matmul(o, T.NIDB[:, :], T.ZV[:, zi, 0:128], False, True)
-            return last
-        P(1024 - 256 * skip, reads + [zk, "IDB", "NIDB"], [bank], sub)
-        AC(512 - 128 * skip, [bank], ["AB%d" % a4], lambda k, T: k.scalar.activation(T.AB[:, a4, 128 * skip:512], T[bank][:, 128 * skip:512], F.Abs))
-        P(256 - 64 * skip, ["AB%d" % a4, "BOK"], [bo_out[0]], lambda k, T: [k.tensor.matmul(bo_out[1](T, kk), T.AB[:, a4, 128 * kk:128 * kk + 128], T.BOK[:, 0:nw], one, one) for kk in range(skip, 4)][-1])
-
-    def lists(T, k, out, B, width, step, xs, rhs, rw):
-        for x in range(xs):
-            last = k.tensor.matmul(out, B[:, width - step * x:width - step * x + 128], rhs[:, rw * x:rw * x + rw], x == 0, x == xs - 1)
-        return last
+    def second(t, h):
+        H, li = str(h), 2 * t + h
+        Z, K, M, Nb = "Z" + H, "K" + H, "M" + H, "N" + H
+        LP = sb("LP", h, al)
+        rab = [sb("RAB", h, s_[v::2]) for v in range(2)]
+        xe = [sb("XE", h, s_[v::2]) for v in range(2)]
+        sec[0] = "two" + H
+        PE(P(sb(Nb, s_[256:512]), [(ones33, pt("CK", s_[0:33], s_[256:512]))], True, False))
+        for v in range(2):
+            for e, a, b in XAP[h, v]:
+                o, i = sb("XA", h, s_[2048 * v + 16 * a:2048 * v + 16 * b]), ind(XW, sb("OF", h, s_[128 * v + a:128 * v + b]))
+                S(act(o, i, F.Copy)) if e == "a" else V(("copy", o, i))
+            for j0 in range(0, 16, 4):
+                xa = lambda j: sb("XA", h, s_[2048 * v + j:2048 * v + 2048:16])
+                my = lambda j: sb("MY", h, s_[2048 * v + 128 * j:2048 * v + 128 * j + 128])
+                V(*[("tt", my(j), xa(j), sb(Z, s_[0:128]), A.max) for j in range(j0, j0 + 4)])
+                PE(*[P(sb(Nb, s_[256 + 16 * v + j::32]), [(xa(j), sb("BON", s_[0:8])), (my(j), sb("BOD", s_[0:8]))], False, v == 1 and j == 15) for j in range(j0, j0 + 4)])
+        sec[0] = "end" + H
+        V(("scan", sb("KF", h, s_[0:256]), sb("RST", al), sb(Nb, s_[256:512]), A.max, A.min))
+        V(ts(sb("RR", h, s_[16:48]), sb("KF", h, s_[15::16]), C7, A.add, -C7, A.add))
+        V(*[("tt", sb("BE", h, s_[14 + v:142:16]), sb("KF", h, s_[15 + 16 * v:256:32]), sb("RR", h, s_[16 + v:32:2]), A.subtract) for v in range(2)])
+        PE(lists(M, 16, 1, "BE", h))
+        V(("copy", sb("OE", h, al), sb(M, s_[16:32])))
+        V(("copy", sb("XE", h, al), ind(sb("XA", h, al), sb("OE", h, al))))
+        PE(P(sb(Nb, s_[0:128]), [(ID16, xe[0]), (NID16, xe[1])]))
+        S(act(sb("XD", h, al), sb(Nb, s_[0:128]), F.Abs))
+        uu = [(sb("NBOF16", al), sb("THT", al)), (sb("BOF", al), sb("XD", h, al))]
+        PE(P(sb(Nb, s_[256:384]), uu))
+        sec[0] = "wr" + H
+        V(("tt", sb("LABP", h, al), sb("LAB", h, al), sb(Nb, s_[256:384]), A.max))
+        V(*[ts(sb("E", h, s_[EW * m + 1 + 16 * m:EW * m + 129]), sb("LABP", h, s_[16 * m:128]), sb("LML", h, s_[m:m + 1]), A.is_equal) for m in range(8)])
+        V(("scan", sb("ES", h, al), sb("E", h, al), sb("KEEP", al), A.add, A.mult))
+        V(("tt", sb("WC", h, al), sb("ES", h, s_[130::EW]), sb("DUM", al), A.min))
+        V(ts(sb("WO", h, al), sb("WC", h, al), 8192.0, A.mult, 2048.0, A.add))
+        V(("tt", ind(RW, sb("WO", h, al)), sb("SVA", h, al), sb("SVB", h, al), A.max))
+        sec[0] = "new" + H
+        V(("tt", sb("VF", h, s_[9::16]), sb("KF", h, s_[271::16]), sb("RR", h, s_[32:48]), A.subtract))
+        V(("tt", sb("VF", h, s_[13::16]), sb("VF", h, s_[9::16]), sb("VF", h, s_[9::16]), A.mult),
+          *[("tt", sb("VF", h, s_[2 + v:128:16]), sb("BE", h, s_[14 + v:142:16]), sb("BE", h, s_[14 + v:142:16]), A.mult) for v in range(2)])
+        PE(P(sb(M, s_[128:256]), [(sb("BE", h, s_[14:142]), IDB), (sb("VF", h, s_[0:128]), IDB), (sb("VF", h, s_[126:254]), IDB)]))
+        S(act(sb("VTU", h, al), sb(M, s_[128:256]), F.Copy))
+        vtu = sb("VTU", h, al)
+        PE(*[P(sb(M, s_[256 + 128 * v:384 + 128 * v]), [(sb("QM", v, al), vtu), (ID16, rab[v])]) for v in range(2)])
+        V(ts(sb("S2", h, al), sb(M, s_[256:512]), -4096.0, A.max))
+        NL = sb("NL", h, al)
+        for v, bk, c0 in ((0, K, 256), (1, M, 0)):
+            PE(*[P(sb(bk, s_[c0 + 128 * u:c0 + 128 * u + 128]), [(sb("QM", 2 + v + 2 * u, al), vtu), (sb("BOF16", al), sb("S2", h, s_[128 * v:128 * v + 128]))]) for u in range(2)])
+        for v, bk, c0 in ((0, K, 256), (1, M, 0)):
+            V(("tt", NL, NL if v else LP, sb(bk, s_[c0:c0 + 128]), A.min))
+            V(("tt", NL, NL, sb(bk, s_[c0 + 128:c0 + 256]), A.max))
+        PE(P(sb(Z, s_[256:384]), [(sb("HID16", al), xe[0]), (sb("HID16", al), xe[1])]))
+        lastv = t == TV - 1
+        V(ts(sb("YZ", rev[h]) if lastv else sb("SZ", li, s_[0:128]), sb(Z, s_[256:384]), C0, A.add, -C0, A.add))
+        PE(P(sb(Z, s_[384:512]), uu))
+        S(act(sb("RU", h, al), sb(Z, s_[384:512]), F.Relu, col(7), 8192.0))
+        if not lastv:
+            S(act(sb("SG", h, al), sb(Z, s_[384:512]), F.Sign, 0.0, 1.0, sb("CNT", h, s_[0:1])))
+            S(act(sb("SZ", li, s_[128:129]), sb("CNT", h, s_[0:1]), F.Copy))
+        PE(*[P(sb(K, s_[128 * u:128 * u + 128]), [(ID16, rab[1]), (sb(("IDB", "NIDB")[u], al), sb("RU", h, al))]) for u in range(2)])
+        V(("tt", NL, NL, sb(K, s_[0:128]), A.min))
+        V(("tt", NL, NL, sb(K, s_[128:256]), A.max))
+        if not lastv:
+            V(ts(sb("SL", li, s_[0:128]), NL, 2048.0, A.add))
+            op("g", [("send", None, sb("SL", li, al), sb("SZ", li, al))], c=1200, send=(t, h))
+        else:
+            V(ts(sb("YL", rev[h]), NL, 2048.0, A.add))
+            half = s_[128 - 128 * h:256 - 128 * h]
+            for nm, y in (("YL", "yl"), ("YZ", "yz")):
+                op("s", [("dma", (y, (al, half)), sb(nm, half))], c=2000, s=("do", 16))
 
     for t in range(TV):
+        vis[0] = t
         if t:
             for h in range(2):
-                op("x", 0, ["send%d%d" % (t - 1, h)], ["L%d%d" % (t, h), "Z%d%d" % (t, h)], None)
-                ops[-1]["s"] = ("ar%d%d" % (t, h), 8)
-                ops[-1]["c"] = 3000
-        hh = []
-        for h in range(2):
-            H = str(h)
-            Lk, Zk = "L%d%d" % (t, h), "Z%d%d" % (t, h)
-
-            def prep(t, h, H, Lk, Zk):
-                li = 2 * t + h
-                V(64, [Lk], ["LP" + H], lambda k, T: k.vector.tensor_scalar(T.LP[:, h, :], T.LV[:, li, 0:128], -2048.0, None, A.add))
-                V(64, [Lk], ["HM" + H], lambda k, T: k.vector.tensor_scalar(T.HM[:, h, :], T.LV[:, li, 0:128], 0.015625, 1025 - 0.4921875, A.mult, A.add))
-                P(128, ["LP" + H, "SEL0"], ["Q0.l" + H], lambda k, T: k.tensor.matmul(T.Q0[:, 128 * h:128 * h + 128], T.SEL[:, 0:128], T.LP[:, h, :], True, True))
-                P(128, [Zk, "IDB"], ["Q0.z" + H], lambda k, T: k.tensor.matmul(T.Q0[:, 256 + 128 * h:384 + 128 * h], T.IDB[:, :], T.ZV[:, li, 0:128], True, True))
-            sec[0] = "prep"
-            prep(t, h, H, Lk, Zk)
-        for h in range(2):
-            H, Lk, Zk = str(h), "L%d%d" % (t, h), "Z%d%d" % (t, h)
-
-            def stage1(t, h, H, Lk, Zk):
-                li = 2 * t + h
-                sec[0] = "one" + H
-                gather("a", 2048, XT + [Lk], ["XG" + H], lambda k, T: k.scalar.activation(T.XG[:, h, :], T.X[:, :].indirect(T.LV[:, li, 0:128]), F.Copy))
-
-                def payload(k, T):
-                    k.tensor.matmul(T.Q3[:, 256:512], T.CKL[:, :], T.CK1[:, :], True, False)
-                    k.tensor.matmul(T.Q3[:, 256:512], T.HM[:, h, :], T.PM[:, :], False, False)
-                    return k.tensor.matmul(T.Q3[:, 384:512], T.LP[:, h, :], T.PM[:, 0:128], False, True)
-                P(640, ["CKL", "CK1", "HM" + H, "LP" + H, "PMa", "PMb"], ["Q3.p"], payload)
-                for q in range(4):
-                    subsum(t, h, 1, lambda T, r: T.XG[:, h, r::16], 4 * q, Zk, ("Q3.d%d" % q, (lambda q: lambda T, kk: T.Q3[:, 8 * (4 * q + kk):8 * (4 * q + kk) + 8])(q)), ["XG" + H], vmax=q in MAXV[1, h])
-                na = RGA[h]
-                gather("a", 16 * na, RT + [Lk], ["RG" + H], lambda k, T: k.scalar.activation(T.RG[:, h, 0:16 * na], T.R[:, :].indirect(T.LV[:, li, 0:na]), F.Copy))
-                if na < 128:
-                    gather("v", 2048 - 16 * na, RT + [Lk], ["RGv" + H], lambda k, T: k.vector.tensor_copy(T.RG[:, h, 16 * na:2048], T.R[:, :].indirect(T.LV[:, li, na:128])))
-                for q in range(3):
-                    V(640, ["RG" + H, "RGv" + H, "Q0.l" + H], ["CE%s%d" % (H, q)], (lambda q: lambda k, T: [k.vector.tensor_tensor(
-                        T.CE[:, h, 128 * kk:128 * kk + 128], T.RG[:, h, kk::16], T.Q0[:, 128 * h:128 * h + 128], A.is_equal) for kk in range(5 * q + 1, 5 * q + 6)][-1])(q))
-                    P(320, ["CE%s%d" % (H, q), "BOC"], ["Q3.c%d" % q], (lambda q: lambda k, T: [k.tensor.matmul(
-                        T.Q3[:, 128 + 8 * kk:136 + 8 * kk], T.CE[:, h, 128 * kk:128 * kk + 128], T.BOC[:, :], True, True) for kk in range(5 * q + 1, 5 * q + 6)][-1])(q))
-                D4 = ["Q3.d0", "Q3.d1", "Q3.d2", "Q3.d3", "Q3.z"]
-                sec[0] = "sel" + H
-                V(120, ["Q3.c0", "Q3.c1", "Q3.c2"], ["KCa" + H], lambda k, T: k.vector.tensor_scalar(T.KC4[:, h, 8:128], T.Q3[:, 136:256], 8388608.0, None, A.min))
-                V(128, D4 + ["CF"], ["KCc" + H], lambda k, T: k.vector.tensor_tensor(T.KC4[:, h, 256:384], T.Q3[:, 0:128], T.CF[:, :], A.add))
-                V(64, [], ["KCz" + H], lambda k, T: k.vector.memset(T.KC4[:, h, 0:8], 0.0)) if t == 0 else None
-                V(128, D4 + ["KCa" + H, "KCz" + H], ["KCb" + H], lambda k, T: k.vector.tensor_tensor(T.KC4[:, h, 128:256], T.Q3[:, 0:128], T.KC4[:, h, 0:128], A.max))
-                for w in range(2):
-                    V(128, ["KCb" + H, "Q3.p"], ["KT%s%d" % (H, w)], (lambda w: lambda k, T: k.vector.tensor_tensor(
-                        T.KT[:, h, w, :], T.Q3[:, 256 + 128 * w:384 + 128 * w], T.KC4[:, h, 128:256], A.add))(w))
-                KT = ["KT" + H + "0", "KT" + H + "1"]
-                V(256, KT, ["m64" + H], lambda k, T: k.vector.tensor_tensor(T.T1[:, h, 0, :, :], T.KT[:, h, :, 0:64], T.KT[:, h, :, 64:128], A.min))
-                V(256, KT, ["s64" + H], lambda k, T: k.vector.tensor_tensor(T.T1[:, h, 1, :, :], T.KT[:, h, :, 0:64], T.KT[:, h, :, 64:128], A.max))
-                for n in (32, 16, 8):
-                    lastlevel = n == 8
-                    o = {32: (2, 0), 16: (2, 32), 8: (2, 48)}[n]
-                    i = {32: (None, 0), 16: (2, 0), 8: (2, 32)}[n]
-                    mi, si = ((0, 1) if n == 32 else (2, 3))
-                    lo = i[1]
-
-                    def lev(n, mi, si, lo, oo, lastlevel):
-                        two = 2 * n
-                        V(4 * n, ["m%d" % two + H], ["x%d" % n + H], lambda k, T: k.vector.tensor_tensor(T.XY[:, h, :, 0:n], T.T1[:, h, mi, :, lo:lo + n], T.T1[:, h, mi, :, lo + n:lo + 2 * n], A.max))
-                        ops[-1]["w"].append("XY" + H)
-                        V(4 * n, ["s%d" % two + H], ["y%d" % n + H], lambda k, T: k.vector.tensor_tensor(T.XY[:, h, :, 64:64 + n], T.T1[:, h, si, :, lo:lo + n], T.T1[:, h, si, :, lo + n:lo + 2 * n], A.min))
-                        ops[-1]["w"].append("XZ" + H)
-                        V(4 * n, ["m%d" % two + H], ["m%d" % n + H], lambda k, T: k.vector.tensor_tensor(
-                            T.KI[:, h, 0:2, :] if lastlevel else T.T1[:, h, 2, :, oo:oo + n], T.T1[:, h, mi, :, lo:lo + n], T.T1[:, h, mi, :, lo + n:lo + 2 * n], A.min))
-                        V(4 * n, ["x%d" % n + H, "y%d" % n + H, "XY" + H, "XZ" + H], ["s%d" % n + H], lambda k, T: k.vector.tensor_tensor(
-                            T.KI[:, h, 2:4, :] if lastlevel else T.T1[:, h, 3, :, oo:oo + n], T.XY[:, h, :, 0:n], T.XY[:, h, :, 64:64 + n], A.min))
-                    lev(n, mi, si, lo, o[1], lastlevel)
-                V(64, ["s8" + H], ["KB" + H], lambda k, T: k.vector.tensor_copy(T.KB[:, h, 0:8], T.KI[:, h, 2, :]))
-                V(64, ["m8" + H, "s8" + H, "KB" + H], ["KJ" + H], lambda k, T: k.vector.tensor_scalar(T.KI[:, h, :, :], T.KI[:, h, :, :], 63, None, A.bitwise_and))
-                ops[-1]["w"].extend(["m8" + H, "s8" + H])
-                V(64, ["KJ" + H], ["TA" + H], lambda k, T: k.vector.tensor_scalar(T.TA[:, h, :, :], T.KI[:, h, 0::2, :], 64.0, -2048.0, A.mult, A.add))
-                V(128, ["TA" + H, "KJ" + H], ["BA" + H], lambda k, T: [k.vector.tensor_tensor(T.BA[:, h, 14 + v:128 + 14:16], T.TA[:, h, v, :], T.KI[:, h, 2 * v + 1, :], A.add) for v in range(2)][-1])
-                P(128, ["BA" + H, "ID16"], ["Q5.vt"], lambda k, T: k.tensor.matmul(T.Q5[:, 384:512], T.BA[:, h, 14:142], T.ID16[:, :], True, True))
-                P(512, ["BA" + H, "RX"], ["Q5.ll" + H], lambda k, T: lists(T, k, T.Q5[:, 256 + 16 * h:272 + 16 * h], T.BA[:, h, :], 14, 2, 8, T.RX, 16))
-                V(64, ["Q5.ll" + H], ["OL" + H], lambda k, T: k.vector.tensor_scalar(T.OL[:, h, :], T.Q5[:, 256 + 16 * h:272 + 16 * h], 2048.0, None, A.add))
-                V(128, ["Q5.vt"], ["LTA" + H], lambda k, T: k.vector.tensor_copy(T.LTA[:, h, :], T.Q5[:, 384:512]))
-                P(128, ["LTA" + H, "SEL0"], ["Q6.a"], lambda k, T: k.tensor.matmul(T.Q6[:, 384:512], T.SEL[:, 0:128], T.LTA[:, h, :], True, True))
-                gather("v", 256, RT + ["OL" + H], ["RAB" + H], lambda k, T: k.vector.tensor_copy(T.RAB[:, h, :], T.R[:, :].indirect(T.OL[:, h, :])))
-                P(256, ["LP" + H, "SEL0", "RAB" + H, "NID16"], ["Q6.c"], lambda k, T: (k.tensor.matmul(T.Q6[:, 256:384], T.SEL[:, 0:128], T.LP[:, h, :], True, False),
-                                                                        k.tensor.matmul(T.Q6[:, 256:384], T.NID16[:, :], T.RAB[:, h, 0::2], False, True))[-1])
-                V(128, ["Q6.a"], ["LAB" + H], lambda k, T: k.vector.tensor_copy(T.LAB[:, 128 * h:128 * h + 128], T.Q6[:, 384:512]))
-                V(128, ["Q6.c", "MT%d" % t], ["SVD" + H], lambda k, T: k.vector.tensor_tensor(T.SVD[:, h, :], T.Q6[:, 256:384], T.MT[:, 128 * t:128 * t + 128], A.mult))
-                P(640, ["SVD" + H, "RAB" + H, "ID16", "ID32"], ["Q6.f"], lambda k, T: (k.tensor.matmul(T.Q6[:, 0:128], T.ID32[:, :], T.SVD[:, h, :], True, False),
-                                                                                 k.tensor.matmul(T.Q6[:, 0:128], T.ID16[:, :], T.RAB[:, h, 0::2], False, True))[-1])
-                if SVV:
-                    V(128, ["Q6.f"], ["SV" + H], lambda k, T: k.vector.tensor_copy(T.SV[:, 128 * h:128 * h + 128], T.Q6[:, 0:128]))
-                else:
-                    AC(128, ["Q6.f"], ["SV" + H], lambda k, T: k.scalar.activation(T.SV[:, 128 * h:128 * h + 128], T.Q6[:, 0:128], F.Copy))
-                V(64, ["BA" + H], ["BM" + H], lambda k, T: k.vector.tensor_copy(T.BM[:, h, 15::16], T.BA[:, h, 14:142:16]))
-                P(1024, ["BM" + H, "PMa"], ["Q5.lm"], lambda k, T: lists(T, k, T.Q5[:, 336:344], T.BM[:, h, :], 15, 1, 16, T.PM, 8))
-                V(64, ["Q5.lm"], ["LML" + H], lambda k, T: k.vector.tensor_copy(T.LML[:, 8 * h:8 * h + 8], T.Q5[:, 336:344]))
-                V(128, ["RAB" + H], ["OF" + H], lambda k, T: k.vector.tensor_scalar(T.OF[:, h, :], T.RAB[:, h, :], 2048.0, None, A.add))
-                V(128, ["RAB" + H], ["HM2" + H], lambda k, T: k.vector.tensor_scalar(T.HM2[:, h, :], T.RAB[:, h, :], 0.015625, 1057 - 0.4921875, A.mult, A.add))
-                b2 = ("Q4", "Q3")[h]
-
-                def payload2(k, T):
-                    k.tensor.matmul(T[b2][:, :], T.CKL[:, :], T.CK2[:, :, :], True, False)
-                    for v in range(2):
-                        k.tensor.matmul(T[b2][:, 256 * v:256 * v + 256], T.HM2[:, h, v::2], T.PM2[:, 0:16, :], False, False)
-                        last = k.tensor.matmul(T[b2][:, 256 * v:256 * v + 256], T.RAB[:, h, v::2], T.PM2[:, 16:32, :], False, False)
-                    return last
-                P(1536, ["CKL", "CK2", "HM2" + H, "RAB" + H, "PM2"], [b2 + ".p"] + [b2 + ".d%d" % j for j in range(8)] + [b2 + ".c%d" % j for j in range(3)], payload2)
-                sec[0] = "far" + H
-                for n in (8, 16, 32, 64):
-                    op("a" if KBA else "v", 60, ["KB" + H], ["KB" + H], (lambda n: lambda k, T: k.scalar.activation(T.KB[:, h, n:2 * n], T.KB[:, h, 0:n], F.Copy) if KBA else
-                                                                         k.vector.tensor_copy(T.KB[:, h, n:2 * n], T.KB[:, h, 0:n]))(n))
-                V(256, ["KB" + H, "KT" + H + "0"], ["KCa" + H, "KCz" + H], lambda k, T: k.vector.tensor_tensor(T.KC4[:, h, 0:128], T.KT[:, h, 0, :], T.KB[:, h, :], A.is_gt))
-                V(256, ["KCa" + H, "KCc" + H], ["KCc" + H], lambda k, T: k.vector.tensor_tensor(T.KC4[:, h, 256:384], T.KC4[:, h, 256:384], T.KC4[:, h, 0:128], A.mult))
-                FT = lambda T, j, a, b: T.FT[:, h, j, a:b]
-                V(128, ["KCc" + H], ["fm64" + H], lambda k, T: k.vector.tensor_tensor(FT(T, 0, 0, 64), T.KC4[:, h, 256:320], T.KC4[:, h, 320:384], A.max))
-                V(128, ["KCc" + H], ["fs64" + H], lambda k, T: k.vector.tensor_tensor(FT(T, 1, 0, 64), T.KC4[:, h, 256:320], T.KC4[:, h, 320:384], A.min))
-                for n, mi, lo, oo in ((32, 0, 0, 0), (16, 2, 0, 32), (8, 2, 32, 48)):
-                    def flev(n, mi, lo, oo):
-                        two = 2 * n
-                        si = mi + 1
-                        V(2 * n, ["fm%d" % two + H, "KCc" + H], ["fx" + H], lambda k, T: k.vector.tensor_tensor(T.KC4[:, h, 0:n], FT(T, mi, lo, lo + n), FT(T, mi, lo + n, lo + 2 * n), A.min))
-                        V(2 * n, ["fs%d" % two + H, "KCc" + H], ["fy" + H], lambda k, T: k.vector.tensor_tensor(T.KC4[:, h, 64:64 + n], FT(T, si, lo, lo + n), FT(T, si, lo + n, lo + 2 * n), A.max))
-                        V(2 * n, ["fm%d" % two + H], ["fm%d" % n + H], lambda k, T: k.vector.tensor_tensor(T.FI[:, h, 0:8] if n == 8 else FT(T, 2, oo, oo + n), FT(T, mi, lo, lo + n), FT(T, mi, lo + n, lo + 2 * n), A.max))
-                        V(2 * n, ["fx" + H, "fy" + H], ["fs%d" % n + H], lambda k, T: k.vector.tensor_tensor(T.FI[:, h, 8:16] if n == 8 else FT(T, 3, oo, oo + n), T.KC4[:, h, 0:n], T.KC4[:, h, 64:64 + n], A.max))
-                    flev(n, mi, lo, oo)
-                V(64, [], ["KCa" + H], lambda k, T: k.vector.memset(T.KC4[:, h, 0:8], 0.0))
-                ops[-1]["r"] = ["fs8" + H]
-                ops[-1]["w"] = ["KCz" + H, "KCa" + H]
-                V(64, ["fm8" + H, "fs8" + H], ["FI" + H], lambda k, T: k.vector.tensor_scalar(T.FI[:, h, :], T.FI[:, h, :], 6, 15, A.logical_shift_right, A.bitwise_and))
-                ops[-1]["w"].extend(["fm8" + H, "fs8" + H])
-                V(128, ["FI" + H, "VT" + H], ["VT2" + H], lambda k, T: [k.vector.tensor_copy(T.VT[:, h, 2 + v::16], T.FI[:, h, 8 * v:8 * v + 8]) for v in range(2)][-1])
-            stage1(t, h, H, Lk, Zk)
-        for h in range(2):
-            def stage2(t, h, H, Lk, Zk):
-                zi = 2 * t + h
-                for q in range(4):
-                    if q in S2V[h]:
-                        gather("v", 1024, XT + ["OF" + H], ["XA%s%d" % (H, q)], (lambda q: lambda k, T: k.vector.tensor_copy(T.XA[:, h, 1024 * q:1024 * q + 1024], T.X[:, :].indirect(T.OF[:, h, 64 * q:64 * q + 64])))(q))
-                    else:
-                        gather("a", 1024, XT + ["OF" + H], ["XA%s%d" % (H, q)], (lambda q: lambda k, T: k.scalar.activation(T.XA[:, h, 1024 * q:1024 * q + 1024], T.X[:, :].indirect(T.OF[:, h, 64 * q:64 * q + 64]), F.Copy))(q))
-
-                sec[0] = "sum" + H
-                bk = ("Q4", "Q3")[h]
-                for q in range(8):
-                    subsum(t, h, 2, lambda T, r: T.XA[:, h, r::32], 4 * q, Zk, (bk + ".d%d" % q, (lambda q: lambda T, kk: T[("Q4", "Q3")[h]][:, 16 * (4 * q + kk):16 * (4 * q + kk) + 16])(q)), ["XA%s%d" % (H, j) for j in range(4)], vmax=q in MAXV[2, h])
-                P(64, [bk + ".d%d" % j for j in range(8)] + ["IDB", "ZERO"], [bk + ".f"], lambda k, T: k.tensor.matmul(T[("Q4", "Q3")[h]][:, 0:16], T.IDB[:, :], T.ZERO[:, 0:16], False, True))
-                if KEA[h]:
-                    AC(276, [bk + ".f"], ["KE" + H], lambda k, T: [k.scalar.activation(T.KE[:, h, v, :], T[("Q4", "Q3")[h]][:, 256 * v:256 * v + 128], F.Copy) for v in range(2)][-1])
-                else:
-                    V(256, [bk + ".f"], ["KE" + H], lambda k, T: [k.vector.tensor_copy(T.KE[:, h, v, :], T[("Q4", "Q3")[h]][:, 256 * v:256 * v + 128]) for v in range(2)][-1])
-                V(256, [bk + ".f", "KE" + H], ["KE" + H], lambda k, T: [k.vector.tensor_tensor(T.KE[:, h, v, :], T.KE[:, h, v, :], T[("Q4", "Q3")[h]][:, 256 * v + 128:256 * v + 256], A.min) for v in range(2)][-1])
-                sec[0] = "end" + H
-                for n in (64, 32):
-                    V(4 * n, ["KE" + H], ["KE" + H], (lambda n: lambda k, T: k.vector.tensor_tensor(T.KE[:, h, :, 0:n], T.KE[:, h, :, 0:n], T.KE[:, h, :, n:2 * n], A.min))(n))
-                V(64, ["KE" + H], ["KI2" + H], lambda k, T: k.vector.tensor_tensor(T.KJ[:, h, :, :], T.KE[:, h, :, 0:16], T.KE[:, h, :, 16:32], A.min))
-                V(64, ["KI2" + H], ["KI2" + H], lambda k, T: k.vector.tensor_scalar(T.KJ[:, h, :, :], T.KJ[:, h, :, :], 63, None, A.bitwise_and))
-                V(64, ["KI2" + H], ["TE" + H], lambda k, T: k.vector.tensor_scalar(T.SM[:, h, 0:2, :], T.KJ[:, h, :, 0:8], 64.0, -2048.0, A.mult, A.add))
-                V(128, ["TE" + H, "KI2" + H], ["BE" + H], lambda k, T: [k.vector.tensor_tensor(T.BE[:, h, 14 + v:128 + 14:16], T.SM[:, h, v, :], T.KJ[:, h, v, 8:16], A.add) for v in range(2)][-1])
-                P(512, ["BE" + H, "RX"], ["Q5.le" + H], lambda k, T: lists(T, k, T.Q5[:, 288 + 16 * h:304 + 16 * h], T.BE[:, h, :], 14, 2, 8, T.RX, 16))
-                V(64, ["Q5.le" + H], ["OE" + H], lambda k, T: k.vector.tensor_scalar(T.OE[:, h, :], T.Q5[:, 288 + 16 * h:304 + 16 * h], 2048.0, None, A.add))
-                gather("v", 256, XT + ["OE" + H], ["XE" + H], lambda k, T: k.vector.tensor_copy(T.XE[:, h, :], T.X[:, :].indirect(T.OE[:, h, :])))
-
-                def sd(k, T):
-                    k.tensor.matmul(T.Q6[:, 128:256], T.IDB[:, :], T.XE[:, h, 0::2], True, False)
-                    k.tensor.matmul(T.Q6[:, 128:256], T.NIDB[:, :], T.XE[:, h, 1::2], False, True)
-                    k.tensor.matmul(T.Q6[:, 0:128], T.IDB[:, :], T.XE[:, h, 0::2], True, False)
-                    return k.tensor.matmul(T.Q6[:, 0:128], T.IDB[:, :], T.XE[:, h, 1::2], False, True)
-                P(512, ["XE" + H, "IDB", "NIDB"], ["Q6.f"], sd)
-                AC(128, ["Q6.f"], ["XD" + H], lambda k, T: k.scalar.activation(T.XD[:, h, :], T.Q6[:, 128:256], F.Abs))
-                V(128, ["Q6.f"], ["ZT" + H], lambda k, T: k.vector.tensor_scalar(T.ZT[:, h, :], T.Q6[:, 0:128], 0.5, 1023.75, A.mult, A.add))
-                zo = "SZ%d%d" % (t, h)
-                V(64, ["ZT" + H, "SZP"], [zo], lambda k, T: k.vector.tensor_scalar(T.SZ[:, zi, 0:128], T.ZT[:, h, :], -1024.0, None, A.add))
-                P(64, ["XD" + H, "BO1"], ["Q5.dt"], lambda k, T: k.tensor.matmul(T.Q5[:, 320:328], T.XD[:, h, :], T.BO1[:, :], True, True))
-                P(1024, ["XD" + H, "BPD"], ["Q5.dl"], lambda k, T: [k.tensor.matmul(T.Q5[:, 352:360], T.BPD[:, 15 - x:143 - x], T.XD[:, h, x::16], x == 0, x == 15) for x in range(16)][-1])
-                if t == 0:
-                    thn = lambda T: T.TH[:, :]
-                    tk = "TH"
-                else:
-                    if h == 0:
-                        nn = ["L%d0" % t, "L%d1" % t]
-                        V(64, nn, ["NF"], lambda k, T: (k.vector.tensor_copy(T.NF[:, 0:1], T.LV[:, 2 * t, 128:129]), k.vector.tensor_copy(T.NF[:, 1:2], T.LV[:, 2 * t + 1, 128:129]))[-1])
-                        V(64, ["NF"], ["NI"], lambda k, T: k.vector.tensor_tensor(T.NI[:, 0:1], T.NF[:, 0:1], T.NF[:, 1:2], A.add))
-                        V(64, ["NI"], ["NI"], lambda k, T: k.vector.tensor_scalar(T.NI[:, 0:1], T.NI[:, 0:1], 63, None, A.bitwise_and))
-                        V(64, ["NI"], ["NM"], lambda k, T: k.vector.tensor_copy(T.NM[:, 0:1], T.NI[:, 0:1]))
-                        V(64, ["NM", "THC0"], ["THC1"], lambda k, T: k.vector.tensor_tensor(T.THC[:, 1:2], T.THC[:, 0:1], T.NM[:, 0:1], A.add))
-                        V(64, ["NM", "TH"], ["THN"], lambda k, T: k.vector.tensor_scalar(T.THN[:, :], T.TH[:, :], T.NM[:, 0:1], None, A.add))
-                    thn = lambda T: T.THN[:, :]
-                    tk = "THN"
-                V(64, ["Q5.dt", tk, "VT" + H], ["VT4" + H], lambda k, T: k.vector.tensor_tensor(T.VT[:, h, 4::16], T.Q5[:, 320:328], thn(T), A.is_lt))
-                tc = 0 if t == 0 else 1
-                V(64, ["Q5.dl", "THC%d" % tc], ["ACL" + H], lambda k, T: k.vector.tensor_scalar(T.ACL[:, 8 * h:8 * h + 8], T.Q5[:, 352:360], T.THC[:, tc:tc + 1], None, A.is_lt))
-                VTK = ["VT%d%s" % (s, H) for s in (2, 4)] + ["VT" + H]
-                P(256, VTK + ["BE" + H, "ID16"], ["Q5.vt"], lambda k, T: (k.tensor.matmul(T.Q5[:, 384:512], T.VT[:, h, :], T.ID16[:, :], True, False),
-                                                                     k.tensor.matmul(T.Q5[:, 384:512], T.BE[:, h, 14:142], T.ID16[:, :], False, True))[-1])
-                V(128, ["Q5.vt"], ["VTT" + H], lambda k, T: k.vector.tensor_copy(T.VTT[:, h, :], T.Q5[:, 384:512]))
-
-                def bc(out, s):
-                    return lambda k, T: k.tensor.matmul(out(T), T.SEL[:, 128 * s:128 * s + 128], T.VTT[:, h, :], True, True)
-                P(256, ["VTT" + H, "SELF"], ["Q6.f"], lambda k, T: [k.tensor.matmul(T.Q6[:, 128 * v:128 * v + 128], T.SELF[:, 128 * v:128 * v + 128], T.VTT[:, h, :], True, True) for v in range(2)][-1])
-                P(128, ["VTT" + H, "SEL4"], ["Q6.c"], bc(lambda T: T.Q6[:, 256:384], 4))
-                P(256, ["VTT" + H, "SEL0", "SEL1"], ["Q7.e"], lambda k, T: (bc(lambda T: T.Q7[:, 0:128], 0)(k, T), bc(lambda T: T.Q7[:, 128:256], 1)(k, T))[-1])
-                V(256, ["Q6.f", "KC"], ["MM" + H], lambda k, T: k.vector.tensor_scalar(T.MM[:, h, :], T.Q6[:, 0:256], T.KC[:, 0:1], None, A.is_equal))
-                V(128, ["Q6.c", "RAB" + H], ["P3" + H], lambda k, T: k.vector.tensor_tensor(T.P34[:, h, 0:128], T.Q6[:, 256:384], T.RAB[:, h, 1::2], A.mult))
-                V(256, ["MM" + H, "Q7.e"], ["P12" + H], lambda k, T: k.vector.tensor_tensor(T.P12[:, h, :], T.MM[:, h, :], T.Q7[:, 0:256], A.mult))
-
-                def kam(k, T):
-                    k.tensor.matmul(T.Q7[:, 256:384], T.ID16[:, :], T.MM[:, h, 0:128], True, False)
-                    k.tensor.matmul(T.Q7[:, 256:384], T.ID16[:, :], T.MM[:, h, 128:256], False, False)
-                    return k.tensor.matmul(T.Q7[:, 256:384], T.SEL[:, 512:640], T.VTT[:, h, :], False, True)
-                P(384, ["MM" + H, "VTT" + H, "ID16", "SEL4"], ["Q7.k"], kam)
-                V(128, ["Q7.k", "LP" + H], ["P4" + H], lambda k, T: k.vector.tensor_tensor(T.P34[:, h, 128:256], T.Q7[:, 256:384], T.LP[:, h, :], A.mult))
-
-                def new(k, T):
-                    o = T.Q7[:, 384:512]
-                    k.tensor.matmul(o, T.ID16[:, :], T.LP[:, h, :], True, False)
-                    k.tensor.matmul(o, T.ID16[:, :], T.P34[:, h, 0:128], False, False)
-                    k.tensor.matmul(o, T.ID16[:, :], T.P12[:, h, 0:128], False, False)
-                    k.tensor.matmul(o, T.ID16[:, :], T.P12[:, h, 128:256], False, False)
-                    return k.tensor.matmul(o, T.NID16[:, :], T.P34[:, h, 128:256], False, True)
-                P(640, ["P12" + H, "P3" + H, "P4" + H, "LP" + H, "ID16", "NID16"], ["Q7.n"], new)
-                if t < TV - 1:
-                    sl = "SL%d%d" % (t, h)
-                    V(128, ["Q7.n", "SLP"], [sl], lambda k, T: k.vector.tensor_scalar(T.SL[:, zi, 0:128], T.Q7[:, 384:512], 2048.0, None, A.add))
-                    P(512, ["VT4" + H, "ONEF"], ["Q5.nc"], lambda k, T: [k.tensor.matmul(T.Q5[:, 328:329], T.ONEF[:, :], T.VT[:, h, 4 + 16 * j:5 + 16 * j], j == 0, j == 7) for j in range(8)][-1])
-                    V(64, ["Q5.nc", "SLP"], [sl + "n"], lambda k, T: k.vector.tensor_copy(T.SL[:, zi, 128:129], T.Q5[:, 328:329]))
-                    op("g", 1200, [sl, sl + "n", zo, "SLP", "SZP"], ["send%d%d" % (t, h)], None)
-                    ops[-1]["send"] = (t, h)
-                else:
-                    V(128, ["Q7.n"], ["YL" + H], lambda k, T: k.vector.tensor_scalar(T.YL[:, 128 * h:128 * h + 128], T.Q7[:, 384:512], 2048.0, None, A.add))
-                    op("s", 50, ["YL" + H], ["yl" + H], lambda k, T: k.sync.dma_start(T.yl[:, 128 * h:128 * h + 128], T.YL[:, 128 * h:128 * h + 128]))
-                    ops[-1]["s"] = ("do", 16)
-                    op("s", 50, [zo], ["yz" + H], lambda k, T: k.sync.dma_start(T.yz[:, 128 * h:128 * h + 128], T.SZ[:, zi, 0:128]))
-                    ops[-1]["s"] = ("do", 16)
-                sec[0] = "wr" + H
-                V(64, ["ACL" + H], ["LU" + H], lambda k, T: k.vector.tensor_scalar(T.WA[:, 8 * h:8 * h + 8], T.ACL[:, 8 * h:8 * h + 8], -16384.0, 18432.0, A.mult, A.add))
-                V(64, ["LU" + H, "LML" + H], ["LV" + H], lambda k, T: k.vector.tensor_tensor(T.WB[:, 8 * h:8 * h + 8], T.WA[:, 8 * h:8 * h + 8], T.LML[:, 8 * h:8 * h + 8], A.add))
-
-                def eq(m, a, b):
-                    return lambda k, T: k.vector.tensor_scalar(T.E[:, m, a - 16 * m:b - 16 * m], T.LAB[:, a:b], T.LML[:, m:m + 1], T.ACL[:, m:m + 1], A.is_equal, A.mult)
-                V(8 * 64 + 300 * (1 - h), ["LAB1", "LAB" + H, "LML" + H, "ACL" + H], ["E%d%d" % (h, h)], lambda k, T: [eq(m, 16 * m, 256)(k, T) for m in range(8 * h, 8 * h + 8)][-1])
-                V(256, ["E%d%d" % (h, h), "TRI"], ["E%d%d" % (h, h)], lambda k, T: k.vector.tensor_tensor(T.E[:, 8 * h:8 * h + 8, 0:16], T.E[:, 8 * h:8 * h + 8, 0:16], T.TRI[:, :, :], A.mult))
-                n = 256 - 128 * h
-                bk = "Q7.e" if h == 0 else "Q7.k"
-                P(1600 - 900 * h, ["E00", "BOS"] if h == 0 else ["E11", "BOS"], [bk],
-                  lambda k, T: [k.tensor.matmul(T.Q7[:, 256 * h + 16 * m:256 * h + n], T.BOS[:, :], T.E[:, 8 * h + m, 0:n - 16 * m], m == 0, m == 7) for m in range(8)][-1])
-                if h == 0:
-                    V(256, [bk, "MT0"], ["PT"], lambda k, T: [k.vector.tensor_tensor(T.PT[:, 128 * j:128 * j + 128], T.Q7[:, 128 * j:128 * j + 128], T.MT[:, 0:128], A.mult) for j in range(2)][-1])
-                else:
-                    V(128, [bk, "MT0"], ["PT"], lambda k, T: k.vector.tensor_tensor(T.PT[:, 0:128], T.Q7[:, 256:384], T.MT[:, 0:128], A.mult))
-                V(n, ["PT", "RS"], ["PS%d" % h], lambda k, T: k.vector.tensor_tensor_scan(T.PS[:, 256 * h:256 * h + n], T.RS[:, 0:n], T.PT[:, 0:n], 0.0, A.mult, A.add))
-                if h == 0:
-                    V(64, ["PS0", "LV0"], ["LW0"], lambda k, T: k.vector.tensor_tensor(T.WB[:, 0:8], T.WB[:, 0:8], T.PS[:, 15:128:16], A.add))
-                else:
-                    V(64, ["PS0", "LV1"], ["LV1"], lambda k, T: k.vector.tensor_tensor(T.WB[:, 8:16], T.WB[:, 8:16], T.PS[:, 143:256:16], A.add))
-                    V(64, ["PS1", "LV1"], ["LW1"], lambda k, T: k.vector.tensor_tensor(T.WB[:, 8:16], T.WB[:, 8:16], T.PS[:, 271:384:16], A.add))
-            stage2(t, h, str(h), "L%d%d" % (t, h), "Z%d%d" % (t, h))
-
-        V(64, ["LW0", "LW1", "CI2"], ["WC"], lambda k, T: k.vector.tensor_tensor(T.WC[:, :], T.WB[:, :], T.CI2[:, :], A.min))
-        ops[-1]["w"].extend(["LV0", "LV1"])
-        V(64, ["WC"], ["WO"], lambda k, T: k.vector.tensor_copy(T.WO[:, :], T.WC[:, :]))
-        op("v", 60 + 256 * 3.5 * CYC, ["WO", "SV0", "SV1"], RT, lambda k, T: k.vector.tensor_copy(T.R[:, :].indirect(T.WO[:, :]), T.SV[:, :]))
+                sec[0] = "arr"
+                op("x", [("land", sb("LV", 2 * t + h, al), sb("ZV", 2 * t + h, al))], c=3000, s=("ar%d%d" % (t, h), 8), after=(t - 1, h))
+        first(t, 0)
+        count(t)
+        first(t, 1)
+        second(t, 0)
+        second(t, 1)
+    sec[0] = "sum"
     for b in range(8):
-        if b % 2:
-            V(512, ["R%d" % (b // 2)], ["R16%d" % b], (lambda b: lambda k, T: k.vector.tensor_copy(T.R16[:, 512 * b:512 * b + 512], T.R[:, 512 * b:512 * b + 512]))(b))
-        else:
-            V(512, ["R%d" % (b // 2)], ["R16%d" % b], (lambda b: lambda k, T: k.vector.tensor_copy(T.R16[:, 512 * b:512 * b + 512], T.R[:, 512 * b:512 * b + 512]))(b))
-    for b in range(8):
-        P(512, ["R16%d" % b, "ID16"], ["Q1"], (lambda b: lambda k, T: k.tensor.matmul(T.Q1[:, :], T.ID16[:, :], T.R16[:, 512 * b:512 * b + 512], b == 0, b == 7))(b))
-    V(512, ["Q1"], ["YR"], lambda k, T: k.vector.tensor_scalar(T.YR[:, :], T.Q1[:, :], 16384.0, None, A.add))
-    op("s", 50, ["YR"], ["yr"], lambda k, T: k.sync.dma_start(T.yr[:, :], T.YR[:, :]))
-    ops[-1]["s"] = ("do", 16)
+        V(("copy", sb("R16", s_[512 * b:512 * b + 512]), sb("R", s_[512 * b:512 * b + 512])))
+        PE(P(sb("K0", al), [(ID16, sb("R16", s_[512 * b:512 * b + 512]))], b == 0, b == 7))
+    V(ts(sb("YR", al), sb("K0", al), 16384.0, A.add))
+    op("s", [("dma", ("yr", s_[:, :]), sb("YR", al))], c=2000, s=("do", 16))
     return ops
 
 
-def callable_(x):
-    return not isinstance(x, (int, float))
+def touches(c):
+    if c[0] == "land":
+        return [], [c[1], c[2]]
+    rd, wr = [], []
+    for j, x in enumerate(c[1:]):
+        if not isap(x) or x[0] in HBM:
+            continue
+        w = j == 0 or (c[0] == "act" and j == 5)
+        if x[0] == "@":
+            rd.append(x[2])
+            x = x[1]
+        (wr if w else rd).append(x)
+    return rd, wr
 
 
 def edges(ops):
-    lastw, readers, bank = {}, {}, {}
+    hist, bank, sends = {}, {}, {}
     for o in ops:
-        pre = set()
-        for k in o["r"]:
-            if k in lastw:
-                pre.add(lastw[k])
-        for k in o["w"]:
-            if k in lastw:
-                pre.add(lastw[k])
-            pre.update(readers.get(k, ()))
-        for b in set(k.split(".")[0] for k in o["r"] + o["w"] if k[0] == "Q"):
-            d = bank.setdefault(b, [None, [], []])
+        pre, acc = set(), []
+        for c in o["calls"]:
+            rd, wr = touches(c)
+            acc += [(x[0], cells(x)[1], False) for x in rd] + [(x[0], cells(x)[1], True) for x in wr]
+        for nm, bits, w in acc:
+            pre.update(e[0] for e in hist.get(nm, ()) if e[1] & bits and (w or e[2]))
+        for nm, bits, w in acc:
+            li = hist.setdefault(nm, [])
+            if w:
+                hist[nm] = li = [[e[0], e[1] & ~bits, e[2]] for e in li if e[1] & ~bits]
+            li.append([o["i"], bits, w])
+        for b in set(x[0] for x in acc if x[0] in BANKS):
+            d = bank.setdefault(b, [None, [], [], None])
             if d[0] != o["e"]:
                 d[0], d[1], d[2] = o["e"], [], d[1]
             d[1].append(o["i"])
             pre.update(d[2])
-        for k in o["r"]:
-            readers.setdefault(k, []).append(o["i"])
-        for k in o["w"]:
-            lastw[k] = o["i"]
-            readers[k] = []
+            if o["e"] == "p":
+                if d[3] is not None:
+                    pre.add(d[3])
+                d[3] = o["i"]
+        if "send" in o:
+            sends[o["send"]] = o["i"]
+        if "after" in o:
+            pre = {sends[o["after"]]}
         pre.discard(o["i"])
         o["pre"] = sorted(pre)
 
 
-def schedule(ops):
+def schedule(ops, bonus=BONUS):
     n = len(ops)
     succ = [[] for _ in ops]
     for o in ops:
         for p in o["pre"]:
             succ[p].append(o["i"])
+    lag = lambda a, b: 0.0 if ops[a]["e"] == "p" and ops[b]["e"] == "p" else DEP
     tail = [0.0] * n
-    rnd = SEED
     for o in reversed(ops):
-        tail[o["i"]] = o["c"] + max([tail[s] + DEP for s in succ[o["i"]]] or [0.0])
-    for i in range(n):
-        rnd = (rnd * 1103515245 + 12345) % 2147483648
-        tail[i] += ops[i]["p"] + SPREAD * (rnd // 65536) / 32768.0
+        tail[o["i"]] = o["c"] + max([tail[s] + lag(o["i"], s) for s in succ[o["i"]]] or [0.0])
+    prio = [tail[i] + bonus.get(ops[i]["sec"], 0.0) for i in range(n)]
     left = [len(o["pre"]) for o in ops]
-    at = [0.0] * n
-    free = {}
-    ready = {}
-    order = {}
+    at, end, free, ready, order = [0.0] * n, [0.0] * n, {}, {}, {}
     for o in ops:
         if not left[o["i"]]:
             ready.setdefault(o["e"], []).append(o["i"])
-    done = 0
-    end = [0.0] * n
-    while done < n:
-        best = None
-        for e, rs in ready.items():
-            if not rs:
-                continue
-            f = free.get(e, 0.0)
-            st = min(max(f, at[i]) for i in rs)
-            if best is None or st < best[0]:
-                best = (st, e)
-        st, e = best
-        cand = [i for i in ready[e] if max(free.get(e, 0.0), at[i]) <= st + 1e-9]
-        i = max(cand, key=lambda j: (tail[j], -j))
-        if e in ("s", "t"):
-            i = min(ready[e])
+    for _ in range(n):
+        st, e = min((min(max(free.get(e, 0.0), at[i]) for i in rs), e) for e, rs in ready.items() if rs)
+        i = min(ready[e]) if e in "st" else max((j for j in ready[e] if at[j] <= st + 1e-9), key=lambda j: (prio[j], -j))
         ready[e].remove(i)
         o = ops[i]
         s0 = max(free.get(e, 0.0), at[i])
         end[i] = s0 + o["c"]
-        free[e] = s0 + (50 if e in ("s", "t", "x") else o["c"])
+        free[e] = s0 + (50 if e in "stx" else o["c"])
         order.setdefault(e, []).append(i)
-        done += 1
         for s in succ[i]:
             left[s] -= 1
-            at[s] = max(at[s], end[i] + DEP)
+            at[s] = max(at[s], end[i] + lag(i, s))
             if not left[s]:
                 ready.setdefault(ops[s]["e"], []).append(s)
-    seq = sorted(range(n), key=lambda i: (end[i] - ops[i]["c"], i))
-    return order, max(end)
+    return order, end
+
+
+def issue(g, q, T, c):
+    def r(x):
+        if not isap(x):
+            return x
+        return r(x[1]).indirect(r(x[2])) if x[0] == "@" else T[x[0]][x[1]]
+    k, a = c[0], [r(x) for x in c[1:]]
+    if k == "mm":
+        return q.matmul(*a)
+    if k == "tt":
+        return q.tensor_tensor(*a)
+    if k == "ts":
+        return q.tensor_scalar(*a) if a[5] is not None else q.tensor_scalar(*a[0:5])
+    if k == "copy":
+        return q.tensor_copy(*a)
+    if k == "memset":
+        return q.memset(*a)
+    if k == "scan":
+        return q.tensor_tensor_scan(a[0], a[1], a[2], 0.0, a[3], a[4])
+    if k == "red":
+        return q.tensor_reduce(a[0], a[1], AxisListType.X, a[2])
+    if k == "act":
+        if a[2] == F.Copy:
+            return q.activation(a[0], a[1], a[2])
+        return q.activation(a[0], a[1], a[2], bias=a[3], scale=a[4], accum_out=a[5])
+    if k == "asel":
+        return q.affine_select(*a)
+    if k == "iota":
+        return q.iota(*a) if SCRATCH[c[1][0]][2] == I32 else q.iota(*a, allow_small_or_imprecise_dtypes=True)
+    if k == "pbc":
+        return q.partition_broadcast(*a)
+    return q.dma_start(*a)
+
+
+PLAN = []
 
 
 def rank_program(g, core, T, topo):
     rank = T.rank_of(core)
     if rank is None:
         return
-    ops = plan()
-    edges(ops)
-    order, _ = schedule(ops)
-    queue = {"v": g.vector, "a": g.scalar, "p": g.tensor, "g": g, "s": g.sync, "t": g.scalar}
+    if not PLAN:
+        ops = plan()
+        edges(ops)
+        PLAN.extend([ops, schedule(ops)[0]])
+    ops, order = PLAN
+    queue = {"v": g.vector, "a": g.scalar, "p": g.tensor, "g": g, "s": g.sync}
     nxt = T.cores[(rank + 1) % N]
-    count = {}
-    seen = {}
+    count, total = {}, {e: 0 for e in "vapg"}
     for e, li in order.items():
-        c = 0
         for i in li:
-            o = ops[i]
-            if "s" in o:
-                if o["s"][0] == "do":
-                    continue
-                count[i] = o["s"]
-            elif "send" in o:
-                count[i] = None
-            else:
-                c += 1
-                count[i] = (SEMOF[e], c)
-    total = {e: 0 for e in "vapg"}
-    known = {}
-    clock = {}
-
-    def merge(a, b):
-        for k, v in b.items():
-            if a.get(k, 0) < v:
-                a[k] = v
-
-    pos = {e: 0 for e in order}
-    lists_ = {e: list(li) for e, li in order.items()}
-    if "t" in lists_:
-        lists_["a"] = lists_["t"] + lists_["a"]
-        del lists_["t"]
-    pos = {e: 0 for e in lists_}
-    emitted = set()
-    do = 0
-    ls = 0
+            if "s" in ops[i]:
+                count[i] = ops[i]["s"]
+            elif "send" not in ops[i]:
+                total[e] += 1
+                count[i] = (SEMOF[e], total[e])
+    lists = {e: list(li) for e, li in order.items() if e != "t"}
+    lists["a"] = order["t"] + order["a"]
+    pos, known, clock, done, stores, sent = {e: 0 for e in lists}, {e: {} for e in lists}, {}, set(), 0, 0
     progress = True
     while progress:
         progress = False
-        for e in list(lists_):
-            while pos[e] < len(lists_[e]):
-                i = lists_[e][pos[e]]
+        for e in lists:
+            while pos[e] < len(lists[e]) and all(p in done for p in ops[lists[e][pos[e]]]["pre"]):
+                i = lists[e][pos[e]]
                 o = ops[i]
-                if any(p not in emitted for p in o["pre"]):
-                    break
                 pos[e] += 1
                 progress = True
-                emitted.add(i)
+                done.add(i)
                 if e == "x":
                     clock[i] = {o["s"][0]: o["s"][1]}
                     continue
-                q = queue[e]
-                kn = known.setdefault(e, {})
+                q, kn = queue[e], known[e]
                 for p in sorted(o["pre"], reverse=True):
-                    po = ops[p]
-                    if po["e"] == "p" and e == "p":
-                        continue
-                    if po["e"] == "g" and "send" in po:
+                    if (ops[p]["e"] == "p" and e == "p") or "send" in ops[p]:
                         continue
                     sem, val = count[p]
                     if kn.get(sem, 0) < val:
                         q.wait_ge(T.sem[sem], val)
-                        merge(kn, clock[p])
-                        kn[sem] = max(kn.get(sem, 0), val)
+                        for k, v in clock[p].items():
+                            kn[k] = max(kn.get(k, 0), v)
                 if "send" in o:
                     t, h = o["send"]
                     rid, pid = topo.addr(nxt)[0:2]
                     eng = topo.engines(core, nxt)
-                    ma = sum(1 << x for x in eng[0:4])
-                    mb = sum(1 << x for x in eng[4:8])
                     dst = DstId(rid=rid, pnc=pid)
-                    arr = T.sem["ar%d%d" % (t + 1, h)]
                     g.remote_dma_fused([
-                        RemoteDMATransfer(dst_ids=[dst], dma_engine_mask=ma, remote_sem=arr, src=T.SL[:, 2 * t + h, :], dst=T.LV[:, 2 * t + 2 + h, :]),
-                        RemoteDMATransfer(dst_ids=[dst], dma_engine_mask=mb, remote_sem=arr, src=T.SZ[:, 2 * t + h, :], dst=T.ZV[:, 2 * t + 2 + h, :]),
-                    ], local_sem=T.sem.ls)
-                    ls += 8
+                        RemoteDMATransfer(dst_ids=[dst], dma_engine_mask=sum(1 << x for x in eng[4 * j:4 * j + 4]), remote_sem=T.sem["ar%d%d" % (t + 1, h)],
+                                          src=T[a][:, 2 * t + h, :], dst=T[b][:, 2 * t + 2 + h, :]) for j, (a, b) in enumerate((("SL", "LV"), ("SZ", "ZV")))],
+                        local_sem=T.sem.ls)
+                    sent += 8
                     continue
-                last = o["f"](g, T)
-                if "s" in o:
-                    sem, val = o["s"]
-                    if sem == "do":
-                        do += 16
-                    for x in (last if isinstance(last, tuple) else (last,)):
-                        x.then_inc(T.sem[sem], 16)
-                    clock[i] = dict(kn)
-                    clock[i][sem] = val
-                else:
-                    sem, val = count[i]
-                    last.then_inc(T.sem[sem], 1)
-                    total[e] += 1
-                    clock[i] = dict(kn)
-                    clock[i][sem] = val
-    g.wait_ge(T.sem.ls, ls)
-    g.sync.wait_ge(T.sem["do"], do)
+                for c in o["calls"]:
+                    last = issue(g, q, T, c)
+                sem, val = count[i]
+                last.then_inc(T.sem[sem], 16 if "s" in o else 1)
+                stores += 16 * (sem == "do")
+                clock[i] = dict(kn)
+                clock[i][sem] = val
+    g.wait_ge(T.sem.ls, sent)
+    g.sync.wait_ge(T.sem["do"], stores)
     for e in "vapg":
-        if total[e]:
-            queue[e].wait_ge(T.sem[SEMOF[e]], total[e])
+        queue[e].wait_ge(T.sem[SEMOF[e]], total[e])

@@ -8,23 +8,23 @@ EW = 131
 B16, H16, F32, I32, U16 = "bfloat16", "float16", "float32", "int32", "uint16"
 SB = {
     "X": ([4096], B16), "R": ([4352], F32), "R16": ([4096], H16), "LI": ([256], I32), "ZI": ([256], B16), "THI": ([8], I32), "THB": ([8], I32),
-    "LV": ([2 * TV, 136], U16), "ZV": ([2 * TV, 136], B16), "SL": ([2 * TV, 136], U16), "SZ": ([2 * TV, 136], B16),
+    "LV": ([2 * TV, 264], H16), "SL": ([2 * TV, 264], H16), "C16": ([128], B16), "S1": ([2, 256], H16), "BOK16": ([16], H16), "ONEH": ([2], H16),
     "ONEB": ([256], B16), "IDB": ([128], B16), "NIDB": ([128], B16), "PID8": ([128], B16), "NID8": ([128], B16), "ID16": ([128], H16), "NID16": ([128], H16),
     "ID32": ([128], F32), "HID16": ([128], H16), "PEN16": ([128], H16), "BOF": ([128], B16), "BOF16": ([128], H16), "NBOF16": ([128], H16), "BOFS16": ([128], H16),
-    "BPD": ([143], H16), "BOD": ([16], B16), "BON": ([16], B16), "BOC": ([8], B16), "BO1": ([8], F32), "SELB": ([128], B16), "SEL0": ([128], H16),
+    "BPD": ([143], H16), "BOD": ([16], B16), "BON": ([16], B16), "BOK": ([16], B16), "BOC": ([8], B16), "BO1": ([8], F32), "SELB": ([128], B16), "SEL0": ([128], H16),
     "RX": ([128], B16), "IK": ([256], F32), "PI": ([4], I32), "IM": ([144], I32), "MTW": ([144], B16), "IN": ([16], F32), "CO": ([24], F32),
     "CL": ([2, 16], B16), "CK": ([512], B16), "CAPK": ([128], F32), "RST": ([256], F32), "RSTN": ([128], F32), "AQ": ([4, 128], B16), "BQ": ([128], B16),
     "QM": ([6, 128], B16), "KEEP": ([8 * EW], H16), "DG": ([2, 16], H16), "DUM": ([8], F32), "TH": ([8], F32), "TH0": ([128], H16), "THT": ([128], H16),
-    "SN": ([128], B16), "SC2": ([128], B16), "NR": ([2], F32), "YL": ([256], F32), "YZ": ([256], B16), "YR": ([512], F32),
+    "SN": ([128], H16), "SC2": ([128], B16), "NR": ([2], F32), "YL": ([256], F32), "YZ": ([256], B16), "YR": ([512], F32),
 }
 for _q in range(4):
     SB["RI%d" % _q] = ([1024], I32)
 for _n, (_s, _d) in {
-    "LP": ([128], H16), "XG": ([2048], B16), "MX": ([2048], B16), "RG": ([2048], F32), "CE": ([2048], B16), "XA": ([4096], B16), "MY": ([4096], B16),
+    "LU": ([128], U16), "VTF": ([128], B16), "XG": ([2048], B16), "MX": ([2048], B16), "RG": ([2048], F32), "CE": ([2048], B16), "XA": ([4096], B16), "MY": ([4096], B16),
     "KS": ([256], F32), "M2": ([128], F32), "KF": ([512], F32), "M2F": ([128], F32), "FS": ([128], F32), "RR": ([48], F32), "BA": ([144], B16), "BE": ([144], B16),
-    "VT": ([128], B16), "VF": ([256], B16), "VTT": ([128], B16), "VTU": ([128], B16), "OL": ([16], U16), "OE": ([16], U16), "RAB": ([256], H16),
-    "XE": ([256], H16), "OF": ([256], U16), "S1": ([256], H16), "S2": ([256], H16), "LAB": ([128], F32), "LML": ([8], F32), "LABP": ([128], H16),
-    "SVA": ([128], F32), "SVB": ([128], F32), "NL": ([128], H16), "XD": ([128], B16), "RU": ([128], B16), "SG": ([128], B16), "CNT": ([2], F32),
+    "VF": ([264], B16), "AB": ([2048], B16), "ZH": ([128], F32), "VTT": ([128], B16), "VTU": ([128], B16), "OL": ([16], U16), "OE": ([16], U16), "RAB": ([256], H16),
+    "XE": ([256], H16), "OF": ([256], U16), "NR2": ([128], F32), "S2": ([256], H16), "LAB": ([128], F32), "LML": ([8], F32), "LABP": ([128], H16),
+    "SVA": ([128], F32), "SVB": ([128], F32), "NL": ([128], F32), "XD": ([128], B16), "RU": ([128], B16), "SG": ([128], B16), "CNT": ([2], F32),
     "E": ([8 * EW], H16), "ES": ([8 * EW], H16), "WC": ([8], F32), "WO": ([8], U16),
 }.items():
     SB[_n] = ([2] + _s, _d)
@@ -37,10 +37,16 @@ SEMOF = {"v": "sv", "a": "sa", "p": "sp", "g": "sg"}
 HBM = ("xt", "z0", "ex", "l0", "th", "yl", "yz", "yr")
 s_ = np.s_
 C7, C6, C0 = 1.5 * 2.0 ** 30, 1.5 * 2.0 ** 29, 1.5 * 2.0 ** 23
+C13 = 1.5 * 2.0 ** 36
 BIG = 2.0 ** 30
-RGP = (((("a", 0, 64), ("a", 64, 128)), ((0, 64), (64, 128))), ((("a", 0, 128),), ((0, 128),)))
-XAP = {(0, 0): (("a", 0, 64), ("a", 64, 128)), (0, 1): (("a", 0, 64), ("a", 64, 128)), (1, 0): (("a", 0, 64), ("a", 64, 128)), (1, 1): (("a", 0, 64), ("a", 64, 128))}
-BONUS = {'arr': -66000, 'cnt': 32000, 'conf0': 15000, 'conf1': 13000, 'end0': 7000, 'end1': 20500, 'far0': 19500, 'far1': 9500, 'init': 2500, 'late': 3000, 'new0': 47000, 'new1': 24000, 'prep0': 500, 'prep1': 19500, 'prew0': 14000, 'prew1': 11000, 'sel0': 37500, 'sel1': 15500, 'sum': 39500, 'two0': 13500, 'two1': 2500, 'wr0': -22500, 'wr1': 74500}
+WHOLE, TWO = (("a", 0, 128),), (("a", 0, 64), ("a", 64, 128))
+OPT = {"xg": [WHOLE, (("a", 0, 96), ("v", 96, 128))], "rg": [TWO, WHOLE], "ce": [((0, 64), (64, 128)), ((0, 128),)], "xa": [TWO, TWO, TWO, TWO], "xe": ["v", "a"], "z": ["a", "a"],
+       "abs": [(), ()], "my": [((0, 128),), ((0, 64), (64, 128)), ((0, 128),), ((0, 64), (64, 128))]}
+SLOW = (1.9, 5.0, 1.3, 0.85, 170.0, 4500.0)
+PERIOD, ROUNDS = 27.0, (16000, 3000)
+PLACE = {"init": -20, "late": -3, "arr": -30, "cnt": 5, "sum": 30, "prep0": -4, "svb0": 0, "conf0": 0, "sel0": 3.5, "far0": 6.5, "prew0": 8, "fq0": 9, "two0": 8.9,
+         "end0": 12.5, "new0": 12.6, "wr0": 20, "prep1": 3.7, "svb1": 8, "conf1": 6.3, "sel1": 10, "far1": 13, "prew1": 14.5, "fq1": 15, "two1": 14.2,
+         "end1": 21, "new1": 21.1, "wr1": 23}
 
 
 def sb(name, *idx):
@@ -80,7 +86,7 @@ def two(ap):
     return SCRATCH[ap[0]][2] in (B16, H16, U16)
 
 
-def cost(e, c):
+def cost(e, c, GA, SCA, PEC):
     k, out = c[0], c[1]
     if k == "mm":
         return max(min(64, cells(c[2])[0]), cells(c[3])[0]) * PEC * (1 if two(c[2]) else 4)
@@ -102,12 +108,13 @@ def cost(e, c):
     return 5 + max(64, n * f) * CYC
 
 
-def plan():
+def plan(TV=TV):
     ops, sec, vis = [], ["init"], [0]
 
     def op(e, calls, **kw):
         o = {"e": e, "calls": calls, "i": len(ops), "t": vis[0], "sec": sec[0]}
-        o["c"] = kw.pop("c") if "c" in kw else sum(cost(e, c) for c in calls)
+        o["c2"] = (SLOW[5] if e == "x" else kw["c"]) if "c" in kw else SLOW[2] * sum(cost(e, c, SLOW[0], SLOW[1], SLOW[3]) for c in calls)
+        o["c"] = kw.pop("c") if "c" in kw else sum(cost(e, c, GA, SCA, PEC) for c in calls)
         o.update(kw)
         ops.append(o)
 
@@ -132,6 +139,9 @@ def plan():
     def act(o, i, f, bias=0.0, scale=1.0, acc=None):
         return ("act", o, i, f, bias, scale, acc)
 
+    def gather(e, o, i):
+        S(act(o, i, F.Copy)) if e == "a" else V(("copy", o, i))
+
     def col(j):
         return sb("CO", s_[j:j + 1])
 
@@ -151,8 +161,8 @@ def plan():
     V(ms(sb("ONEB", al), 1.0))
     rev = (s_[255:127:-1], s_[127::-1])
     for h in range(2):
-        V(("copy", sb("LV", h, s_[0:128]), sb("LI", rev[h])))
-        V(("copy", sb("ZV", h, s_[0:128]), sb("ZI", rev[h])))
+        V(ts(sb("LV", h, s_[0:128]), sb("LI", rev[h]), -2048.0, A.add))
+        V(("copy", sb("LV", h, s_[128:256]), sb("ZI", rev[h])))
     G(("asel", sb("IDB", al), one, [[-1, 128]], A.is_equal, 0.0, 0, 1))
     G(("asel", sb("BOF", al), one, [[-16, 8], [0, 16]], A.is_ge, 0.0, 0, 1))
     G(("asel", sb("BOF", al), sb("BOF", al), [[16, 8], [0, 16]], A.is_ge, 0.0, 15, -1))
@@ -170,14 +180,13 @@ def plan():
     b8 = sb("BOF", s_[0::16])
     V(ms(sb("BPD", al), 0.0))
     V(ts(sb("BPD", s_[15::16]), b8, 2.0 ** -13, A.mult))
-    V(*[ts(sb(nm, s_[c:c + 8]), b8, x, A.mult) for nm, x in (("BOD", 256.0), ("BON", -128.0)) for c in (0, 8)])
+    V(*[ts(sb(nm, s_[c:c + 8]), b8, x, A.mult) for nm, x in (("BOD", 256.0), ("BON", -128.0), ("BOK", 128.0), ("BOK16", 128.0)) for c in (0, 8)])
     V(ts(sb("BOC", al), b8, 2.0 ** 21, A.mult), ("copy", sb("BO1", al), b8))
     V(ts(sb("PI", s_[0:1]), sb("PI", s_[0:1]), 15, A.bitwise_and), ts(sb("PI", s_[1:2]), sb("PI", s_[1:2]), 14, A.bitwise_and),
       ts(sb("PI", s_[2:3]), sb("PI", s_[2:3]), 1, A.bitwise_and))
     V(("copy", col(0), sb("PI", s_[0:1])), ts(col(4), sb("PI", s_[1:2]), 8.0, A.mult), ts(col(5), sb("PI", s_[2:3]), 2048.0, A.mult))
     V(*[ts(col(1 + j), col(0), float(j), A.is_equal) for j in range(3)])
-    V(ts(col(6), col(0), 6.0, A.is_equal, 2.0, A.mult), ts(col(8), col(0), 2.0 ** -12, A.mult, 0.25, A.add))
-    V(ts(col(6), col(6), -1.0, A.add), ts(col(7), col(1), 2.0 ** 26, A.mult))
+    V(ts(col(8), col(0), 2.0 ** -12, A.mult, 0.25, A.add), ts(col(7), col(1), 2.0 ** 29, A.mult))
     V(ts(sb("CL", 0, al), sb("IN", al), col(4), A.add), ts(sb("CL", 1, al), sb("IN", al), col(4), A.add, col(5), A.add))
     V(ts(sb("DUM", al), sb("IN", s_[0:8]), 2.0 ** -15, A.mult, col(8), A.add))
     r0, r32, r64 = s_[0:1], s_[32:33], s_[64:65]
@@ -191,21 +200,21 @@ def plan():
     V(ms(sb("RST", s_[0::16]), BIG), ms(sb("RSTN", s_[0::16]), -BIG), ms(sb("M2", al, s_[0:1]), BIG), ms(sb("M2F", al, s_[0:1]), -BIG))
     V(ts(sb("IM", al), sb("IM", al), 15, A.bitwise_and))
     V(ts(sb("MTW", al), sb("IM", al), 0.0, A.is_equal))
-    for nm in ("BA", "BE", "VT", "VF"):
+    for nm in ("BA", "BE", "VF"):
         V(ms(sb(nm, al, al), 0.0))
-    V(ms(sb("VT", al, s_[4::16]), 1.0), ms(sb("VF", al, s_[4:128:16]), 1.0), ms(sb("VF", al, s_[6:128:16]), 1.0))
-    V(ms(sb("R", s_[4096:4352]), 0.0), ms(sb("SL", al, s_[128:136]), 0), ms(sb("SZ", al, s_[128:136]), 0.0))
+    V(ms(sb("R", s_[4096:4352]), 0.0), ms(sb("SL", al, s_[256:264]), 0.0), ms(pt("C16", r0, al), 16384.0))
     sec[0] = "late"
     V(ms(pt("AQ", s_[0:96], al, al), 0.0), ms(pt("BQ", s_[0:96], al), 0.0))
-    q8 = 8192.0
+    q8, qf = 8192.0, -16384.0
     V(*[ms(pt("AQ", r, m, s_[sl::16]), x) for r, m, sl, x in (
-        (r0, 0, 0, 2 * q8), (r0, 1, 1, 2 * q8), (r64, 0, 2, -q8), (r64, 1, 3, -q8), (r32, s_[0:2], 4, -q8),
-        (r0, 2, 9, 2 * q8), (r0, 3, 11, 2 * q8), (r0, s_[2:4], 4, -30 * q8), (r32, s_[2:4], 4, q8), (r64, 2, 9, -30 * q8), (r64, 3, 11, -30 * q8),
-        (r64, 2, 13, q8), (r64, 3, 15, q8), (r64, s_[2:4], 4, 225 * q8), (r64, s_[2:4], 6, 61440.0))])
+        (r0, 0, 0, q8), (r0, 1, 1, q8), (r0, 0, 2, -q8), (r0, 1, 3, -q8), (r64, 0, 2, -q8), (r64, 1, 3, -q8), (r32, s_[0:2], 4, -q8), (r0, s_[0:2], 4, -q8),
+        (r0, 2, 9, qf), (r0, 3, 11, qf), (r64, 2, 9, -15 * qf), (r64, 3, 11, -15 * qf), (r0, 2, 13, -qf), (r0, 3, 15, -qf), (r64, 2, 13, 16 * qf), (r64, 3, 15, 16 * qf),
+        (r0, s_[2:4], 4, -31 * qf), (r32, s_[2:4], 4, qf), (r64, s_[2:4], 4, 240 * qf), (r64, s_[2:4], 6, 61440.0 + q8))])
+    V(ts(col(13), col(0), 2.0, A.not_equal), ts(col(14), col(0), 3.0, A.not_equal), ts(col(15), col(0), 13.0, A.is_lt))
+    V(ts(col(13), col(13), col(14), A.mult, col(15), A.mult))
     V(("copy", pt("BQ", r0, al), pt("IK", r0, s_[0:128])), ("tt", pt("BQ", r32, al), pt("IK", r32, s_[0:128]), pt("IK", r32, s_[0:128]), A.mult), ms(pt("BQ", r64, al), 1.0))
     PE(*[P(sb("M1", s_[128 * m:128 * m + 128]), [(pt("AQ", s_[0:96], m, al), pt("BQ", s_[0:96], al))]) for m in range(4)])
     V(*[("tt", sb("QM", m, al), sb("M1", s_[128 * m:128 * m + 128]), sb("BOF", al), A.mult) for m in range(4)])
-    V(*[ts(sb("QM", 2 + m, al), sb("QM", m, al), col(6), A.mult) for m in (2, 3)])
     V(ms(sb("KEEP", al), 1.0))
     V(ms(sb("E", al, al), 0.0))
     V(ms(sb("E", al, s_[129::EW]), 1.0), ms(sb("KEEP", s_[0::EW + 16]), 0.0))
@@ -235,21 +244,33 @@ def plan():
         H, li = str(h), 2 * t + h
         Z, K, M, Nb = "Z" + H, "K" + H, "M" + H, "N" + H
         mt = sb("MTW", s_[16 - t:144 - t])
-        LP = sb("LP", h, al)
+        LP = sb("LV", li, s_[0:128])
         sec[0] = "prep" + H
-        V(ts(LP, sb("LV", li, s_[0:128]), -2048.0, A.add))
-        PE(P(sb(Z, s_[0:128]), [(IDB, sb("ZV", li, s_[0:128]))]), P(sb(Z, s_[128:256]), [(sb("SEL0", al), LP)]))
-        S(act(sb("XG", h, al), ind(XW, sb("LV", li, s_[0:128])), F.Copy))
+        V(ts(sb("LU", h, al), LP, 2048.0, A.add))
+        ZP = sb("LV", li, s_[128:256])
+        PE(P(sb(Z, s_[0:128]), [(ID16, ZP)]), P(sb(Z, s_[128:256]), [(sb("SEL0", al), LP)]))
+        sec[0] = "svb" + H
+        PE(P(sb(Nb, s_[0:128]), [(sb("SEL0", al), LP), (sb("PID8", al), mt)]))
+        S(act(sb("SVB", h, al), sb(Nb, s_[0:128]), F.Identity, -8192.0))
+        sec[0] = "prep" + H
+        for e, a, b in OPT["xg"][h]:
+            gather(e, sb("XG", h, s_[16 * a:16 * b]), ind(XW, sb("LU", h, s_[a:b])))
         PE(P(sb(K, s_[0:256]), [(ones33, pt("CK", s_[0:33], s_[0:256]))], True, False))
-        for rows in ((1, 2, 3), (4, 5, 6, 7), (8, 9, 10, 11), (12, 13, 14, 15)):
+        for q, rows in enumerate(((1, 2, 3), (4, 5, 6, 7), (8, 9, 10, 11), (12, 13, 14, 15))):
+            if q in OPT["abs"][h]:
+                bk, k0, k1 = (Nb, M)[q % 2], rows[0], rows[-1] + 1
+                PE(*[P(sb(bk, s_[128 * (k - k0):128 * (k - k0) + 128]), [(IDB, sb("XG", h, s_[k::16])), (NID16, ZP)]) for k in rows])
+                S(act(sb("MX", h, s_[128 * k0:128 * k1]), sb(bk, s_[0:128 * (k1 - k0)]), F.Abs))
+                PE(*[P(sb(K, s_[k:256:16]), [(sb("MX", h, s_[128 * k:128 * k + 128]), sb("BOK", al))]
+                       + ([(ZP, sb("BOK16", al))] if len(OPT["abs"][h]) < 4 else []), False, False) for k in rows])
+                continue
             V(*[("tt", sb("MX", h, s_[128 * k:128 * k + 128]), sb("XG", h, s_[k::16]), sb(Z, s_[0:128]), A.max) for k in rows])
             PE(*[P(sb(K, s_[k:256:16]), [(sb("XG", h, s_[k::16]), sb("BON", al)), (sb("MX", h, s_[128 * k:128 * k + 128]), sb("BOD", al))], False, False) for k in rows])
         sec[0] = "conf" + H
-        for e, a, b in RGP[h][0]:
-            o, i = sb("RG", h, s_[16 * a:16 * b]), ind(RW, sb("LV", li, s_[a:b]))
-            S(act(o, i, F.Copy)) if e == "a" else V(("copy", o, i))
-        for n_, (a, b) in enumerate(RGP[h][1]):
-            last = n_ == len(RGP[h][1]) - 1
+        for e, a, b in OPT["rg"][h]:
+            gather(e, sb("RG", h, s_[16 * a:16 * b]), ind(RW, sb("LU", h, s_[a:b])))
+        for n_, (a, b) in enumerate(OPT["ce"][h]):
+            last = n_ == len(OPT["ce"][h]) - 1
             for rows in (((1, 2, 3, 4, 5), (6, 7, 8, 9, 10), (11, 12, 13), (14, 15)) if last else (tuple(range(1, 16)),)):
                 V(*[("tt", sb("CE", h, s_[128 * k + a:128 * k + b]), sb("RG", h, s_[16 * a + k:16 * b:16]), sb(Z, s_[128 + a:128 + b]), A.is_equal) for k in rows])
                 if last:
@@ -268,98 +289,114 @@ def plan():
         for v in range(2):
             V(ts(sb("OF", h, s_[128 * v:128 * v + 128]), rab[v], 2048.0, A.add))
         sec[0] = "far" + H
-        V(*[("tt", sb("VT", h, s_[2 + v::16]), sb("BA", h, s_[14 + v:142:16]), sb("BA", h, s_[14 + v:142:16]), A.mult) for v in range(2)])
-        PE(P(sb(M, s_[128:256]), [(sb("BA", h, s_[14:142]), IDB), (sb("VT", h, al), IDB)]))
-        S(act(sb("VTT", h, al), sb(M, s_[128:256]), F.Copy))
+        PE(P(sb(M, s_[128:256]), [(sb("BA", h, s_[14:142]), IDB), (sb("BA", h, s_[12:140]), IDB)]))
+        S(act(sb("VTT", h, al), sb(M, s_[128:256]), F.Square, col(13)))
         PE(*[P(sb(M, s_[256 + 128 * v:384 + 128 * v]), [(sb("QM", v, al), sb("VTT", h, al)), (ID16, LP)]) for v in range(2)])
-        V(ts(sb("S1", h, al), sb(M, s_[256:512]), -4096.0, A.max))
+        s1 = [sb("S1", v, s_[128 * h:128 * h + 128]) for v in range(2)]
+        V(*[ts(s1[v], sb(M, s_[256 + 128 * v:384 + 128 * v]), -4096.0, A.max) for v in range(2)])
         S(act(sb("FS", h, al), sb(K, s_[128:256]), F.Copy))
         PE(P(sb(K, s_[128:256]), [(sb("ID32", al), sb("FS", h, al))], True, False))
-        PE(P(sb(K, s_[128:256]), [(sb("S1", h, s_[128 * v:128 * v + 128]), sb("PEN16", al)) for v in range(2)], False, True))
+        PE(P(sb(K, s_[128:256]), [(s1[v], sb("PEN16", al)) for v in range(2)], False, True))
         V(("scan", sb("KF", h, s_[256:384]), sb("RSTN", al), sb(K, s_[128:256]), A.min, A.max))
         V(("tt", sb("M2F", h, s_[1:128]), sb(K, s_[129:256]), sb("KF", h, s_[256:383]), A.min))
         V(("scan", sb("KF", h, s_[384:512]), sb("RSTN", al), sb("M2F", h, al), A.min, A.max))
         sec[0] = "prew" + H
-        PE(P(sb(M, s_[128:256]), [(sb("BOFS16", al), sb("S1", h, s_[0:128]))]),
-           P(sb(M, s_[32:40]), [(sb("BPD", s_[15 - x:143 - x]), sb("S1", h, s_[x:128:16])) for x in range(16)]))
-        S(act(sb("LAB", h, al), sb(M, s_[128:256]), F.Identity, 7.5), act(sb("LML", h, al), sb(M, s_[32:40]), F.Identity, 7.5))
-        V(("copy", sb("E", h, s_[130::EW]), sb("LML", h, al)))
-        PE(P(sb(Nb, s_[0:128]), [(sb("SEL0", al), LP), (sb("PID8", al), mt)]), P(sb(Nb, s_[128:256]), [(ID16, rab[0]), (sb("NID8", al), mt)]))
-        S(act(sb("SVB", h, al), sb(Nb, s_[0:128]), F.Identity, -8192.0), act(sb("SVA", h, al), sb(Nb, s_[128:256]), F.Copy))
+        PE(P(sb(M, s_[128:256]), [(sb("BOFS16", al), s1[0])]), P(sb(M, s_[384:512]), [(ID16, rab[0]), (sb("NID8", al), mt)]))
+        if h:
+            PE(P(sb(M, s_[32:48]), [(sb("BPD", s_[15 - x:143 - x]), sb("S1", 0, s_[x::16])) for x in range(16)]))
+            S(*[act(o, sb(M, s_[32 + 8 * u:40 + 8 * u]), F.Identity, 7.5) for u in range(2) for o in (sb("LML", u, al), sb("E", u, s_[130::EW]))])
+        S(act(sb("LAB", h, al), sb(M, s_[128:256]), F.Identity, 7.5), act(sb("SVA", h, al), sb(M, s_[384:512]), F.Copy))
+        sec[0] = "fq" + H
+        V(ts(sb("RR", h, s_[32:48]), sb("KF", h, s_[271::16]), C7, A.add, -C7, A.add))
+        V(("tt", sb("VF", h, s_[13::16]), sb("KF", h, s_[271::16]), sb("RR", h, s_[32:48]), A.subtract))
+        PE(P(sb(M, s_[128:256]), [(sb("VF", h, s_[c:c + 128]), IDB) for c in (4, 0, 130, 126)]))
+        S(act(sb("VTF", h, al), sb(M, s_[128:256]), F.Square, col(13)))
+        PE(P(sb(K, s_[0:128]), [(sb("QM", 2, al), sb("VTF", h, al))], True, False))
 
     def count(t):
         sec[0] = "cnt"
         v = sb("M1", s_[40:41])
-        PE(P(v, [(pt("SC2", r0, al), pt("ONEB", r0, s_[0:1]))] + ([(sb("SN", al), sb("ZV", 2 * t + h, s_[128:129])) for h in range(2)] if t else [])))
+        PE(P(v, [(pt("SC2", r0, al), pt("ONEB", r0, s_[0:1]))] + ([(sb("SN", al), sb("LV", 2 * t + h, s_[256:257])) for h in range(2)] if t else [])))
         V(ts(sb("NR", s_[0:1]), v, C6, A.add, -C6, A.add))
         V(ts(sb("THT", al), sb("TH0", al), v, A.add, sb("NR", s_[0:1]), A.subtract))
 
     def second(t, h):
         H, li = str(h), 2 * t + h
         Z, K, M, Nb = "Z" + H, "K" + H, "M" + H, "N" + H
-        LP = sb("LP", h, al)
+        LP = sb("LV", li, s_[0:128])
+        lastv = t == TV - 1
         rab = [sb("RAB", h, s_[v::2]) for v in range(2)]
         xe = [sb("XE", h, s_[v::2]) for v in range(2)]
         sec[0] = "two" + H
         PE(P(sb(Nb, s_[256:512]), [(ones33, pt("CK", s_[0:33], s_[256:512]))], True, False))
         for v in range(2):
-            for e, a, b in XAP[h, v]:
-                o, i = sb("XA", h, s_[2048 * v + 16 * a:2048 * v + 16 * b]), ind(XW, sb("OF", h, s_[128 * v + a:128 * v + b]))
-                S(act(o, i, F.Copy)) if e == "a" else V(("copy", o, i))
-            for j0 in range(0, 16, 4):
-                xa = lambda j: sb("XA", h, s_[2048 * v + j:2048 * v + 2048:16])
-                my = lambda j: sb("MY", h, s_[2048 * v + 128 * j:2048 * v + 128 * j + 128])
-                V(*[("tt", my(j), xa(j), sb(Z, s_[0:128]), A.max) for j in range(j0, j0 + 4)])
-                PE(*[P(sb(Nb, s_[256 + 16 * v + j::32]), [(xa(j), sb("BON", s_[0:8])), (my(j), sb("BOD", s_[0:8]))], False, v == 1 and j == 15) for j in range(j0, j0 + 4)])
+            for e, a, b in OPT["xa"][2 * h + v]:
+                gather(e, sb("XA", h, s_[2048 * v + 16 * a:2048 * v + 16 * b]), ind(XW, sb("OF", h, s_[128 * v + a:128 * v + b])))
+            xa = lambda j, a=0, b=128: sb("XA", h, s_[2048 * v + 16 * a + j:2048 * v + 16 * b:16])
+            my = lambda j, a=0, b=128: sb("MY", h, s_[2048 * v + 128 * j + a:2048 * v + 128 * j + b])
+            key = lambda j: sb(Nb, s_[256 + 16 * v + j::32])
+            for a, b in OPT["my"][2 * h + v]:
+                for j0 in range(0, 16, 4):
+                    V(*[("tt", my(j, a, b), xa(j, a, b), sb(Z, s_[a:b]), A.max) for j in range(j0, j0 + 4)])
+                    if b == 128:
+                        PE(*[P(key(j), [(xa(j), sb("BON", s_[0:8]))], False, False) for j in range(j0, j0 + 4)])
+                        PE(*[P(key(j), [(my(j), sb("BOD", s_[0:8]))], False, v == 1 and j == 15) for j in range(j0, j0 + 4)])
+        sec[0] = "new" + H
+        PE(P(sb(Z, s_[256:512]), [(ID16, sb("RAB", h, al))], True, False))
         sec[0] = "end" + H
         V(("scan", sb("KF", h, s_[0:256]), sb("RST", al), sb(Nb, s_[256:512]), A.max, A.min))
-        V(ts(sb("RR", h, s_[16:48]), sb("KF", h, s_[15::16]), C7, A.add, -C7, A.add))
+        V(ts(sb("RR", h, s_[16:32]), sb("KF", h, s_[15:256:16]), C7, A.add, -C7, A.add))
         V(*[("tt", sb("BE", h, s_[14 + v:142:16]), sb("KF", h, s_[15 + 16 * v:256:32]), sb("RR", h, s_[16 + v:32:2]), A.subtract) for v in range(2)])
         PE(lists(M, 16, 1, "BE", h))
         V(("copy", sb("OE", h, al), sb(M, s_[16:32])))
-        V(("copy", sb("XE", h, al), ind(sb("XA", h, al), sb("OE", h, al))))
-        PE(P(sb(Nb, s_[0:128]), [(ID16, xe[0]), (NID16, xe[1])]))
-        S(act(sb("XD", h, al), sb(Nb, s_[0:128]), F.Abs))
+        gather(OPT["xe"][h], sb("XE", h, al), ind(sb("XA", h, al), sb("OE", h, al)))
+        sec[0] = "new" + H
+        PE(P(sb(M, s_[128:256]), [(sb("BE", h, s_[c:c + 128]), IDB) for c in (14, 12)]))
+        S(act(sb("VTU", h, al), sb(M, s_[128:256]), F.Square, col(13)))
         uu = [(sb("NBOF16", al), sb("THT", al)), (sb("BOF", al), sb("XD", h, al))]
+        PE(P(sb(M, s_[256:384]), uu[0:1], True, False))
+        PE(*[P(sb(Z, s_[256 + v::2]), [(sb("QM", v, al), sb("VTU", h, al))], False, v == 1) for v in range(2)])
+        V(ts(sb("S2", h, al), sb(Z, s_[256:512]), -4096.0, A.max))
+        PE(P(sb(K, s_[0:128]), [(sb("BOF16", al), sb("S2", h, s_[0::2]))], False, True),
+           P(sb(K, s_[128:256]), [(sb("QM", 3, al), sb("VTF", h, al)), (sb("BOF16", al), sb("S2", h, s_[1::2]))]))
+        PE(P(sb(Z, s_[0:128]), [(ID16, rab[1]), (pt("ONEB", r0, s_[0:128]), pt("C16", r0, al))], True, False))
+        NL = sb("NL", h, al)
+        for q in range(2):
+            V(("tt", NL, NL if q else LP, sb(K, s_[128 * q:128 * q + 128]), A.max))
+        sec[0] = "end" + H
+        PE(P(sb(Nb, s_[0:128]), [(ID16, xe[0]), (NID16, xe[1])]))
+        PE(P(sb(Nb, s_[128:256]), [(sb("HID16", al), xe[0]), (sb("HID16", al), xe[1])]))
+        S(act(sb("XD", h, al), sb(Nb, s_[0:128]), F.Abs))
+        PE(P(sb(M, s_[256:384]), uu[1:2], False, True))
+        sec[0] = "new" + H
+        zo = sb("YZ", rev[h]) if lastv else sb("SL", li, s_[128:256])
+        if OPT["z"][h] == "v":
+            V(ts(zo, sb(Nb, s_[128:256]), C0, A.add, -C0, A.add))
+        else:
+            S(act(sb("ZH", h, al), sb(Nb, s_[128:256]), F.Identity, C0))
+            S(act(zo, sb("ZH", h, al), F.Identity, -C0))
         PE(P(sb(Nb, s_[256:384]), uu))
         sec[0] = "wr" + H
-        V(("tt", sb("LABP", h, al), sb("LAB", h, al), sb(Nb, s_[256:384]), A.max))
+        V(("tt", sb("LABP", h, al), sb("LAB", h, al), sb(M, s_[256:384]), A.max))
         V(*[ts(sb("E", h, s_[EW * m + 1 + 16 * m:EW * m + 129]), sb("LABP", h, s_[16 * m:128]), sb("LML", h, s_[m:m + 1]), A.is_equal) for m in range(8)])
         V(("scan", sb("ES", h, al), sb("E", h, al), sb("KEEP", al), A.add, A.mult))
         V(("tt", sb("WC", h, al), sb("ES", h, s_[130::EW]), sb("DUM", al), A.min))
         V(ts(sb("WO", h, al), sb("WC", h, al), 8192.0, A.mult, 2048.0, A.add))
         V(("tt", ind(RW, sb("WO", h, al)), sb("SVA", h, al), sb("SVB", h, al), A.max))
         sec[0] = "new" + H
-        V(("tt", sb("VF", h, s_[9::16]), sb("KF", h, s_[271::16]), sb("RR", h, s_[32:48]), A.subtract))
-        V(("tt", sb("VF", h, s_[13::16]), sb("VF", h, s_[9::16]), sb("VF", h, s_[9::16]), A.mult),
-          *[("tt", sb("VF", h, s_[2 + v:128:16]), sb("BE", h, s_[14 + v:142:16]), sb("BE", h, s_[14 + v:142:16]), A.mult) for v in range(2)])
-        PE(P(sb(M, s_[128:256]), [(sb("BE", h, s_[14:142]), IDB), (sb("VF", h, s_[0:128]), IDB), (sb("VF", h, s_[126:254]), IDB)]))
-        S(act(sb("VTU", h, al), sb(M, s_[128:256]), F.Copy))
-        vtu = sb("VTU", h, al)
-        PE(*[P(sb(M, s_[256 + 128 * v:384 + 128 * v]), [(sb("QM", v, al), vtu), (ID16, rab[v])]) for v in range(2)])
-        V(ts(sb("S2", h, al), sb(M, s_[256:512]), -4096.0, A.max))
-        NL = sb("NL", h, al)
-        for v, bk, c0 in ((0, K, 256), (1, M, 0)):
-            PE(*[P(sb(bk, s_[c0 + 128 * u:c0 + 128 * u + 128]), [(sb("QM", 2 + v + 2 * u, al), vtu), (sb("BOF16", al), sb("S2", h, s_[128 * v:128 * v + 128]))]) for u in range(2)])
-        for v, bk, c0 in ((0, K, 256), (1, M, 0)):
-            V(("tt", NL, NL if v else LP, sb(bk, s_[c0:c0 + 128]), A.min))
-            V(("tt", NL, NL, sb(bk, s_[c0 + 128:c0 + 256]), A.max))
-        PE(P(sb(Z, s_[256:384]), [(sb("HID16", al), xe[0]), (sb("HID16", al), xe[1])]))
-        lastv = t == TV - 1
-        V(ts(sb("YZ", rev[h]) if lastv else sb("SZ", li, s_[0:128]), sb(Z, s_[256:384]), C0, A.add, -C0, A.add))
-        PE(P(sb(Z, s_[384:512]), uu))
-        S(act(sb("RU", h, al), sb(Z, s_[384:512]), F.Relu, col(7), 8192.0))
+        S(act(sb("RU", h, al), sb(Nb, s_[256:384]), F.Relu, col(7), 65536.0))
         if not lastv:
-            S(act(sb("SG", h, al), sb(Z, s_[384:512]), F.Sign, 0.0, 1.0, sb("CNT", h, s_[0:1])))
-            S(act(sb("SZ", li, s_[128:129]), sb("CNT", h, s_[0:1]), F.Copy))
-        PE(*[P(sb(K, s_[128 * u:128 * u + 128]), [(ID16, rab[1]), (sb(("IDB", "NIDB")[u], al), sb("RU", h, al))]) for u in range(2)])
-        V(("tt", NL, NL, sb(K, s_[0:128]), A.min))
-        V(("tt", NL, NL, sb(K, s_[128:256]), A.max))
+            S(act(sb("SG", h, al), sb(Nb, s_[256:384]), F.Sign, 0.0, 1.0, sb("CNT", h, s_[0:1])))
+            S(act(sb("SL", li, s_[256:257]), sb("CNT", h, s_[0:1]), F.Copy))
+        PE(P(sb(Z, s_[0:128]), [(sb("NIDB", al), sb("RU", h, al))], False, True))
+        V(("tt", sb(Z, s_[0:128]), NL, sb(Z, s_[0:128]), A.max))
+        V(ts(sb("NR2", h, al), sb(Z, s_[0:128]), C13, A.add, -C13, A.add))
         if not lastv:
-            V(ts(sb("SL", li, s_[0:128]), NL, 2048.0, A.add))
-            op("g", [("send", None, sb("SL", li, al), sb("SZ", li, al))], c=1200, send=(t, h))
+            V(("tt", sb("SL", li, s_[0:128]), sb(Z, s_[0:128]), sb("NR2", h, al), A.subtract))
+            op("g", [("send", None, sb("SL", li, al))], c=1200, send=(t, h))
         else:
-            V(ts(sb("YL", rev[h]), NL, 2048.0, A.add))
+            V(ts(sb("NR2", h, al), sb("NR2", h, al), -2048.0, A.add))
+            V(("tt", sb("YL", rev[h]), sb(Z, s_[0:128]), sb("NR2", h, al), A.subtract))
             half = s_[128 - 128 * h:256 - 128 * h]
             for nm, y in (("YL", "yl"), ("YZ", "yz")):
                 op("s", [("dma", (y, (al, half)), sb(nm, half))], c=2000, s=("do", 16))
@@ -369,7 +406,7 @@ def plan():
         if t:
             for h in range(2):
                 sec[0] = "arr"
-                op("x", [("land", sb("LV", 2 * t + h, al), sb("ZV", 2 * t + h, al))], c=3000, s=("ar%d%d" % (t, h), 8), after=(t - 1, h))
+                op("x", [("land", sb("LV", 2 * t + h, al))], c=3000, s=("ar%d%d" % (t, h), 8), after=(t - 1, h))
         first(t, 0)
         count(t)
         first(t, 1)
@@ -377,7 +414,7 @@ def plan():
         second(t, 1)
     sec[0] = "sum"
     for b in range(8):
-        V(("copy", sb("R16", s_[512 * b:512 * b + 512]), sb("R", s_[512 * b:512 * b + 512])))
+        gather("va"[b % 2], sb("R16", s_[512 * b:512 * b + 512]), sb("R", s_[512 * b:512 * b + 512]))
         PE(P(sb("K0", al), [(ID16, sb("R16", s_[512 * b:512 * b + 512]))], b == 0, b == 7))
     V(ts(sb("YR", al), sb("K0", al), 16384.0, A.add))
     op("s", [("dma", ("yr", s_[:, :]), sb("YR", al))], c=2000, s=("do", 16))
@@ -386,7 +423,7 @@ def plan():
 
 def touches(c):
     if c[0] == "land":
-        return [], [c[1], c[2]]
+        return [], [c[1]]
     rd, wr = [], []
     for j, x in enumerate(c[1:]):
         if not isap(x) or x[0] in HBM:
@@ -431,37 +468,134 @@ def edges(ops):
         o["pre"] = sorted(pre)
 
 
-def schedule(ops, bonus=BONUS):
+def place(ops, pre, succ, prio):
+    left, at, st, busy = [len(p) for p in pre], [0.0] * len(ops), [0.0] * len(ops), {}
+    ready = [i for i in range(len(ops)) if not left[i]]
+    while ready:
+        i = min(ready, key=lambda j: prio[j])
+        ready.remove(i)
+        e, c, s = ops[i]["e"], ops[i]["c"], at[i]
+        if e not in "stx":
+            li, k = busy.setdefault(e, []), 0
+            while k < len(li) and s + c > li[k][0]:
+                s, k = max(s, li[k][1]), k + 1
+            li.insert(k, (s, s + c))
+        st[i] = s
+        for j in succ[i]:
+            left[j] -= 1
+            at[j] = max(at[j], s + c + (0.0 if e == "p" == ops[j]["e"] else DEP))
+            if not left[j]:
+                ready.append(j)
+    return st
+
+
+def times(order, npre, out, occ, cs, want):
+    n = len(npre)
+    left, nxt = list(npre), [-1] * n
+    for li in order.values():
+        for a, b in zip(li, li[1:]):
+            nxt[a] = b
+            left[b] += 1
+    top = [i for i in range(n) if not left[i]]
+    s0, s1, why = [0.0] * n, [0.0] * n, [None] * n
+    for i in top:
+        a, b = s0[i], s1[i]
+        j = nxt[i]
+        for j, x, y, q in out[i] + ([(j, occ[i][0], occ[i][1], True)] if j >= 0 else []):
+            if a + x > s0[j]:
+                s0[j] = a + x
+                if not want:
+                    why[j] = (i, q)
+            if b + y > s1[j]:
+                s1[j] = b + y
+                if want:
+                    why[j] = (i, q)
+            left[j] -= 1
+            if not left[j]:
+                top.append(j)
+    if len(top) < n:
+        return None, None
+    ends = [max((s[i] + cs[i][m], i) for i in order["s"][-5:]) for m, s in enumerate((s0, s1))]
+    arcs, i = [], ends[want][1]
+    while why[i]:
+        if why[i][1]:
+            arcs.append((why[i][0], i))
+        i = why[i][0]
+    return (ends[0][0], ends[1][0], s0), arcs
+
+
+def orders(rounds=ROUNDS, seed=1):
+    short, ops = plan(3), plan()
+    edges(short)
+    edges(ops)
+    st = schedule(short, rounds[0], seed)[1][2]
+    at = {(o["t"], o["k"]): st[o["i"]] for o in short}
+    per = at[2, ("conf0", "a", 1)] - at[1, ("conf0", "a", 1)]
+    return ops, schedule(ops, rounds[1], seed, lambda t, k: at[0, k] if t == 0 else at[2, k] + (TV - 3) * per if t == TV - 1 else at[1, k] + (t - 1) * per)
+
+
+def schedule(ops, rounds, seed, start=None):
     n = len(ops)
-    succ = [[] for _ in ops]
+    pre, succ, head, key, seen = [o["pre"] for o in ops], [[] for _ in ops], [0.0] * n, {}, {}
     for o in ops:
         for p in o["pre"]:
             succ[p].append(o["i"])
-    lag = lambda a, b: 0.0 if ops[a]["e"] == "p" and ops[b]["e"] == "p" else DEP
-    tail = [0.0] * n
-    for o in reversed(ops):
-        tail[o["i"]] = o["c"] + max([tail[s] + lag(o["i"], s) for s in succ[o["i"]]] or [0.0])
-    prio = [tail[i] + bonus.get(ops[i]["sec"], 0.0) for i in range(n)]
-    left = [len(o["pre"]) for o in ops]
-    at, end, free, ready, order = [0.0] * n, [0.0] * n, {}, {}, {}
-    for o in ops:
-        if not left[o["i"]]:
-            ready.setdefault(o["e"], []).append(o["i"])
-    for _ in range(n):
-        st, e = min((min(max(free.get(e, 0.0), at[i]) for i in rs), e) for e, rs in ready.items() if rs)
-        i = min(ready[e]) if e in "st" else max((j for j in ready[e] if at[j] <= st + 1e-9), key=lambda j: (prio[j], -j))
-        ready[e].remove(i)
-        o = ops[i]
-        s0 = max(free.get(e, 0.0), at[i])
-        end[i] = s0 + o["c"]
-        free[e] = s0 + (50 if e in "stx" else o["c"])
-        order.setdefault(e, []).append(i)
-        for s in succ[i]:
-            left[s] -= 1
-            at[s] = max(at[s], end[i] + lag(i, s))
-            if not left[s]:
-                ready.setdefault(ops[s]["e"], []).append(s)
-    return order, end
+            if (ops[p]["sec"], ops[p]["t"]) == (o["sec"], o["t"]):
+                head[o["i"]] = max(head[o["i"]], head[p] + ops[p]["c"] + DEP)
+        k = (o["t"], o["sec"], o["e"])
+        seen[k] = seen.get(k, 0) + 1
+        o["k"] = (o["sec"], o["e"], seen[k])
+        key[o["t"], o["k"]] = o["i"]
+    if start:
+        prio, left, st = [start(o["t"], o["k"]) + o["i"] * 1e-3 for o in ops], [len(p) for p in pre], [0] * n
+        ready = [i for i in range(n) if not left[i]]
+        for r in range(n):
+            i = min(ready, key=lambda j: prio[j])
+            ready.remove(i)
+            st[i] = r
+            for j in succ[i]:
+                left[j] -= 1
+                if not left[j]:
+                    ready.append(j)
+    else:
+        st = place(ops, pre, succ, [1000.0 * (o["t"] * PERIOD + PLACE[o["sec"]]) + head[o["i"]] + o["i"] * 1e-3 for o in ops])
+        back = place(ops, succ, pre, [-st[i] - ops[i]["c"] + i * 1e-3 for i in range(n)])
+        st = place(ops, pre, succ, [-back[i] - ops[i]["c"] + i * 1e-3 for i in range(n)])
+    order = {}
+    for i in sorted(range(n), key=lambda i: (i if ops[i]["e"] in "st" else st[i], i)):
+        order.setdefault(ops[i]["e"], []).append(i)
+    cs = [(o["c"], o["c2"]) for o in ops]
+    occ = [(50.0, 50.0) if o["e"] in "stx" else cs[o["i"]] for o in ops]
+    out = [[(j, cs[i][0] + w * DEP, cs[i][1] + w * SLOW[4], False) for j in succ[i] for w in (0 if ops[i]["e"] == "p" == ops[j]["e"] else 1,)] for i in range(n)]
+    npre = [len(p) for p in pre]
+    rnd = np.random.RandomState(seed).random_sample(8 * rounds + 8).tolist()
+    val = lambda r: r[0] + 0.5 * r[1]
+    res, arcs = times(order, npre, out, occ, cs, 0)
+    cur, best = val(res), (val(res), res, {e: list(li) for e, li in order.items()})
+    for it in range(rounds):
+        r = rnd[8 * it:8 * it + 8]
+        cand = [a for a in arcs if ops[a[0]]["e"] in "vapg" and a[0] not in pre[a[1]]]
+        u, v = cand[int(r[0] * len(cand))]
+        e = ops[u]["e"]
+        li, old = order[e], list(order[e])
+        if r[1] < 0.3:
+            u = li[max(0, li.index(u) - 1 - int(3 * r[2]))]
+        elif r[1] < 0.6:
+            v = li[min(len(li) - 1, li.index(v) + 1 + int(3 * r[2]))]
+        d = ops[v]["t"] - ops[u]["t"]
+        for a, b in [(u, v)] if r[3] < 0.25 else [(key.get((t, ops[u]["k"])), key.get((t + d, ops[v]["k"]))) for t in range(TV)]:
+            if a is not None and b is not None:
+                ia, ib = li.index(a), li.index(b)
+                if ia < ib <= ia + 12:
+                    li.insert(ib, li.pop(ia)) if 0.3 <= r[1] < 0.6 else li.insert(ia, li.pop(ib))
+        res, a2 = times(order, npre, out, occ, cs, int(r[4] < 0.35))
+        if res and val(res) <= cur * (1 + 0.004 * r[5] * (1 - it / rounds)):
+            cur, arcs = val(res), a2
+            if cur < best[0]:
+                best = (cur, res, {e: list(li) for e, li in order.items()})
+        else:
+            order[e] = old
+    return best[2], best[1]
 
 
 def issue(g, q, T, c):
@@ -505,9 +639,8 @@ def rank_program(g, core, T, topo):
     if rank is None:
         return
     if not PLAN:
-        ops = plan()
-        edges(ops)
-        PLAN.extend([ops, schedule(ops)[0]])
+        ops, found = orders()
+        PLAN.extend([ops, found[0]])
     ops, order = PLAN
     queue = {"v": g.vector, "a": g.scalar, "p": g.tensor, "g": g, "s": g.sync}
     nxt = T.cores[(rank + 1) % N]
@@ -547,13 +680,8 @@ def rank_program(g, core, T, topo):
                 if "send" in o:
                     t, h = o["send"]
                     rid, pid = topo.addr(nxt)[0:2]
-                    eng = topo.engines(core, nxt)
-                    dst = DstId(rid=rid, pnc=pid)
-                    g.remote_dma_fused([
-                        RemoteDMATransfer(dst_ids=[dst], dma_engine_mask=sum(1 << x for x in eng[4 * j:4 * j + 4]), remote_sem=T.sem["ar%d%d" % (t + 1, h)],
-                                          src=T[a][:, 2 * t + h, :], dst=T[b][:, 2 * t + 2 + h, :]) for j, (a, b) in enumerate((("SL", "LV"), ("SZ", "ZV")))],
-                        local_sem=T.sem.ls)
-                    sent += 8
+                    g.remote_dma(T.LV[:, 2 * t + 2 + h, :], T.SL[:, 2 * t + h, :], T.sem["ar%d%d" % (t + 1, h)], T.sem.ls, pid, rid, topo.mask(core, nxt))
+                    sent += len(topo.engines(core, nxt))
                     continue
                 for c in o["calls"]:
                     last = issue(g, q, T, c)

@@ -1,31 +1,29 @@
 import numpy as np
-from concourse.bass import DstId, RemoteDMATransfer
 from concourse.mybir import AluOpType as A, ActivationFunctionType as F, AxisListType
 
 N, TV = 4, 5
-CYC, PEC, GA, SCA, DEP = 0.83, 0.71, 1.5, 3.5, 100.0
-EW = 131
+CYC = 0.83
+FIGURES, WEIGHTS = ((1.56, 3.8, 1.0, 0.71, 100.0, 3000.0), (1.1, 2.0, 1.0, 0.6, 70.0, 2500.0), (2.0, 5.5, 1.3, 0.8, 150.0, 4000.0)), (0.5, 0.3)
+ROUNDS, SEED = (4000, 600), 1
 B16, H16, F32, I32, U16 = "bfloat16", "float16", "float32", "int32", "uint16"
 SB = {
-    "X": ([4096], B16), "R": ([4352], F32), "R16": ([4096], H16), "LI": ([256], I32), "ZI": ([256], B16), "THI": ([8], I32), "THB": ([8], I32),
-    "LV": ([2 * TV, 264], H16), "SL": ([2 * TV, 264], H16), "C16": ([128], B16), "S1": ([2, 256], H16), "BOK16": ([16], H16), "ONEH": ([2], H16),
-    "ONEB": ([256], B16), "IDB": ([128], B16), "NIDB": ([128], B16), "PID8": ([128], B16), "NID8": ([128], B16), "ID16": ([128], H16), "NID16": ([128], H16),
-    "ID32": ([128], F32), "HID16": ([128], H16), "PEN16": ([128], H16), "BOF": ([128], B16), "BOF16": ([128], H16), "NBOF16": ([128], H16), "BOFS16": ([128], H16),
-    "BPD": ([143], H16), "BOD": ([16], B16), "BON": ([16], B16), "BOK": ([16], B16), "BOC": ([8], B16), "BO1": ([8], F32), "SELB": ([128], B16), "SEL0": ([128], H16),
-    "RX": ([128], B16), "IK": ([256], F32), "PI": ([4], I32), "IM": ([144], I32), "MTW": ([144], B16), "IN": ([16], F32), "CO": ([24], F32),
-    "CL": ([2, 16], B16), "CK": ([512], B16), "CAPK": ([128], F32), "RST": ([256], F32), "RSTN": ([128], F32), "AQ": ([4, 128], B16), "BQ": ([128], B16),
-    "QM": ([6, 128], B16), "KEEP": ([8 * EW], H16), "DG": ([2, 16], H16), "DUM": ([8], F32), "TH": ([8], F32), "TH0": ([128], H16), "THT": ([128], H16),
-    "SN": ([128], H16), "SC2": ([128], B16), "NR": ([2], F32), "YL": ([256], F32), "YZ": ([256], B16), "YR": ([512], F32),
+    "X": ([4096], B16), "R": ([4160], I32), "R16": ([4096], H16), "LI": ([256], I32), "ZI": ([256], B16), "THI": ([8], I32), "THB": ([8], I32),
+    "LV": ([2 * TV, 264], H16), "SL": ([2 * TV, 264], H16), "C16": ([128], B16), "ONEB": ([256], B16), "IDB": ([128], B16), "NIDB": ([128], B16),
+    "ID16": ([128], H16), "NID16": ([128], H16), "ID32": ([128], F32), "HID16": ([128], H16), "PEN16": ([128], H16), "BOF": ([128], B16), "BOF16": ([128], H16),
+    "NBOU16": ([128], H16), "BOU": ([128], H16), "NBH16": ([128], H16), "BOD": ([16], B16), "BON": ([16], B16), "BOC": ([8], B16), "BO1": ([8], F32),
+    "SELB": ([128], B16), "SEL0": ([128], H16), "RX": ([128], B16), "IK": ([256], F32), "PI": ([4], I32), "IM": ([144], I32), "MT": ([2, 144], B16), "IN": ([16], F32),
+    "CO": ([24], F32), "CL": ([2, 16], B16), "CK": ([512], B16), "CAPK": ([2, 128], F32), "IG": ([128], F32), "CNT": ([2], F32), "RST": ([256], B16), "RSTN": ([128], B16),
+    "AQ": ([4, 128], B16), "BQ": ([128], B16), "QM": ([4, 128], B16), "MK": ([2, 256], B16), "IJ": ([256], B16), "RS2": ([256], B16), "BL": ([256], B16),
+    "BL16": ([256], H16), "DM": ([128], B16), "TH": ([8], F32), "TH0": ([128], H16), "THT": ([128], H16), "SN": ([128], H16), "SC2": ([128], B16), "NR": ([2], F32),
+    "YL": ([256], F32), "YZ": ([256], B16), "YR": ([512], F32),
 }
-for _q in range(4):
-    SB["RI%d" % _q] = ([1024], I32)
 for _n, (_s, _d) in {
     "LU": ([128], U16), "VTF": ([128], B16), "XG": ([2048], B16), "MX": ([2048], B16), "RG": ([2048], F32), "CE": ([2048], B16), "XA": ([4096], B16), "MY": ([4096], B16),
     "KS": ([256], F32), "M2": ([128], F32), "KF": ([512], F32), "M2F": ([128], F32), "FS": ([128], F32), "RR": ([48], F32), "BA": ([144], B16), "BE": ([144], B16),
-    "VF": ([264], B16), "AB": ([2048], B16), "ZH": ([128], F32), "VTT": ([128], B16), "VTU": ([128], B16), "OL": ([16], U16), "OE": ([16], U16), "RAB": ([256], H16),
-    "XE": ([256], H16), "OF": ([256], U16), "NR2": ([128], F32), "S2": ([256], H16), "LAB": ([128], F32), "LML": ([8], F32), "LABP": ([128], H16),
-    "SVA": ([128], F32), "SVB": ([128], F32), "NL": ([128], F32), "XD": ([128], B16), "RU": ([128], B16), "SG": ([128], B16), "CNT": ([2], F32),
-    "E": ([8 * EW], H16), "ES": ([8 * EW], H16), "WC": ([8], F32), "WO": ([8], U16),
+    "VF": ([264], B16), "ZH": ([128], F32), "VTT": ([128], B16), "VTU": ([128], B16), "OL": ([16], U16), "OE": ([16], U16), "RAB": ([256], H16),
+    "XE": ([256], H16), "OF": ([256], U16), "NR2": ([128], F32), "S1": ([256], H16), "S2": ([256], H16), "LD": ([128], H16), "LMS": ([8], F32),
+    "SV": ([128], F32), "SVB": ([128], F32), "NL": ([128], F32), "XD": ([128], H16), "SG": ([128], B16),
+    "AD": ([256], B16), "WT": ([256], B16), "WS": ([256], B16), "WC": ([8], F32), "WO": ([8], U16),
 }.items():
     SB[_n] = ([2] + _s, _d)
 SCRATCH = {_n: ("sbuf", [128] + _s, _d) for _n, (_s, _d) in SB.items()}
@@ -39,14 +37,18 @@ s_ = np.s_
 C7, C6, C0 = 1.5 * 2.0 ** 30, 1.5 * 2.0 ** 29, 1.5 * 2.0 ** 23
 C13 = 1.5 * 2.0 ** 36
 BIG = 2.0 ** 30
-WHOLE, TWO = (("a", 0, 128),), (("a", 0, 64), ("a", 64, 128))
-OPT = {"xg": [WHOLE, (("a", 0, 96), ("v", 96, 128))], "rg": [TWO, WHOLE], "ce": [((0, 64), (64, 128)), ((0, 128),)], "xa": [TWO, TWO, TWO, TWO], "xe": ["v", "a"], "z": ["a", "a"],
-       "abs": [(), ()], "my": [((0, 128),), ((0, 64), (64, 128)), ((0, 128),), ((0, 64), (64, 128))]}
-SLOW = (1.9, 5.0, 1.3, 0.85, 170.0, 4500.0)
-PERIOD, ROUNDS = 27.0, (16000, 3000)
-PLACE = {"init": -20, "late": -3, "arr": -30, "cnt": 5, "sum": 30, "prep0": -4, "svb0": 0, "conf0": 0, "sel0": 3.5, "far0": 6.5, "prew0": 8, "fq0": 9, "two0": 8.9,
-         "end0": 12.5, "new0": 12.6, "wr0": 20, "prep1": 3.7, "svb1": 8, "conf1": 6.3, "sel1": 10, "far1": 13, "prew1": 14.5, "fq1": 15, "two1": 14.2,
-         "end1": 21, "new1": 21.1, "wr1": 23}
+TWO, FOUR, T2 = (("a", 0, 64), ("a", 64, 128)), tuple(("a", 32 * _q, 32 * _q + 32) for _q in range(4)), ((0, 64), (64, 128))
+OPT = {"xg": [FOUR, TWO], "rg": [(("v", 0, 48), ("a", 48, 88), ("a", 88, 128)), (("v", 0, 32), ("a", 32, 80), ("a", 80, 128))], "xa": [TWO, TWO, FOUR, FOUR],
+       "mx": [T2, T2], "ce": [T2, T2], "my": [T2] * 4, "rab": ["a", "a"], "xe": ["v", "a"], "xd": ["v", "v"],
+       "z": ["v", "v"], "ru": ["m", "m"], "prew": ["late", "early"], "gr": 2, "cefirst": [False, False], "sum": "vavavava"}
+AHEAD, PERIOD = (250.0, 150.0, 100.0, 500.0), 26.0
+RANK = {"init": dict(v=-30, g=-30, p=-30, a=-30), "late": dict(v=5, p=-10, g=-30), "cnt": dict(p=7, v=7), "sum": dict(v=40, p=40, a=40),
+        "lu0": dict(v=-30), "prep0": dict(p=-2, a=-3, v=0), "svb0": dict(p=2, a=2), "conf0": dict(p=-2, a=-2, v=0.5), "qq0": dict(p=1), "sel0": dict(v=-5, p=-5, a=-5),
+        "far0": dict(p=2, a=2, v=7.5), "fq0": dict(v=7.6, p=2, a=2), "two0": dict(p=3, a=3, v=8), "end0": dict(v=-3, p=-3, a=-3), "new0": dict(v=-2.9, p=-2.9, a=-2.9, g=0),
+        "zz0": dict(p=-2.8, v=-2.8, a=-2.8), "prew0": dict(a=13, p=9, v=13), "wr0": dict(v=13),
+        "lu1": dict(v=-30), "prep1": dict(p=4, a=1, v=6), "svb1": dict(p=5, a=5), "conf1": dict(v=6.5, p=4, a=1.5), "qq1": dict(p=5), "sel1": dict(v=-4, p=-4, a=-4),
+        "far1": dict(a=11, p=11, v=13.5), "fq1": dict(v=13.5, p=11, a=13), "prew1": dict(a=14, p=12, v=14), "two1": dict(p=10, a=12, v=14),
+        "end1": dict(v=5, p=5, a=5), "new1": dict(p=5.5, a=5.5, v=5.5, g=0), "zz1": dict(p=5.6, a=5.6, v=5.6), "sg1": dict(a=5.7), "wr1": dict(v=6)}
 
 
 def sb(name, *idx):
@@ -65,18 +67,13 @@ def isap(x):
     return isinstance(x, tuple) and isinstance(x[0], str)
 
 
-def shape_of(name):
-    return SCRATCH[name][1]
-
-
 CELLS = {}
 
 
 def cells(ap):
     key = (ap[0], str(ap[1]))
     if key not in CELLS:
-        sh = shape_of(ap[0])[1:]
-        m = np.zeros(sh, bool)
+        m = np.zeros(SCRATCH[ap[0]][1][1:], bool)
         m[ap[1][1:]] = True
         CELLS[key] = (int(m.sum()), int.from_bytes(np.packbits(m.reshape(-1)).tobytes(), "big"))
     return CELLS[key]
@@ -113,8 +110,6 @@ def plan(TV=TV):
 
     def op(e, calls, **kw):
         o = {"e": e, "calls": calls, "i": len(ops), "t": vis[0], "sec": sec[0]}
-        o["c2"] = (SLOW[5] if e == "x" else kw["c"]) if "c" in kw else SLOW[2] * sum(cost(e, c, SLOW[0], SLOW[1], SLOW[3]) for c in calls)
-        o["c"] = kw.pop("c") if "c" in kw else sum(cost(e, c, GA, SCA, PEC) for c in calls)
         o.update(kw)
         ops.append(o)
 
@@ -139,8 +134,11 @@ def plan(TV=TV):
     def act(o, i, f, bias=0.0, scale=1.0, acc=None):
         return ("act", o, i, f, bias, scale, acc)
 
-    def gather(e, o, i):
-        S(act(o, i, F.Copy)) if e == "a" else V(("copy", o, i))
+    def move(e, o, i, add=0.0, times=1.0):
+        if e == "a":
+            S(act(o, i, F.Identity, add, times) if add or times != 1.0 else act(o, i, F.Copy))
+        else:
+            V(ts(o, i, times, A.mult, add, A.add) if add or times != 1.0 else ("copy", o, i))
 
     def col(j):
         return sb("CO", s_[j:j + 1])
@@ -153,7 +151,7 @@ def plan(TV=TV):
     load("t", "dx1", 3500, sb("X", s_[2048:4096]), ("xt", s_[:, 2048:4096]))
     load("s", "dz", 4000, sb("ZI", al), ("z0", s_[:, :]))
     for q in range(4):
-        load("s" if q % 2 else "t", "dr%d" % q, 6000 + 1500 * q, sb("RI%d" % q, al), ("ex", s_[:, 1024 * q:1024 * q + 1024]))
+        load("s" if q % 2 else "t", "dr%d" % q, 6000 + 1500 * q, sb("R", s_[32 + 1024 * q:1056 + 1024 * q]), ("ex", s_[:, 1024 * q:1024 * q + 1024]))
     load("s", "dt", 9000, pt("THI", s_[0:1], al), ("th", s_[:, :]))
 
     ms = lambda o, x: ("memset", o, x)
@@ -168,58 +166,61 @@ def plan(TV=TV):
     G(("asel", sb("BOF", al), sb("BOF", al), [[16, 8], [0, 16]], A.is_ge, 0.0, 15, -1))
     G(("asel", sb("SELB", al), one, [[-16, 8], [0, 16]], A.is_equal, 0.0, 0, 1))
     G(("iota", sb("IK", al), [[0, 16], [1, 16]], 0, 0))
+    G(("iota", sb("IG", al), [[-3, 8], [0, 16]], 12, 0))
     G(("iota", sb("PI", al), [[0, 4]], 0, 1))
     G(("asel", sb("RX", al), one, [[-1, 8], [-8, 16]], A.is_equal, 0.0, 0, 1))
     G(("iota", sb("IN", al), [[128, 16]], 0, 0))
-    G(("iota", sb("IM", al), [[1, 144]], 1, 1))
-    G(("pbc", sb("THB", al), pt("THI", s_[0:1], al), 128))
-    for nm, src, x in (("ID16", "IDB", 1.0), ("ID32", "IDB", 1.0), ("NID16", "IDB", -1.0), ("HID16", "IDB", 0.5 - 2.0 ** -12), ("PEN16", "IDB", -512.0), ("NIDB", "IDB", -1.0),
-                       ("PID8", "IDB", 8192.0), ("NID8", "IDB", -8192.0), ("SEL0", "SELB", 1.0), ("BOF16", "BOF", 1.0), ("NBOF16", "BOF", -1.0),
-                       ("BOFS16", "BOF", 2.0 ** -13)):
+    for nm, src, x in (("ID16", "IDB", 1.0), ("SEL0", "SELB", 1.0)):
         V(ts(sb(nm, al), sb(src, al), x, A.mult))
     b8 = sb("BOF", s_[0::16])
-    V(ms(sb("BPD", al), 0.0))
-    V(ts(sb("BPD", s_[15::16]), b8, 2.0 ** -13, A.mult))
-    V(*[ts(sb(nm, s_[c:c + 8]), b8, x, A.mult) for nm, x in (("BOD", 256.0), ("BON", -128.0), ("BOK", 128.0), ("BOK16", 128.0)) for c in (0, 8)])
-    V(ts(sb("BOC", al), b8, 2.0 ** 21, A.mult), ("copy", sb("BO1", al), b8))
+    V(*[ts(sb(nm, s_[c:c + 8]), b8, x, A.mult) for nm, x in (("BOD", 256.0), ("BON", -128.0)) for c in (0, 8)], ts(sb("BOC", al), b8, 2.0 ** 21, A.mult))
     V(ts(sb("PI", s_[0:1]), sb("PI", s_[0:1]), 15, A.bitwise_and), ts(sb("PI", s_[1:2]), sb("PI", s_[1:2]), 14, A.bitwise_and),
       ts(sb("PI", s_[2:3]), sb("PI", s_[2:3]), 1, A.bitwise_and))
     V(("copy", col(0), sb("PI", s_[0:1])), ts(col(4), sb("PI", s_[1:2]), 8.0, A.mult), ts(col(5), sb("PI", s_[2:3]), 2048.0, A.mult))
-    V(*[ts(col(1 + j), col(0), float(j), A.is_equal) for j in range(3)])
-    V(ts(col(8), col(0), 2.0 ** -12, A.mult, 0.25, A.add), ts(col(7), col(1), 2.0 ** 29, A.mult))
     V(ts(sb("CL", 0, al), sb("IN", al), col(4), A.add), ts(sb("CL", 1, al), sb("IN", al), col(4), A.add, col(5), A.add))
-    V(ts(sb("DUM", al), sb("IN", s_[0:8]), 2.0 ** -15, A.mult, col(8), A.add))
     r0, r32, r64 = s_[0:1], s_[32:33], s_[64:65]
     V(ms(pt("CK", s_[0:64], al), 0.0))
     V(("copy", pt("CK", r0, s_[0:128]), pt("IK", r0, s_[0:128])), ts(pt("CK", r0, s_[128:256]), pt("IK", r0, s_[0:128]), -1.0, A.mult, 15.0, A.add),
-      ("copy", pt("CK", r0, s_[256:512]), pt("IK", r0, al)), ms(pt("CK", r32, s_[0:128:16]), 2.0 ** 21), ms(pt("CK", r32, s_[128:256]), -2.0 ** 22))
-    V(ms(pt("CK", r32, s_[128:256:16]), -2.0 ** 23))
-    V(ts(sb("CAPK", al), sb("IK", s_[0:128]), 2.0 ** 20, A.add))
-    V(ms(sb("CAPK", s_[0::16]), 1.5 * 2.0 ** 20))
-    V(ms(sb("RST", al), -BIG), ms(sb("RSTN", al), BIG))
-    V(ms(sb("RST", s_[0::16]), BIG), ms(sb("RSTN", s_[0::16]), -BIG), ms(sb("M2", al, s_[0:1]), BIG), ms(sb("M2F", al, s_[0:1]), -BIG))
-    V(ts(sb("IM", al), sb("IM", al), 15, A.bitwise_and))
-    V(ts(sb("MTW", al), sb("IM", al), 0.0, A.is_equal))
-    for nm in ("BA", "BE", "VF"):
-        V(ms(sb(nm, al, al), 0.0))
-    V(ms(sb("R", s_[4096:4352]), 0.0), ms(sb("SL", al, s_[256:264]), 0.0), ms(pt("C16", r0, al), 16384.0))
+      ("copy", pt("CK", r0, s_[256:512]), pt("IK", r0, al)), ts(pt("CK", r32, s_[0:128]), pt("IG", r32, al), 2.0 ** 19, A.mult), ms(pt("CK", r32, s_[128:256]), -2.0 ** 22))
+    V(ms(pt("CK", r32, s_[128:256:16]), -2.0 ** 23), ms(pt("CK", r32, s_[0:128:16]), BIG))
+    V(ts(sb("IG", al), sb("IG", al), 2.0, A.add, 2.0 ** 19, A.mult))
+    V(*[("tt", sb("CAPK", u, al), sb("IG", al), sb("IK", s_[0:128]), A.add) for u in range(2)])
+    V(ms(sb("CAPK", al, s_[0::16]), BIG), ms(sb("CAPK", 1, s_[1::16]), BIG), ms(sb("M2", al, s_[0:1]), BIG), ms(sb("BA", al, al), 0.0))
+    V(ms(sb("R", s_[0:32]), 0), ms(sb("R", s_[4128:4160]), 0))
     sec[0] = "late"
+    G(("iota", sb("IM", al), [[1, 144]], 1, 1))
+    G(("pbc", sb("THB", al), pt("THI", s_[0:1], al), 128))
+    for nm, src, x in (("ID32", "IDB", 1.0), ("NID16", "IDB", -1.0), ("HID16", "IDB", 0.25 - 2.0 ** -13), ("PEN16", "IDB", -512.0), ("NIDB", "IDB", -16384.0),
+                       ("NBH16", "BOF", -16384.0), ("BOF16", "BOF", 1.0), ("NBOU16", "BOF", -32768.0), ("BOU", "BOF", 32768.0)):
+        V(ts(sb(nm, al), sb(src, al), x, A.mult))
+    V(*[ts(col(1 + j), col(0), float(j), A.is_equal) for j in range(3)], ("copy", sb("BO1", al), b8))
+    V(*[ts(col(16 + j), col(0), x, A.add) for j, x in enumerate((0.0, 16.0, 4128.0, 4144.0))], ts(col(7), col(1), 2.0 ** 29, A.mult))
+    V(ms(sb("RST", al), -BIG), ms(sb("RSTN", al), BIG), ms(sb("RS2", al), -BIG))
+    V(ms(sb("RST", s_[0::16]), BIG), ms(sb("RSTN", s_[0::16]), -BIG), ms(sb("RS2", s_[0::32]), BIG), ms(sb("M2F", al, s_[0:1]), -BIG))
+    V(ts(sb("IM", al), sb("IM", al), 15, A.bitwise_and))
+    V(ts(sb("MT", 0, al), sb("IM", al), 0.0, A.is_equal, -8192.0, A.mult), ts(sb("MT", 1, al), sb("IM", al), 0.0, A.not_equal, -8192.0, A.mult))
+    V(ts(sb("MT", al, al), sb("MT", al, al), 2048.0, A.add))
+    for nm in ("BE", "VF"):
+        V(ms(sb(nm, al, al), 0.0))
+    V(ms(sb("SL", al, s_[256:264]), 0.0), ms(pt("C16", r0, al), 61440.0))
     V(ms(pt("AQ", s_[0:96], al, al), 0.0), ms(pt("BQ", s_[0:96], al), 0.0))
     q8, qf = 8192.0, -16384.0
-    V(*[ms(pt("AQ", r, m, s_[sl::16]), x) for r, m, sl, x in (
-        (r0, 0, 0, q8), (r0, 1, 1, q8), (r0, 0, 2, -q8), (r0, 1, 3, -q8), (r64, 0, 2, -q8), (r64, 1, 3, -q8), (r32, s_[0:2], 4, -q8), (r0, s_[0:2], 4, -q8),
-        (r0, 2, 9, qf), (r0, 3, 11, qf), (r64, 2, 9, -15 * qf), (r64, 3, 11, -15 * qf), (r0, 2, 13, -qf), (r0, 3, 15, -qf), (r64, 2, 13, 16 * qf), (r64, 3, 15, 16 * qf),
-        (r0, s_[2:4], 4, -31 * qf), (r32, s_[2:4], 4, qf), (r64, s_[2:4], 4, 240 * qf), (r64, s_[2:4], 6, 61440.0 + q8))])
+    for part in (((r0, 0, 0, q8), (r0, 1, 1, q8), (r0, 0, 2, -q8), (r64, 0, 2, -q8)), ((r0, 1, 3, -q8), (r64, 1, 3, -q8)), ((r32, s_[0:2], 4, -q8), (r0, s_[0:2], 4, -q8)),
+                 ((r0, 2, 9, qf), (r64, 2, 9, -15 * qf)), ((r0, 3, 11, qf), (r64, 3, 11, -15 * qf)), ((r0, 2, 13, -qf), (r64, 2, 13, 16 * qf)),
+                 ((r0, 3, 15, -qf), (r64, 3, 15, 16 * qf)), ((r0, s_[2:4], 4, -31 * qf), (r32, s_[2:4], 4, qf), (r64, s_[2:4], 4, 240 * qf), (r64, s_[2:4], 6, 61440.0 + q8))):
+        V(*[ms(pt("AQ", r, m, s_[sl::16]), x) for r, m, sl, x in part])
     V(ts(col(13), col(0), 2.0, A.not_equal), ts(col(14), col(0), 3.0, A.not_equal), ts(col(15), col(0), 13.0, A.is_lt))
     V(ts(col(13), col(13), col(14), A.mult, col(15), A.mult))
     V(("copy", pt("BQ", r0, al), pt("IK", r0, s_[0:128])), ("tt", pt("BQ", r32, al), pt("IK", r32, s_[0:128]), pt("IK", r32, s_[0:128]), A.mult), ms(pt("BQ", r64, al), 1.0))
     PE(*[P(sb("M1", s_[128 * m:128 * m + 128]), [(pt("AQ", s_[0:96], m, al), pt("BQ", s_[0:96], al))]) for m in range(4)])
-    V(*[("tt", sb("QM", m, al), sb("M1", s_[128 * m:128 * m + 128]), sb("BOF", al), A.mult) for m in range(4)])
-    V(ms(sb("KEEP", al), 1.0))
-    V(ms(sb("E", al, al), 0.0))
-    V(ms(sb("E", al, s_[129::EW]), 1.0), ms(sb("KEEP", s_[0::EW + 16]), 0.0))
-    V(ts(sb("DG", 0, al), sb("IK", s_[0:16]), col(0), A.is_gt), ts(sb("DG", 1, al), sb("IK", s_[0:16]), col(0), A.is_equal))
-    V(*[("tt", sb("KEEP", s_[(EW + 16) * m + 1:(EW + 16) * m + 17]), sb("DG", 0, al), sb("DG", 1, al), A.subtract) for m in range(8)])
+    for m in range(4):
+        V(("tt", sb("QM", m, al), sb("M1", s_[128 * m:128 * m + 128]), sb("BOF", al), A.mult))
+    G(("iota", sb("IJ", al), [[-16, 2], [0, 4], [1, 32]], 0, 0))
+    G(("asel", sb("BL", al), sb("ONEB", al), [[-16, 2], [-32, 4], [0, 32]], A.is_ge, 0.0, 0, 1))
+    G(("asel", sb("BL", al), sb("BL", al), [[16, 2], [32, 4], [0, 32]], A.is_ge, 0.0, 15, -1))
+    V(ts(sb("MK", 0, al), sb("IJ", al), col(0), A.is_lt, 8192.0, A.mult), ts(sb("MK", 1, al), sb("IJ", al), col(0), A.is_equal, 0.5, A.mult))
+    V(("tt", sb("MK", 0, al), sb("MK", 0, al), sb("MK", 1, al), A.add))
+    V(("copy", sb("BL16", al), sb("BL", al)), ts(sb("DM", al), sb("IK", s_[0:128]), col(0), A.is_equal, -1.0, A.mult))
     V(("copy", sb("TH", al), sb("THB", al)))
     V(("tt", sb("TH", al), sb("TH", al), sb("BO1", al), A.mult))
     V(("red", col(9), sb("TH", al), A.add))
@@ -229,12 +230,14 @@ def plan(TV=TV):
     V(ts(sb("TH0", al), one, col(11), A.mult, col(12), A.add))
     V(ms(sb("SN", al), 0.0), ms(pt("SC2", r0, al), 0.0))
     V(ts(sb("SN", s_[2::16]), sb("ONEB", s_[0:8]), col(2), A.mult, -0.5, A.mult), ms(pt("SC2", r0, s_[2::16]), -31.5))
-    sec[0] = "init"
-    for q in range(4):
-        V(ts(sb("R", s_[1024 * q:1024 * q + 1024]), sb("RI%d" % q, al), -2048.0, A.add))
-    IDB, ID16, NID16 = sb("IDB", al), sb("ID16", al), sb("NID16", al)
-    XW, RW = sb("X", al), sb("R", al)
+    IDB, ID16, NID16, BOF16 = sb("IDB", al), sb("ID16", al), sb("NID16", al), sb("BOF16", al)
+    XW, RW = sb("X", al), sb("R", s_[32:4128])
     ones33 = pt("ONEB", s_[0:33], s_[0:128])
+    wide = (s_[0:256], al)
+    groups = ((1, 2, 3), (4, 5, 6, 7), (8, 9, 10, 11), (12, 13, 14, 15))
+
+    def column(h, v):
+        return sb("RAB", h, s_[v::2])
 
     def lists(bank, c0, which, tile, h):
         out = sb(bank, s_[c0:c0 + 16])
@@ -243,80 +246,98 @@ def plan(TV=TV):
     def first(t, h):
         H, li = str(h), 2 * t + h
         Z, K, M, Nb = "Z" + H, "K" + H, "M" + H, "N" + H
-        mt = sb("MTW", s_[16 - t:144 - t])
-        LP = sb("LV", li, s_[0:128])
-        sec[0] = "prep" + H
+        LP, ZP = sb("LV", li, s_[0:128]), sb("LV", li, s_[128:256])
+        sec[0] = "lu" + H
         V(ts(sb("LU", h, al), LP, 2048.0, A.add))
-        ZP = sb("LV", li, s_[128:256])
+        sec[0] = "prep" + H
         PE(P(sb(Z, s_[0:128]), [(ID16, ZP)]), P(sb(Z, s_[128:256]), [(sb("SEL0", al), LP)]))
         sec[0] = "svb" + H
-        PE(P(sb(Nb, s_[0:128]), [(sb("SEL0", al), LP), (sb("PID8", al), mt)]))
-        S(act(sb("SVB", h, al), sb(Nb, s_[0:128]), F.Identity, -8192.0))
+        PE(P(sb(Nb, s_[0:128]), [(sb("SEL0", al), LP), (IDB, sb("MT", 1, s_[16 - t:144 - t]))]))
+        S(act(sb("SVB", h, al), sb(Nb, s_[0:128]), F.Copy))
         sec[0] = "prep" + H
         for e, a, b in OPT["xg"][h]:
-            gather(e, sb("XG", h, s_[16 * a:16 * b]), ind(XW, sb("LU", h, s_[a:b])))
+            move(e, sb("XG", h, s_[16 * a:16 * b]), ind(XW, sb("LU", h, s_[a:b])))
         PE(P(sb(K, s_[0:256]), [(ones33, pt("CK", s_[0:33], s_[0:256]))], True, False))
-        for q, rows in enumerate(((1, 2, 3), (4, 5, 6, 7), (8, 9, 10, 11), (12, 13, 14, 15))):
-            if q in OPT["abs"][h]:
-                bk, k0, k1 = (Nb, M)[q % 2], rows[0], rows[-1] + 1
-                PE(*[P(sb(bk, s_[128 * (k - k0):128 * (k - k0) + 128]), [(IDB, sb("XG", h, s_[k::16])), (NID16, ZP)]) for k in rows])
-                S(act(sb("MX", h, s_[128 * k0:128 * k1]), sb(bk, s_[0:128 * (k1 - k0)]), F.Abs))
-                PE(*[P(sb(K, s_[k:256:16]), [(sb("MX", h, s_[128 * k:128 * k + 128]), sb("BOK", al))]
-                       + ([(ZP, sb("BOK16", al))] if len(OPT["abs"][h]) < 4 else []), False, False) for k in rows])
-                continue
-            V(*[("tt", sb("MX", h, s_[128 * k:128 * k + 128]), sb("XG", h, s_[k::16]), sb(Z, s_[0:128]), A.max) for k in rows])
-            PE(*[P(sb(K, s_[k:256:16]), [(sb("XG", h, s_[k::16]), sb("BON", al)), (sb("MX", h, s_[128 * k:128 * k + 128]), sb("BOD", al))], False, False) for k in rows])
-        sec[0] = "conf" + H
-        for e, a, b in OPT["rg"][h]:
-            gather(e, sb("RG", h, s_[16 * a:16 * b]), ind(RW, sb("LU", h, s_[a:b])))
-        for n_, (a, b) in enumerate(OPT["ce"][h]):
-            last = n_ == len(OPT["ce"][h]) - 1
-            for rows in (((1, 2, 3, 4, 5), (6, 7, 8, 9, 10), (11, 12, 13), (14, 15)) if last else (tuple(range(1, 16)),)):
-                V(*[("tt", sb("CE", h, s_[128 * k + a:128 * k + b]), sb("RG", h, s_[16 * a + k:16 * b:16]), sb(Z, s_[128 + a:128 + b]), A.is_equal) for k in rows])
-                if last:
-                    PE(*[P(sb(K, s_[k:128:16]), [(sb("CE", h, s_[128 * k:128 * k + 128]), sb("BOC", al))], False, k == 15) for k in rows])
+        for rows in groups:
+            PE(*[P(sb(K, s_[k:256:16]), [(sb("XG", h, s_[k::16]), sb("BON", al))], False, False) for k in rows])
+
+        def conflicts(last):
+            sec[0] = "conf" + H
+            for e, a, b in OPT["rg"][h]:
+                move(e, sb("RG", h, s_[16 * a:16 * b]), ind(RW, sb("LU", h, s_[a:b])), -2048.0)
+            for a, b in OPT["ce"][h]:
+                for rows in groups:
+                    for u in range(0, len(rows), OPT["gr"]):
+                        V(*[("tt", sb("CE", h, s_[128 * k + a:128 * k + b]), sb("RG", h, s_[16 * a + k:16 * b:16]), sb(Z, s_[128 + a:128 + b]), A.is_equal)
+                            for k in rows[u:u + OPT["gr"]]])
+                    if b == 128:
+                        PE(*[P(sb(K, s_[k:128:16]), [(sb("CE", h, s_[128 * k:128 * k + 128]), sb("BOC", al))], False, last and k == 15) for k in rows])
+
+        def maxima(last):
+            sec[0] = "prep" + H
+            for a, b in OPT["mx"][h]:
+                for rows in groups:
+                    for u in range(0, len(rows), OPT["gr"]):
+                        V(*[("tt", sb("MX", h, s_[128 * k + a:128 * k + b]), sb("XG", h, s_[16 * a + k:16 * b:16]), sb(Z, s_[a:b]), A.max) for k in rows[u:u + OPT["gr"]]])
+                    if b == 128:
+                        PE(*[P(sb(K, s_[k:256:16]), [(sb("MX", h, s_[128 * k:128 * k + 128]), sb("BOD", al))], False, last and k == 15) for k in rows])
+        for n_, part in enumerate((conflicts, maxima) if OPT["cefirst"][h] else (maxima, conflicts)):
+            part(n_ == 1)
+        sec[0] = "qq" + H
+        qq = (sb(M, s_[256:384]), sb(Nb, s_[0:128]))
+        for v in range(2):
+            PE(P(qq[v], [(ID16, LP)], True, False))
         sec[0] = "sel" + H
-        V(("tt", sb(K, s_[0:128]), sb(K, s_[0:128]), sb("CAPK", al), A.min))
-        V(("scan", sb("KS", h, s_[0:128]), sb("RST", s_[0:128]), sb(K, s_[0:128]), A.max, A.min))
+        V(("scan", sb("KS", h, s_[0:128]), sb("CAPK", 0, al), sb(K, s_[0:128]), A.min, A.min))
         V(("tt", sb("M2", h, s_[1:128]), sb(K, s_[1:128]), sb("KS", h, s_[0:127]), A.max))
-        V(("scan", sb("KS", h, s_[128:256]), sb("RST", s_[0:128]), sb("M2", h, al), A.max, A.min))
+        V(("scan", sb("KS", h, s_[128:256]), sb("CAPK", 1, al), sb("M2", h, al), A.min, A.min))
         V(ts(sb("RR", h, s_[0:16]), sb("KS", h, s_[15::16]), C7, A.add, -C7, A.add))
         V(*[("tt", sb("BA", h, s_[14 + v:142:16]), sb("KS", h, s_[128 * v + 15:128 * v + 128:16]), sb("RR", h, s_[8 * v:8 * v + 8]), A.subtract) for v in range(2)])
-        PE(lists(M, 0, 0, "BA", h))
-        V(("copy", sb("OL", h, al), sb(M, s_[0:16])))
-        V(("copy", sb("RAB", h, al), ind(sb("RG", h, al), sb("OL", h, al))))
-        rab = [sb("RAB", h, s_[v::2]) for v in range(2)]
+        PE(lists(Z, 256, 0, "BA", h))
+        V(("copy", sb("OL", h, al), sb(Z, s_[256:272])))
+        move(OPT["rab"][h], sb("RAB", h, al), ind(sb("RG", h, al), sb("OL", h, al)))
         for v in range(2):
-            V(ts(sb("OF", h, s_[128 * v:128 * v + 128]), rab[v], 2048.0, A.add))
+            V(ts(sb("OF", h, s_[128 * v:128 * v + 128]), column(h, v), 2048.0, A.add))
         sec[0] = "far" + H
-        PE(P(sb(M, s_[128:256]), [(sb("BA", h, s_[14:142]), IDB), (sb("BA", h, s_[12:140]), IDB)]))
-        S(act(sb("VTT", h, al), sb(M, s_[128:256]), F.Square, col(13)))
-        PE(*[P(sb(M, s_[256 + 128 * v:384 + 128 * v]), [(sb("QM", v, al), sb("VTT", h, al)), (ID16, LP)]) for v in range(2)])
-        s1 = [sb("S1", v, s_[128 * h:128 * h + 128]) for v in range(2)]
-        V(*[ts(s1[v], sb(M, s_[256 + 128 * v:384 + 128 * v]), -4096.0, A.max) for v in range(2)])
+        PE(P(sb(Z, s_[128:256]), [(sb("BA", h, s_[14:142]), IDB), (sb("BA", h, s_[12:140]), IDB)]))
+        S(act(sb("VTT", h, al), sb(Z, s_[128:256]), F.Square, col(13)))
+        s1 = [sb("S1", h, s_[128 * v:128 * v + 128]) for v in range(2)]
+        for v in range(2):
+            PE(P(qq[v], [(sb("QM", v, al), sb("VTT", h, al))], False, True))
+        for v in range(2):
+            V(ts(s1[v], qq[v], -4096.0, A.max))
         S(act(sb("FS", h, al), sb(K, s_[128:256]), F.Copy))
         PE(P(sb(K, s_[128:256]), [(sb("ID32", al), sb("FS", h, al))], True, False))
         PE(P(sb(K, s_[128:256]), [(s1[v], sb("PEN16", al)) for v in range(2)], False, True))
         V(("scan", sb("KF", h, s_[256:384]), sb("RSTN", al), sb(K, s_[128:256]), A.min, A.max))
         V(("tt", sb("M2F", h, s_[1:128]), sb(K, s_[129:256]), sb("KF", h, s_[256:383]), A.min))
         V(("scan", sb("KF", h, s_[384:512]), sb("RSTN", al), sb("M2F", h, al), A.min, A.max))
-        sec[0] = "prew" + H
-        PE(P(sb(M, s_[128:256]), [(sb("BOFS16", al), s1[0])]), P(sb(M, s_[384:512]), [(ID16, rab[0]), (sb("NID8", al), mt)]))
-        if h:
-            PE(P(sb(M, s_[32:48]), [(sb("BPD", s_[15 - x:143 - x]), sb("S1", 0, s_[x::16])) for x in range(16)]))
-            S(*[act(o, sb(M, s_[32 + 8 * u:40 + 8 * u]), F.Identity, 7.5) for u in range(2) for o in (sb("LML", u, al), sb("E", u, s_[130::EW]))])
-        S(act(sb("LAB", h, al), sb(M, s_[128:256]), F.Identity, 7.5), act(sb("SVA", h, al), sb(M, s_[384:512]), F.Copy))
         sec[0] = "fq" + H
         V(ts(sb("RR", h, s_[32:48]), sb("KF", h, s_[271::16]), C7, A.add, -C7, A.add))
         V(("tt", sb("VF", h, s_[13::16]), sb("KF", h, s_[271::16]), sb("RR", h, s_[32:48]), A.subtract))
-        PE(P(sb(M, s_[128:256]), [(sb("VF", h, s_[c:c + 128]), IDB) for c in (4, 0, 130, 126)]))
-        S(act(sb("VTF", h, al), sb(M, s_[128:256]), F.Square, col(13)))
+        PE(P(sb(K, s_[256:384]), [(sb("VF", h, s_[c:c + 128]), IDB) for c in (4, 0, 130, 126)]))
+        S(act(sb("VTF", h, al), sb(K, s_[256:384]), F.Square, col(13)))
         PE(P(sb(K, s_[0:128]), [(sb("QM", 2, al), sb("VTF", h, al))], True, False))
+        if OPT["prew"][h] == "early":
+            writers(t, h)
+
+    def writers(t, h):
+        M, s1 = "M" + str(h), sb("S1", h, s_[0:128])
+        sec[0] = "prew" + str(h)
+        bk, c0 = (M, 128) if OPT["prew"][h] == "early" else ("N" + str(h), 256)
+        PE(P(sb(M, s_[384:512]), [(s1, BOF16), (pt("ONEB", r0, s_[0:128]), pt("C16", r0, al))]))
+        V(("tt", sb("LD", h, al), sb(M, s_[384:512]), sb("DM", al), A.mult))
+        PE(P(sb(M, s_[0:8]), [(sb("LD", h, al), sb("BL16", s_[0::32]))]), P(sb(M, s_[384:512]), [(ID16, column(h, 0)), (IDB, sb("MT", 0, s_[16 - t:144 - t]))]))
+        PE(P(sb(bk, s_[c0:c0 + 256]), [(IDB, sb("MK", 0, al)), (sb("LD", h, al), sb("BL16", al))], True, False),
+           *[P(sb(bk, s_[c0 + 128 * u:c0 + 128 * u + 128]), [(BOF16, s1)], False, u == 1) for u in range(2)])
+        S(act(sb("AD", h, al), sb(bk, s_[c0:c0 + 256]), F.Abs, 61440.0 * 16384.0, 16384.0))
+        S(act(sb("LMS", h, al), sb(M, s_[0:8]), F.Identity, 2048.0 + 32.0 - 8192.0, -1.0))
+        V(("tt", sb("SV", h, al), sb("SVB", h, al), sb(M, s_[384:512]), A.max))
 
     def count(t):
         sec[0] = "cnt"
         v = sb("M1", s_[40:41])
-        PE(P(v, [(pt("SC2", r0, al), pt("ONEB", r0, s_[0:1]))] + ([(sb("SN", al), sb("LV", 2 * t + h, s_[256:257])) for h in range(2)] if t else [])))
+        PE(P(v, [(pt("SC2", r0, al), pt("ONEB", r0, s_[0:1]))] + ([(sb("SN", al), sb("LV", 2 * t + 1, s_[256 + h:257 + h])) for h in range(2)] if t else [])))
         V(ts(sb("NR", s_[0:1]), v, C6, A.add, -C6, A.add))
         V(ts(sb("THT", al), sb("TH0", al), v, A.add, sb("NR", s_[0:1]), A.subtract))
 
@@ -325,21 +346,22 @@ def plan(TV=TV):
         Z, K, M, Nb = "Z" + H, "K" + H, "M" + H, "N" + H
         LP = sb("LV", li, s_[0:128])
         lastv = t == TV - 1
-        rab = [sb("RAB", h, s_[v::2]) for v in range(2)]
         xe = [sb("XE", h, s_[v::2]) for v in range(2)]
         sec[0] = "two" + H
         PE(P(sb(Nb, s_[256:512]), [(ones33, pt("CK", s_[0:33], s_[256:512]))], True, False))
         for v in range(2):
             for e, a, b in OPT["xa"][2 * h + v]:
-                gather(e, sb("XA", h, s_[2048 * v + 16 * a:2048 * v + 16 * b]), ind(XW, sb("OF", h, s_[128 * v + a:128 * v + b])))
+                move(e, sb("XA", h, s_[2048 * v + 16 * a:2048 * v + 16 * b]), ind(XW, sb("OF", h, s_[128 * v + a:128 * v + b])))
             xa = lambda j, a=0, b=128: sb("XA", h, s_[2048 * v + 16 * a + j:2048 * v + 16 * b:16])
             my = lambda j, a=0, b=128: sb("MY", h, s_[2048 * v + 128 * j + a:2048 * v + 128 * j + b])
             key = lambda j: sb(Nb, s_[256 + 16 * v + j::32])
+            for j0 in range(0, 16, 4):
+                PE(*[P(key(j), [(xa(j), sb("BON", s_[0:8]))], False, False) for j in range(j0, j0 + 4)])
             for a, b in OPT["my"][2 * h + v]:
                 for j0 in range(0, 16, 4):
-                    V(*[("tt", my(j, a, b), xa(j, a, b), sb(Z, s_[a:b]), A.max) for j in range(j0, j0 + 4)])
+                    for j1 in range(j0, j0 + 4, OPT["gr"]):
+                        V(*[("tt", my(j, a, b), xa(j, a, b), sb(Z, s_[a:b]), A.max) for j in range(j1, j1 + OPT["gr"])])
                     if b == 128:
-                        PE(*[P(key(j), [(xa(j), sb("BON", s_[0:8]))], False, False) for j in range(j0, j0 + 4)])
                         PE(*[P(key(j), [(my(j), sb("BOD", s_[0:8]))], False, v == 1 and j == 15) for j in range(j0, j0 + 4)])
         sec[0] = "new" + H
         PE(P(sb(Z, s_[256:512]), [(ID16, sb("RAB", h, al))], True, False))
@@ -349,51 +371,62 @@ def plan(TV=TV):
         V(*[("tt", sb("BE", h, s_[14 + v:142:16]), sb("KF", h, s_[15 + 16 * v:256:32]), sb("RR", h, s_[16 + v:32:2]), A.subtract) for v in range(2)])
         PE(lists(M, 16, 1, "BE", h))
         V(("copy", sb("OE", h, al), sb(M, s_[16:32])))
-        gather(OPT["xe"][h], sb("XE", h, al), ind(sb("XA", h, al), sb("OE", h, al)))
+        move(OPT["xe"][h], sb("XE", h, al), ind(sb("XA", h, al), sb("OE", h, al)), 0.0, 2.0)
         sec[0] = "new" + H
-        PE(P(sb(M, s_[128:256]), [(sb("BE", h, s_[c:c + 128]), IDB) for c in (14, 12)]))
-        S(act(sb("VTU", h, al), sb(M, s_[128:256]), F.Square, col(13)))
-        uu = [(sb("NBOF16", al), sb("THT", al)), (sb("BOF", al), sb("XD", h, al))]
+        PE(P(sb(Nb, s_[0:128]), [(sb("BE", h, s_[c:c + 128]), IDB) for c in (14, 12)]))
+        S(act(sb("VTU", h, al), sb(Nb, s_[0:128]), F.Square, col(13)))
+        uu = [(sb("NBOU16", al), sb("THT", al))] + ([(sb("NBH16", al), x) for x in xe] if OPT["xd"][h] == "v" else []) + [(sb("BOU", al), sb("XD", h, al))]
         PE(P(sb(M, s_[256:384]), uu[0:1], True, False))
         PE(*[P(sb(Z, s_[256 + v::2]), [(sb("QM", v, al), sb("VTU", h, al))], False, v == 1) for v in range(2)])
         V(ts(sb("S2", h, al), sb(Z, s_[256:512]), -4096.0, A.max))
-        PE(P(sb(K, s_[0:128]), [(sb("BOF16", al), sb("S2", h, s_[0::2]))], False, True),
-           P(sb(K, s_[128:256]), [(sb("QM", 3, al), sb("VTF", h, al)), (sb("BOF16", al), sb("S2", h, s_[1::2]))]))
-        PE(P(sb(Z, s_[0:128]), [(ID16, rab[1]), (pt("ONEB", r0, s_[0:128]), pt("C16", r0, al))], True, False))
+        PE(P(sb(K, s_[0:128]), [(BOF16, sb("S2", h, s_[0::2]))], False, True),
+           P(sb(K, s_[128:256]), [(sb("QM", 3, al), sb("VTF", h, al)), (BOF16, sb("S2", h, s_[1::2]))]))
+        PE(P(sb(Z, s_[0:128]), [(ID16, column(h, 1))], True, False))
         NL = sb("NL", h, al)
         for q in range(2):
             V(("tt", NL, NL if q else LP, sb(K, s_[128 * q:128 * q + 128]), A.max))
         sec[0] = "end" + H
-        PE(P(sb(Nb, s_[0:128]), [(ID16, xe[0]), (NID16, xe[1])]))
+        if OPT["xd"][h] == "v":
+            V(("tt", sb("XD", h, al), xe[0], xe[1], A.max))
+            PE(P(sb(M, s_[256:384]), uu[1:3], False, False))
+        else:
+            PE(P(sb(Nb, s_[0:128]), [(ID16, xe[0]), (NID16, xe[1])]))
+            S(act(sb("XD", h, al), sb(Nb, s_[0:128]), F.Abs, 0.0, 0.5))
+        PE(P(sb(M, s_[256:384]), uu[-1:], False, True))
+        sec[0] = "zz" + H
         PE(P(sb(Nb, s_[128:256]), [(sb("HID16", al), xe[0]), (sb("HID16", al), xe[1])]))
-        S(act(sb("XD", h, al), sb(Nb, s_[0:128]), F.Abs))
-        PE(P(sb(M, s_[256:384]), uu[1:2], False, True))
-        sec[0] = "new" + H
         zo = sb("YZ", rev[h]) if lastv else sb("SL", li, s_[128:256])
         if OPT["z"][h] == "v":
             V(ts(zo, sb(Nb, s_[128:256]), C0, A.add, -C0, A.add))
         else:
             S(act(sb("ZH", h, al), sb(Nb, s_[128:256]), F.Identity, C0))
             S(act(zo, sb("ZH", h, al), F.Identity, -C0))
-        PE(P(sb(Nb, s_[256:384]), uu))
-        sec[0] = "wr" + H
-        V(("tt", sb("LABP", h, al), sb("LAB", h, al), sb(M, s_[256:384]), A.max))
-        V(*[ts(sb("E", h, s_[EW * m + 1 + 16 * m:EW * m + 129]), sb("LABP", h, s_[16 * m:128]), sb("LML", h, s_[m:m + 1]), A.is_equal) for m in range(8)])
-        V(("scan", sb("ES", h, al), sb("E", h, al), sb("KEEP", al), A.add, A.mult))
-        V(("tt", sb("WC", h, al), sb("ES", h, s_[130::EW]), sb("DUM", al), A.min))
-        V(ts(sb("WO", h, al), sb("WC", h, al), 8192.0, A.mult, 2048.0, A.add))
-        V(("tt", ind(RW, sb("WO", h, al)), sb("SVA", h, al), sb("SVB", h, al), A.max))
         sec[0] = "new" + H
-        S(act(sb("RU", h, al), sb(Nb, s_[256:384]), F.Relu, col(7), 65536.0))
-        if not lastv:
-            S(act(sb("SG", h, al), sb(Nb, s_[256:384]), F.Sign, 0.0, 1.0, sb("CNT", h, s_[0:1])))
-            S(act(sb("SL", li, s_[256:257]), sb("CNT", h, s_[0:1]), F.Copy))
-        PE(P(sb(Z, s_[0:128]), [(sb("NIDB", al), sb("RU", h, al))], False, True))
+        ub = sb(M, s_[256:384])
+        if OPT["ru"][h] == "n":
+            ub = sb(Nb, s_[256:384])
+            PE(P(ub, uu))
+        S(act(sb("SG", h, al), ub, F.Sign, col(7), 1.0, None if lastv else sb("CNT", s_[h:h + 1])))
+        if h and not lastv:
+            sec[0] = "sg" + H
+            S(act(sb("SL", li, s_[256:258]), sb("CNT", al), F.Copy))
+        if OPT["prew"][h] == "late":
+            writers(t, h)
+        sec[0] = "wr" + H
+        for u in range(2):
+            V(("tt", sb("WT", h, s_[128 * u:128 * u + 128]), sb("AD", h, s_[128 * u:128 * u + 128]), sb(M, s_[256:384]), A.max))
+        V(("scan", sb("WS", h, al), sb("RS2", al), sb("WT", h, al), A.max, A.min))
+        V(("tt", sb("WC", h, al), sb("WS", h, s_[31::32]), sb("LMS", h, al), A.add))
+        V(*[ts(sb("WO", h, s_[u::2]), sb("WC", h, s_[4 * u:4 * u + 4]), col(16 + u), A.max, col(18 + u), A.min) for u in range(2)])
+        for q in range(4):
+            V(("copy", ind(sb("R", al), sb("WO", h, s_[2 * q:2 * q + 2])), sb("SV", h, s_[32 * q:32 * q + 32])))
+        sec[0] = "new" + H
+        PE(P(sb(Z, s_[0:128]), [(sb("NIDB", al), sb("SG", h, al))], False, True))
         V(("tt", sb(Z, s_[0:128]), NL, sb(Z, s_[0:128]), A.max))
         V(ts(sb("NR2", h, al), sb(Z, s_[0:128]), C13, A.add, -C13, A.add))
         if not lastv:
             V(("tt", sb("SL", li, s_[0:128]), sb(Z, s_[0:128]), sb("NR2", h, al), A.subtract))
-            op("g", [("send", None, sb("SL", li, al))], c=1200, send=(t, h))
+            op("g", [("send", None, sb("SL", li, wide[h]))], c=1200, send=(t, h), to=[(1, sb("LV", li + 2, wide[h]))], sem="ar%d%d" % (t + 1, h))
         else:
             V(ts(sb("NR2", h, al), sb("NR2", h, al), -2048.0, A.add))
             V(("tt", sb("YL", rev[h]), sb(Z, s_[0:128]), sb("NR2", h, al), A.subtract))
@@ -406,7 +439,7 @@ def plan(TV=TV):
         if t:
             for h in range(2):
                 sec[0] = "arr"
-                op("x", [("land", sb("LV", 2 * t + h, al))], c=3000, s=("ar%d%d" % (t, h), 8), after=(t - 1, h))
+                op("x", [("land", sb("LV", 2 * t + h, wide[h]))], c=3000, s=("ar%d%d" % (t, h), 1), after=(t - 1, h))
         first(t, 0)
         count(t)
         first(t, 1)
@@ -414,7 +447,7 @@ def plan(TV=TV):
         second(t, 1)
     sec[0] = "sum"
     for b in range(8):
-        gather("va"[b % 2], sb("R16", s_[512 * b:512 * b + 512]), sb("R", s_[512 * b:512 * b + 512]))
+        move(OPT["sum"][b], sb("R16", s_[512 * b:512 * b + 512]), sb("R", s_[32 + 512 * b:544 + 512 * b]), -2048.0)
         PE(P(sb("K0", al), [(ID16, sb("R16", s_[512 * b:512 * b + 512]))], b == 0, b == 7))
     V(ts(sb("YR", al), sb("K0", al), 16384.0, A.add))
     op("s", [("dma", ("yr", s_[:, :]), sb("YR", al))], c=2000, s=("do", 16))
@@ -468,134 +501,146 @@ def edges(ops):
         o["pre"] = sorted(pre)
 
 
-def place(ops, pre, succ, prio):
-    left, at, st, busy = [len(p) for p in pre], [0.0] * len(ops), [0.0] * len(ops), {}
-    ready = [i for i in range(len(ops)) if not left[i]]
-    while ready:
-        i = min(ready, key=lambda j: prio[j])
-        ready.remove(i)
-        e, c, s = ops[i]["e"], ops[i]["c"], at[i]
-        if e not in "stx":
-            li, k = busy.setdefault(e, []), 0
-            while k < len(li) and s + c > li[k][0]:
-                s, k = max(s, li[k][1]), k + 1
-            li.insert(k, (s, s + c))
-        st[i] = s
-        for j in succ[i]:
-            left[j] -= 1
-            at[j] = max(at[j], s + c + (0.0 if e == "p" == ops[j]["e"] else DEP))
-            if not left[j]:
-                ready.append(j)
-    return st
-
-
-def times(order, npre, out, occ, cs, want):
-    n = len(npre)
-    left, nxt = list(npre), [-1] * n
-    for li in order.values():
-        for a, b in zip(li, li[1:]):
-            nxt[a] = b
-            left[b] += 1
-    top = [i for i in range(n) if not left[i]]
-    s0, s1, why = [0.0] * n, [0.0] * n, [None] * n
-    for i in top:
-        a, b = s0[i], s1[i]
-        j = nxt[i]
-        for j, x, y, q in out[i] + ([(j, occ[i][0], occ[i][1], True)] if j >= 0 else []):
-            if a + x > s0[j]:
-                s0[j] = a + x
-                if not want:
-                    why[j] = (i, q)
-            if b + y > s1[j]:
-                s1[j] = b + y
-                if want:
-                    why[j] = (i, q)
-            left[j] -= 1
-            if not left[j]:
-                top.append(j)
-    if len(top) < n:
-        return None, None
-    ends = [max((s[i] + cs[i][m], i) for i in order["s"][-5:]) for m, s in enumerate((s0, s1))]
-    arcs, i = [], ends[want][1]
-    while why[i]:
-        if why[i][1]:
-            arcs.append((why[i][0], i))
-        i = why[i][0]
-    return (ends[0][0], ends[1][0], s0), arcs
-
-
-def orders(rounds=ROUNDS, seed=1):
-    short, ops = plan(3), plan()
-    edges(short)
-    edges(ops)
-    st = schedule(short, rounds[0], seed)[1][2]
-    at = {(o["t"], o["k"]): st[o["i"]] for o in short}
-    per = at[2, ("conf0", "a", 1)] - at[1, ("conf0", "a", 1)]
-    return ops, schedule(ops, rounds[1], seed, lambda t, k: at[0, k] if t == 0 else at[2, k] + (TV - 3) * per if t == TV - 1 else at[1, k] + (t - 1) * per)
-
-
-def schedule(ops, rounds, seed, start=None):
-    n = len(ops)
-    pre, succ, head, key, seen = [o["pre"] for o in ops], [[] for _ in ops], [0.0] * n, {}, {}
+def chains(ops):
+    last, pairs = {}, []
     for o in ops:
-        for p in o["pre"]:
-            succ[p].append(o["i"])
-            if (ops[p]["sec"], ops[p]["t"]) == (o["sec"], o["t"]):
-                head[o["i"]] = max(head[o["i"]], head[p] + ops[p]["c"] + DEP)
+        if o["e"] in "va" and o["calls"][0][1][0] in ("XG", "RG", "XA", "MX", "CE", "MY"):
+            key = (o["t"], o["sec"], o["e"], o["calls"][0][1][0])
+            if key in last:
+                pairs.append((last[key], o["i"]))
+            last[key] = o["i"]
+    return pairs
+
+
+def graph(ops, figures):
+    ga, sca, every, pec, wake, way = figures
+    c = [way if o["e"] == "x" else o["c"] if "c" in o else every * sum(cost(o["e"], x, ga, sca, pec) for x in o["calls"]) for o in ops]
+    fore, back = [[] for _ in ops], [[] for _ in ops]
+    for a, b, wait in ops[0]["arcs"]:
+        fore[a].append((b, c[a] + wait * wake if wait >= 0 else 0.0))
+        back[b].append((a, c[b] + wait * wake if wait >= 0 else 0.0))
+    return ["vapg".find(o["e"]) for o in ops], c, fore, back
+
+
+def play(queue, c, out, into, rank):
+    left, at, st, seq, end = [len(x) for x in into], [0.0] * len(c), [0.0] * len(c), [], 0.0
+    free, ready, soon, new = [0.0] * 4, [[], [], [], []], [None] * 4, [i for i in range(len(c)) if not into[i]]
+    while True:
+        i = new.pop() if new else -1
+        if i >= 0 and queue[i] >= 0:
+            ready[queue[i]].append(i)
+            soon[queue[i]] = None
+            continue
+        if i >= 0:
+            s = at[i]
+        else:
+            first = 1e18
+            for q in range(4):
+                if soon[q] is None:
+                    f, a, b = free[q], 1e18, 1e18
+                    for j in ready[q]:
+                        s = at[j] if at[j] > f else f
+                        a, b = (s if s < a else a), (s + c[j] if s + c[j] < b else b)
+                    soon[q] = (a, b)
+                if soon[q][1] < first:
+                    first, e = soon[q][1], q
+            if first == 1e18:
+                return st, end, seq
+            f, a, low = free[e], soon[e][0], 1e18
+            for j in ready[e]:
+                if at[j] <= a + AHEAD[e] and rank[j] < low:
+                    i, low = j, rank[j]
+            if at[i] > a:
+                b, low = at[i] + 30, 1e18
+                for j in ready[e]:
+                    if rank[j] < low and (at[j] if at[j] > f else f) + c[j] <= b:
+                        i, low = j, rank[j]
+            ready[e].remove(i)
+            s = at[i] if at[i] > f else f
+            free[e], soon[e] = s + c[i], None
+        st[i] = s
+        seq.append(i)
+        end = s + c[i] if s + c[i] > end else end
+        for j, x in out[i]:
+            left[j] -= 1
+            if s + x > at[j]:
+                at[j] = s + x
+            if not left[j]:
+                new.append(j)
+
+
+def replay(g, seq):
+    queue, c, out = g[0:3]
+    at, free, end = [0.0] * len(c), [0.0] * 5, 0.0
+    for i in seq:
+        s = at[i] if at[i] > free[queue[i]] else free[queue[i]]
+        free[queue[i]], free[4] = s + c[i], 0.0
+        end = s + c[i] if s + c[i] > end else end
+        for j, x in out[i]:
+            if s + x > at[j]:
+                at[j] = s + x
+    return end
+
+
+def search(ops, rank, rounds, heat, seed):
+    gs = [graph(ops, f) for f in FIGURES]
+    queue, c, fore, back = gs[0]
+    parts = {}
+    for o in ops:
+        parts.setdefault(o["sec"] + o["e"], []).append(o["i"])
+    parts = [parts[k] for k in sorted(parts)]
+
+    def value(rank, tight):
+        st, end, seq = play(queue, c, fore, back, rank)
+        if tight:
+            bk = play(queue, c, back, fore, [-s - x for s, x in zip(st, c)])[0]
+            s2, e2, q2 = play(queue, c, fore, back, [-s - x for s, x in zip(bk, c)])
+            if e2 < end:
+                st, end, seq = s2, e2, q2
+        return end + sum(w * replay(g, seq) for w, g in zip(WEIGHTS, gs[1:])), st, seq
+    rnd = np.random.RandomState(seed)
+    steps, draws = rnd.standard_normal(3 * rounds).tolist(), rnd.random_sample(8 * rounds).tolist()
+    cur = best = value(rank, True)
+    for it in range(rounds):
+        r, rank = draws[8 * it:8 * it + 8], list(cur[1])
+        for u in range(1 + int(3 * r[0])):
+            for i in parts[int(r[1 + u] * len(parts))]:
+                rank[i] += steps[3 * it + u] * (400.0 if r[4] < 0.5 else 1600.0)
+        new = value(rank, r[5] < 0.5)
+        if new[0] <= cur[0] - heat * 0.1 ** (it / rounds) * float(np.log(1.0 - r[6])):
+            cur = new
+            best = min(best, cur, key=lambda x: x[0])
+    return best
+
+
+def prepared(visits):
+    ops = plan(visits)
+    edges(ops)
+    reach, arcs, seen = [], [], {}
+    for o in ops:
+        r = 0
+        for p in sorted(o["pre"], reverse=True):
+            if not r >> p & 1:
+                arcs.append((p, o["i"], 0 if ops[p]["e"] == "p" == o["e"] else 1))
+                r |= reach[p] | 1 << p
+        reach.append(r)
         k = (o["t"], o["sec"], o["e"])
         seen[k] = seen.get(k, 0) + 1
-        o["k"] = (o["sec"], o["e"], seen[k])
-        key[o["t"], o["k"]] = o["i"]
-    if start:
-        prio, left, st = [start(o["t"], o["k"]) + o["i"] * 1e-3 for o in ops], [len(p) for p in pre], [0] * n
-        ready = [i for i in range(n) if not left[i]]
-        for r in range(n):
-            i = min(ready, key=lambda j: prio[j])
-            ready.remove(i)
-            st[i] = r
-            for j in succ[i]:
-                left[j] -= 1
-                if not left[j]:
-                    ready.append(j)
-    else:
-        st = place(ops, pre, succ, [1000.0 * (o["t"] * PERIOD + PLACE[o["sec"]]) + head[o["i"]] + o["i"] * 1e-3 for o in ops])
-        back = place(ops, succ, pre, [-st[i] - ops[i]["c"] + i * 1e-3 for i in range(n)])
-        st = place(ops, pre, succ, [-back[i] - ops[i]["c"] + i * 1e-3 for i in range(n)])
-    order = {}
-    for i in sorted(range(n), key=lambda i: (i if ops[i]["e"] in "st" else st[i], i)):
-        order.setdefault(ops[i]["e"], []).append(i)
-    cs = [(o["c"], o["c2"]) for o in ops]
-    occ = [(50.0, 50.0) if o["e"] in "stx" else cs[o["i"]] for o in ops]
-    out = [[(j, cs[i][0] + w * DEP, cs[i][1] + w * SLOW[4], False) for j in succ[i] for w in (0 if ops[i]["e"] == "p" == ops[j]["e"] else 1,)] for i in range(n)]
-    npre = [len(p) for p in pre]
-    rnd = np.random.RandomState(seed).random_sample(8 * rounds + 8).tolist()
-    val = lambda r: r[0] + 0.5 * r[1]
-    res, arcs = times(order, npre, out, occ, cs, 0)
-    cur, best = val(res), (val(res), res, {e: list(li) for e, li in order.items()})
-    for it in range(rounds):
-        r = rnd[8 * it:8 * it + 8]
-        cand = [a for a in arcs if ops[a[0]]["e"] in "vapg" and a[0] not in pre[a[1]]]
-        u, v = cand[int(r[0] * len(cand))]
-        e = ops[u]["e"]
-        li, old = order[e], list(order[e])
-        if r[1] < 0.3:
-            u = li[max(0, li.index(u) - 1 - int(3 * r[2]))]
-        elif r[1] < 0.6:
-            v = li[min(len(li) - 1, li.index(v) + 1 + int(3 * r[2]))]
-        d = ops[v]["t"] - ops[u]["t"]
-        for a, b in [(u, v)] if r[3] < 0.25 else [(key.get((t, ops[u]["k"])), key.get((t + d, ops[v]["k"]))) for t in range(TV)]:
-            if a is not None and b is not None:
-                ia, ib = li.index(a), li.index(b)
-                if ia < ib <= ia + 12:
-                    li.insert(ib, li.pop(ia)) if 0.3 <= r[1] < 0.6 else li.insert(ia, li.pop(ib))
-        res, a2 = times(order, npre, out, occ, cs, int(r[4] < 0.35))
-        if res and val(res) <= cur * (1 + 0.004 * r[5] * (1 - it / rounds)):
-            cur, arcs = val(res), a2
-            if cur < best[0]:
-                best = (cur, res, {e: list(li) for e, li in order.items()})
-        else:
-            order[e] = old
-    return best[2], best[1]
+        o["k"] = k[1:] + (seen[k],)
+    ops[0]["arcs"] = arcs + [(a, b, -1) for a, b in chains(ops)]
+    return ops
+
+
+def orders(rounds=ROUNDS, seed=SEED):
+    short, ops = prepared(3), prepared(TV)
+    st = search(short, [o["t"] * PERIOD + RANK.get(o["sec"], {}).get(o["e"], 0) + o["i"] * 1e-6 for o in short], rounds[0], 500.0, seed)[1]
+    at = {(o["t"], o["k"]): st[o["i"]] for o in short}
+    per = at[2, ("sel0", "v", 1)] - at[1, ("sel0", "v", 1)]
+    rank = [at[0, o["k"]] if o["t"] == 0 else at[2, o["k"]] + (TV - 3) * per if o["t"] == TV - 1 else at[1, o["k"]] + (o["t"] - 1) * per for o in ops]
+    value, st, seq = search(ops, rank, rounds[1], 200.0, seed)
+    order = {e: [o["i"] for o in ops if o["e"] == e] for e in "stx"}
+    order.update({e: [i for i in seq if ops[i]["e"] == e] for e in "vapg"})
+    return ops, order, st
 
 
 def issue(g, q, T, c):
@@ -615,7 +660,7 @@ def issue(g, q, T, c):
     if k == "memset":
         return q.memset(*a)
     if k == "scan":
-        return q.tensor_tensor_scan(a[0], a[1], a[2], 0.0, a[3], a[4])
+        return q.tensor_tensor_scan(a[0], a[1], a[2], BIG, a[3], a[4])
     if k == "red":
         return q.tensor_reduce(a[0], a[1], AxisListType.X, a[2])
     if k == "act":
@@ -639,16 +684,15 @@ def rank_program(g, core, T, topo):
     if rank is None:
         return
     if not PLAN:
-        ops, found = orders()
-        PLAN.extend([ops, found[0]])
+        PLAN.extend(orders()[0:2])
     ops, order = PLAN
     queue = {"v": g.vector, "a": g.scalar, "p": g.tensor, "g": g, "s": g.sync}
-    nxt = T.cores[(rank + 1) % N]
+    nxt, prv = T.cores[(rank + 1) % N], T.cores[(rank - 1) % N]
     count, total = {}, {e: 0 for e in "vapg"}
     for e, li in order.items():
         for i in li:
             if "s" in ops[i]:
-                count[i] = ops[i]["s"]
+                count[i] = (ops[i]["s"][0], ops[i]["s"][1] * (len(topo.engines(prv, core)) if e == "x" else 1))
             elif "send" not in ops[i]:
                 total[e] += 1
                 count[i] = (SEMOF[e], total[e])
@@ -666,7 +710,7 @@ def rank_program(g, core, T, topo):
                 progress = True
                 done.add(i)
                 if e == "x":
-                    clock[i] = {o["s"][0]: o["s"][1]}
+                    clock[i] = {count[i][0]: count[i][1]}
                     continue
                 q, kn = queue[e], known[e]
                 for p in sorted(o["pre"], reverse=True):
@@ -678,9 +722,8 @@ def rank_program(g, core, T, topo):
                         for k, v in clock[p].items():
                             kn[k] = max(kn.get(k, 0), v)
                 if "send" in o:
-                    t, h = o["send"]
-                    rid, pid = topo.addr(nxt)[0:2]
-                    g.remote_dma(T.LV[:, 2 * t + 2 + h, :], T.SL[:, 2 * t + h, :], T.sem["ar%d%d" % (t + 1, h)], T.sem.ls, pid, rid, topo.mask(core, nxt))
+                    src, dst, (rid, pid) = o["calls"][0][2], o["to"][0][1], topo.addr(nxt)[0:2]
+                    g.remote_dma(T[dst[0]][dst[1]], T[src[0]][src[1]], T.sem[o["sem"]], T.sem.ls, pid, rid, topo.mask(core, nxt))
                     sent += len(topo.engines(core, nxt))
                     continue
                 for c in o["calls"]:

@@ -3,24 +3,26 @@ from concourse.mybir import AluOpType as A, ActivationFunctionType as F, AxisLis
 
 N, TV = 4, 5
 CYC = 0.83
-FIGURES, WEIGHTS = ((1.56, 3.8, 1.0, 0.71, 100.0, 3000.0), (1.1, 2.0, 1.0, 0.6, 70.0, 2500.0), (2.0, 5.5, 1.3, 0.8, 150.0, 4000.0)), (0.5, 0.3)
-ROUNDS, SEED = (4000, 600), 1
+FIGURES = ((1.62, 3.8, 1.25, 0.7, 100.0, 3000.0), (1.12, 3.9, 1.35, 0.73, 70.0, 3000.0), (2.05, 4.5, 1.15, 0.71, 100.0, 3000.0), (1.25, 3.0, 1.1, 0.7, 120.0, 4000.0),
+           (1.8, 4.0, 1.45, 0.9, 150.0, 4500.0))
+WEIGHTS = (1.5, 0.35, 0.8, 0.35)
+ROUNDS, SEED = (1000, 2000, 2500), 7
 B16, H16, F32, I32, U16 = "bfloat16", "float16", "float32", "int32", "uint16"
 SB = {
     "X": ([4096], B16), "R": ([4160], I32), "R16": ([4096], H16), "LI": ([256], I32), "ZI": ([256], B16), "THI": ([8], I32), "THB": ([8], I32),
-    "LV": ([2 * TV, 264], H16), "SL": ([2 * TV, 264], H16), "C16": ([128], B16), "ONEB": ([256], B16), "IDB": ([128], B16), "NIDB": ([128], B16),
-    "ID16": ([128], H16), "NID16": ([128], H16), "ID32": ([128], F32), "HID16": ([128], H16), "PEN16": ([128], H16), "BOF": ([128], B16), "BOF16": ([128], H16),
-    "NBOU16": ([128], H16), "BOU": ([128], H16), "NBH16": ([128], H16), "BOD": ([16], B16), "BON": ([16], B16), "BOC": ([8], B16), "BO1": ([8], F32),
-    "SELB": ([128], B16), "SEL0": ([128], H16), "RX": ([128], B16), "IK": ([256], F32), "PI": ([4], I32), "IM": ([144], I32), "MT": ([2, 144], B16), "IN": ([16], F32),
-    "CO": ([24], F32), "CL": ([2, 16], B16), "CK": ([512], B16), "CAPK": ([2, 128], F32), "IG": ([128], F32), "CNT": ([2], F32), "RST": ([256], B16), "RSTN": ([128], B16),
-    "AQ": ([4, 128], B16), "BQ": ([128], B16), "QM": ([4, 128], B16), "MK": ([2, 256], B16), "IJ": ([256], B16), "RS2": ([256], B16), "BL": ([256], B16),
-    "BL16": ([256], H16), "DM": ([128], B16), "TH": ([8], F32), "TH0": ([128], H16), "THT": ([128], H16), "SN": ([128], H16), "SC2": ([128], B16), "NR": ([2], F32),
+    "LV": ([2 * TV, 264], H16), "SL": ([2 * TV, 264], H16), "ONEB": ([128], B16), "ZERO": ([136], B16), "CZ": ([640], B16), "ACC": ([512], F32), "IDB": ([128], B16), "NIDB": ([128], B16),
+    "ID16": ([128], H16), "ID32": ([128], F32), "NID16": ([128], H16), "HID16": ([128], H16), "PEN16": ([136], H16), "BOF": ([128], B16), "BOX": ([128], H16),
+    "BOF16": ([128], H16), "BOU": ([128], H16), "NBH16": ([128], H16), "BOD": ([16], B16), "BON": ([16], B16), "BOC": ([8], B16), "BO1": ([8], F32),
+    "SEL0": ([128], H16), "RX": ([128], B16), "IK": ([128], F32), "PI": ([4], I32), "IM": ([144], I32), "MT": ([2, 144], B16), "IN": ([16], F32),
+    "CO": ([24], F32), "CL": ([2, 16], B16), "CK": ([528], B16), "CAPK": ([136], F32), "IG": ([272], F32), "CNT": ([2], F32), "RST": ([256], B16), "NEG": ([136], B16),
+    "AQ": ([512], B16), "BQ": ([128], B16), "QM": ([4, 128], B16), "RS2": ([2, 256], B16), "IJ": ([256], B16), "BL": ([256], B16), "BL16": ([256], H16), "MK": ([8], B16),
+    "DM": ([128], B16), "LOW": ([256], B16), "TH": ([8], F32), "TH0": ([128], H16), "THT": ([128], H16), "SN": ([128], H16), "SC2": ([128], B16), "NR": ([2], F32),
     "YL": ([256], F32), "YZ": ([256], B16), "YR": ([512], F32),
 }
 for _n, (_s, _d) in {
     "LU": ([128], U16), "VTF": ([128], B16), "XG": ([2048], B16), "MX": ([2048], B16), "RG": ([2048], F32), "CE": ([2048], B16), "XA": ([4096], B16), "MY": ([4096], B16),
-    "KS": ([256], F32), "M2": ([128], F32), "KF": ([512], F32), "M2F": ([128], F32), "FS": ([128], F32), "RR": ([48], F32), "BA": ([144], B16), "BE": ([144], B16),
-    "VF": ([264], B16), "ZH": ([128], F32), "VTT": ([128], B16), "VTU": ([128], B16), "OL": ([16], U16), "OE": ([16], U16), "RAB": ([256], H16),
+    "KS": ([273], F32), "KF": ([529], F32), "FS": ([136], F32), "RR": ([48], F32), "BA": ([144], B16), "BE": ([144], B16),
+    "VF": ([264], B16), "VTT": ([128], B16), "VTU": ([128], B16), "OL": ([16], U16), "OE": ([16], U16), "RAB": ([256], H16),
     "XE": ([256], H16), "OF": ([256], U16), "NR2": ([128], F32), "S1": ([256], H16), "S2": ([256], H16), "LD": ([128], H16), "LMS": ([8], F32),
     "SV": ([128], F32), "SVB": ([128], F32), "NL": ([128], F32), "XD": ([128], H16), "SG": ([128], B16),
     "AD": ([256], B16), "WT": ([256], B16), "WS": ([256], B16), "WC": ([8], F32), "WO": ([8], U16),
@@ -36,17 +38,23 @@ HBM = ("xt", "z0", "ex", "l0", "th", "yl", "yz", "yr")
 s_ = np.s_
 C7, C6, C0 = 1.5 * 2.0 ** 30, 1.5 * 2.0 ** 29, 1.5 * 2.0 ** 23
 C13 = 1.5 * 2.0 ** 36
-BIG = 2.0 ** 30
-TWO, FOUR, T2 = (("a", 0, 64), ("a", 64, 128)), tuple(("a", 32 * _q, 32 * _q + 32) for _q in range(4)), ((0, 64), (64, 128))
-OPT = {"xg": [FOUR, TWO], "rg": [(("v", 0, 48), ("a", 48, 88), ("a", 88, 128)), (("v", 0, 32), ("a", 32, 80), ("a", 80, 128))], "xa": [TWO, TWO, FOUR, FOUR],
-       "mx": [T2, T2], "ce": [T2, T2], "my": [T2] * 4, "rab": ["a", "a"], "xe": ["v", "a"], "xd": ["v", "v"],
-       "z": ["v", "v"], "ru": ["m", "m"], "prew": ["late", "early"], "gr": 2, "cefirst": [False, False], "sum": "vavavava"}
+BIG, TOP = 2.0 ** 30, 2.0 ** 23
+
+
+def pieces(who):
+    return tuple((e, 2 * (64 * q // len(who)), 2 * (64 * (q + 1) // len(who))) for q, e in enumerate(who))
+
+
+OPT = {"xg": ["avaa", "aa"], "rg": ["vaa", "vaa"], "xa": ["av", "aa", "aaa", "aaa"], "mx": ["vv", "vv"], "ce": ["vv", "vv"], "my": ["vv"] * 4,
+       "flip": 0.1, "join": [True, True],
+       "rab": "aa", "xe": "aa", "xd": "av", "z": "aa", "prew": ["late", "early"], "sum": 4, "const": "vag"}
 AHEAD, PERIOD = (250.0, 150.0, 100.0, 500.0), 26.0
-RANK = {"init": dict(v=-30, g=-30, p=-30, a=-30), "late": dict(v=5, p=-10, g=-30), "cnt": dict(p=7, v=7), "sum": dict(v=40, p=40, a=40),
-        "lu0": dict(v=-30), "prep0": dict(p=-2, a=-3, v=0), "svb0": dict(p=2, a=2), "conf0": dict(p=-2, a=-2, v=0.5), "qq0": dict(p=1), "sel0": dict(v=-5, p=-5, a=-5),
+RANK = {"init": dict(v=-30, g=-30, p=-30, a=-30), "mid": dict(v=1, g=-29, a=1), "sq": dict(v=4, p=-10, g=-28, a=4), "late": dict(v=5, p=-10, g=-27, a=5),
+        "thr": dict(v=6, g=-26, a=6), "cnt": dict(p=7, v=7), "sum": dict(v=40, p=40, a=40, g=-40), "add": dict(v=40),
+        "lu0": dict(v=-30), "prep0": dict(p=-2, a=-3, v=0), "svb0": dict(p=2, a=2), "conf0": dict(p=-2, a=-2, v=0.5), "sel0": dict(v=-5, p=-5, a=-5),
         "far0": dict(p=2, a=2, v=7.5), "fq0": dict(v=7.6, p=2, a=2), "two0": dict(p=3, a=3, v=8), "end0": dict(v=-3, p=-3, a=-3), "new0": dict(v=-2.9, p=-2.9, a=-2.9, g=0),
         "zz0": dict(p=-2.8, v=-2.8, a=-2.8), "prew0": dict(a=13, p=9, v=13), "wr0": dict(v=13),
-        "lu1": dict(v=-30), "prep1": dict(p=4, a=1, v=6), "svb1": dict(p=5, a=5), "conf1": dict(v=6.5, p=4, a=1.5), "qq1": dict(p=5), "sel1": dict(v=-4, p=-4, a=-4),
+        "lu1": dict(v=-30), "prep1": dict(p=4, a=1, v=6), "svb1": dict(p=5, a=5), "conf1": dict(v=6.5, p=4, a=1.5), "sel1": dict(v=-4, p=-4, a=-4),
         "far1": dict(a=11, p=11, v=13.5), "fq1": dict(v=13.5, p=11, a=13), "prew1": dict(a=14, p=12, v=14), "two1": dict(p=10, a=12, v=14),
         "end1": dict(v=5, p=5, a=5), "new1": dict(p=5.5, a=5.5, v=5.5, g=0), "zz1": dict(p=5.6, a=5.6, v=5.6), "sg1": dict(a=5.7), "wr1": dict(v=6)}
 
@@ -83,26 +91,26 @@ def two(ap):
     return SCRATCH[ap[0]][2] in (B16, H16, U16)
 
 
-def cost(e, c, GA, SCA, PEC):
+def cost(e, c, GA, SCA, PEC, PHI):
     k, out = c[0], c[1]
     if k == "mm":
         return max(min(64, cells(c[2])[0]), cells(c[3])[0]) * PEC * (1 if two(c[2]) else 4)
     if out[0] == "@":
-        return 50 + 16 * cells(out[2])[0] * SCA * CYC
+        return 50 + max(40, 16 * cells(out[2])[0]) * SCA * CYC
     n = cells(out)[0]
     if e == "g":
-        return 170 + 2 * n * CYC
+        return (170 + 2 * n * CYC) * PHI
     if k != "memset" and c[2][0] == "@":
-        return 60 + n * GA * CYC
+        return (70 if e == "a" else 50) + n * GA * CYC
     if e == "a":
-        return 20 + max(64, n) * CYC
+        return (40 + max(64, n) * CYC) * PHI
     if k == "tt":
         f = 1 if c[2][0] in BANKS or c[3][0] in BANKS else 2
     elif k == "red":
         n, f = cells(c[2])[0], 1
     else:
         f = 0.5 if all(two(x) for x in ((out,) if k == "memset" else c[1:4] if k == "scan" else c[1:3])) else 1
-    return 5 + max(64, n * f) * CYC
+    return (1 + max(64, n * f) * CYC) * (PHI if k in ("ts", "scan", "red") else 1.0)
 
 
 def plan(TV=TV):
@@ -134,16 +142,26 @@ def plan(TV=TV):
     def act(o, i, f, bias=0.0, scale=1.0, acc=None):
         return ("act", o, i, f, bias, scale, acc)
 
-    def move(e, o, i, add=0.0, times=1.0):
-        if e == "a":
-            S(act(o, i, F.Identity, add, times) if add or times != 1.0 else act(o, i, F.Copy))
-        else:
-            V(ts(o, i, times, A.mult, add, A.add) if add or times != 1.0 else ("copy", o, i))
+    def either(first, forms):
+        op("f", [c for e in forms for c in forms[e]], forms=forms, first=first if first in forms else "v")
+
+    def move(e, *jobs):
+        either(e, {"v": [ts(o, i, times, A.mult, add, A.add) if add or times != 1.0 else ("copy", o, i) for o, i, add, times in jobs],
+                   "a": [act(o, i, F.Identity, add, times) if add or times != 1.0 else act(o, i, F.Copy) for o, i, add, times in jobs]})
+
+    def fill(e, *jobs):
+        forms = {"v": [("memset", o, x) for o, x in jobs]}
+        if "g" in OPT["const"] and all(SCRATCH[o[0]][2] != H16 and not o[1][0].start for o, x in jobs):
+            forms["g"] = [("iota", o, [[0, cells(o)[0]]], int(x), 0) for o, x in jobs]
+        if all(cells(o)[0] <= 128 and sum(isinstance(x, slice) for x in o[1]) == 2 and SCRATCH[o[0]][2] != I32 for o, x in jobs):
+            forms["a"] = [act(o, pt("ONEB", o[1][0], s_[0:cells(o)[0]]), F.Identity, 0.0, x) for o, x in jobs]
+        either(e, forms)
 
     def col(j):
         return sb("CO", s_[j:j + 1])
 
     al = s_[:]
+    part = lambda v: s_[128 * v:128 * v + 128]
     def load(q, sem, c, out, src):
         op(q, [("dma", out, src)], c=c, s=(sem, 16))
     load("s", "dl", 2500, sb("LI", al), ("l0", s_[:, :]))
@@ -155,84 +173,110 @@ def plan(TV=TV):
     load("s", "dt", 9000, pt("THI", s_[0:1], al), ("th", s_[:, :]))
 
     ms = lambda o, x: ("memset", o, x)
-    one = sb("ONEB", s_[0:128])
-    V(ms(sb("ONEB", al), 1.0))
+    one, b8 = sb("ONEB", s_[0:128]), sb("BOF", s_[0::16])
+    r0, r32, r64 = s_[0:1], s_[32:33], s_[64:65]
+    V(ms(one, 1.0), ms(sb("ZERO", al), 0.0))
     rev = (s_[255:127:-1], s_[127::-1])
     for h in range(2):
-        V(ts(sb("LV", h, s_[0:128]), sb("LI", rev[h]), -2048.0, A.add))
-        V(("copy", sb("LV", h, s_[128:256]), sb("ZI", rev[h])))
+        move("va"[h], (sb("LV", h, s_[0:128]), sb("LI", rev[h]), -2048.0, 1.0))
+        move("v", (sb("LV", h, s_[128:256]), sb("ZI", rev[h]), 1024.0, 1.0))
+    fill("a", (pt("CZ", r0, part(0)), -1024.0))
+
+    def diagonal(e, nm, x):
+        forms = {"v": [ts(sb(nm, al), sb("IDB", al), x, A.mult)], "a": [act(sb(nm, al), sb("IDB", al), F.Identity, 0.0, x)]}
+        if "g" in OPT["const"]:
+            forms["g"] = [("asel", sb(nm, al), sb("ZERO", part(0)), [[-1, 128]], A.not_equal, x, 0, 1)]
+        either(e, forms)
+    G(("iota", sb("PI", al), [[0, 4]], 0, 1))
     G(("asel", sb("IDB", al), one, [[-1, 128]], A.is_equal, 0.0, 0, 1))
     G(("asel", sb("BOF", al), one, [[-16, 8], [0, 16]], A.is_ge, 0.0, 0, 1))
     G(("asel", sb("BOF", al), sb("BOF", al), [[16, 8], [0, 16]], A.is_ge, 0.0, 15, -1))
-    G(("asel", sb("SELB", al), one, [[-16, 8], [0, 16]], A.is_equal, 0.0, 0, 1))
-    G(("iota", sb("IK", al), [[0, 16], [1, 16]], 0, 0))
-    G(("iota", sb("IG", al), [[-3, 8], [0, 16]], 12, 0))
-    G(("iota", sb("PI", al), [[0, 4]], 0, 1))
-    G(("asel", sb("RX", al), one, [[-1, 8], [-8, 16]], A.is_equal, 0.0, 0, 1))
-    G(("iota", sb("IN", al), [[128, 16]], 0, 0))
-    for nm, src, x in (("ID16", "IDB", 1.0), ("SEL0", "SELB", 1.0)):
-        V(ts(sb(nm, al), sb(src, al), x, A.mult))
-    b8 = sb("BOF", s_[0::16])
-    V(*[ts(sb(nm, s_[c:c + 8]), b8, x, A.mult) for nm, x in (("BOD", 256.0), ("BON", -128.0)) for c in (0, 8)], ts(sb("BOC", al), b8, 2.0 ** 21, A.mult))
+    G(("asel", sb("SEL0", al), one, [[-16, 8], [0, 16]], A.is_equal, 0.0, 0, 1))
+    G(("iota", pt("IG", s_[0:64], s_[0:136]), [[-6, 8], [0, 17]], 24, 0), ("iota", pt("IG", s_[0:64], s_[136:272]), [[13, 8], [0, 17]], -52, 0))
+    G(*[("iota", pt("IG", s_[0:64], s_[c:c // 136 * 136 + 136:17]), [[x, 8]], base, 0) for c, x, base in ((0, -6, 29), (16, -6, 23), (136, 13, -60), (152, 13, -68))])
+    G(("iota", sb("IK", al), [[0, 8], [1, 16]], 0, 0))
+    diagonal("v", "ID16", 1.0)
+    move("v", *[(sb(nm, s_[c:c + 8]), b8, 0.0, x) for nm, x in (("BON", -128.0), ("BOD", 256.0)) for c in (0, 8)])
+    move("v", (sb("BOC", al), b8, 0.0, 2.0 ** 21))
+    V(ms(pt("CK", s_[0:64], al), 0.0))
+    G(("iota", pt("CK", r0, s_[0:136]), [[0, 8], [1, 17]], 0, 0), ("iota", pt("CK", r0, s_[136:272]), [[0, 8], [-1, 17]], 15, 0))
+    fill("a", (pt("CK", r0, s_[0:136:17]), 2.0), (pt("CK", r0, s_[16:136:17]), 2.0))
+    move("a", (pt("CK", r32, s_[0:272]), pt("IG", r32, al), 0.0, 2.0 ** 18))
+    ones33 = pt("ONEB", s_[0:33], s_[0:128])
+    PE(P(sb("M0", s_[0:136]), [(ones33, pt("CK", s_[0:33], s_[0:136]))]))
+    move("v", (sb("CAPK", al), sb("M0", s_[0:136]), 2.0 ** 20, 1.0))
+    fill("v", (sb("KS", al, 0), 29.0 * 2 ** 18 + 2.0))
+    fill("g", (sb("R", s_[0:32]), 0), (sb("R", s_[4128:4160]), 0))
+    sec[0] = "mid"
     V(ts(sb("PI", s_[0:1]), sb("PI", s_[0:1]), 15, A.bitwise_and), ts(sb("PI", s_[1:2]), sb("PI", s_[1:2]), 14, A.bitwise_and),
       ts(sb("PI", s_[2:3]), sb("PI", s_[2:3]), 1, A.bitwise_and))
     V(("copy", col(0), sb("PI", s_[0:1])), ts(col(4), sb("PI", s_[1:2]), 8.0, A.mult), ts(col(5), sb("PI", s_[2:3]), 2048.0, A.mult))
+    G(("asel", sb("RX", al), one, [[-1, 8], [-8, 16]], A.is_equal, 0.0, 0, 1))
+    G(("iota", sb("IN", al), [[128, 16]], 0, 0))
     V(ts(sb("CL", 0, al), sb("IN", al), col(4), A.add), ts(sb("CL", 1, al), sb("IN", al), col(4), A.add, col(5), A.add))
-    r0, r32, r64 = s_[0:1], s_[32:33], s_[64:65]
-    V(ms(pt("CK", s_[0:64], al), 0.0))
-    V(("copy", pt("CK", r0, s_[0:128]), pt("IK", r0, s_[0:128])), ts(pt("CK", r0, s_[128:256]), pt("IK", r0, s_[0:128]), -1.0, A.mult, 15.0, A.add),
-      ("copy", pt("CK", r0, s_[256:512]), pt("IK", r0, al)), ts(pt("CK", r32, s_[0:128]), pt("IG", r32, al), 2.0 ** 19, A.mult), ms(pt("CK", r32, s_[128:256]), -2.0 ** 22))
-    V(ms(pt("CK", r32, s_[128:256:16]), -2.0 ** 23), ms(pt("CK", r32, s_[0:128:16]), BIG))
-    V(ts(sb("IG", al), sb("IG", al), 2.0, A.add, 2.0 ** 19, A.mult))
-    V(*[("tt", sb("CAPK", u, al), sb("IG", al), sb("IK", s_[0:128]), A.add) for u in range(2)])
-    V(ms(sb("CAPK", al, s_[0::16]), BIG), ms(sb("CAPK", 1, s_[1::16]), BIG), ms(sb("M2", al, s_[0:1]), BIG), ms(sb("BA", al, al), 0.0))
-    V(ms(sb("R", s_[0:32]), 0), ms(sb("R", s_[4128:4160]), 0))
-    sec[0] = "late"
-    G(("iota", sb("IM", al), [[1, 144]], 1, 1))
-    G(("pbc", sb("THB", al), pt("THI", s_[0:1], al), 128))
-    for nm, src, x in (("ID32", "IDB", 1.0), ("NID16", "IDB", -1.0), ("HID16", "IDB", 0.25 - 2.0 ** -13), ("PEN16", "IDB", -512.0), ("NIDB", "IDB", -16384.0),
-                       ("NBH16", "BOF", -16384.0), ("BOF16", "BOF", 1.0), ("NBOU16", "BOF", -32768.0), ("BOU", "BOF", 32768.0)):
-        V(ts(sb(nm, al), sb(src, al), x, A.mult))
-    V(*[ts(col(1 + j), col(0), float(j), A.is_equal) for j in range(3)], ("copy", sb("BO1", al), b8))
-    V(*[ts(col(16 + j), col(0), x, A.add) for j, x in enumerate((0.0, 16.0, 4128.0, 4144.0))], ts(col(7), col(1), 2.0 ** 29, A.mult))
-    V(ms(sb("RST", al), -BIG), ms(sb("RSTN", al), BIG), ms(sb("RS2", al), -BIG))
-    V(ms(sb("RST", s_[0::16]), BIG), ms(sb("RSTN", s_[0::16]), -BIG), ms(sb("RS2", s_[0::32]), BIG), ms(sb("M2F", al, s_[0:1]), -BIG))
-    V(ts(sb("IM", al), sb("IM", al), 15, A.bitwise_and))
-    V(ts(sb("MT", 0, al), sb("IM", al), 0.0, A.is_equal, -8192.0, A.mult), ts(sb("MT", 1, al), sb("IM", al), 0.0, A.not_equal, -8192.0, A.mult))
-    V(ts(sb("MT", al, al), sb("MT", al, al), 2048.0, A.add))
-    for nm in ("BE", "VF"):
-        V(ms(sb(nm, al, al), 0.0))
-    V(ms(sb("SL", al, s_[256:264]), 0.0), ms(pt("C16", r0, al), 61440.0))
-    V(ms(pt("AQ", s_[0:96], al, al), 0.0), ms(pt("BQ", s_[0:96], al), 0.0))
+    fill("g", (sb("BA", al, al), 0.0))
+    G(("iota", pt("CK", r0, s_[272:528]), [[0, 16], [1, 16]], 0, 0))
+    sec[0] = "sq"
+    fill("v", (pt("AQ", s_[0:96], al), 0.0))
+    fill("a", (pt("BQ", s_[0:96], al), 0.0))
     q8, qf = 8192.0, -16384.0
-    for part in (((r0, 0, 0, q8), (r0, 1, 1, q8), (r0, 0, 2, -q8), (r64, 0, 2, -q8)), ((r0, 1, 3, -q8), (r64, 1, 3, -q8)), ((r32, s_[0:2], 4, -q8), (r0, s_[0:2], 4, -q8)),
-                 ((r0, 2, 9, qf), (r64, 2, 9, -15 * qf)), ((r0, 3, 11, qf), (r64, 3, 11, -15 * qf)), ((r0, 2, 13, -qf), (r64, 2, 13, 16 * qf)),
-                 ((r0, 3, 15, -qf), (r64, 3, 15, 16 * qf)), ((r0, s_[2:4], 4, -31 * qf), (r32, s_[2:4], 4, qf), (r64, s_[2:4], 4, 240 * qf), (r64, s_[2:4], 6, 61440.0 + q8))):
-        V(*[ms(pt("AQ", r, m, s_[sl::16]), x) for r, m, sl, x in part])
+    for r, job in ((r0, ((0, q8), (129, q8), (2, -q8), (131, -q8))), (r0, ((265, qf), (395, qf), (269, -qf), (399, -qf))), (r64, ((2, -q8), (131, -q8))),
+                   (r64, ((265, -15 * qf), (395, -15 * qf), (269, 16 * qf), (399, 16 * qf)))):
+        fill("a", *[(pt("AQ", r, s_[c:c // 128 * 128 + 128:16]), x) for c, x in job])
+    for job in (((r0, 4, -q8), (r32, 4, -q8), (r32, 260, qf)), ((r0, 260, -31 * qf), (r64, 260, 240 * qf), (r64, 262, 61440.0 + q8))):
+        fill("a", *[(pt("AQ", r, s_[c:c // 128 * 128 + 256:16]), x) for r, c, x in job])
     V(ts(col(13), col(0), 2.0, A.not_equal), ts(col(14), col(0), 3.0, A.not_equal), ts(col(15), col(0), 13.0, A.is_lt))
     V(ts(col(13), col(13), col(14), A.mult, col(15), A.mult))
-    V(("copy", pt("BQ", r0, al), pt("IK", r0, s_[0:128])), ("tt", pt("BQ", r32, al), pt("IK", r32, s_[0:128]), pt("IK", r32, s_[0:128]), A.mult), ms(pt("BQ", r64, al), 1.0))
-    PE(*[P(sb("M1", s_[128 * m:128 * m + 128]), [(pt("AQ", s_[0:96], m, al), pt("BQ", s_[0:96], al))]) for m in range(4)])
+    G(("iota", pt("BQ", r0, al), [[0, 8], [1, 16]], 0, 0))
+    fill("a", (pt("BQ", r64, al), 1.0))
+    S(act(pt("BQ", r32, al), pt("IK", r32, s_[0:128]), F.Square))
+    PE(*[P(sb("M1", part(m)), [(pt("AQ", s_[0:96], part(m)), pt("BQ", s_[0:96], al))]) for m in range(4)])
     for m in range(4):
-        V(("tt", sb("QM", m, al), sb("M1", s_[128 * m:128 * m + 128]), sb("BOF", al), A.mult))
+        V(("tt", sb("QM", m, al), sb("M1", part(m)), sb("BOF", al), A.mult))
+    fill("g", (sb("LOW", al), -4096.0))
+    sec[0] = "late"
+    G(("iota", sb("IM", al), [[1, 144]], 1, 1))
+    G(("asel", sb("PEN16", al), sb("ZERO", al), [[-16, 8], [-1, 17]], A.not_equal, -256.0, 0, 1))
+    for nm, x in (("ID32", 1.0), ("NID16", -1.0), ("HID16", 0.25 - 2.0 ** -13), ("NIDB", -16384.0)):
+        if nm != "NID16" or "a" in OPT["xd"]:
+            diagonal("g", nm, x)
+    for nm, x in (("BOF16", 1.0), ("NBH16", -16384.0), ("BOU", 32768.0)):
+        move("v", (sb(nm, al), sb("BOF", al), 0.0, x))
+    V(*[ts(col(1 + j), col(0), float(j), A.is_equal) for j in range(3)], ("copy", sb("BO1", al), b8), ts(col(18), col(0), 0.0, A.is_equal, -15.0, A.mult))
+    V(ts(sb("DM", al), sb("IK", s_[0:128]), col(0), A.is_equal, -1.0, A.mult), ts(col(18), col(18), 1.0, A.add))
+    V(ts(sb("BOX", al), sb("BOF", al), col(18), A.mult))
+    move("v", *[(col(j), col(0), x, 1.0) for j, x in ((16, 16.0), (17, 4128.0), (21, 4144.0), (19, 1.0))], (col(7), col(1), 0.0, 2.0 ** 29))
+    V(ts(col(20), col(0), 15.0, A.is_equal, -8192.0, A.mult))
+    fill("g", (sb("RST", al), -TOP))
+    fill("g", (sb("RST", s_[0::16]), TOP))
+    V(ms(sb("NEG", al), -BIG), ms(sb("KF", al, 256), -BIG))
+    V(ts(sb("IM", al), sb("IM", al), 15, A.bitwise_and))
+    V(ts(sb("MT", 0, al), sb("IM", al), 0.0, A.is_equal, -8192.0, A.mult))
+    move("v", (sb("MT", 1, al), sb("MT", 0, al), -6144.0, -1.0))
+    move("v", (sb("MT", 0, al), sb("MT", 0, al), 2048.0, 1.0))
+    for nm in ("BE", "VF"):
+        fill("g", (sb(nm, al, al), 0.0))
+    V(ms(sb("SL", s_[1::2], s_[258:264]), 0.0))
     G(("iota", sb("IJ", al), [[-16, 2], [0, 4], [1, 32]], 0, 0))
-    G(("asel", sb("BL", al), sb("ONEB", al), [[-16, 2], [-32, 4], [0, 32]], A.is_ge, 0.0, 0, 1))
-    G(("asel", sb("BL", al), sb("BL", al), [[16, 2], [32, 4], [0, 32]], A.is_ge, 0.0, 15, -1))
-    V(ts(sb("MK", 0, al), sb("IJ", al), col(0), A.is_lt, 8192.0, A.mult), ts(sb("MK", 1, al), sb("IJ", al), col(0), A.is_equal, 0.5, A.mult))
-    V(("tt", sb("MK", 0, al), sb("MK", 0, al), sb("MK", 1, al), A.add))
-    V(("copy", sb("BL16", al), sb("BL", al)), ts(sb("DM", al), sb("IK", s_[0:128]), col(0), A.is_equal, -1.0, A.mult))
-    V(("copy", sb("TH", al), sb("THB", al)))
-    V(("tt", sb("TH", al), sb("TH", al), sb("BO1", al), A.mult))
+    for u in range(2):
+        G(("asel", sb("BL", part(u)), one, [[-32, 4], [0, 32]], A.is_ge, 0.0, -16 * u, 1))
+    G(("asel", sb("BL16", al), sb("BL", al), [[16, 2], [32, 4], [0, 32]], A.is_ge, 0.0, 15, -1))
+    V(ms(sb("MK", s_[0:4]), 0.0), ts(sb("MK", s_[4:8]), sb("ONEB", s_[0:4]), col(20), A.mult))
+    V(ts(sb("RS2", 0, al), sb("IJ", al), col(0), A.is_equal, BIG, A.mult), ts(sb("RS2", 1, al), sb("IJ", al), col(19), A.is_equal, 8192.0, A.mult))
+    PE(P(sb("N1", s_[0:256]), [(sb("IDB", al), sb("RS2", u, al)) for u in range(2)]))
+    move("a", (sb("RS2", 0, al), sb("N1", s_[0:256]), 0.0, 1.0))
+    sec[0] = "thr"
+    G(("pbc", sb("THB", al), pt("THI", s_[0:1], al), 128))
+    V(("tt", sb("TH", al), sb("THB", al), sb("BO1", al), A.mult))
     V(("red", col(9), sb("TH", al), A.add))
     V(ts(col(10), col(9), C6, A.add, -C6, A.add))
-    V(("tt", col(11), col(9), col(10), A.subtract), ("tt", col(12), col(10), col(1), A.mult))
-    V(ts(col(11), col(11), -0.5, A.add, col(2), A.mult), ts(col(12), col(3), 31.5, A.mult, col(12), A.add))
+    V(("tt", col(11), col(10), col(9), A.subtract), ts(col(12), col(10), -1.0, A.mult, col(1), A.mult))
+    V(ts(col(11), col(11), 0.5, A.add, col(2), A.mult), ts(col(12), col(3), -31.5, A.mult, col(12), A.add))
     V(ts(sb("TH0", al), one, col(11), A.mult, col(12), A.add))
-    V(ms(sb("SN", al), 0.0), ms(pt("SC2", r0, al), 0.0))
+    fill("a", (sb("SN", al), 0.0), (pt("SC2", r0, al), 0.0))
     V(ts(sb("SN", s_[2::16]), sb("ONEB", s_[0:8]), col(2), A.mult, -0.5, A.mult), ms(pt("SC2", r0, s_[2::16]), -31.5))
-    IDB, ID16, NID16, BOF16 = sb("IDB", al), sb("ID16", al), sb("NID16", al), sb("BOF16", al)
+    IDB, ID16, BOF16, BOX, SEL0 = sb("IDB", al), sb("ID16", al), sb("BOF16", al), sb("BOX", al), sb("SEL0", al)
     XW, RW = sb("X", al), sb("R", s_[32:4128])
-    ones33 = pt("ONEB", s_[0:33], s_[0:128])
     wide = (s_[0:256], al)
     groups = ((1, 2, 3), (4, 5, 6, 7), (8, 9, 10, 11), (12, 13, 14, 15))
 
@@ -240,106 +284,88 @@ def plan(TV=TV):
         return sb("RAB", h, s_[v::2])
 
     def lists(bank, c0, which, tile, h):
-        out = sb(bank, s_[c0:c0 + 16])
-        return P(out, [(IDB, sb("CL", which, al))] + [(sb(tile, h, s_[14 - 2 * x:142 - 2 * x]), sb("RX", s_[16 * x:16 * x + 16])) for x in range(8)])
+        return P(sb(bank, s_[c0:c0 + 16]), [(IDB, sb("CL", which, al))] + [(sb(tile, h, s_[14 - 2 * x:142 - 2 * x]), sb("RX", s_[16 * x:16 * x + 16])) for x in range(8)])
+
+    def rowwise(h, out, src, c0, other, alu, cut, rows_in, sums):
+        for e, a, b in pieces(cut):
+            for rows in rows_in:
+                for u in range(0, len(rows), 2):
+                    V(*[("tt", sb(out, h, s_[c0 + 128 * k + a:c0 + 128 * k + b]), sb(src, h, s_[c0 + 16 * a + k:c0 + 16 * b:16]),
+                         sb("Z" + str(h), s_[other + a:other + b]), alu) for k in rows[u:u + 2]])
+                if b == 128:
+                    PE(*[sums(k, sb(out, h, s_[c0 + 128 * k:c0 + 128 * k + 128])) for k in rows])
 
     def first(t, h):
         H, li = str(h), 2 * t + h
-        Z, K, M, Nb = "Z" + H, "K" + H, "M" + H, "N" + H
+        Z, K, M = "Z" + H, "K" + H, "M" + H
         LP, ZP = sb("LV", li, s_[0:128]), sb("LV", li, s_[128:256])
         sec[0] = "lu" + H
         V(ts(sb("LU", h, al), LP, 2048.0, A.add))
         sec[0] = "prep" + H
-        PE(P(sb(Z, s_[0:128]), [(ID16, ZP)]), P(sb(Z, s_[128:256]), [(sb("SEL0", al), LP)]))
+        PE(P(sb(Z, part(0)), [(pt("ONEB", r0, part(0)), pt("CZ", r0, part(0))), (ID16, ZP)]), P(sb(Z, part(1)), [(SEL0, LP)]))
         sec[0] = "svb" + H
-        PE(P(sb(Nb, s_[0:128]), [(sb("SEL0", al), LP), (IDB, sb("MT", 1, s_[16 - t:144 - t]))]))
-        S(act(sb("SVB", h, al), sb(Nb, s_[0:128]), F.Copy))
+        PE(P(sb(M, part(1)), [(SEL0, LP), (IDB, sb("MT", 1, s_[16 - t:144 - t]))]))
+        S(act(sb("SVB", h, al), sb(M, part(1)), F.Copy))
         sec[0] = "prep" + H
-        for e, a, b in OPT["xg"][h]:
-            move(e, sb("XG", h, s_[16 * a:16 * b]), ind(XW, sb("LU", h, s_[a:b])))
-        PE(P(sb(K, s_[0:256]), [(ones33, pt("CK", s_[0:33], s_[0:256]))], True, False))
+        for e, a, b in pieces(OPT["xg"][h]):
+            move(e, (sb("XG", h, s_[16 * a:16 * b]), ind(XW, sb("LU", h, s_[a:b])), 0.0, 1.0))
+        PE(P(sb(K, s_[0:272]), [(ones33, pt("CK", s_[0:33], s_[0:272]))], True, False))
         for rows in groups:
-            PE(*[P(sb(K, s_[k:256:16]), [(sb("XG", h, s_[k::16]), sb("BON", al))], False, False) for k in rows])
-
-        def conflicts(last):
-            sec[0] = "conf" + H
-            for e, a, b in OPT["rg"][h]:
-                move(e, sb("RG", h, s_[16 * a:16 * b]), ind(RW, sb("LU", h, s_[a:b])), -2048.0)
-            for a, b in OPT["ce"][h]:
-                for rows in groups:
-                    for u in range(0, len(rows), OPT["gr"]):
-                        V(*[("tt", sb("CE", h, s_[128 * k + a:128 * k + b]), sb("RG", h, s_[16 * a + k:16 * b:16]), sb(Z, s_[128 + a:128 + b]), A.is_equal)
-                            for k in rows[u:u + OPT["gr"]]])
-                    if b == 128:
-                        PE(*[P(sb(K, s_[k:128:16]), [(sb("CE", h, s_[128 * k:128 * k + 128]), sb("BOC", al))], False, last and k == 15) for k in rows])
-
-        def maxima(last):
-            sec[0] = "prep" + H
-            for a, b in OPT["mx"][h]:
-                for rows in groups:
-                    for u in range(0, len(rows), OPT["gr"]):
-                        V(*[("tt", sb("MX", h, s_[128 * k + a:128 * k + b]), sb("XG", h, s_[16 * a + k:16 * b:16]), sb(Z, s_[a:b]), A.max) for k in rows[u:u + OPT["gr"]]])
-                    if b == 128:
-                        PE(*[P(sb(K, s_[k:256:16]), [(sb("MX", h, s_[128 * k:128 * k + 128]), sb("BOD", al))], False, last and k == 15) for k in rows])
-        for n_, part in enumerate((conflicts, maxima) if OPT["cefirst"][h] else (maxima, conflicts)):
-            part(n_ == 1)
-        sec[0] = "qq" + H
-        qq = (sb(M, s_[256:384]), sb(Nb, s_[0:128]))
-        for v in range(2):
-            PE(P(qq[v], [(ID16, LP)], True, False))
+            PE(*[P(sb(K, s_[k:272:17]), [(sb("XG", h, s_[k::16]), sb("BON", al))], False, False) for k in rows])
+        rowwise(h, "MX", "XG", 0, 0, A.max, OPT["mx"][h], groups, lambda k, x: P(sb(K, s_[k:272:17]), [(x, sb("BOD", al))], False, False))
+        sec[0] = "conf" + H
+        for e, a, b in pieces(OPT["rg"][h]):
+            move(e, (sb("RG", h, s_[16 * a:16 * b]), ind(RW, sb("LU", h, s_[a:b])), -2048.0, 1.0))
+        rowwise(h, "CE", "RG", 0, 128, A.is_equal, OPT["ce"][h], groups, lambda k, x: P(sb(K, s_[k:136:17]), [(x, sb("BOC", al))], False, k == 15))
         sec[0] = "sel" + H
-        V(("scan", sb("KS", h, s_[0:128]), sb("CAPK", 0, al), sb(K, s_[0:128]), A.min, A.min))
-        V(("tt", sb("M2", h, s_[1:128]), sb(K, s_[1:128]), sb("KS", h, s_[0:127]), A.max))
-        V(("scan", sb("KS", h, s_[128:256]), sb("CAPK", 1, al), sb("M2", h, al), A.min, A.min))
-        V(ts(sb("RR", h, s_[0:16]), sb("KS", h, s_[15::16]), C7, A.add, -C7, A.add))
-        V(*[("tt", sb("BA", h, s_[14 + v:142:16]), sb("KS", h, s_[128 * v + 15:128 * v + 128:16]), sb("RR", h, s_[8 * v:8 * v + 8]), A.subtract) for v in range(2)])
+        V(("scan", sb("KS", h, s_[1:137]), sb("CAPK", al), sb(K, s_[0:136]), A.min, A.min, BIG))
+        V(("scan", sb("KS", h, s_[137:273]), sb(K, s_[0:136]), sb("KS", h, s_[0:136]), A.min, A.max, BIG))
+        V(ts(sb("RR", h, s_[0:16]), sb("KS", h, s_[16::17]), C7, A.add, -C7, A.add))
+        V(*[("tt", sb("BA", h, s_[14 + v:142:16]), sb("KS", h, s_[136 * v + 16:136 * v + 137:17]), sb("RR", h, s_[8 * v:8 * v + 8]), A.subtract) for v in range(2)])
         PE(lists(Z, 256, 0, "BA", h))
         V(("copy", sb("OL", h, al), sb(Z, s_[256:272])))
-        move(OPT["rab"][h], sb("RAB", h, al), ind(sb("RG", h, al), sb("OL", h, al)))
+        move(OPT["rab"][h], (sb("RAB", h, al), ind(sb("RG", h, al), sb("OL", h, al)), 0.0, 1.0))
         for v in range(2):
-            V(ts(sb("OF", h, s_[128 * v:128 * v + 128]), column(h, v), 2048.0, A.add))
+            V(ts(sb("OF", h, part(v)), column(h, v), 2048.0, A.add))
         sec[0] = "far" + H
-        PE(P(sb(Z, s_[128:256]), [(sb("BA", h, s_[14:142]), IDB), (sb("BA", h, s_[12:140]), IDB)]))
-        S(act(sb("VTT", h, al), sb(Z, s_[128:256]), F.Square, col(13)))
-        s1 = [sb("S1", h, s_[128 * v:128 * v + 128]) for v in range(2)]
-        for v in range(2):
-            PE(P(qq[v], [(sb("QM", v, al), sb("VTT", h, al))], False, True))
-        for v in range(2):
-            V(ts(s1[v], qq[v], -4096.0, A.max))
-        S(act(sb("FS", h, al), sb(K, s_[128:256]), F.Copy))
-        PE(P(sb(K, s_[128:256]), [(sb("ID32", al), sb("FS", h, al))], True, False))
-        PE(P(sb(K, s_[128:256]), [(s1[v], sb("PEN16", al)) for v in range(2)], False, True))
-        V(("scan", sb("KF", h, s_[256:384]), sb("RSTN", al), sb(K, s_[128:256]), A.min, A.max))
-        V(("tt", sb("M2F", h, s_[1:128]), sb(K, s_[129:256]), sb("KF", h, s_[256:383]), A.min))
-        V(("scan", sb("KF", h, s_[384:512]), sb("RSTN", al), sb("M2F", h, al), A.min, A.max))
+        PE(P(sb(M, part(1)), [(sb("BA", h, s_[c:c + 128]), IDB) for c in (14, 12)]))
+        S(act(sb("VTT", h, al), sb(M, part(1)), F.Square, col(13)))
+        PE(*[P(sb(M, part(2 + v)), [(ID16, LP), (sb("QM", v, al), sb("VTT", h, al))]) for v in range(2)])
+        V(("tt", sb("S1", h, al), sb(M, s_[256:512]), sb("LOW", al), A.max))
+        far = sb(K, s_[136:272])
+        move("a", (sb("FS", h, al), far, 0.0, 1.0))
+        PE(P(far, [(sb("ID32", al), sb("FS", h, al))], True, False))
+        PE(P(far, [(sb("S1", h, part(v)), sb("PEN16", al)) for v in range(2)], False, True))
+        V(("scan", sb("KF", h, s_[257:393]), far, sb("NEG", al), A.max, A.max, -BIG))
+        V(("scan", sb("KF", h, s_[393:529]), far, sb("KF", h, s_[256:392]), A.max, A.min, -BIG))
         sec[0] = "fq" + H
-        V(ts(sb("RR", h, s_[32:48]), sb("KF", h, s_[271::16]), C7, A.add, -C7, A.add))
-        V(("tt", sb("VF", h, s_[13::16]), sb("KF", h, s_[271::16]), sb("RR", h, s_[32:48]), A.subtract))
-        PE(P(sb(K, s_[256:384]), [(sb("VF", h, s_[c:c + 128]), IDB) for c in (4, 0, 130, 126)]))
-        S(act(sb("VTF", h, al), sb(K, s_[256:384]), F.Square, col(13)))
-        PE(P(sb(K, s_[0:128]), [(sb("QM", 2, al), sb("VTF", h, al))], True, False))
+        V(ts(sb("RR", h, s_[32:48]), sb("KF", h, s_[272::17]), C7, A.add, -C7, A.add))
+        V(("tt", sb("VF", h, s_[13::16]), sb("KF", h, s_[272::17]), sb("RR", h, s_[32:48]), A.subtract))
+        PE(P(sb(K, part(3)), [(sb("VF", h, s_[c:c + 128]), IDB) for c in (4, 0, 130, 126)], True, not OPT["join"][h]))
+        if not OPT["join"][h]:
+            S(act(sb("VTF", h, al), sb(K, part(3)), F.Square, col(13)))
+            PE(P(sb(K, part(0)), [(sb("QM", 2, al), sb("VTF", h, al))], True, False))
         if OPT["prew"][h] == "early":
             writers(t, h)
 
     def writers(t, h):
-        M, s1 = "M" + str(h), sb("S1", h, s_[0:128])
+        M = "M" + str(h)
         sec[0] = "prew" + str(h)
-        bk, c0 = (M, 128) if OPT["prew"][h] == "early" else ("N" + str(h), 256)
-        PE(P(sb(M, s_[384:512]), [(s1, BOF16), (pt("ONEB", r0, s_[0:128]), pt("C16", r0, al))]))
-        V(("tt", sb("LD", h, al), sb(M, s_[384:512]), sb("DM", al), A.mult))
-        PE(P(sb(M, s_[0:8]), [(sb("LD", h, al), sb("BL16", s_[0::32]))]), P(sb(M, s_[384:512]), [(ID16, column(h, 0)), (IDB, sb("MT", 0, s_[16 - t:144 - t]))]))
-        PE(P(sb(bk, s_[c0:c0 + 256]), [(IDB, sb("MK", 0, al)), (sb("LD", h, al), sb("BL16", al))], True, False),
-           *[P(sb(bk, s_[c0 + 128 * u:c0 + 128 * u + 128]), [(BOF16, s1)], False, u == 1) for u in range(2)])
-        S(act(sb("AD", h, al), sb(bk, s_[c0:c0 + 256]), F.Abs, 61440.0 * 16384.0, 16384.0))
-        S(act(sb("LMS", h, al), sb(M, s_[0:8]), F.Identity, 2048.0 + 32.0 - 8192.0, -1.0))
-        V(("tt", sb("SV", h, al), sb("SVB", h, al), sb(M, s_[384:512]), A.max))
+        s1, LD, bk = sb("S1", h, part(0)), sb("LD", h, al), M if OPT["prew"][h] == "early" else "N" + str(h)
+        PE(P(sb(M, part(3)), [(s1, BOX)]))
+        V(("tt", LD, sb(M, part(3)), sb("DM", al), A.mult))
+        PE(P(sb(bk, s_[256:264]), [(IDB, sb("MK", al)), (LD, sb("BL16", s_[0::32]))]), P(sb(bk, part(3)), [(ID16, column(h, 0)), (IDB, sb("MT", 0, s_[16 - t:144 - t]))]))
+        PE(P(sb(M, s_[0:256]), [(LD, sb("BL16", al))], True, False), *[P(sb(M, part(u)), [(BOX, s1)], False, u == 1) for u in range(2)])
+        S(act(sb("AD", h, al), sb(M, s_[0:256]), F.Abs, 0.0, 16384.0))
+        S(act(sb("LMS", h, al), sb(bk, s_[256:264]), F.Identity, 2048.0 + 32.0 - 8192.0, -1.0))
+        V(("tt", sb("SV", h, al), sb("SVB", h, al), sb(bk, part(3)), A.max))
 
     def count(t):
         sec[0] = "cnt"
         v = sb("M1", s_[40:41])
         PE(P(v, [(pt("SC2", r0, al), pt("ONEB", r0, s_[0:1]))] + ([(sb("SN", al), sb("LV", 2 * t + 1, s_[256 + h:257 + h])) for h in range(2)] if t else [])))
         V(ts(sb("NR", s_[0:1]), v, C6, A.add, -C6, A.add))
-        V(ts(sb("THT", al), sb("TH0", al), v, A.add, sb("NR", s_[0:1]), A.subtract))
+        V(ts(sb("THT", al), sb("TH0", al), v, A.subtract, sb("NR", s_[0:1]), A.add))
 
     def second(t, h):
         H, li = str(h), 2 * t + h
@@ -347,66 +373,55 @@ def plan(TV=TV):
         LP = sb("LV", li, s_[0:128])
         lastv = t == TV - 1
         xe = [sb("XE", h, s_[v::2]) for v in range(2)]
+        fours = tuple(tuple(range(j, j + 4)) for j in range(0, 16, 4))
         sec[0] = "two" + H
-        PE(P(sb(Nb, s_[256:512]), [(ones33, pt("CK", s_[0:33], s_[256:512]))], True, False))
+        PE(P(sb(Nb, s_[256:512]), [(ones33, pt("CK", s_[0:33], s_[272:528]))], True, False))
         for v in range(2):
-            for e, a, b in OPT["xa"][2 * h + v]:
-                move(e, sb("XA", h, s_[2048 * v + 16 * a:2048 * v + 16 * b]), ind(XW, sb("OF", h, s_[128 * v + a:128 * v + b])))
-            xa = lambda j, a=0, b=128: sb("XA", h, s_[2048 * v + 16 * a + j:2048 * v + 16 * b:16])
-            my = lambda j, a=0, b=128: sb("MY", h, s_[2048 * v + 128 * j + a:2048 * v + 128 * j + b])
+            for e, a, b in pieces(OPT["xa"][2 * h + v]):
+                move(e, (sb("XA", h, s_[2048 * v + 16 * a:2048 * v + 16 * b]), ind(XW, sb("OF", h, s_[128 * v + a:128 * v + b])), 0.0, 1.0))
             key = lambda j: sb(Nb, s_[256 + 16 * v + j::32])
-            for j0 in range(0, 16, 4):
-                PE(*[P(key(j), [(xa(j), sb("BON", s_[0:8]))], False, False) for j in range(j0, j0 + 4)])
-            for a, b in OPT["my"][2 * h + v]:
-                for j0 in range(0, 16, 4):
-                    for j1 in range(j0, j0 + 4, OPT["gr"]):
-                        V(*[("tt", my(j, a, b), xa(j, a, b), sb(Z, s_[a:b]), A.max) for j in range(j1, j1 + OPT["gr"])])
-                    if b == 128:
-                        PE(*[P(key(j), [(my(j), sb("BOD", s_[0:8]))], False, v == 1 and j == 15) for j in range(j0, j0 + 4)])
+            for rows in fours:
+                PE(*[P(key(j), [(sb("XA", h, s_[2048 * v + j:2048 * v + 2048:16]), sb("BON", s_[0:8]))], False, False) for j in rows])
+            rowwise(h, "MY", "XA", 2048 * v, 0, A.max, OPT["my"][2 * h + v], fours, lambda j, x: P(key(j), [(x, sb("BOD", s_[0:8]))], False, v == 1 and j == 15))
         sec[0] = "new" + H
         PE(P(sb(Z, s_[256:512]), [(ID16, sb("RAB", h, al))], True, False))
         sec[0] = "end" + H
-        V(("scan", sb("KF", h, s_[0:256]), sb("RST", al), sb(Nb, s_[256:512]), A.max, A.min))
+        V(("scan", sb("KF", h, s_[0:256]), sb("RST", al), sb(Nb, s_[256:512]), A.max, A.min, BIG))
         V(ts(sb("RR", h, s_[16:32]), sb("KF", h, s_[15:256:16]), C7, A.add, -C7, A.add))
         V(*[("tt", sb("BE", h, s_[14 + v:142:16]), sb("KF", h, s_[15 + 16 * v:256:32]), sb("RR", h, s_[16 + v:32:2]), A.subtract) for v in range(2)])
         PE(lists(M, 16, 1, "BE", h))
         V(("copy", sb("OE", h, al), sb(M, s_[16:32])))
-        move(OPT["xe"][h], sb("XE", h, al), ind(sb("XA", h, al), sb("OE", h, al)), 0.0, 2.0)
+        move(OPT["xe"][h], (sb("XE", h, al), ind(sb("XA", h, al), sb("OE", h, al)), 0.0, 2.0))
         sec[0] = "new" + H
-        PE(P(sb(Nb, s_[0:128]), [(sb("BE", h, s_[c:c + 128]), IDB) for c in (14, 12)]))
-        S(act(sb("VTU", h, al), sb(Nb, s_[0:128]), F.Square, col(13)))
-        uu = [(sb("NBOU16", al), sb("THT", al))] + ([(sb("NBH16", al), x) for x in xe] if OPT["xd"][h] == "v" else []) + [(sb("BOU", al), sb("XD", h, al))]
-        PE(P(sb(M, s_[256:384]), uu[0:1], True, False))
+        join = OPT["join"][h]
+        places, VTF = sb(K, part(3)) if join else sb(Nb, part(0)), sb("VTU" if join else "VTF", h, al)
+        PE(P(places, [(sb("BE", h, s_[c:c + 128]), IDB) for c in (14, 12)], not join, True))
+        S(act(sb("VTU", h, al), places, F.Square, col(13)))
+        PE(P(sb(M, part(2)), [(sb("BOU", al), sb("THT", al))], True, False))
         PE(*[P(sb(Z, s_[256 + v::2]), [(sb("QM", v, al), sb("VTU", h, al))], False, v == 1) for v in range(2)])
-        V(ts(sb("S2", h, al), sb(Z, s_[256:512]), -4096.0, A.max))
-        PE(P(sb(K, s_[0:128]), [(BOF16, sb("S2", h, s_[0::2]))], False, True),
-           P(sb(K, s_[128:256]), [(sb("QM", 3, al), sb("VTF", h, al)), (BOF16, sb("S2", h, s_[1::2]))]))
-        PE(P(sb(Z, s_[0:128]), [(ID16, column(h, 1))], True, False))
+        V(("tt", sb("S2", h, al), sb(Z, s_[256:512]), sb("LOW", al), A.max))
+        if join:
+            PE(P(sb(K, part(0)), [(sb("QM", 2, al), VTF)], True, False))
+        PE(P(sb(K, part(0)), [(BOF16, sb("S2", h, s_[0::2]))], False, True), P(sb(K, part(1)), [(sb("QM", 3, al), VTF), (BOF16, sb("S2", h, s_[1::2]))]))
+        PE(P(sb(Z, part(0)), [(ID16, column(h, 1))], True, False))
         NL = sb("NL", h, al)
         for q in range(2):
-            V(("tt", NL, NL if q else LP, sb(K, s_[128 * q:128 * q + 128]), A.max))
+            V(("tt", NL, NL if q else LP, sb(K, part(q)), A.max))
         sec[0] = "end" + H
         if OPT["xd"][h] == "v":
             V(("tt", sb("XD", h, al), xe[0], xe[1], A.max))
-            PE(P(sb(M, s_[256:384]), uu[1:3], False, False))
+            PE(P(sb(M, part(2)), [(sb("NBH16", al), x) for x in xe], False, False))
         else:
-            PE(P(sb(Nb, s_[0:128]), [(ID16, xe[0]), (NID16, xe[1])]))
-            S(act(sb("XD", h, al), sb(Nb, s_[0:128]), F.Abs, 0.0, 0.5))
-        PE(P(sb(M, s_[256:384]), uu[-1:], False, True))
+            PE(P(sb(Nb, part(0)), [(ID16, xe[0]), (sb("NID16", al), xe[1])]))
+            S(act(sb("XD", h, al), sb(Nb, part(0)), F.Abs, 0.0, 0.5))
+        PE(P(sb(M, part(2)), [(sb("BOU", al), sb("XD", h, al))], False, True))
         sec[0] = "zz" + H
-        PE(P(sb(Nb, s_[128:256]), [(sb("HID16", al), xe[0]), (sb("HID16", al), xe[1])]))
-        zo = sb("YZ", rev[h]) if lastv else sb("SL", li, s_[128:256])
-        if OPT["z"][h] == "v":
-            V(ts(zo, sb(Nb, s_[128:256]), C0, A.add, -C0, A.add))
-        else:
-            S(act(sb("ZH", h, al), sb(Nb, s_[128:256]), F.Identity, C0))
-            S(act(zo, sb("ZH", h, al), F.Identity, -C0))
+        PE(P(sb(Nb, part(1)), [(sb("HID16", al), x) for x in xe]))
+        move(OPT["z"][h], (sb("SL", li, s_[128:256]), sb(Nb, part(1)), 1024.0, 1.0))
+        if lastv:
+            move(OPT["z"][h], (sb("YZ", rev[h]), sb("SL", li, s_[128:256]), -1024.0, 1.0))
         sec[0] = "new" + H
-        ub = sb(M, s_[256:384])
-        if OPT["ru"][h] == "n":
-            ub = sb(Nb, s_[256:384])
-            PE(P(ub, uu))
-        S(act(sb("SG", h, al), ub, F.Sign, col(7), 1.0, None if lastv else sb("CNT", s_[h:h + 1])))
+        S(act(sb("SG", h, al), sb(M, part(2)), F.Sign, col(7), 1.0, None if lastv else sb("CNT", s_[h:h + 1])))
         if h and not lastv:
             sec[0] = "sg" + H
             S(act(sb("SL", li, s_[256:258]), sb("CNT", al), F.Copy))
@@ -414,22 +429,22 @@ def plan(TV=TV):
             writers(t, h)
         sec[0] = "wr" + H
         for u in range(2):
-            V(("tt", sb("WT", h, s_[128 * u:128 * u + 128]), sb("AD", h, s_[128 * u:128 * u + 128]), sb(M, s_[256:384]), A.max))
-        V(("scan", sb("WS", h, al), sb("RS2", al), sb("WT", h, al), A.max, A.min))
+            V(("tt", sb("WT", h, part(u)), sb("AD", h, part(u)), sb(M, part(2)), A.max))
+        V(("scan", sb("WS", h, al), sb("RS2", 0, al), sb("WT", h, al), A.max, A.min, BIG))
         V(("tt", sb("WC", h, al), sb("WS", h, s_[31::32]), sb("LMS", h, al), A.add))
-        V(*[ts(sb("WO", h, s_[u::2]), sb("WC", h, s_[4 * u:4 * u + 4]), col(16 + u), A.max, col(18 + u), A.min) for u in range(2)])
+        V(*[ts(sb("WO", h, s_[u::2]), sb("WC", h, s_[4 * u:4 * u + 4]), col(16 * u), A.max, col(17 + 4 * u), A.min) for u in range(2)])
         for q in range(4):
             V(("copy", ind(sb("R", al), sb("WO", h, s_[2 * q:2 * q + 2])), sb("SV", h, s_[32 * q:32 * q + 32])))
         sec[0] = "new" + H
-        PE(P(sb(Z, s_[0:128]), [(sb("NIDB", al), sb("SG", h, al))], False, True))
-        V(("tt", sb(Z, s_[0:128]), NL, sb(Z, s_[0:128]), A.max))
-        V(ts(sb("NR2", h, al), sb(Z, s_[0:128]), C13, A.add, -C13, A.add))
+        PE(P(sb(Z, part(0)), [(sb("NIDB", al), sb("SG", h, al))], False, True))
+        V(("tt", sb(Z, part(0)), NL, sb(Z, part(0)), A.max))
+        V(ts(sb("NR2", h, al), sb(Z, part(0)), C13, A.add, -C13 - (2048.0 * 4 if False else 0.0), A.add))
         if not lastv:
-            V(("tt", sb("SL", li, s_[0:128]), sb(Z, s_[0:128]), sb("NR2", h, al), A.subtract))
-            op("g", [("send", None, sb("SL", li, wide[h]))], c=1200, send=(t, h), to=[(1, sb("LV", li + 2, wide[h]))], sem="ar%d%d" % (t + 1, h))
+            V(("tt", sb("SL", li, s_[0:128]), sb(Z, part(0)), sb("NR2", h, al), A.subtract))
+            op("g", [("send", None, sb("SL", li, wide[h]))], c=1200, send="ar%d%d" % (t + 1, h), to=[(1, sb("LV", li + 2, wide[h]))])
         else:
             V(ts(sb("NR2", h, al), sb("NR2", h, al), -2048.0, A.add))
-            V(("tt", sb("YL", rev[h]), sb(Z, s_[0:128]), sb("NR2", h, al), A.subtract))
+            V(("tt", sb("YL", rev[h]), sb(Z, part(0)), sb("NR2", h, al), A.subtract))
             half = s_[128 - 128 * h:256 - 128 * h]
             for nm, y in (("YL", "yl"), ("YZ", "yz")):
                 op("s", [("dma", (y, (al, half)), sb(nm, half))], c=2000, s=("do", 16))
@@ -439,17 +454,24 @@ def plan(TV=TV):
         if t:
             for h in range(2):
                 sec[0] = "arr"
-                op("x", [("land", sb("LV", 2 * t + h, wide[h]))], c=3000, s=("ar%d%d" % (t, h), 1), after=(t - 1, h))
+                op("x", [("land", sb("LV", 2 * t + h, wide[h]))], c=3000, s=("ar%d%d" % (t, h), 1), after="ar%d%d" % (t, h))
         first(t, 0)
         count(t)
         first(t, 1)
         second(t, 0)
         second(t, 1)
     sec[0] = "sum"
-    for b in range(8):
-        move(OPT["sum"][b], sb("R16", s_[512 * b:512 * b + 512]), sb("R", s_[32 + 512 * b:544 + 512 * b]), -2048.0)
-        PE(P(sb("K0", al), [(ID16, sb("R16", s_[512 * b:512 * b + 512]))], b == 0, b == 7))
-    V(ts(sb("YR", al), sb("K0", al), 16384.0, A.add))
+    n, block = OPT["sum"], lambda b: sb("R", s_[32 + 512 * b:544 + 512 * b])
+    fill("g", (pt("CZ", r0, s_[128:640]), 2048.0 * n))
+    PE(P(sb("K0", al), [(pt("ONEB", r0, part(0)), pt("CZ", r0, s_[128:640]))], True, False))
+    for b in range(n):
+        S(act(sb("R16", s_[512 * b:512 * b + 512]), block(b), F.Identity, -2048.0))
+        PE(P(sb("K0", al), [(ID16, sb("R16", s_[512 * b:512 * b + 512]))], False, b == n - 1))
+    sec[0] = "add"
+    V(("copy", sb("N0", al), block(n)))
+    for b in range(n + 1, 8):
+        V(("tt", sb("N0" if b < 7 else "ACC", al), sb("N0", al), block(b), A.add))
+    V(("tt", sb("YR", al), sb("K0", al), sb("ACC", al), A.add))
     op("s", [("dma", ("yr", s_[:, :]), sb("YR", al))], c=2000, s=("do", 16))
     return ops
 
@@ -485,7 +507,7 @@ def edges(ops):
             li.append([o["i"], bits, w])
         for b in set(x[0] for x in acc if x[0] in BANKS):
             d = bank.setdefault(b, [None, [], [], None])
-            if d[0] != o["e"]:
+            if d[0] != o["e"] or o["e"] == "f":
                 d[0], d[1], d[2] = o["e"], [], d[1]
             d[1].append(o["i"])
             pre.update(d[2])
@@ -504,7 +526,7 @@ def edges(ops):
 def chains(ops):
     last, pairs = {}, []
     for o in ops:
-        if o["e"] in "va" and o["calls"][0][1][0] in ("XG", "RG", "XA", "MX", "CE", "MY"):
+        if o["e"] in "vf" and o["calls"][0][1][0] in ("XG", "RG", "XA", "MX", "CE", "MY"):
             key = (o["t"], o["sec"], o["e"], o["calls"][0][1][0])
             if key in last:
                 pairs.append((last[key], o["i"]))
@@ -512,14 +534,18 @@ def chains(ops):
     return pairs
 
 
-def graph(ops, figures):
-    ga, sca, every, pec, wake, way = figures
-    c = [way if o["e"] == "x" else o["c"] if "c" in o else every * sum(cost(o["e"], x, ga, sca, pec) for x in o["calls"]) for o in ops]
+def times(ops, figures):
+    ga, sca, phi, pec, wake, way = figures
+    return [{-1: way if o["e"] == "x" else o["c"], 3: o["c"]} if "c" in o else
+            {"vapg".find(e): sum(cost(e, x, ga, sca, pec, phi) for x in calls) for e, calls in o.get("forms", {o["e"]: o["calls"]}).items()} for o in ops]
+
+
+def links(ops, wake):
     fore, back = [[] for _ in ops], [[] for _ in ops]
     for a, b, wait in ops[0]["arcs"]:
-        fore[a].append((b, c[a] + wait * wake if wait >= 0 else 0.0))
-        back[b].append((a, c[b] + wait * wake if wait >= 0 else 0.0))
-    return ["vapg".find(o["e"]) for o in ops], c, fore, back
+        fore[a].append((b, wait * wake if wait >= 0 else -1))
+        back[b].append((a, wait * wake if wait >= 0 else -1))
+    return fore, back
 
 
 def play(queue, c, out, into, rank):
@@ -560,57 +586,142 @@ def play(queue, c, out, into, rank):
             free[e], soon[e] = s + c[i], None
         st[i] = s
         seq.append(i)
-        end = s + c[i] if s + c[i] > end else end
+        b = s + c[i]
+        end = b if b > end else end
         for j, x in out[i]:
             left[j] -= 1
-            if s + x > at[j]:
-                at[j] = s + x
+            a = b + x if x >= 0 else s
+            if a > at[j]:
+                at[j] = a
             if not left[j]:
                 new.append(j)
 
 
-def replay(g, seq):
-    queue, c, out = g[0:3]
+def replay(queue, c, out, seq):
     at, free, end = [0.0] * len(c), [0.0] * 5, 0.0
     for i in seq:
-        s = at[i] if at[i] > free[queue[i]] else free[queue[i]]
-        free[queue[i]], free[4] = s + c[i], 0.0
-        end = s + c[i] if s + c[i] > end else end
+        e = queue[i]
+        s = at[i] if at[i] > free[e] else free[e]
+        b = s + c[i]
+        free[e], free[4] = b, 0.0
+        end = b if b > end else end
         for j, x in out[i]:
-            if s + x > at[j]:
-                at[j] = s + x
+            a = b + x if x >= 0 else s
+            if a > at[j]:
+                at[j] = a
     return end
 
 
-def search(ops, rank, rounds, heat, seed):
-    gs = [graph(ops, f) for f in FIGURES]
-    queue, c, fore, back = gs[0]
-    parts = {}
+def search(ops, rank, queue, rounds, heat, seed):
+    ts, ls = [times(ops, f) for f in FIGURES], [links(ops, f[4]) for f in FIGURES]
+    fore, back = ls[0]
+    parts, free = {}, {}
     for o in ops:
         parts.setdefault(o["sec"] + o["e"], []).append(o["i"])
-    parts = [parts[k] for k in sorted(parts)]
+        if len(o.get("forms", "")) > 1:
+            free.setdefault(o["k"], []).append(o["i"])
+    parts, free = [parts[k] for k in sorted(parts)], [free[k] for k in sorted(free)]
 
-    def value(rank, tight):
+    def value(rank, queue, cs, tight):
+        c = cs[0]
         st, end, seq = play(queue, c, fore, back, rank)
         if tight:
             bk = play(queue, c, back, fore, [-s - x for s, x in zip(st, c)])[0]
             s2, e2, q2 = play(queue, c, fore, back, [-s - x for s, x in zip(bk, c)])
             if e2 < end:
                 st, end, seq = s2, e2, q2
-        return end + sum(w * replay(g, seq) for w, g in zip(WEIGHTS, gs[1:])), st, seq
+        return end + sum(w * replay(queue, c, l[0], seq) for w, c, l in zip(WEIGHTS, cs[1:], ls[1:])), st, seq, queue, cs
     rnd = np.random.RandomState(seed)
-    steps, draws = rnd.standard_normal(3 * rounds).tolist(), rnd.random_sample(8 * rounds).tolist()
-    cur = best = value(rank, True)
+    steps, draws = rnd.standard_normal(3 * rounds).tolist(), rnd.random_sample(14 * rounds).tolist()
+    cur = best = value(rank, queue, [[x[e] for x, e in zip(t, queue)] for t in ts], True)
     for it in range(rounds):
-        r, rank = draws[8 * it:8 * it + 8], list(cur[1])
+        r, rank, queue, cs = draws[14 * it:14 * it + 14], list(cur[1]), cur[3], cur[4]
         for u in range(1 + int(3 * r[0])):
             for i in parts[int(r[1 + u] * len(parts))]:
                 rank[i] += steps[3 * it + u] * (400.0 if r[4] < 0.5 else 1600.0)
-        new = value(rank, r[5] < 0.5)
+        if r[7] < OPT["flip"]:
+            queue, cs = list(queue), [list(c) for c in cs]
+            for u in range(1 + int(2 * r[8])):
+                some = free[int(r[9 + u] * len(free))]
+                other = [e for e in ts[0][some[0]] if e != queue[some[0]]]
+                for i in some:
+                    queue[i] = other[int(r[11 + u] * len(other))]
+                    for c, t in zip(cs, ts):
+                        c[i] = t[i][queue[i]]
+        new = value(rank, queue, cs, r[5] < 0.5)
         if new[0] <= cur[0] - heat * 0.1 ** (it / rounds) * float(np.log(1.0 - r[6])):
             cur = new
             best = min(best, cur, key=lambda x: x[0])
     return best
+
+
+def polish(ops, seq, queue, cs, rounds, heat, seed):
+    ls = [links(ops, f[4]) for f in FIGURES]
+    n, need = len(ops), [len(x) for x in ls[0][1]]
+    same = {}
+    for o in ops:
+        same[o["t"], o["k"]] = o["i"]
+    lines = [[i for i in seq if queue[i] == e] for e in range(4)]
+
+    def run(lines, f):
+        nxt, left = [-1] * n, list(need)
+        for li in lines:
+            for a, b in zip(li, li[1:]):
+                nxt[a] = b
+                left[b] += 1
+        c, out, at, why, seq, end, last = cs[f], ls[f][0], [0.0] * n, [-1] * n, [i for i in range(n) if not left[i]], 0.0, 0
+        for i in seq:
+            s = at[i]
+            b = s + c[i]
+            if b > end:
+                end, last = b, i
+            for j, x in out[i]:
+                a = b + x if x >= 0 else s
+                if a > at[j]:
+                    at[j], why[j] = a, i
+                left[j] -= 1
+                if not left[j]:
+                    seq.append(j)
+            j = nxt[i]
+            if j >= 0:
+                if b > at[j]:
+                    at[j], why[j] = b, i
+                left[j] -= 1
+                if not left[j]:
+                    seq.append(j)
+        if len(seq) < n:
+            return None
+        pairs = []
+        while why[last] >= 0:
+            if nxt[why[last]] == last:
+                pairs.append((why[last], last))
+            last = why[last]
+        return seq, end, pairs
+
+    def value(lines, f):
+        r = run(lines, f)
+        return r and (sum(w * (r[1] if g == f else replay(queue, cs[g], ls[g][0], r[0])) for g, w in enumerate((1.0,) + WEIGHTS)), lines, r[0], r[2])
+    draws = np.random.RandomState(seed).random_sample(6 * rounds).tolist()
+    cur = best = value(lines, 0)
+    for it in range(rounds):
+        r = draws[6 * it:6 * it + 6]
+        a, b = cur[3][int(r[0] * len(cur[3]))]
+        e, far = queue[a], 1 + int(4 * r[3] * r[3])
+        li = list(cur[1][e])
+        for t in range(TV) if r[1] < 0.8 else (ops[a]["t"],):
+            i, j = same.get((t, ops[a]["k"])), same.get((t + ops[b]["t"] - ops[a]["t"], ops[b]["k"]))
+            if i is not None and j is not None:
+                p, q = li.index(i), li.index(j)
+                if 0 < q - p < 4:
+                    if r[4] < 0.5:
+                        li.insert(max(0, p - far + 1), li.pop(q))
+                    else:
+                        li.insert(q + far - 1, li.pop(p))
+        new = value(cur[1][:e] + [li] + cur[1][e + 1:], int(r[2] * len(FIGURES)))
+        if new and new[0] <= cur[0] - heat * 0.1 ** (it / rounds) * float(np.log(1.0 - r[5])):
+            cur = new
+            best = min(best, cur, key=lambda x: x[0])
+    return best[2]
 
 
 def prepared(visits):
@@ -633,11 +744,17 @@ def prepared(visits):
 
 def orders(rounds=ROUNDS, seed=SEED):
     short, ops = prepared(3), prepared(TV)
-    st = search(short, [o["t"] * PERIOD + RANK.get(o["sec"], {}).get(o["e"], 0) + o["i"] * 1e-6 for o in short], rounds[0], 500.0, seed)[1]
-    at = {(o["t"], o["k"]): st[o["i"]] for o in short}
+    rank = [o["t"] * PERIOD + RANK.get(o["sec"], {}).get(o.get("first", o["e"]), 0) + o["i"] * 1e-6 for o in short]
+    value, st, seq, queue, cs = search(short, rank, ["vapg".find(o.get("first", o["e"])) for o in short], rounds[0], 500.0, seed)
+    at, who = {(o["t"], o["k"]): st[o["i"]] for o in short}, {o["k"]: queue[o["i"]] for o in short}
     per = at[2, ("sel0", "v", 1)] - at[1, ("sel0", "v", 1)]
     rank = [at[0, o["k"]] if o["t"] == 0 else at[2, o["k"]] + (TV - 3) * per if o["t"] == TV - 1 else at[1, o["k"]] + (o["t"] - 1) * per for o in ops]
-    value, st, seq = search(ops, rank, rounds[1], 200.0, seed)
+    value, st, seq, queue, cs = search(ops, rank, [who[o["k"]] for o in ops], rounds[1], 200.0, seed)
+    seq = polish(ops, seq, queue, cs, rounds[2], 150.0, seed)
+    for o in ops:
+        if o["e"] == "f":
+            o.update(e="vapg"[queue[o["i"]]], calls=o["forms"]["vapg"[queue[o["i"]]]])
+            o["forms"] = {o["e"]: o["calls"]}
     order = {e: [o["i"] for o in ops if o["e"] == e] for e in "stx"}
     order.update({e: [i for i in seq if ops[i]["e"] == e] for e in "vapg"})
     return ops, order, st
@@ -660,7 +777,7 @@ def issue(g, q, T, c):
     if k == "memset":
         return q.memset(*a)
     if k == "scan":
-        return q.tensor_tensor_scan(a[0], a[1], a[2], BIG, a[3], a[4])
+        return q.tensor_tensor_scan(a[0], a[1], a[2], a[5], a[3], a[4])
     if k == "red":
         return q.tensor_reduce(a[0], a[1], AxisListType.X, a[2])
     if k == "act":
@@ -691,14 +808,17 @@ def rank_program(g, core, T, topo):
     count, total = {}, {e: 0 for e in "vapg"}
     for e, li in order.items():
         for i in li:
-            if "s" in ops[i]:
-                count[i] = (ops[i]["s"][0], ops[i]["s"][1] * (len(topo.engines(prv, core)) if e == "x" else 1))
+            if e == "x":
+                count[i] = (ops[i]["s"][0], len(topo.engines(prv, core)))
+            elif "s" in ops[i]:
+                count[i] = ops[i]["s"]
             elif "send" not in ops[i]:
                 total[e] += 1
                 count[i] = (SEMOF[e], total[e])
-    lists = {e: list(li) for e, li in order.items() if e != "t"}
+    lists = {e: list(li) for e, li in order.items() if e not in "tx"}
     lists["a"] = order["t"] + order["a"]
-    pos, known, clock, done, stores, sent = {e: 0 for e in lists}, {e: {} for e in lists}, {}, set(), 0, 0
+    pos, known, clock, done, stores, sent = {e: 0 for e in lists}, {e: {} for e in lists}, {}, set(order["x"]), 0, 0
+    clock.update({i: {count[i][0]: count[i][1]} for i in order["x"]})
     progress = True
     while progress:
         progress = False
@@ -709,9 +829,6 @@ def rank_program(g, core, T, topo):
                 pos[e] += 1
                 progress = True
                 done.add(i)
-                if e == "x":
-                    clock[i] = {count[i][0]: count[i][1]}
-                    continue
                 q, kn = queue[e], known[e]
                 for p in sorted(o["pre"], reverse=True):
                     if (ops[p]["e"] == "p" and e == "p") or "send" in ops[p]:
@@ -723,7 +840,7 @@ def rank_program(g, core, T, topo):
                             kn[k] = max(kn.get(k, 0), v)
                 if "send" in o:
                     src, dst, (rid, pid) = o["calls"][0][2], o["to"][0][1], topo.addr(nxt)[0:2]
-                    g.remote_dma(T[dst[0]][dst[1]], T[src[0]][src[1]], T.sem[o["sem"]], T.sem.ls, pid, rid, topo.mask(core, nxt))
+                    g.remote_dma(T[dst[0]][dst[1]], T[src[0]][src[1]], T.sem[o["send"]], T.sem.ls, pid, rid, topo.mask(core, nxt))
                     sent += len(topo.engines(core, nxt))
                     continue
                 for c in o["calls"]:

import numpy as np
from concourse.mybir import AluOpType as A, ActivationFunctionType as F, AxisListType

N, TV = 4, 5
CYC = 0.83
FIGURES = ((1.62, 3.8, 1.25, 0.7, 100.0, 3000.0), (1.12, 3.9, 1.35, 0.73, 70.0, 3000.0), (2.05, 4.5, 1.15, 0.71, 100.0, 3000.0), (1.25, 3.0, 1.1, 0.7, 120.0, 4000.0),
           (1.8, 4.0, 1.45, 0.9, 150.0, 4500.0))
WEIGHTS = (1.5, 0.35, 0.8, 0.35)
ROUNDS, SEED = (1000, 2000, 2500), 7
B16, H16, F32, I32, U16 = "bfloat16", "float16", "float32", "int32", "uint16"
SB = {
    "X": ([4096], B16), "R": ([4160], I32), "R16": ([4096], H16), "LI": ([256], I32), "ZI": ([256], B16), "THI": ([8], I32), "THB": ([8], I32),
    "LV": ([2 * TV, 264], H16), "SL": ([2 * TV, 264], H16), "ONEB": ([128], B16), "ZERO": ([136], B16), "CZ": ([640], B16), "ACC": ([512], F32), "IDB": ([128], B16), "NIDB": ([128], B16),
    "ID16": ([128], H16), "ID32": ([128], F32), "NID16": ([128], H16), "HID16": ([128], H16), "PEN16": ([136], H16), "BOF": ([128], B16), "BOX": ([128], H16),
    "BOF16": ([128], H16), "BOU": ([128], H16), "NBH16": ([128], H16), "BOD": ([16], B16), "BON": ([16], B16), "BOC": ([8], B16), "BO1": ([8], F32),
    "SEL0": ([128], H16), "RX": ([128], B16), "IK": ([128], F32), "PI": ([4], I32), "IM": ([144], I32), "MT": ([2, 144], B16), "IN": ([16], F32),
    "CO": ([24], F32), "CL": ([2, 16], B16), "CK": ([528], B16), "CAPK": ([136], F32), "IG": ([272], F32), "CNT": ([2], F32), "RST": ([256], B16), "NEG": ([136], B16),
    "AQ": ([512], B16), "BQ": ([128], B16), "QM": ([4, 128], B16), "RS2": ([2, 256], B16), "IJ": ([256], B16), "BL": ([256], B16), "BL16": ([256], H16), "MK": ([8], B16),
    "DM": ([128], B16), "LOW": ([256], B16), "TH": ([8], F32), "TH0": ([128], H16), "THT": ([128], H16), "SN": ([128], H16), "SC2": ([128], B16), "NR": ([2], F32),
    "YL": ([256], F32), "YZ": ([256], B16), "YR": ([512], F32),
}
for _n, (_s, _d) in {
    "LU": ([128], U16), "VTF": ([128], B16), "XG": ([2048], B16), "MX": ([2048], B16), "RG": ([2048], F32), "CE": ([2048], B16), "XA": ([4096], B16), "MY": ([4096], B16),
    "KS": ([273], F32), "KF": ([529], F32), "FS": ([136], F32), "RR": ([48], F32), "BA": ([144], B16), "BE": ([144], B16),
    "VF": ([264], B16), "VTT": ([128], B16), "VTU": ([128], B16), "OL": ([16], U16), "OE": ([16], U16), "RAB": ([256], H16),
    "XE": ([256], H16), "OF": ([256], U16), "NR2": ([128], F32), "S1": ([256], H16), "S2": ([256], H16), "LD": ([128], H16), "LMS": ([8], F32),
    "SV": ([128], F32), "SVB": ([128], F32), "NL": ([128], F32), "XD": ([128], H16), "SG": ([128], B16),
    "AD": ([256], B16), "WT": ([256], B16), "WS": ([256], B16), "WC": ([8], F32), "WO": ([8], U16),
}.items():
    SB[_n] = ([2] + _s, _d)
SCRATCH = {_n: ("sbuf", [128] + _s, _d) for _n, (_s, _d) in SB.items()}
BANKS = [_b + _h for _b in "ZKMN" for _h in "01"]
for _b in BANKS:
    SCRATCH[_b] = ("psum", [128, 512], F32)
SEMAPHORES = ["sv", "sa", "sp", "sg", "dz", "dl", "dt", "ls", "do", "dx0", "dx1", "dr0", "dr1", "dr2", "dr3"] + ["ar%d%d" % (t, h) for t in range(1, TV) for h in range(2)]
SEMOF = {"v": "sv", "a": "sa", "p": "sp", "g": "sg"}
HBM = ("xt", "z0", "ex", "l0", "th", "yl", "yz", "yr")
s_ = np.s_
C7, C6, C0 = 1.5 * 2.0 ** 30, 1.5 * 2.0 ** 29, 1.5 * 2.0 ** 23
C13 = 1.5 * 2.0 ** 36
BIG, TOP = 2.0 ** 30, 2.0 ** 23


def pieces(who):
    return tuple((e, 2 * (64 * q // len(who)), 2 * (64 * (q + 1) // len(who))) for q, e in enumerate(who))


OPT = {"xg": ["avaa", "aa"], "rg": ["vaa", "vaa"], "xa": ["av", "aa", "aaa", "aaa"], "mx": ["vv", "vv"], "ce": ["vv", "vv"], "my": ["vv"] * 4,
       "flip": 0.1, "join": [True, True],
       "rab": "aa", "xe": "aa", "xd": "av", "z": "aa", "prew": ["late", "early"], "sum": 4, "const": "vag"}
AHEAD, PERIOD = (250.0, 150.0, 100.0, 500.0), 26.0
RANK = {"init": dict(v=-30, g=-30, p=-30, a=-30), "mid": dict(v=1, g=-29, a=1), "sq": dict(v=4, p=-10, g=-28, a=4), "late": dict(v=5, p=-10, g=-27, a=5),
        "thr": dict(v=6, g=-26, a=6), "cnt": dict(p=7, v=7), "sum": dict(v=40, p=40, a=40, g=-40), "add": dict(v=40),
        "lu0": dict(v=-30), "prep0": dict(p=-2, a=-3, v=0), "svb0": dict(p=2, a=2), "conf0": dict(p=-2, a=-2, v=0.5), "sel0": dict(v=-5, p=-5, a=-5),
        "far0": dict(p=2, a=2, v=7.5), "fq0": dict(v=7.6, p=2, a=2), "two0": dict(p=3, a=3, v=8), "end0": dict(v=-3, p=-3, a=-3), "new0": dict(v=-2.9, p=-2.9, a=-2.9, g=0),
        "zz0": dict(p=-2.8, v=-2.8, a=-2.8), "prew0": dict(a=13, p=9, v=13), "wr0": dict(v=13),
        "lu1": dict(v=-30), "prep1": dict(p=4, a=1, v=6), "svb1": dict(p=5, a=5), "conf1": dict(v=6.5, p=4, a=1.5), "sel1": dict(v=-4, p=-4, a=-4),
        "far1": dict(a=11, p=11, v=13.5), "fq1": dict(v=13.5, p=11, a=13), "prew1": dict(a=14, p=12, v=14), "two1": dict(p=10, a=12, v=14),
        "end1": dict(v=5, p=5, a=5), "new1": dict(p=5.5, a=5.5, v=5.5, g=0), "zz1": dict(p=5.6, a=5.6, v=5.6), "sg1": dict(a=5.7), "wr1": dict(v=6)}


def sb(name, *idx):
    return (name, (slice(None),) + idx)


def pt(name, p, *idx):
    return (name, (p,) + idx)


def ind(win, off):
    return ("@", win, off)


def isap(x):
    return isinstance(x, tuple) and isinstance(x[0], str)


CELLS = {}


def cells(ap):
    key = (ap[0], str(ap[1]))
    if key not in CELLS:
        m = np.zeros(SCRATCH[ap[0]][1][1:], bool)
        m[ap[1][1:]] = True
        CELLS[key] = (int(m.sum()), int.from_bytes(np.packbits(m.reshape(-1)).tobytes(), "big"))
    return CELLS[key]


def two(ap):
    return SCRATCH[ap[0]][2] in (B16, H16, U16)


def cost(e, c, GA, SCA, PEC, PHI):
    k, out = c[0], c[1]
    if k == "mm":
        return max(min(64, cells(c[2])[0]), cells(c[3])[0]) * PEC * (1 if two(c[2]) else 4)
    if out[0] == "@":
        return 50 + max(40, 16 * cells(out[2])[0]) * SCA * CYC
    n = cells(out)[0]
    if e == "g":
        return (170 + 2 * n * CYC) * PHI
    if k != "memset" and c[2][0] == "@":
        return (70 if e == "a" else 50) + n * GA * CYC
    if e == "a":
        return (40 + max(64, n) * CYC) * PHI
    if k == "tt":
        f = 1 if c[2][0] in BANKS or c[3][0] in BANKS else 2
    elif k == "red":
        n, f = cells(c[2])[0], 1
    else:
        f = 0.5 if all(two(x) for x in ((out,) if k == "memset" else c[1:4] if k == "scan" else c[1:3])) else 1
    return (1 + max(64, n * f) * CYC) * (PHI if k in ("ts", "scan", "red") else 1.0)


def plan(TV=TV):
    ops, sec, vis = [], ["init"], [0]

    def op(e, calls, **kw):
        o = {"e": e, "calls": calls, "i": len(ops), "t": vis[0], "sec": sec[0]}
        o.update(kw)
        ops.append(o)

    def V(*calls):
        op("v", list(calls))

    def S(*calls):
        op("a", list(calls))

    def G(*calls):
        op("g", list(calls))

    def P(out, pairs, start=True, stop=True):
        return [("mm", out, l, r, start and j == 0, stop and j == len(pairs) - 1) for j, (l, r) in enumerate(pairs)]

    def PE(*groups):
        op("p", [c for gr in groups for c in gr])

    def ts(o, i, s1, o0, s2=None, o1=None):
        return ("ts", o, i, s1, s2, o0, o1)

    def act(o, i, f, bias=0.0, scale=1.0, acc=None):
        return ("act", o, i, f, bias, scale, acc)

    def either(first, forms):
        op("f", [c for e in forms for c in forms[e]], forms=forms, first=first if first in forms else "v")

    def move(e, *jobs):
        either(e, {"v": [ts(o, i, times, A.mult, add, A.add) if add or times != 1.0 else ("copy", o, i) for o, i, add, times in jobs],
                   "a": [act(o, i, F.Identity, add, times) if add or times != 1.0 else act(o, i, F.Copy) for o, i, add, times in jobs]})

    def fill(e, *jobs):
        forms = {"v": [("memset", o, x) for o, x in jobs]}
        if "g" in OPT["const"] and all(SCRATCH[o[0]][2] != H16 and not o[1][0].start for o, x in jobs):
            forms["g"] = [("iota", o, [[0, cells(o)[0]]], int(x), 0) for o, x in jobs]
        if all(cells(o)[0] <= 128 and sum(isinstance(x, slice) for x in o[1]) == 2 and SCRATCH[o[0]][2] != I32 for o, x in jobs):
            forms["a"] = [act(o, pt("ONEB", o[1][0], s_[0:cells(o)[0]]), F.Identity, 0.0, x) for o, x in jobs]
        either(e, forms)

    def col(j):
        return sb("CO", s_[j:j + 1])

    al = s_[:]
    part = lambda v: s_[128 * v:128 * v + 128]
    def load(q, sem, c, out, src):
        op(q, [("dma", out, src)], c=c, s=(sem, 16))
    load("s", "dl", 2500, sb("LI", al), ("l0", s_[:, :]))
    load("s", "dx0", 3500, sb("X", s_[0:2048]), ("xt", s_[:, 0:2048]))
    load("t", "dx1", 3500, sb("X", s_[2048:4096]), ("xt", s_[:, 2048:4096]))
    load("s", "dz", 4000, sb("ZI", al), ("z0", s_[:, :]))
    for q in range(4):
        load("s" if q % 2 else "t", "dr%d" % q, 6000 + 1500 * q, sb("R", s_[32 + 1024 * q:1056 + 1024 * q]), ("ex", s_[:, 1024 * q:1024 * q + 1024]))
    load("s", "dt", 9000, pt("THI", s_[0:1], al), ("th", s_[:, :]))

    ms = lambda o, x: ("memset", o, x)
    one, b8 = sb("ONEB", s_[0:128]), sb("BOF", s_[0::16])
    r0, r32, r64 = s_[0:1], s_[32:33], s_[64:65]
    V(ms(one, 1.0), ms(sb("ZERO", al), 0.0))
    rev = (s_[255:127:-1], s_[127::-1])
    for h in range(2):
        move("va"[h], (sb("LV", h, s_[0:128]), sb("LI", rev[h]), -2048.0, 1.0))
        move("v", (sb("LV", h, s_[128:256]), sb("ZI", rev[h]), 1024.0, 1.0))
    fill("a", (pt("CZ", r0, part(0)), -1024.0))

    def diagonal(e, nm, x):
        forms = {"v": [ts(sb(nm, al), sb("IDB", al), x, A.mult)], "a": [act(sb(nm, al), sb("IDB", al), F.Identity, 0.0, x)]}
        if "g" in OPT["const"]:
            forms["g"] = [("asel", sb(nm, al), sb("ZERO", part(0)), [[-1, 128]], A.not_equal, x, 0, 1)]
        either(e, forms)
    G(("iota", sb("PI", al), [[0, 4]], 0, 1))
    G(("asel", sb("IDB", al), one, [[-1, 128]], A.is_equal, 0.0, 0, 1))
    G(("asel", sb("BOF", al), one, [[-16, 8], [0, 16]], A.is_ge, 0.0, 0, 1))
    G(("asel", sb("BOF", al), sb("BOF", al), [[16, 8], [0, 16]], A.is_ge, 0.0, 15, -1))
    G(("asel", sb("SEL0", al), one, [[-16, 8], [0, 16]], A.is_equal, 0.0, 0, 1))
    G(("iota", pt("IG", s_[0:64], s_[0:136]), [[-6, 8], [0, 17]], 24, 0), ("iota", pt("IG", s_[0:64], s_[136:272]), [[13, 8], [0, 17]], -52, 0))
    G(*[("iota", pt("IG", s_[0:64], s_[c:c // 136 * 136 + 136:17]), [[x, 8]], base, 0) for c, x, base in ((0, -6, 29), (16, -6, 23), (136, 13, -60), (152, 13, -68))])
    G(("iota", sb("IK", al), [[0, 8], [1, 16]], 0, 0))
    diagonal("v", "ID16", 1.0)
    move("v", *[(sb(nm, s_[c:c + 8]), b8, 0.0, x) for nm, x in (("BON", -128.0), ("BOD", 256.0)) for c in (0, 8)])
    move("v", (sb("BOC", al), b8, 0.0, 2.0 ** 21))
    V(ms(pt("CK", s_[0:64], al), 0.0))
    G(("iota", pt("CK", r0, s_[0:136]), [[0, 8], [1, 17]], 0, 0), ("iota", pt("CK", r0, s_[136:272]), [[0, 8], [-1, 17]], 15, 0))
    fill("a", (pt("CK", r0, s_[0:136:17]), 2.0), (pt("CK", r0, s_[16:136:17]), 2.0))
    move("a", (pt("CK", r32, s_[0:272]), pt("IG", r32, al), 0.0, 2.0 ** 18))
    ones33 = pt("ONEB", s_[0:33], s_[0:128])
    PE(P(sb("M0", s_[0:136]), [(ones33, pt("CK", s_[0:33], s_[0:136]))]))
    move("v", (sb("CAPK", al), sb("M0", s_[0:136]), 2.0 ** 20, 1.0))
    fill("v", (sb("KS", al, 0), 29.0 * 2 ** 18 + 2.0))
    fill("g", (sb("R", s_[0:32]), 0), (sb("R", s_[4128:4160]), 0))
    sec[0] = "mid"
    V(ts(sb("PI", s_[0:1]), sb("PI", s_[0:1]), 15, A.bitwise_and), ts(sb("PI", s_[1:2]), sb("PI", s_[1:2]), 14, A.bitwise_and),
      ts(sb("PI", s_[2:3]), sb("PI", s_[2:3]), 1, A.bitwise_and))
    V(("copy", col(0), sb("PI", s_[0:1])), ts(col(4), sb("PI", s_[1:2]), 8.0, A.mult), ts(col(5), sb("PI", s_[2:3]), 2048.0, A.mult))
    G(("asel", sb("RX", al), one, [[-1, 8], [-8, 16]], A.is_equal, 0.0, 0, 1))
    G(("iota", sb("IN", al), [[128, 16]], 0, 0))
    V(ts(sb("CL", 0, al), sb("IN", al), col(4), A.add), ts(sb("CL", 1, al), sb("IN", al), col(4), A.add, col(5), A.add))
    fill("g", (sb("BA", al, al), 0.0))
    G(("iota", pt("CK", r0, s_[272:528]), [[0, 16], [1, 16]], 0, 0))
    sec[0] = "sq"
    fill("v", (pt("AQ", s_[0:96], al), 0.0))
    fill("a", (pt("BQ", s_[0:96], al), 0.0))
    q8, qf = 8192.0, -16384.0
    for r, job in ((r0, ((0, q8), (129, q8), (2, -q8), (131, -q8))), (r0, ((265, qf), (395, qf), (269, -qf), (399, -qf))), (r64, ((2, -q8), (131, -q8))),
                   (r64, ((265, -15 * qf), (395, -15 * qf), (269, 16 * qf), (399, 16 * qf)))):
        fill("a", *[(pt("AQ", r, s_[c:c // 128 * 128 + 128:16]), x) for c, x in job])
    for job in (((r0, 4, -q8), (r32, 4, -q8), (r32, 260, qf)), ((r0, 260, -31 * qf), (r64, 260, 240 * qf), (r64, 262, 61440.0 + q8))):
        fill("a", *[(pt("AQ", r, s_[c:c // 128 * 128 + 256:16]), x) for r, c, x in job])
    V(ts(col(13), col(0), 2.0, A.not_equal), ts(col(14), col(0), 3.0, A.not_equal), ts(col(15), col(0), 13.0, A.is_lt))
    V(ts(col(13), col(13), col(14), A.mult, col(15), A.mult))
    G(("iota", pt("BQ", r0, al), [[0, 8], [1, 16]], 0, 0))
    fill("a", (pt("BQ", r64, al), 1.0))
    S(act(pt("BQ", r32, al), pt("IK", r32, s_[0:128]), F.Square))
    PE(*[P(sb("M1", part(m)), [(pt("AQ", s_[0:96], part(m)), pt("BQ", s_[0:96], al))]) for m in range(4)])
    for m in range(4):
        V(("tt", sb("QM", m, al), sb("M1", part(m)), sb("BOF", al), A.mult))
    fill("g", (sb("LOW", al), -4096.0))
    sec[0] = "late"
    G(("iota", sb("IM", al), [[1, 144]], 1, 1))
    G(("asel", sb("PEN16", al), sb("ZERO", al), [[-16, 8], [-1, 17]], A.not_equal, -256.0, 0, 1))
    for nm, x in (("ID32", 1.0), ("NID16", -1.0), ("HID16", 0.25 - 2.0 ** -13), ("NIDB", -16384.0)):
        if nm != "NID16" or "a" in OPT["xd"]:
            diagonal("g", nm, x)
    for nm, x in (("BOF16", 1.0), ("NBH16", -16384.0), ("BOU", 32768.0)):
        move("v", (sb(nm, al), sb("BOF", al), 0.0, x))
    V(*[ts(col(1 + j), col(0), float(j), A.is_equal) for j in range(3)], ("copy", sb("BO1", al), b8), ts(col(18), col(0), 0.0, A.is_equal, -15.0, A.mult))
    V(ts(sb("DM", al), sb("IK", s_[0:128]), col(0), A.is_equal, -1.0, A.mult), ts(col(18), col(18), 1.0, A.add))
    V(ts(sb("BOX", al), sb("BOF", al), col(18), A.mult))
    move("v", *[(col(j), col(0), x, 1.0) for j, x in ((16, 16.0), (17, 4128.0), (21, 4144.0), (19, 1.0))], (col(7), col(1), 0.0, 2.0 ** 29))
    V(ts(col(20), col(0), 15.0, A.is_equal, -8192.0, A.mult))
    fill("g", (sb("RST", al), -TOP))
    fill("g", (sb("RST", s_[0::16]), TOP))
    V(ms(sb("NEG", al), -BIG), ms(sb("KF", al, 256), -BIG))
    V(ts(sb("IM", al), sb("IM", al), 15, A.bitwise_and))
    V(ts(sb("MT", 0, al), sb("IM", al), 0.0, A.is_equal, -8192.0, A.mult))
    move("v", (sb("MT", 1, al), sb("MT", 0, al), -6144.0, -1.0))
    move("v", (sb("MT", 0, al), sb("MT", 0, al), 2048.0, 1.0))
    for nm in ("BE", "VF"):
        fill("g", (sb(nm, al, al), 0.0))
    V(ms(sb("SL", s_[1::2], s_[258:264]), 0.0))
    G(("iota", sb("IJ", al), [[-16, 2], [0, 4], [1, 32]], 0, 0))
    for u in range(2):
        G(("asel", sb("BL", part(u)), one, [[-32, 4], [0, 32]], A.is_ge, 0.0, -16 * u, 1))
    G(("asel", sb("BL16", al), sb("BL", al), [[16, 2], [32, 4], [0, 32]], A.is_ge, 0.0, 15, -1))
    V(ms(sb("MK", s_[0:4]), 0.0), ts(sb("MK", s_[4:8]), sb("ONEB", s_[0:4]), col(20), A.mult))
    V(ts(sb("RS2", 0, al), sb("IJ", al), col(0), A.is_equal, BIG, A.mult), ts(sb("RS2", 1, al), sb("IJ", al), col(19), A.is_equal, 8192.0, A.mult))
    PE(P(sb("N1", s_[0:256]), [(sb("IDB", al), sb("RS2", u, al)) for u in range(2)]))
    move("a", (sb("RS2", 0, al), sb("N1", s_[0:256]), 0.0, 1.0))
    sec[0] = "thr"
    G(("pbc", sb("THB", al), pt("THI", s_[0:1], al), 128))
    V(("tt", sb("TH", al), sb("THB", al), sb("BO1", al), A.mult))
    V(("red", col(9), sb("TH", al), A.add))
    V(ts(col(10), col(9), C6, A.add, -C6, A.add))
    V(("tt", col(11), col(10), col(9), A.subtract), ts(col(12), col(10), -1.0, A.mult, col(1), A.mult))
    V(ts(col(11), col(11), 0.5, A.add, col(2), A.mult), ts(col(12), col(3), -31.5, A.mult, col(12), A.add))
    V(ts(sb("TH0", al), one, col(11), A.mult, col(12), A.add))
    fill("a", (sb("SN", al), 0.0), (pt("SC2", r0, al), 0.0))
    V(ts(sb("SN", s_[2::16]), sb("ONEB", s_[0:8]), col(2), A.mult, -0.5, A.mult), ms(pt("SC2", r0, s_[2::16]), -31.5))
    IDB, ID16, BOF16, BOX, SEL0 = sb("IDB", al), sb("ID16", al), sb("BOF16", al), sb("BOX", al), sb("SEL0", al)
    XW, RW = sb("X", al), sb("R", s_[32:4128])
    wide = (s_[0:256], al)
    groups = ((1, 2, 3), (4, 5, 6, 7), (8, 9, 10, 11), (12, 13, 14, 15))

    def column(h, v):
        return sb("RAB", h, s_[v::2])

    def lists(bank, c0, which, tile, h):
        return P(sb(bank, s_[c0:c0 + 16]), [(IDB, sb("CL", which, al))] + [(sb(tile, h, s_[14 - 2 * x:142 - 2 * x]), sb("RX", s_[16 * x:16 * x + 16])) for x in range(8)])

    def rowwise(h, out, src, c0, other, alu, cut, rows_in, sums):
        for e, a, b in pieces(cut):
            for rows in rows_in:
                for u in range(0, len(rows), 2):
                    V(*[("tt", sb(out, h, s_[c0 + 128 * k + a:c0 + 128 * k + b]), sb(src, h, s_[c0 + 16 * a + k:c0 + 16 * b:16]),
                         sb("Z" + str(h), s_[other + a:other + b]), alu) for k in rows[u:u + 2]])
                if b == 128:
                    PE(*[sums(k, sb(out, h, s_[c0 + 128 * k:c0 + 128 * k + 128])) for k in rows])

    def first(t, h):
        H, li = str(h), 2 * t + h
        Z, K, M = "Z" + H, "K" + H, "M" + H
        LP, ZP = sb("LV", li, s_[0:128]), sb("LV", li, s_[128:256])
        sec[0] = "lu" + H
        V(ts(sb("LU", h, al), LP, 2048.0, A.add))
        sec[0] = "prep" + H
        PE(P(sb(Z, part(0)), [(pt("ONEB", r0, part(0)), pt("CZ", r0, part(0))), (ID16, ZP)]), P(sb(Z, part(1)), [(SEL0, LP)]))
        sec[0] = "svb" + H
        PE(P(sb(M, part(1)), [(SEL0, LP), (IDB, sb("MT", 1, s_[16 - t:144 - t]))]))
        S(act(sb("SVB", h, al), sb(M, part(1)), F.Copy))
        sec[0] = "prep" + H
        for e, a, b in pieces(OPT["xg"][h]):
            move(e, (sb("XG", h, s_[16 * a:16 * b]), ind(XW, sb("LU", h, s_[a:b])), 0.0, 1.0))
        PE(P(sb(K, s_[0:272]), [(ones33, pt("CK", s_[0:33], s_[0:272]))], True, False))
        for rows in groups:
            PE(*[P(sb(K, s_[k:272:17]), [(sb("XG", h, s_[k::16]), sb("BON", al))], False, False) for k in rows])
        rowwise(h, "MX", "XG", 0, 0, A.max, OPT["mx"][h], groups, lambda k, x: P(sb(K, s_[k:272:17]), [(x, sb("BOD", al))], False, False))
        sec[0] = "conf" + H
        for e, a, b in pieces(OPT["rg"][h]):
            move(e, (sb("RG", h, s_[16 * a:16 * b]), ind(RW, sb("LU", h, s_[a:b])), -2048.0, 1.0))
        rowwise(h, "CE", "RG", 0, 128, A.is_equal, OPT["ce"][h], groups, lambda k, x: P(sb(K, s_[k:136:17]), [(x, sb("BOC", al))], False, k == 15))
        sec[0] = "sel" + H
        V(("scan", sb("KS", h, s_[1:137]), sb("CAPK", al), sb(K, s_[0:136]), A.min, A.min, BIG))
        V(("scan", sb("KS", h, s_[137:273]), sb(K, s_[0:136]), sb("KS", h, s_[0:136]), A.min, A.max, BIG))
        V(ts(sb("RR", h, s_[0:16]), sb("KS", h, s_[16::17]), C7, A.add, -C7, A.add))
        V(*[("tt", sb("BA", h, s_[14 + v:142:16]), sb("KS", h, s_[136 * v + 16:136 * v + 137:17]), sb("RR", h, s_[8 * v:8 * v + 8]), A.subtract) for v in range(2)])
        PE(lists(Z, 256, 0, "BA", h))
        V(("copy", sb("OL", h, al), sb(Z, s_[256:272])))
        move(OPT["rab"][h], (sb("RAB", h, al), ind(sb("RG", h, al), sb("OL", h, al)), 0.0, 1.0))
        for v in range(2):
            V(ts(sb("OF", h, part(v)), column(h, v), 2048.0, A.add))
        sec[0] = "far" + H
        PE(P(sb(M, part(1)), [(sb("BA", h, s_[c:c + 128]), IDB) for c in (14, 12)]))
        S(act(sb("VTT", h, al), sb(M, part(1)), F.Square, col(13)))
        PE(*[P(sb(M, part(2 + v)), [(ID16, LP), (sb("QM", v, al), sb("VTT", h, al))]) for v in range(2)])
        V(("tt", sb("S1", h, al), sb(M, s_[256:512]), sb("LOW", al), A.max))
        far = sb(K, s_[136:272])
        move("a", (sb("FS", h, al), far, 0.0, 1.0))
        PE(P(far, [(sb("ID32", al), sb("FS", h, al))], True, False))
        PE(P(far, [(sb("S1", h, part(v)), sb("PEN16", al)) for v in range(2)], False, True))
        V(("scan", sb("KF", h, s_[257:393]), far, sb("NEG", al), A.max, A.max, -BIG))
        V(("scan", sb("KF", h, s_[393:529]), far, sb("KF", h, s_[256:392]), A.max, A.min, -BIG))
        sec[0] = "fq" + H
        V(ts(sb("RR", h, s_[32:48]), sb("KF", h, s_[272::17]), C7, A.add, -C7, A.add))
        V(("tt", sb("VF", h, s_[13::16]), sb("KF", h, s_[272::17]), sb("RR", h, s_[32:48]), A.subtract))
        PE(P(sb(K, part(3)), [(sb("VF", h, s_[c:c + 128]), IDB) for c in (4, 0, 130, 126)], True, not OPT["join"][h]))
        if not OPT["join"][h]:
            S(act(sb("VTF", h, al), sb(K, part(3)), F.Square, col(13)))
            PE(P(sb(K, part(0)), [(sb("QM", 2, al), sb("VTF", h, al))], True, False))
        if OPT["prew"][h] == "early":
            writers(t, h)

    def writers(t, h):
        M = "M" + str(h)
        sec[0] = "prew" + str(h)
        s1, LD, bk = sb("S1", h, part(0)), sb("LD", h, al), M if OPT["prew"][h] == "early" else "N" + str(h)
        PE(P(sb(M, part(3)), [(s1, BOX)]))
        V(("tt", LD, sb(M, part(3)), sb("DM", al), A.mult))
        PE(P(sb(bk, s_[256:264]), [(IDB, sb("MK", al)), (LD, sb("BL16", s_[0::32]))]), P(sb(bk, part(3)), [(ID16, column(h, 0)), (IDB, sb("MT", 0, s_[16 - t:144 - t]))]))
        PE(P(sb(M, s_[0:256]), [(LD, sb("BL16", al))], True, False), *[P(sb(M, part(u)), [(BOX, s1)], False, u == 1) for u in range(2)])
        S(act(sb("AD", h, al), sb(M, s_[0:256]), F.Abs, 0.0, 16384.0))
        S(act(sb("LMS", h, al), sb(bk, s_[256:264]), F.Identity, 2048.0 + 32.0 - 8192.0, -1.0))
        V(("tt", sb("SV", h, al), sb("SVB", h, al), sb(bk, part(3)), A.max))

    def count(t):
        sec[0] = "cnt"
        v = sb("M1", s_[40:41])
        PE(P(v, [(pt("SC2", r0, al), pt("ONEB", r0, s_[0:1]))] + ([(sb("SN", al), sb("LV", 2 * t + 1, s_[256 + h:257 + h])) for h in range(2)] if t else [])))
        V(ts(sb("NR", s_[0:1]), v, C6, A.add, -C6, A.add))
        V(ts(sb("THT", al), sb("TH0", al), v, A.subtract, sb("NR", s_[0:1]), A.add))

    def second(t, h):
        H, li = str(h), 2 * t + h
        Z, K, M, Nb = "Z" + H, "K" + H, "M" + H, "N" + H
        LP = sb("LV", li, s_[0:128])
        lastv = t == TV - 1
        xe = [sb("XE", h, s_[v::2]) for v in range(2)]
        fours = tuple(tuple(range(j, j + 4)) for j in range(0, 16, 4))
        sec[0] = "two" + H
        PE(P(sb(Nb, s_[256:512]), [(ones33, pt("CK", s_[0:33], s_[272:528]))], True, False))
        for v in range(2):
            for e, a, b in pieces(OPT["xa"][2 * h + v]):
                move(e, (sb("XA", h, s_[2048 * v + 16 * a:2048 * v + 16 * b]), ind(XW, sb("OF", h, s_[128 * v + a:128 * v + b])), 0.0, 1.0))
            key = lambda j: sb(Nb, s_[256 + 16 * v + j::32])
            for rows in fours:
                PE(*[P(key(j), [(sb("XA", h, s_[2048 * v + j:2048 * v + 2048:16]), sb("BON", s_[0:8]))], False, False) for j in rows])
            rowwise(h, "MY", "XA", 2048 * v, 0, A.max, OPT["my"][2 * h + v], fours, lambda j, x: P(key(j), [(x, sb("BOD", s_[0:8]))], False, v == 1 and j == 15))
        sec[0] = "new" + H
        PE(P(sb(Z, s_[256:512]), [(ID16, sb("RAB", h, al))], True, False))
        sec[0] = "end" + H
        V(("scan", sb("KF", h, s_[0:256]), sb("RST", al), sb(Nb, s_[256:512]), A.max, A.min, BIG))
        V(ts(sb("RR", h, s_[16:32]), sb("KF", h, s_[15:256:16]), C7, A.add, -C7, A.add))
        V(*[("tt", sb("BE", h, s_[14 + v:142:16]), sb("KF", h, s_[15 + 16 * v:256:32]), sb("RR", h, s_[16 + v:32:2]), A.subtract) for v in range(2)])
        PE(lists(M, 16, 1, "BE", h))
        V(("copy", sb("OE", h, al), sb(M, s_[16:32])))
        move(OPT["xe"][h], (sb("XE", h, al), ind(sb("XA", h, al), sb("OE", h, al)), 0.0, 2.0))
        sec[0] = "new" + H
        join = OPT["join"][h]
        places, VTF = sb(K, part(3)) if join else sb(Nb, part(0)), sb("VTU" if join else "VTF", h, al)
        PE(P(places, [(sb("BE", h, s_[c:c + 128]), IDB) for c in (14, 12)], not join, True))
        S(act(sb("VTU", h, al), places, F.Square, col(13)))
        PE(P(sb(M, part(2)), [(sb("BOU", al), sb("THT", al))], True, False))
        PE(*[P(sb(Z, s_[256 + v::2]), [(sb("QM", v, al), sb("VTU", h, al))], False, v == 1) for v in range(2)])
        V(("tt", sb("S2", h, al), sb(Z, s_[256:512]), sb("LOW", al), A.max))
        if join:
            PE(P(sb(K, part(0)), [(sb("QM", 2, al), VTF)], True, False))
        PE(P(sb(K, part(0)), [(BOF16, sb("S2", h, s_[0::2]))], False, True), P(sb(K, part(1)), [(sb("QM", 3, al), VTF), (BOF16, sb("S2", h, s_[1::2]))]))
        PE(P(sb(Z, part(0)), [(ID16, column(h, 1))], True, False))
        NL = sb("NL", h, al)
        for q in range(2):
            V(("tt", NL, NL if q else LP, sb(K, part(q)), A.max))
        sec[0] = "end" + H
        if OPT["xd"][h] == "v":
            V(("tt", sb("XD", h, al), xe[0], xe[1], A.max))
            PE(P(sb(M, part(2)), [(sb("NBH16", al), x) for x in xe], False, False))
        else:
            PE(P(sb(Nb, part(0)), [(ID16, xe[0]), (sb("NID16", al), xe[1])]))
            S(act(sb("XD", h, al), sb(Nb, part(0)), F.Abs, 0.0, 0.5))
        PE(P(sb(M, part(2)), [(sb("BOU", al), sb("XD", h, al))], False, True))
        sec[0] = "zz" + H
        PE(P(sb(Nb, part(1)), [(sb("HID16", al), x) for x in xe]))
        move(OPT["z"][h], (sb("SL", li, s_[128:256]), sb(Nb, part(1)), 1024.0, 1.0))
        if lastv:
            move(OPT["z"][h], (sb("YZ", rev[h]), sb("SL", li, s_[128:256]), -1024.0, 1.0))
        sec[0] = "new" + H
        S(act(sb("SG", h, al), sb(M, part(2)), F.Sign, col(7), 1.0, None if lastv else sb("CNT", s_[h:h + 1])))
        if h and not lastv:
            sec[0] = "sg" + H
            S(act(sb("SL", li, s_[256:258]), sb("CNT", al), F.Copy))
        if OPT["prew"][h] == "late":
            writers(t, h)
        sec[0] = "wr" + H
        for u in range(2):
            V(("tt", sb("WT", h, part(u)), sb("AD", h, part(u)), sb(M, part(2)), A.max))
        V(("scan", sb("WS", h, al), sb("RS2", 0, al), sb("WT", h, al), A.max, A.min, BIG))
        V(("tt", sb("WC", h, al), sb("WS", h, s_[31::32]), sb("LMS", h, al), A.add))
        V(*[ts(sb("WO", h, s_[u::2]), sb("WC", h, s_[4 * u:4 * u + 4]), col(16 * u), A.max, col(17 + 4 * u), A.min) for u in range(2)])
        for q in range(4):
            V(("copy", ind(sb("R", al), sb("WO", h, s_[2 * q:2 * q + 2])), sb("SV", h, s_[32 * q:32 * q + 32])))
        sec[0] = "new" + H
        PE(P(sb(Z, part(0)), [(sb("NIDB", al), sb("SG", h, al))], False, True))
        V(("tt", sb(Z, part(0)), NL, sb(Z, part(0)), A.max))
        V(ts(sb("NR2", h, al), sb(Z, part(0)), C13, A.add, -C13 - (2048.0 * 4 if False else 0.0), A.add))
        if not lastv:
            V(("tt", sb("SL", li, s_[0:128]), sb(Z, part(0)), sb("NR2", h, al), A.subtract))
            op("g", [("send", None, sb("SL", li, wide[h]))], c=1200, send="ar%d%d" % (t + 1, h), to=[(1, sb("LV", li + 2, wide[h]))])
        else:
            V(ts(sb("NR2", h, al), sb("NR2", h, al), -2048.0, A.add))
            V(("tt", sb("YL", rev[h]), sb(Z, part(0)), sb("NR2", h, al), A.subtract))
            half = s_[128 - 128 * h:256 - 128 * h]
            for nm, y in (("YL", "yl"), ("YZ", "yz")):
                op("s", [("dma", (y, (al, half)), sb(nm, half))], c=2000, s=("do", 16))

    for t in range(TV):
        vis[0] = t
        if t:
            for h in range(2):
                sec[0] = "arr"
                op("x", [("land", sb("LV", 2 * t + h, wide[h]))], c=3000, s=("ar%d%d" % (t, h), 1), after="ar%d%d" % (t, h))
        first(t, 0)
        count(t)
        first(t, 1)
        second(t, 0)
        second(t, 1)
    sec[0] = "sum"
    n, block = OPT["sum"], lambda b: sb("R", s_[32 + 512 * b:544 + 512 * b])
    fill("g", (pt("CZ", r0, s_[128:640]), 2048.0 * n))
    PE(P(sb("K0", al), [(pt("ONEB", r0, part(0)), pt("CZ", r0, s_[128:640]))], True, False))
    for b in range(n):
        S(act(sb("R16", s_[512 * b:512 * b + 512]), block(b), F.Identity, -2048.0))
        PE(P(sb("K0", al), [(ID16, sb("R16", s_[512 * b:512 * b + 512]))], False, b == n - 1))
    sec[0] = "add"
    V(("copy", sb("N0", al), block(n)))
    for b in range(n + 1, 8):
        V(("tt", sb("N0" if b < 7 else "ACC", al), sb("N0", al), block(b), A.add))
    V(("tt", sb("YR", al), sb("K0", al), sb("ACC", al), A.add))
    op("s", [("dma", ("yr", s_[:, :]), sb("YR", al))], c=2000, s=("do", 16))
    return ops


def touches(c):
    if c[0] == "land":
        return [], [c[1]]
    rd, wr = [], []
    for j, x in enumerate(c[1:]):
        if not isap(x) or x[0] in HBM:
            continue
        w = j == 0 or (c[0] == "act" and j == 5)
        if x[0] == "@":
            rd.append(x[2])
            x = x[1]
        (wr if w else rd).append(x)
    return rd, wr


def edges(ops):
    hist, bank, sends = {}, {}, {}
    for o in ops:
        pre, acc = set(), []
        for c in o["calls"]:
            rd, wr = touches(c)
            acc += [(x[0], cells(x)[1], False) for x in rd] + [(x[0], cells(x)[1], True) for x in wr]
        for nm, bits, w in acc:
            pre.update(e[0] for e in hist.get(nm, ()) if e[1] & bits and (w or e[2]))
        for nm, bits, w in acc:
            li = hist.setdefault(nm, [])
            if w:
                hist[nm] = li = [[e[0], e[1] & ~bits, e[2]] for e in li if e[1] & ~bits]
            li.append([o["i"], bits, w])
        for b in set(x[0] for x in acc if x[0] in BANKS):
            d = bank.setdefault(b, [None, [], [], None])
            if d[0] != o["e"] or o["e"] == "f":
                d[0], d[1], d[2] = o["e"], [], d[1]
            d[1].append(o["i"])
            pre.update(d[2])
            if o["e"] == "p":
                if d[3] is not None:
                    pre.add(d[3])
                d[3] = o["i"]
        if "send" in o:
            sends[o["send"]] = o["i"]
        if "after" in o:
            pre = {sends[o["after"]]}
        pre.discard(o["i"])
        o["pre"] = sorted(pre)


def chains(ops):
    last, pairs = {}, []
    for o in ops:
        if o["e"] in "vf" and o["calls"][0][1][0] in ("XG", "RG", "XA", "MX", "CE", "MY"):
            key = (o["t"], o["sec"], o["e"], o["calls"][0][1][0])
            if key in last:
                pairs.append((last[key], o["i"]))
            last[key] = o["i"]
    return pairs


def times(ops, figures):
    ga, sca, phi, pec, wake, way = figures
    return [{-1: way if o["e"] == "x" else o["c"], 3: o["c"]} if "c" in o else
            {"vapg".find(e): sum(cost(e, x, ga, sca, pec, phi) for x in calls) for e, calls in o.get("forms", {o["e"]: o["calls"]}).items()} for o in ops]


def links(ops, wake):
    fore, back = [[] for _ in ops], [[] for _ in ops]
    for a, b, wait in ops[0]["arcs"]:
        fore[a].append((b, wait * wake if wait >= 0 else -1))
        back[b].append((a, wait * wake if wait >= 0 else -1))
    return fore, back


def play(queue, c, out, into, rank):
    left, at, st, seq, end = [len(x) for x in into], [0.0] * len(c), [0.0] * len(c), [], 0.0
    free, ready, soon, new = [0.0] * 4, [[], [], [], []], [None] * 4, [i for i in range(len(c)) if not into[i]]
    while True:
        i = new.pop() if new else -1
        if i >= 0 and queue[i] >= 0:
            ready[queue[i]].append(i)
            soon[queue[i]] = None
            continue
        if i >= 0:
            s = at[i]
        else:
            first = 1e18
            for q in range(4):
                if soon[q] is None:
                    f, a, b = free[q], 1e18, 1e18
                    for j in ready[q]:
                        s = at[j] if at[j] > f else f
                        a, b = (s if s < a else a), (s + c[j] if s + c[j] < b else b)
                    soon[q] = (a, b)
                if soon[q][1] < first:
                    first, e = soon[q][1], q
            if first == 1e18:
                return st, end, seq
            f, a, low = free[e], soon[e][0], 1e18
            for j in ready[e]:
                if at[j] <= a + AHEAD[e] and rank[j] < low:
                    i, low = j, rank[j]
            if at[i] > a:
                b, low = at[i] + 30, 1e18
                for j in ready[e]:
                    if rank[j] < low and (at[j] if at[j] > f else f) + c[j] <= b:
                        i, low = j, rank[j]
            ready[e].remove(i)
            s = at[i] if at[i] > f else f
            free[e], soon[e] = s + c[i], None
        st[i] = s
        seq.append(i)
        b = s + c[i]
        end = b if b > end else end
        for j, x in out[i]:
            left[j] -= 1
            a = b + x if x >= 0 else s
            if a > at[j]:
                at[j] = a
            if not left[j]:
                new.append(j)


def replay(queue, c, out, seq):
    at, free, end = [0.0] * len(c), [0.0] * 5, 0.0
    for i in seq:
        e = queue[i]
        s = at[i] if at[i] > free[e] else free[e]
        b = s + c[i]
        free[e], free[4] = b, 0.0
        end = b if b > end else end
        for j, x in out[i]:
            a = b + x if x >= 0 else s
            if a > at[j]:
                at[j] = a
    return end


def search(ops, rank, queue, rounds, heat, seed):
    ts, ls = [times(ops, f) for f in FIGURES], [links(ops, f[4]) for f in FIGURES]
    fore, back = ls[0]
    parts, free = {}, {}
    for o in ops:
        parts.setdefault(o["sec"] + o["e"], []).append(o["i"])
        if len(o.get("forms", "")) > 1:
            free.setdefault(o["k"], []).append(o["i"])
    parts, free = [parts[k] for k in sorted(parts)], [free[k] for k in sorted(free)]

    def value(rank, queue, cs, tight):
        c = cs[0]
        st, end, seq = play(queue, c, fore, back, rank)
        if tight:
            bk = play(queue, c, back, fore, [-s - x for s, x in zip(st, c)])[0]
            s2, e2, q2 = play(queue, c, fore, back, [-s - x for s, x in zip(bk, c)])
            if e2 < end:
                st, end, seq = s2, e2, q2
        return end + sum(w * replay(queue, c, l[0], seq) for w, c, l in zip(WEIGHTS, cs[1:], ls[1:])), st, seq, queue, cs
    rnd = np.random.RandomState(seed)
    steps, draws = rnd.standard_normal(3 * rounds).tolist(), rnd.random_sample(14 * rounds).tolist()
    cur = best = value(rank, queue, [[x[e] for x, e in zip(t, queue)] for t in ts], True)
    for it in range(rounds):
        r, rank, queue, cs = draws[14 * it:14 * it + 14], list(cur[1]), cur[3], cur[4]
        for u in range(1 + int(3 * r[0])):
            for i in parts[int(r[1 + u] * len(parts))]:
                rank[i] += steps[3 * it + u] * (400.0 if r[4] < 0.5 else 1600.0)
        if r[7] < OPT["flip"]:
            queue, cs = list(queue), [list(c) for c in cs]
            for u in range(1 + int(2 * r[8])):
                some = free[int(r[9 + u] * len(free))]
                other = [e for e in ts[0][some[0]] if e != queue[some[0]]]
                for i in some:
                    queue[i] = other[int(r[11 + u] * len(other))]
                    for c, t in zip(cs, ts):
                        c[i] = t[i][queue[i]]
        new = value(rank, queue, cs, r[5] < 0.5)
        if new[0] <= cur[0] - heat * 0.1 ** (it / rounds) * float(np.log(1.0 - r[6])):
            cur = new
            best = min(best, cur, key=lambda x: x[0])
    return best


def polish(ops, seq, queue, cs, rounds, heat, seed):
    ls = [links(ops, f[4]) for f in FIGURES]
    n, need = len(ops), [len(x) for x in ls[0][1]]
    same = {}
    for o in ops:
        same[o["t"], o["k"]] = o["i"]
    lines = [[i for i in seq if queue[i] == e] for e in range(4)]

    def run(lines, f):
        nxt, left = [-1] * n, list(need)
        for li in lines:
            for a, b in zip(li, li[1:]):
                nxt[a] = b
                left[b] += 1
        c, out, at, why, seq, end, last = cs[f], ls[f][0], [0.0] * n, [-1] * n, [i for i in range(n) if not left[i]], 0.0, 0
        for i in seq:
            s = at[i]
            b = s + c[i]
            if b > end:
                end, last = b, i
            for j, x in out[i]:
                a = b + x if x >= 0 else s
                if a > at[j]:
                    at[j], why[j] = a, i
                left[j] -= 1
                if not left[j]:
                    seq.append(j)
            j = nxt[i]
            if j >= 0:
                if b > at[j]:
                    at[j], why[j] = b, i
                left[j] -= 1
                if not left[j]:
                    seq.append(j)
        if len(seq) < n:
            return None
        pairs = []
        while why[last] >= 0:
            if nxt[why[last]] == last:
                pairs.append((why[last], last))
            last = why[last]
        return seq, end, pairs

    def value(lines, f):
        r = run(lines, f)
        return r and (sum(w * (r[1] if g == f else replay(queue, cs[g], ls[g][0], r[0])) for g, w in enumerate((1.0,) + WEIGHTS)), lines, r[0], r[2])
    draws = np.random.RandomState(seed).random_sample(6 * rounds).tolist()
    cur = best = value(lines, 0)
    for it in range(rounds):
        r = draws[6 * it:6 * it + 6]
        a, b = cur[3][int(r[0] * len(cur[3]))]
        e, far = queue[a], 1 + int(4 * r[3] * r[3])
        li = list(cur[1][e])
        for t in range(TV) if r[1] < 0.8 else (ops[a]["t"],):
            i, j = same.get((t, ops[a]["k"])), same.get((t + ops[b]["t"] - ops[a]["t"], ops[b]["k"]))
            if i is not None and j is not None:
                p, q = li.index(i), li.index(j)
                if 0 < q - p < 4:
                    if r[4] < 0.5:
                        li.insert(max(0, p - far + 1), li.pop(q))
                    else:
                        li.insert(q + far - 1, li.pop(p))
        new = value(cur[1][:e] + [li] + cur[1][e + 1:], int(r[2] * len(FIGURES)))
        if new and new[0] <= cur[0] - heat * 0.1 ** (it / rounds) * float(np.log(1.0 - r[5])):
            cur = new
            best = min(best, cur, key=lambda x: x[0])
    return best[2]


def prepared(visits):
    ops = plan(visits)
    edges(ops)
    reach, arcs, seen = [], [], {}
    for o in ops:
        r = 0
        for p in sorted(o["pre"], reverse=True):
            if not r >> p & 1:
                arcs.append((p, o["i"], 0 if ops[p]["e"] == "p" == o["e"] else 1))
                r |= reach[p] | 1 << p
        reach.append(r)
        k = (o["t"], o["sec"], o["e"])
        seen[k] = seen.get(k, 0) + 1
        o["k"] = k[1:] + (seen[k],)
    ops[0]["arcs"] = arcs + [(a, b, -1) for a, b in chains(ops)]
    return ops


def orders(rounds=ROUNDS, seed=SEED):
    short, ops = prepared(3), prepared(TV)
    rank = [o["t"] * PERIOD + RANK.get(o["sec"], {}).get(o.get("first", o["e"]), 0) + o["i"] * 1e-6 for o in short]
    value, st, seq, queue, cs = search(short, rank, ["vapg".find(o.get("first", o["e"])) for o in short], rounds[0], 500.0, seed)
    at, who = {(o["t"], o["k"]): st[o["i"]] for o in short}, {o["k"]: queue[o["i"]] for o in short}
    per = at[2, ("sel0", "v", 1)] - at[1, ("sel0", "v", 1)]
    rank = [at[0, o["k"]] if o["t"] == 0 else at[2, o["k"]] + (TV - 3) * per if o["t"] == TV - 1 else at[1, o["k"]] + (o["t"] - 1) * per for o in ops]
    value, st, seq, queue, cs = search(ops, rank, [who[o["k"]] for o in ops], rounds[1], 200.0, seed)
    seq = polish(ops, seq, queue, cs, rounds[2], 150.0, seed)
    for o in ops:
        if o["e"] == "f":
            o.update(e="vapg"[queue[o["i"]]], calls=o["forms"]["vapg"[queue[o["i"]]]])
            o["forms"] = {o["e"]: o["calls"]}
    order = {e: [o["i"] for o in ops if o["e"] == e] for e in "stx"}
    order.update({e: [i for i in seq if ops[i]["e"] == e] for e in "vapg"})
    return ops, order, st


def issue(g, q, T, c):
    def r(x):
        if not isap(x):
            return x
        return r(x[1]).indirect(r(x[2])) if x[0] == "@" else T[x[0]][x[1]]
    k, a = c[0], [r(x) for x in c[1:]]
    if k == "mm":
        return q.matmul(*a)
    if k == "tt":
        return q.tensor_tensor(*a)
    if k == "ts":
        return q.tensor_scalar(*a) if a[5] is not None else q.tensor_scalar(*a[0:5])
    if k == "copy":
        return q.tensor_copy(*a)
    if k == "memset":
        return q.memset(*a)
    if k == "scan":
        return q.tensor_tensor_scan(a[0], a[1], a[2], a[5], a[3], a[4])
    if k == "red":
        return q.tensor_reduce(a[0], a[1], AxisListType.X, a[2])
    if k == "act":
        if a[2] == F.Copy:
            return q.activation(a[0], a[1], a[2])
        return q.activation(a[0], a[1], a[2], bias=a[3], scale=a[4], accum_out=a[5])
    if k == "asel":
        return q.affine_select(*a)
    if k == "iota":
        return q.iota(*a) if SCRATCH[c[1][0]][2] == I32 else q.iota(*a, allow_small_or_imprecise_dtypes=True)
    if k == "pbc":
        return q.partition_broadcast(*a)
    return q.dma_start(*a)


PLAN = []


def rank_program(g, core, T, topo):
    rank = T.rank_of(core)
    if rank is None:
        return
    if not PLAN:
        PLAN.extend(orders()[0:2])
    ops, order = PLAN
    queue = {"v": g.vector, "a": g.scalar, "p": g.tensor, "g": g, "s": g.sync}
    nxt, prv = T.cores[(rank + 1) % N], T.cores[(rank - 1) % N]
    count, total = {}, {e: 0 for e in "vapg"}
    for e, li in order.items():
        for i in li:
            if e == "x":
                count[i] = (ops[i]["s"][0], len(topo.engines(prv, core)))
            elif "s" in ops[i]:
                count[i] = ops[i]["s"]
            elif "send" not in ops[i]:
                total[e] += 1
                count[i] = (SEMOF[e], total[e])
    lists = {e: list(li) for e, li in order.items() if e not in "tx"}
    lists["a"] = order["t"] + order["a"]
    pos, known, clock, done, stores, sent = {e: 0 for e in lists}, {e: {} for e in lists}, {}, set(order["x"]), 0, 0
    clock.update({i: {count[i][0]: count[i][1]} for i in order["x"]})
    progress = True
    while progress:
        progress = False
        for e in lists:
            while pos[e] < len(lists[e]) and all(p in done for p in ops[lists[e][pos[e]]]["pre"]):
                i = lists[e][pos[e]]
                o = ops[i]
                pos[e] += 1
                progress = True
                done.add(i)
                q, kn = queue[e], known[e]
                for p in sorted(o["pre"], reverse=True):
                    if (ops[p]["e"] == "p" and e == "p") or "send" in ops[p]:
                        continue
                    sem, val = count[p]
                    if kn.get(sem, 0) < val:
                        q.wait_ge(T.sem[sem], val)
                        for k, v in clock[p].items():
                            kn[k] = max(kn.get(k, 0), v)
                if "send" in o:
                    src, dst, (rid, pid) = o["calls"][0][2], o["to"][0][1], topo.addr(nxt)[0:2]
                    g.remote_dma(T[dst[0]][dst[1]], T[src[0]][src[1]], T.sem[o["send"]], T.sem.ls, pid, rid, topo.mask(core, nxt))
                    sent += len(topo.engines(core, nxt))
                    continue
                for c in o["calls"]:
                    last = issue(g, q, T, c)
                sem, val = count[i]
                last.then_inc(T.sem[sem], 16 if "s" in o else 1)
                stores += 16 * (sem == "do")
                clock[i] = dict(kn)
                clock[i][sem] = val
    g.wait_ge(T.sem.ls, sent)
    g.sync.wait_ge(T.sem["do"], stores)
    for e in "vapg":
        queue[e].wait_ge(T.sem[SEMOF[e]], total[e])
